import numpy as np, ml_dtypes
CORES = [3,11,19,27,35,43,51,59]
N = 8
BF = ml_dtypes.bfloat16
def gentries(a):
    return np.ascontiguousarray(a.reshape(8, 16, -1).transpose(0, 2, 1)).reshape(8, -1)
def gtable(e):
    e = np.asarray(e); return np.ascontiguousarray(e.reshape(8, -1, 16).transpose(0, 2, 1)).reshape(128, -1).astype(np.int32)
E, G, M, S, R = 2048, 128, 256, 3, 5
V, W = S * M, E + (N - 1) * G
def pick(rng, shape, lo, hi):
    return np.where(rng.random(shape) < 0.5, lo, hi)
def parts(rng):
    a = np.minimum((16 * (0.25 + 0.75 * rng.random((N, 8, 1, E))) * rng.random((N, 8, 16, E))).astype(np.int64), 15)
    hot = rng.integers(0, W, (N, 8, 128)); hot[..., :64] = rng.integers(0, V, (N, 8, 64))
    h = np.take_along_axis(hot, rng.integers(0, 128, (N, 8, V * 16)), 2).reshape(N, 8, V, 16)
    return {"a": a, "k": rng.integers(0, 8, (N, 8, 16, 2048)), "be": np.exp2(-10 + 3 * rng.random((N, 8, 16))),
            "ti": rng.integers(0, 1024, (N, 8, E)), "kd": rng.integers(0, 8, (N, 8, E)), "cl": rng.integers(0, 16, (N, 8, V)), "bg": rng.integers(0, 4096, (N, 8, V)), "us": rng.integers(0, 256, (N, 8, R * M)),
            "lp": np.where(rng.random((N, 8, E)) < 0.25, -1, rng.integers(0, W, (N, 8, E))),
            "ca": np.where(rng.random((N, 8, V, 16)) < 0.4, h, rng.integers(0, W, (N, 8, V, 16))),
            "snd": np.ascontiguousarray(np.argsort(rng.random((N, 8, N - 1, E)), axis=-1)[..., :G])}
def pack(p):
    d = {"a0": p["a"].reshape(N, 128, E).astype(np.float32).astype(BF), "k0": p["k"].reshape(N, 128, 2048).astype(np.float32).astype(BF), "be": p["be"].reshape(N, 128, 1).astype(np.float32)}
    for k in ("ti", "kd", "cl", "bg", "us", "lp"): d[k] = p[k].astype(np.int32)
    d["ca"] = np.stack([gtable(x.reshape(8, -1)) for x in p["ca"]]); d["snd"] = np.stack([gtable(x.reshape(8, -1)) for x in p["snd"]])
    return d
def setup_inputs(rng):
    return pack(parts(rng))
def setup_inputs_spread(rng):
    p = parts(rng)
    p["a"] = np.minimum((16 * np.exp2(-3 * rng.random((N, 8, 1, E))) * rng.random((N, 8, 16, E))).astype(np.int64), 15)
    p["k"] = np.minimum((8 * np.exp2(-2 * rng.random((N, 8, 1, 2048))) * rng.random((N, 8, 16, 2048))).astype(np.int64), 7)
    for k, n, e in (("ti", 1024, 3.0), ("bg", 4096, 4.0), ("us", 256, 0.5), ("cl", 16, 2.0), ("ca", W, 2.0)):
        p[k] = np.minimum((n * rng.random(p[k].shape) ** e).astype(np.int64), n - 1)
    p["lp"] = np.where(rng.random((N, 8, E)) < 0.5, -1, rng.integers(0, W, (N, 8, E)))
    r = int(rng.integers(0, N)); p["be"][r] = 2.0 ** -7
    p["ti"][r, :, :V] = rng.integers(0, 48, (8, V)); p["ti"][r, :, V:] = rng.integers(976, 1024, (8, E - V))
    tw = ghosts(p["ti"][:, :, None], p["snd"])[r, :, 0]
    for g in range(8):
        far = np.flatnonzero(tw[g] >= 976)
        p["ca"][r, g] = rng.choice(far, (V, 16)); p["lp"][r, g] = np.where(p["lp"][r, g] < 0, -1, rng.choice(far, E))
    return pack(p)
def setup_inputs_ends(rng):
    p = parts(rng)
    s = rng.random((N, 8, 1, E)); p["a"] = np.where(s < 0.25, 0, np.where(s < 0.5, 15, pick(rng, (N, 8, 16, E), 0, 15)))
    s = rng.random((N, 8, 1, 2048)); p["k"] = np.where(s < 0.25, 0, np.where(s < 0.5, 7, pick(rng, (N, 8, 16, 2048), 0, 7)))
    p["a"][:, ::2, :, 0] = 15; p["a"][..., 2] = 0; p["a"][..., E - 1] = 15
    for j in (0, 63, 1984, 2047): p["k"][..., j] = 7
    p["k"][..., 1991] = 0
    p["be"] = pick(rng, (N, 8, 16), 2.0 ** -10, 2.0 ** -7)
    for k, lo, hi in (("ti", 0, 1023), ("kd", 0, 7), ("us", 0, 255), ("lp", -1, W - 1)):
        p[k] = np.where(rng.random(p[k].shape) < 0.8, pick(rng, p[k].shape, lo, hi), p[k])
    p["cl"] = pick(rng, (N, 8, V), 0, 15); p["bg"] = pick(rng, (N, 8, V), 0, 4095)
    for j in (0, V - 1, E - 1): p["kd"][..., j] = 7
    p["ti"][..., 0] = 1023; p["ti"][..., V - 1] = 0; p["ti"][..., E - 1] = 1023
    p["bg"][..., V - 1] = 4095 * ((np.arange(N)[:, None] + np.arange(8)[None, :]) % 2)
    at = (rng.random((N, 8, V, 1)) < 0.45) | (rng.random((N, 8, V, 16)) < 0.4)
    p["ca"] = np.where(at, pick(rng, (N, 8, V, 16), 0, W - 1), rng.integers(0, W, (N, 8, V, 16)))
    p["ca"][:, :, 0] = W - 1; p["ca"][:, :, V - 1] = W - 1; p["ca"][:, :, 1] = 2
    both = np.concatenate([np.arange(G // 2), np.arange(E - (G - G // 2), E)])
    s = both[np.argsort(rng.random((N, 8, N - 1, G)), axis=-1)]; j = np.argmax(s == E - 1, axis=-1)[..., None]
    np.put_along_axis(s, j, s[..., -1:].copy(), -1); s[..., -1] = E - 1
    p["snd"] = s
    return pack(p)
def setup_inputs_corners(rng):
    p = parts(rng)
    for r in range(N):
        for g in range(8):
            x = (g + r) % 8
            for k, cap, n, kind in (("a", 15, E, x % 4), ("k", 7, 2048, (x // 2) % 4)):
                if kind == 0: p[k][r, g] = cap - rng.integers(0, 2, (16, n))
                elif kind == 1: p[k][r, g] = rng.integers(0, 2, (16, n))
                elif kind == 2: p[k][r, g] = np.broadcast_to(pick(rng, (1, n), 0, cap), (16, n))
    e = np.broadcast_to(np.arange(E), (N, 8, E)); o = rng.integers(0, 8, (N, 8, E))
    p["lp"] = np.choose(o, [np.full_like(e, -1), e, (e + 1) % E, np.zeros_like(e), np.full_like(e, E - 1), np.full_like(e, E), np.full_like(e, W - 1), p["lp"]])
    v = np.broadcast_to(np.arange(V)[:, None], (N, 8, V, 16)); o = rng.integers(0, 10, (N, 8, V, 16))
    for i, c in enumerate((0, V - 1, E - 1, E, W - 1)): p["ca"] = np.where(o == i, c, p["ca"])
    p["ca"] = np.where(o == 5, v, p["ca"])
    p["us"] = rng.choice(np.array([0, 1, 127, 128, 254, 255]), (N, 8, R * M)); p["bg"] = rng.choice(np.array([0, 0, 0, 1, 4094, 4095]), (N, 8, V))
    return pack(p)
def setup_inputs_crowd(rng):
    p = parts(rng); h = int(rng.integers(0, N)); x = rng.integers(V, E, 8); x[0] = E - 1; x[1] -= x[1] % 2; x[3] = 0
    tv = rng.integers(100, 900, 8); kv = rng.integers(0, 8, 8); cv = rng.integers(0, 16, 8)
    for g in range(8):
        p["a"][h, g, :, x[g]] = np.maximum(p["a"][h, g, :, x[g]], 1); p["a"][h, g, cv[g], x[g]] = 1
        for d in range(1, N):
            row = p["snd"][h, g, d - 1]; j = np.flatnonzero(row == x[g])
            if j.size: row[j[0]] = row[G - 1]
            row[G - 1] = x[g]
    for r in range(N):
        for g in range(8):
            w = g if r == h else (g - 1) % 8
            if w == 7: continue
            c = int(x[w]) if r == h else E + ((r - h) % N - 1) * G + G - 1
            p["ti"][r, g, :V] = tv[w]; p["kd"][r, g, :V] = kv[w]; p["bg"][r, g] = 0; p["k"][r, g] = np.maximum(p["k"][r, g], 1)
            if w % 2 == 0: p["cl"][r, g] = cv[w]
            if w == 6: p["ca"][r, g] = rng.choice(np.array([0, c, E, W - 1]), (V, 16)); continue
            p["ca"][r, g] = c
            if w >= 3:
                for s in range(S):
                    i = (0, M - 1, int(rng.integers(0, M)))[w - 3]; p["ca"][r, g, s * M + i] = rng.integers(0, W, 16)
    for g in range(7):
        if x[g] >= V: p["ti"][h, g, x[g]] = tv[g] + rng.integers(0, 65)
    p["cl"][h, 1, ::M] = cv[1]
    q = (h + 1) % N; i = np.arange(M); n = min(G, M); ev = p["snd"][h, 7, 0, :n]; o = V + i[n:]
    tc = 400 + 32 * (i >> 6) + rng.integers(0, 32, M); kc = (i >> 3) % 8
    p["ti"][q, 0, :V] = 400; p["kd"][q, 0, :V] = np.tile(i % 8, S); p["bg"][q, 0] = 0; p["k"][q, 0] = rng.integers(1, 3, (16, 2048))
    p["ca"][q, 0] = np.tile(np.where(i < n, E + i, V + i), S)[:, None]; p["lp"][q, 0, o] = -1
    for b, g, c, lo, hi in ((h, 7, ev, 0, n), (q, 0, o, n, M)):
        p["a"][b, g][:, c] = rng.integers(1, 3, (16, hi - lo)); p["ti"][b, g, c] = tc[lo:hi]; p["kd"][b, g, c] = kc[lo:hi]
    return pack(p)
def setup_inputs_calm(rng):
    p = parts(rng)
    for r in range(N):
        for g in range(8):
            kind = (g + r) % 4
            if kind == 0: p["a"][r, g] = (np.arange(16)[:, None] == rng.integers(0, 16, (1, E))) & (rng.random((1, E)) < 0.5)
            elif kind == 3: p["a"][r, g] = rng.integers(0, 4, (16, E))
            else: p["a"][r, g] = kind
            p["k"][r, g] = (1, 1, 0, 3)[kind]
            if kind == 2: p["k"][r, g] = rng.integers(0, 3, (16, 2048))
    p["ca"] = rng.integers(0, W, (N, 8, V, 16)); p["us"] = 16 * rng.integers(0, 16, (N, 8, R * M)); p["bg"] = rng.choice(np.array([0, 0, 0, 1, 16, 256]), (N, 8, V))
    r = int(rng.integers(0, N)); p["k"][r, (1 - r) % 4] = 0
    g = 4 + (2 - r) % 4; p["us"][r, g] = 255; p["bg"][r, g] = 4095
    return pack(p)
def check_ranges(d):
    bad = []
    for k, lo, hi in (("a0", 0, 15), ("k0", 0, 7), ("be", 2.0 ** -10, 2.0 ** -7), ("ti", 0, 1023), ("kd", 0, 7), ("cl", 0, 15), ("bg", 0, 4095), ("us", 0, 255), ("lp", -1, W - 1), ("ca", 0, W - 1), ("snd", 0, E - 1)):
        v = np.asarray(d[k]).astype(np.float64)
        if not np.all((v >= lo) & (v <= hi)): bad.append("range of " + k)
        elif k in ("a0", "k0") and np.any(v != np.floor(v)): bad.append("whole numbers of " + k)
    s = np.sort(np.stack([gentries(x) for x in np.asarray(d["snd"])]).reshape(N, 8, N - 1, G), axis=-1)
    if np.any(s[..., 1:] == s[..., :-1]): bad.append("repeated event in a block of snd")
    return bad
def ghosts(x, sl):
    out = []
    for r in range(N):
        w = [x[r]]
        for d in range(1, N):
            q = (r - d) % N
            w.append(np.roll(np.take_along_axis(x[q], sl[q, :, d - 1][:, None, :], 2), 1, axis=0))
        out.append(np.concatenate(w, axis=2))
    return np.stack(out)
def reference(a0, k0, be, ti, kd, cl, bg, us, lp, ca, snd):
    A = a0.astype(np.float32).astype(np.int64).reshape(N, 8, 16, E); K = k0.astype(np.float32).astype(np.int64).reshape(N, 8, 16, 2048)
    beta = be.astype(np.float64).reshape(N, 8, 16, 1); T, D, cls, B, U, L = [v.astype(np.int64) for v in (ti, kd, cl, bg, us, lp)]
    C = np.stack([gentries(x) for x in ca]).astype(np.int64); sl = np.stack([gentries(x) for x in snd]).astype(np.int64).reshape(N, 8, N - 1, G)
    TW = ghosts(T[:, :, None], sl)[:, :, 0]; DW = ghosts(D[:, :, None], sl)[:, :, 0]
    lam = []
    for t in range(R):
        lo = (t % S) * M; AW = ghosts(A, sl)
        c = C[:, :, 16 * lo:16 * (lo + M)]
        lag = np.abs(np.repeat(T[:, :, lo:lo + M], 16, axis=2) - np.take_along_axis(TW, c, 2))
        bn = 64 * (lag >> 5) + 8 * np.repeat(D[:, :, lo:lo + M], 16, axis=2) + np.take_along_axis(DW, c, 2)
        pr = np.take_along_axis(AW, c[:, :, None], 3) * np.take_along_axis(K, bn[:, :, None], 3)
        lam.append(np.add.reduce((np.exp(-beta * lag[:, :, None]) * pr).reshape(N, 8, 16, M, 16), axis=4))
        w = np.add.reduce(pr, axis=2).reshape(N, 8, M, 16); cum = np.add.accumulate(w, axis=3)
        hit = 256 * cum > (U[:, :, t * M:(t + 1) * M] * (B[:, :, lo:lo + M] + cum[..., 15]))[..., None]
        el = np.any(hit, axis=3); first = np.argmax(hit, axis=3)[..., None]
        cc = c.reshape(N, 8, M, 16); par = np.take_along_axis(cc, first, 3)[..., 0]; pb = np.take_along_axis(bn.reshape(N, 8, M, 16), first, 3)[..., 0]
        add = np.zeros_like(A)
        for r in range(N):
            for g in range(8):
                i = np.flatnonzero(el[r, g]); cg = cls[r, g, lo:lo + M]
                col, j = np.unique(par[r, g, i], return_index=True); z = cg[i[j]]; own = col < E
                np.add.at(add, (r, g, z[own], col[own]), 1)
                y = col[~own] - E; d = y // G + 1; q = (r - d) % N; h = (g - 1) % 8
                np.add.at(add, (q, h, z[~own], sl[q, h, d - 1, y % G]), 1)
                if t < R - 1:
                    b, j = np.unique(pb[r, g, i], return_index=True); z = cg[i[j]]
                    K[r, g, z, b] = np.minimum(K[r, g, z, b] + 1, 7)
        A = np.minimum(A + add, 15)
        if t < R - S:
            L[:, :, lo:lo + M] = np.where(el, par, L[:, :, lo:lo + M])
            up = np.where(el & (par < E), np.take_along_axis(L, np.minimum(par, E - 1), 2), -1)[..., None]
            least = np.argmin(w, axis=3)[..., None]
            C[:, :, 16 * lo:16 * (lo + M)] = np.where((np.arange(16) == least) & (up >= 0), up, cc).reshape(N, 8, 16 * M)
    return {"yl": np.concatenate(lam, axis=3).reshape(N, 128, R * M).astype(np.float32), "ya": A.reshape(N, 128, E).astype(np.float32)}

def check_inputs(d):
    bad = list(check_ranges(d))
    if not bad:
        for name, y in reference(**d).items():
            for q in range(N):
                v = np.abs(np.asarray(y[q], np.float64)); s = np.sqrt(np.mean(v * v))
                if v.max() > 9 * s or s < 2.0 ** -6: bad.append('%s of rank %d is uneven or too small' % (name, q))
    return bad

@@ -1,0 +1,686 @@
+from concourse.bass import DstId, RemoteDMATransfer
+from concourse.mybir import AluOpType, ActivationFunctionType
+
+N, E, GH, NG, R = 8, 2048, 128, 896, 5
+HOLE, GUN, DUMPB, GHO, DUMPA = 2048, 2064, 2960, 2976, 3872
+F32, BF, I32, U16, F16 = "float32", "bfloat16", "int32", "uint16", "float16"
+SB = {
+    "AW": (3872, BF), "INC": (3888, BF), "TW": (2944, BF), "KW": (2064, BF), "BUF": (3840, BF), "GN": (NG, BF), "GT": (NG, BF),
+    "X0": (NG, BF), "VV": (NG, BF), "GS": (NG, BF), "SL": (NG, BF), "HI": (NG, BF), "LO": (NG, BF), "YY": (1792, BF), "XB": (NG, BF),
+    "XX": (4096, BF), "KG": (4096, BF), "PR0_": (4096, BF), "PR1_": (4096, BF), "RG0": (4096, F32), "RG1": (4096, F32), "SC": (4096, F32), "RT": (2048, F32),
+    "LP": (2064, I32), "CA": (768, I32), "CAL": (768, U16), "SN": (56, I32), "SNL": (56, U16), "SI": (256, I32), "S2": (640, I32), "S3": (640, BF),
+    "QI": (1280, I32), "QF": (1280, F32), "JF": (656, F32), "FQ": (656, F32), "KI": (256, F32), "J16": (128, F32), "PI": (8, I32), "PC": (128, F32),
+    "F0": (144, BF), "FT": (144, BF), "FK": (144, BF), "FM": (144, BF), "FC": (144, BF), "I2": (256, BF), "RLT": (128, BF), "D11": (128, BF), "D12": (128, BF), "AG": (2048, BF), "I32F": (384, F32),
+    "GO": (128, F32), "GC": (128, F32), "SH": (2048, BF), "DG": (256, F32), "KF": (256, F32), "SEG": (256, F32), "BSEG": (256, F32),
+    "REP": (48, U16), "REP15": (16, U16), "LAML": (16, U16), "PERM": (48, U16), "SIX": (56, F32), "T48": (48, F32),
+    "UL": (80, F32), "BGL": (48, F32), "NTV": (48, F32), "KV": (48, F32), "TVR": (768, F32), "KVR": (768, F32), "OH": (768, BF),
+    "YU": (112, F32), "YT": (168, F32), "PRV": (56, U16), "LST": (56, U16), "MSN": (56, U16), "MAPL": (128, U16), "BE": (8, F32), "BT": (16, F32),
+    "LAG": (256, F32), "YI": (256, BF), "SS": (256, F32), "MT": (256, F32), "CT0": (256, F32), "CT1": (256, F32), "CL0": (256, U16), "CL1": (256, U16),
+    "ML": (256, U16), "BNL": (256, U16), "RL0": (256, U16), "RL1": (256, U16), "EL0": (16, U16), "EL1": (16, U16), "E150": (256, F32), "E151": (256, F32),
+    "CUM": (256, F32), "S1": (16, F32), "THR": (16, F32), "HIT": (256, F32), "PD": (256, F32), "PDK": (256, F32), "XS": (256, F16), "XK": (256, F16),
+    "LB": (256, F32), "LBK": (256, F32), "EE": (256, F32), "EEK": (256, F32), "OF": (256, F32), "OFK": (256, F32),
+    "L1": (32, U16), "L2": (32, U16), "L2C": (16, U16), "LK": (32, U16), "LKC": (16, U16), "NV": (256, BF), "NW": (256, BF), "NV2": (256, BF), "NW2": (256, BF),
+    "LAM": (256, F32), "KEY": (256, F32), "MN": (256, F32), "W1": (256, F32), "W2": (256, F32), "W3": (256, F32), "W4": (256, F32), "W5": (256, F32),
+    "W6": (256, F32), "SM": (64, F32), "IX": (16, U16),
+}
+PS = ["PW", "PD_", "PR0", "PR1", "PT", "PK", "PX", "PM"]
+POOL, _n = {}, 0
+for _k, (_c, _d) in SB.items():
+    if _d == U16:
+        POOL[_k] = _n
+        _n += (_c + 15) // 16 * 16
+SCRATCH = {k: ("sbuf", [128, n], d) for k, (n, d) in SB.items() if k not in POOL}
+SCRATCH["UP"] = ("sbuf", [128, _n], U16)
+for _k in PS:
+    SCRATCH[_k] = ("psum", [128, 512], F32)
+SEMAPHORES = ["ev", "ea", "et", "eg", "ls", "h0t", "h1", "h2"] + ["hh%d" % _k for _k in range(1, 2 * R + 1)] + ["d%d" % _k for _k in range(40)]
+SIZE = {F32: 4, I32: 4, BF: 2, U16: 2, F16: 2}
+A = AluOpType
+AF = ActivationFunctionType
+CYC, FIX, GATHER, SCATTER, PEC, SYNC, DMALAT, HOP = 1.04, 60.0, 1.56, 3.8, 0.55, 120.0, 2200.0, 7000.0
+LOOK, DEPTH, LEAD, LEAD0, SHORT, PASSES, MIX, ORDER = 0.8, 8, 2500.0, 2500.0, 250.0, 5, 0.6, {}
+
+
+PARTS = ((8, 16), (0, 8))
+HELP = True
+EXCHANGES = [("TW", E, 1, "h0t"), ("AW", GHO, 1, "h2")] + [("BUF", NG, -1, "h1"), ("AW", GHO, 1, "h2")] * (R - 1) + [("BUF", NG, -1, "h1")]
+
+
+def transfer(T, topo, core, peer, engines, sem, src, dst):
+    rid, pid, _ = topo.addr(peer)
+    mask = sum(1 << topo.engines(core, peer)[e] for e in engines)
+    return RemoteDMATransfer(dst_ids=[DstId(rid=rid, pnc=pid)], dma_engine_mask=mask, remote_sem=T.sem[sem], src=src, dst=dst)
+
+
+def helpers(T, topo, core):
+    return [c for c in topo.cores_of(core) if T.rank_of(c) is None and all(topo.may_write(c, x) for x in T.cores)][:3]
+
+
+def hand_on(g, core, T, topo):
+    boss = [c for c in topo.cores_of(core) if T.rank_of(c) is not None]
+    if not HELP or not boss or core not in helpers(T, topo, boss[0]):
+        return
+    rank, j = T.rank_of(boss[0]), helpers(T, topo, boss[0]).index(core)
+    for k in range(1, len(EXCHANGES)):
+        dst, d0, sign, sem = EXCHANGES[k]
+        g.wait_ge(T.sem["hh%d" % k], 4)
+        g.remote_dma_fused([transfer(T, topo, core, T.cores[(rank + sign * d) % N], range(4 * h, 4 * h + 4), sem,
+                                     T.XX[:, GH * (2 * k + h):GH * (2 * k + h + 1)], T[dst][:, d0 + GH * (d - 1):d0 + GH * d])
+                            for h, d in enumerate((2 * j + 1, 2 * j + 2))], local_sem=T.sem.ls)
+    g.wait_ge(T.sem.ls, 8 * (len(EXCHANGES) - 1))
+
+
+def rank_program(g, core, T, topo):
+    rank = T.rank_of(core)
+    if rank is None:
+        hand_on(g, core, T, topo)
+        return
+    Q = {"v": g.vector, "a": g.scalar, "t": g.tensor, "g": g, "s": g.sync}
+    ops, hist, ndma = [], {}, [0]
+
+    def v(name, c0=0, c1=None, step=1, p=None):
+        n, sz = (SB[name][0], SIZE[SB[name][1]]) if name in SB else (512, 4)
+        c1 = n if c1 is None else c1
+        rows = slice(None) if p is None else p
+        ten, b = (T.UP, POOL[name]) if name in POOL else (T[name], 0)
+        ap_ = ten[rows, b + c0:b + c1:step] if step != 1 else ten[rows, b + c0:b + c1]
+        return {"ap": ap_, "reg": [(name, (c0 * sz) // 16 * 16, (c1 * sz + 15) // 16 * 16)], "n": len(range(c0, c1, step)), "sz": sz, "ps": name in PS}
+
+    def ind(win, off):
+        return {"ap": win["ap"].indirect(off["ap"]), "reg": win["reg"], "off": off["reg"], "n": 16 * off["n"], "sz": win["sz"], "ps": False}
+
+    def regs(xs):
+        return [r for x in xs if isinstance(x, dict) for r in x["reg"] + x.get("off", [])]
+
+    def ap(x):
+        return x["ap"] if isinstance(x, dict) else x
+
+    def add(q, calls, rd, wr, cost, lat=0.0, kind="c", after=(), free=False):
+        me, deps = len(ops), set(after)
+        if not free:
+            for rs, w in ((rd, False), (wr, True)):
+                for name, lo, hi in rs:
+                    for (o, l2, h2, w2) in hist.get(name, []):
+                        if (name in PS and (ops[o]["q"] != q or q == "t")) or (l2 < hi and lo < h2 and (w or w2)):
+                            deps.add(o)
+        for name, lo, hi in wr:
+            keep = [r for r in hist.get(name, []) if kind == "d" or name in PS or not (lo <= r[1] and r[2] <= hi)]
+            hist[name] = keep + [(me, lo, hi, True)]
+        for name, lo, hi in rd:
+            hist.setdefault(name, []).append((me, lo, hi, False))
+        ops.append({"q": q, "calls": calls, "deps": deps, "cost": cost, "lat": lat, "kind": kind})
+        return me
+
+    def run(q, call, o, ins, per, after=()):
+        xs = [x for x in [o] + ins if isinstance(x, dict)]
+        if "off" in o:
+            per = SCATTER
+        elif any("off" in x for x in xs):
+            per = GATHER
+        elif per == 0.5 and any(x["sz"] == 4 and x["n"] > 1 for x in xs):
+            per = 1.0
+        return add(q, [call], regs(ins) + o.get("off", []), o["reg"], FIX + CYC * per * max(o["n"], 16), after=after)
+
+    def tt(o, a, b, op):
+        run("v", lambda: g.vector.tensor_tensor(ap(o), ap(a), ap(b), op), o, [a, b], 1.0 if a["ps"] or b["ps"] else 2.0)
+
+    def ts(o, a, s1, op0, s2=None, op1=None):
+        if op1 is None:
+            run("v", lambda: g.vector.tensor_scalar(ap(o), ap(a), ap(s1), None, op0), o, [a, s1], 0.5)
+        else:
+            run("v", lambda: g.vector.tensor_scalar(ap(o), ap(a), ap(s1), ap(s2), op0, op1), o, [a, s1, s2], 0.5)
+
+    def cp(o, a):
+        run("v", lambda: g.vector.tensor_copy(ap(o), ap(a)), o, [a], 0.5)
+
+    def scan(o, d0, d1, init, op0, op1):
+        run("v", lambda: g.vector.tensor_tensor_scan(ap(o), ap(d0), ap(d1), ap(init), op0, op1), o, [d0, d1, init], 0.5)
+
+    def fill(o, c):
+        run("v", lambda: g.vector.memset(ap(o), c), o, [], 0.5)
+
+    def act(o, a, f=AF.Copy, bias=None, scale=1.0):
+        if bias is None:
+            run("a", lambda: g.scalar.activation(ap(o), ap(a), f, scale=ap(scale)), o, [a, scale], 1.0)
+        else:
+            run("a", lambda: g.scalar.activation(ap(o), ap(a), f, bias=ap(bias), scale=ap(scale)), o, [a, bias, scale], 1.0)
+
+    def mm(items):
+        def one(x):
+            return lambda: g.tensor.matmul(ap(x[0]), ap(x[1]), ap(x[2]), x[3], x[4])
+        cost = sum(max(64, x[2]["n"]) * (4 if x[2]["sz"] == 4 else 1) * PEC for x in items)
+        add("t", [one(x) for x in items], regs([y for x in items for y in x[1:3]]), list(set(regs([x[0] for x in items]))), cost, 150.0)
+
+    def iota(o, pat, base, cm, small=True):
+        if small:
+            run("g", lambda: g.iota(ap(o), pat, base, cm, allow_small_or_imprecise_dtypes=True), o, [], 2.0)
+        else:
+            run("g", lambda: g.iota(ap(o), pat, base, cm), o, [], 2.0)
+
+    def sel(o, a, pat, op, fl, base, cm, after=()):
+        run("g", lambda: g.affine_select(ap(o), ap(a), pat, op, fl, base, cm), o, [a], 2.0, after)
+
+    def dma(q, pairs, other_rows=False):
+        def one(o, a):
+            return lambda: Q[q].dma_start(ap(o), ap(a))
+        rd, wr = regs([a for o, a in pairs]), list(set(regs([o for o, a in pairs])))
+        me = add(q, [one(o, a) for o, a in pairs], rd, wr, 150.0 * len(pairs), DMALAT, "d")
+        if other_rows:
+            ops[me]["deps"] = set(o for o in ops[me]["deps"] if ops[o]["kind"] != "d")
+        ops[me]["sem"] = "d%d" % ndma[0]
+        ndma[0] += 1
+        return me
+
+    last_send = []
+
+    def exchange(src, s0, dst, d0, sign, sem):
+        k = len(last_send)
+        assert EXCHANGES[k] == (dst, d0, sign, sem)
+        handed = HELP and k > 0
+
+        def block(d, engines):
+            return transfer(T, topo, core, T.cores[(rank + sign * d) % N], engines, sem, T[src][:, s0 + GH * (d - 1):s0 + GH * d], T[dst][:, d0 + GH * (d - 1):d0 + GH * d])
+
+        def call():
+            if handed:
+                g.remote_dma_fused([transfer(T, topo, core, h, range(4 * j + 4, 4 * j + 8), "hh%d" % k, T[src][:, s0 + 2 * GH * j:s0 + 2 * GH * (j + 1)], T.XX[:, 2 * GH * k:2 * GH * (k + 1)])
+                                    for j, h in enumerate(helpers(T, topo, core))], local_sem=T.sem.ls)
+                g.remote_dma_fused([block(N - 1, range(4))], local_sem=T.sem.ls)
+            else:
+                g.remote_dma_fused([block(d, [d - 1]) for d in range(1, N)], local_sem=T.sem.ls)
+        me = add("g", [call], v(src, s0, s0 + NG)["reg"], [], 300.0, HOP - 1000.0, "x", after=last_send[-1:])
+        last_send.append(me)
+        arr = add(None, [], [], v(dst, d0, d0 + NG)["reg"], 0.0, HOP, "r", free=True)
+        ops[arr]["sem"], ops[arr]["with"] = sem, me
+        ops[me]["n"], ops[arr]["n"] = (16, 4 * (N - 1)) if handed else (N - 1, N - 1)
+        return me
+
+    def col(j):
+        return v("PC", 4 * j, 4 * j + 1)
+
+    def win(name, a):
+        return v(name, 15 - a, 143 - a)
+
+    dma("s", [(v("SI", 0, 128), T.ti[:])])
+    dma("s", [(v("S2", 512, 640), T.kd[:])])
+    dma("s", [(v("SN"), T.snd[:])])
+    dma("a", [(v("AW", 0, E), T.a0[:])])
+    dma("a", [(v("CA"), T.ca[:])])
+    dma("s", [(v("BE", 0, 1), T.be[:])])
+    dma("a", [(v("KW", 0, E), T.k0[:])])
+    fill(v("TW", 0, E), 0.0)
+    fill(v("KW", E, E + 16), 0.0)
+    fill(v("AW", HOLE, GUN), 0.0)
+    fill(v("AW", DUMPB, GHO), 0.0)
+    iota(v("SI", 128, 256), [[1, 128]], 0, 128, False)
+    iota(v("PI", 0, 1), [[0, 1]], 0, 1, False)
+    iota(v("JF", 0, 144), [[1, 144]], 0, 0)
+    iota(v("JF", 144, 656), [[1, 512]], 144, 0)
+    iota(v("HI"), [[64, 14], [0, 64]], 0, 0)
+    iota(v("LO"), [[0, 14], [1, 64]], 0, 0)
+    iota(v("KI"), [[0, 16], [1, 16]], 0, 0)
+    iota(v("J16"), [[16, 8], [0, 16]], 0, 0)
+    iota(v("T48"), [[256, 3], [1, 16]], 0, 0)
+    for c0 in (128, 0):
+        ts(v("S2", c0, c0 + 128), v("SI", c0, c0 + 128), 0x7C0, A.bitwise_and)
+        ts(v("S2", c0 + 256, c0 + 384), v("SI", c0, c0 + 128), 63, A.bitwise_and)
+        cp(v("S3", c0, c0 + 128), v("S2", c0, c0 + 128))
+        cp(v("S3", c0 + 256, c0 + 384), v("S2", c0 + 256, c0 + 384))
+    cp(v("S3", 512, 640), v("S2", 512, 640))
+    rows = [dma(q, [(v("TW", 0, E, p=slice(row, 128, 16)), v("S3", c, c + 128))], True)
+            for q, row, c in (("s", 3, 128), ("a", 4, 384), ("s", 5, 128), ("a", 6, 384), ("s", 0, 0), ("a", 1, 256), ("s", 2, 512))]
+    small = dma("s", [(v("QI", 0, n, p=slice(8 * j, 8 * j + 8)), src[:, 0:n]) for j, (src, n) in enumerate(((T.us, 1280), (T.bg, 768), (T.cl, 768), (T.ti, 768), (T.kd, 768)))])
+    ops[small]["deps"].update(rows)
+    last = dma("s", [(v("LP", 0, E, p=slice(p, 128, 16)), T.lp[:]) for p in range(16)])
+    ops[last]["deps"].add(small)
+    cp(v("SNL"), v("SN"))
+    fill(col(26), 1.0)
+    fill(col(27), -1.0)
+    fill(col(28), 15.0)
+    fill(col(29), 160.0 - 15.5 / 32)
+    fill(col(30), -160.0)
+    ts(v("PI", 4, 5), v("PI", 0, 1), 15, A.bitwise_and)
+    cp(col(0), v("PI", 0, 1))
+    cp(col(1), v("PI", 4, 5))
+    tt(col(2), col(0), col(1), A.subtract)
+    ts(col(3), col(1), 3.0, A.is_equal)
+    ts(col(4), col(1), 4.0, A.is_equal)
+    ts(col(5), col(1), 5.0, A.is_equal)
+    ts(col(6), col(1), 6.0, A.is_equal)
+    tt(col(7), col(3), col(5), A.add)
+    tt(col(8), col(4), col(6), A.add)
+    ts(col(9), col(3), float(GHO - E), A.mult)
+    ts(col(10), col(7), float(E), A.mult, col(9), A.add)
+    tt(col(11), col(3), col(4), A.add)
+    ts(col(12), col(11), -1.0, A.mult, 1.0, A.add)
+    ts(col(13), col(3), float(GUN - GHO), A.mult)
+    ts(col(14), col(1), 2.5, A.is_lt)
+    ts(v("I2", 0, 128), v("JF", 0, 128), col(0), A.is_equal)
+    act(v("I2", 128, 256), v("I2", 0, 128))
+    act(v("RLT"), v("I2", 112, 240), scale=col(14))
+    ts(v("GS"), v("HI"), col(7), A.mult, col(10), A.add)
+    ts(v("SL"), v("LO"), col(8), A.mult)
+    act(v("D11"), v("I2", 0, 128), scale=col(11))
+    act(v("D12"), v("I2", 0, 128), scale=col(12))
+    ident, roll, unroll = v("I2", 0, 128), v("I2", 112, 240), v("I2", 16, 144)
+    pos32, roll32, neg32 = v("I32F", 0, 128), v("I32F", 112, 240), v("I32F", 256, 384)
+
+    def through(dst, d0, terms, bias=None, banks=("PR0", "PR1"), both=False):
+        for h, bank in enumerate(banks):
+            c = 448 * h
+            for j, (lhs, src, s0) in enumerate(terms):
+                mm([(v(bank, 0, 448), lhs, v(src, s0 + c, s0 + c + 448), j == 0, j == len(terms) - 1)])
+        for h, bank in enumerate(banks):
+            o = v(dst, d0 + 448 * h, d0 + 448 * h + 448)
+            if bias is not None:
+                ts(o, v(bank, 0, 448), bias, A.add)
+            else:
+                (cp if both and h else act)(o, v(bank, 0, 448))
+
+    cp(v("X0"), ind(v("TW", 0, E), v("SNL")))
+    through("GT", 0, [(ident, "GS", 0), (ident, "SL", 0), (v("RLT"), "X0", 0)], both=True)
+    exchange("GT", 0, "TW", E, 1, "h0t")
+    through("VV", 0, [(v("D11"), "GS", 0), (v("D11"), "SL", 0), (v("D12"), "X0", 0)], col(13), ("PT", "PK"))
+    act(v("AW", GUN, GUN + NG), ind(v("AW", 0, E), v("SNL")))
+    through("GN", 0, [(roll, "AW", GUN)])
+    sent = exchange("GN", 0, "AW", GHO, 1, "h2")
+    act(v("YY", 0, GH), v("X0", 0, GH))
+    for d in range(7):
+        lst = v("SNL", 8 * d, 8 * d + 8)
+        if d:
+            act(v("YY", GH * d, GH * d + GH), ind(v("TW", 0, E), lst))
+        cp(ind(v("TW", 0, E), lst), v("VV", GH * d, GH * d + GH))
+    act(v("YY", NG, 2 * NG), ind(v("TW", 0, E), v("SNL")))
+    ts(col(15), col(2), 15.0, A.add)
+    ts(v("F0"), v("JF", 0, 144), col(15), A.is_equal)
+    ts(col(16), col(1), 1.5, A.is_lt)
+    ts(col(17), col(1), 2.0, A.is_equal, 1.0 / 64, A.mult)
+    tt(col(18), col(5), col(6), A.add)
+    act(v("FT"), v("F0"), scale=col(16))
+    act(v("FK"), v("F0"), scale=col(17))
+    act(v("FM"), v("F0"), scale=col(11))
+    act(v("FC"), v("F0"), scale=col(18))
+    ts(col(19), col(0), 16.0, A.mult, 15.0, A.add)
+    p40, p24 = slice(0, 40), slice(0, 24)
+    ts(v("FQ", p=p40), v("JF", p=p40), v("PC", 76, 77, p=p40), A.is_equal)
+    cp(v("QF", 0, 768, p=p40), v("QI", 0, 768, p=p40))
+    cp(v("QF", 768, 1280, p=slice(0, 8)), v("QI", 768, 1280, p=slice(0, 8)))
+    act(v("I32F", 0, 256), v("I2"))
+    act(neg32, ident, scale=-1.0)
+    cp(v("REP"), v("JF", 0, 48))
+    ts(col(20), col(1), 16.0, A.mult)
+    ts(v("PERM"), v("T48"), col(20), A.add)
+    for s in range(3):
+        cp(v("CAL", 256 * s, 256 * s + 256), ind(v("CA"), v("PERM", 16 * s, 16 * s + 16)))
+
+    def lists(j, n, o):
+        ps = slice(0, 8 * j + 8)
+        mm([(o, v("FQ", 128 * j + 15 - a, 128 * j + 143 - a, p=ps), v("QF", a, 16 * n, 16, p=ps), a == 0, a == 15) for a in range(16)])
+
+    lists(3, 48, v("PX", 0, 48))
+    lists(4, 48, v("PX", 48, 96))
+    act(v("NTV"), v("PX", 0, 48), scale=-1.0)
+    act(v("KV"), v("PX", 48, 96), AF.Identity, bias=col(30), scale=0.125)
+    for s in range(3):
+        act(v("TVR", 256 * s, 256 * s + 256), ind(v("NTV"), v("REP", 16 * s, 16 * s + 16)))
+        act(v("KVR", 256 * s, 256 * s + 256), ind(v("KV"), v("REP", 16 * s, 16 * s + 16)))
+    sha = v("AG", 0, 1920)
+    act(sha, v("KW", 0, 1920), AF.Identity, bias=col(26), scale=0.0)
+    fill(v("SH", 0, 128), 0.0)
+    sel(v("SH", 128, 2048), sha, [[-1, 15], [0, 8], [1, 16]], A.is_ge, 0.0, -1, 0, [sent])
+    sel(sha, v("SH", 128, 2048), [[1, 15], [-1, 128]], A.is_equal, 0.0, 1, 1)
+    sel(v("SH", 128, 2048), sha, [[0, 15], [-1, 128]], A.not_equal, -1.0, 0, 1)
+
+    def tk_gather(t, chunks, eng):
+        lst = ("CAL", 256 * t) if t < 3 else ("CL%d" % (t - 3), 0)
+        for c in chunks:
+            src = ind(v("TW"), v(lst[0], lst[1] + 64 * c, lst[1] + 64 * c + 64))
+            (cp if eng == "v" else act)(v("XX", 1024 * c, 1024 * c + 1024), src)
+
+    def diff(bank, c0, src):
+        o = v(bank, c0, c0 + 255)
+        mm([(o, pos32, v(src, 0, 255), True, False), (o, neg32, v(src, 1, 256), False, True)])
+
+    def prep(t):
+        s = t % 3
+
+        def extract(bank, c0, f, pre):
+            o = v(bank, c0, c0 + 256)
+            if pre:
+                mm([(o, pos32, v(pre, 256 * s, 256 * s + 256), True, False)])
+            for q4 in (0, 2, 1, 3):
+                mm([(o, win(f, a), v("XX", 256 * a, 256 * a + 256) if t < 3 else v("XX", a, 4096, 16), a == 0 and not pre, a == 15 and f != "FK") for a in range(4 * q4, 4 * q4 + 4)])
+
+        extract("PT", 0, "FT", "TVR")
+        extract("PK", 0, "FK", "KVR")
+        extract("PM", 0, "FM", None)
+        act(v("LAG"), v("PT", 0, 256), AF.Abs)
+        act(v("YI"), v("LAG"), AF.Identity, bias=col(29), scale=1.0 / 32)
+        mm([(v("PK", 0, 256), ident, v("YI"), False, True)])
+        ts(v("BNL"), v("PK", 0, 256), 64.0, A.mult)
+        act(v("SS"), v("PK", 0, 256))
+        cp(v("ML"), v("PM", 0, 256))
+        act(v("MT"), v("PM", 0, 256))
+        if t < 2:
+            extract("PM", 256, "FC", None)
+            act(v("CT%d" % t), v("PM", 256, 512))
+        rl = "RL%d" % (t % 2)
+        diff("PT", 256, "LAG")
+        ts(v(rl, 1, 256), v("PT", 256, 511), 1023.0, A.add)
+        fill(v(rl, 0, 256, 16), 2047)
+        ts(v("EL%d" % (t % 2)), v("LAG", 15, 256, 16), 1023.0, A.add)
+
+    def prep2(t):
+        diff("PX", 0, "MT")
+        if t < R - 1:
+            diff("PX", 256, "SS")
+        ts(v("PX", 15, 256, 16), v("MT", 15, 256, 16), float(HOLE), A.subtract)
+        if t < R - 1:
+            ts(v("PX", 271, 512, 16), v("SS", 15, 256, 16), E / 64.0, A.subtract)
+
+    def k_gather():
+        for c in range(3, -1, -1):
+            act(v("KG", 1024 * c, 1024 * c + 1024), ind(v("KW"), v("BNL", 64 * c, 64 * c + 64)))
+
+    def r_gather(t):
+        for c in range(4):
+            act(v("RG%d" % (t % 2), 1024 * c, 1024 * c + 1024), ind(v("RT"), v("RL%d" % (t % 2), 64 * c, 64 * c + 64)))
+        act(v("E15%d" % (t % 2)), ind(v("RT"), v("EL%d" % (t % 2))))
+
+    def weights(t, b0, b1):
+        pr = "PR%d_" % (t % 2)
+        for c0 in range(16 * b1 - 64, 16 * b0 - 1, -64):
+            c1 = c0 + 64
+            tt(v(pr, 16 * c0, 16 * c1), ind(v("AW"), v("ML", c0, c1)), v("KG", 16 * c0, 16 * c1), A.mult)
+            mm([(v("PW", c0, c1), win("F0", a), v(pr, 16 * c0 + a, 16 * c1, 16), a == 0, a == 15) for a in range(16)])
+
+    def elect(px0, bank, sfx, xs, lb, scale, dump, c0=0, c1=256):
+        tt(v("PD" + sfx, c0, c1), v("HIT", c0, c1), v("PX", px0 + c0, px0 + c1), A.mult)
+        scan(v(xs, c0, c1), v("SEG", c0, c1), v("PD" + sfx, c0, c1), 0.0, A.mult, A.add)
+        mm([(v(bank, px0 + c0 + dl, px0 + c1, 16), v("SH", 128 * dl, 128 * dl + 128), v(xs, c0 + 15, c1, 16), True, True) for dl in range(16)])
+        ts(v(lb, c0, c1, 16), v(xs, c0 + 15, c1, 16), scale, A.mult, float(HOLE), A.add)
+        ts(v("EE" + sfx, c0, c1), v(bank, px0 + c0, px0 + c1), 0.0, A.is_equal, dump, A.mult)
+        scan(v("OF" + sfx, c0, c1), v("EE" + sfx, c0, c1), v(lb, c0, c1), 0.0, A.max, A.min)
+
+    def scatter(window, lst, val, c0, b):
+        cp(ind(window, v(lst, 2 * b, 2 * b + 1)), v(val, c0 + 16 * b, c0 + 16 * b + 16))
+
+    def raised(window, lc, oh, nv, cap, b0=0, b1=16):
+        tt(v(nv, 16 * b0, 16 * b1), ind(window, v(lc, b0, b1)), v("OH", oh + 16 * b0, oh + 16 * b1), A.add)
+        ts(v(nv + "2", 16 * b0, 16 * b1), v(nv, 16 * b0, 16 * b1), cap, A.min)
+
+    def lam(t):
+        for a in range(16):
+            scan(v("SC", 256 * a, 256 * a + 256), v("RG%d" % (t % 2), a, 4096, 16), v("PR%d_" % (t % 2), a, 4096, 16), 0.0, A.mult, A.add)
+        tt(v("LAM"), ind(v("SC"), v("LAML")), v("E15%d" % (t % 2)), A.mult)
+        dma("s", [(T.yl[:, 256 * t:256 * t + 256], v("LAM"))])
+
+    def candidates(t):
+        ct, lp = "CT%d" % t, v("LP", 256 * t, 256 * t + 256)
+        tt(v("KEY"), v("PW", 0, 256), v("KF"), A.add)
+        scan(v("MN"), v("BSEG"), v("KEY"), 0.0, A.add, A.min)
+        diff("PK", 256, ct)
+        ts(v("PK", 271, 512, 16), v(ct, 15, 256, 16), 1.0, A.add)
+        tt(v("W2"), v("HIT"), v("PK", 256, 512), A.mult)
+        scan(v("W1"), v("SEG"), v("W2"), 0.0, A.mult, A.add)
+        tt(v("W3"), ind(v("W1"), v("REP15")), v("DG"), A.mult)
+        mm([(v("PK", 256, 512), v("GO"), v("W3"), True, True)])
+        ts(v("SM", 0, 16), v("W1", 15, 256, 16), 0.0, A.is_equal, 4096.0, A.mult)
+        tt(v("SM", 16, 32), v("SM", 0, 16), v("W1", 15, 256, 16), A.add)
+        ts(v("IX"), v("SM", 16, 32), 1.0, A.subtract, float(E), A.min)
+        act(v("W4"), v("PK", 256, 512), AF.Relu, bias=col(26), scale=-1.0)
+        act(v("W5"), v("PK", 256, 512), AF.Relu, bias=col(27), scale=1.0)
+        tt(v("W6"), v("W4"), lp, A.mult)
+        tt(lp, v("W6"), v("W5"), A.add)
+        tt(v("W2"), ind(v("LP"), v("IX")), v("DG"), A.mult)
+        scan(v("W1"), v("SEG"), v("W2"), 0.0, A.mult, A.add)
+        ts(v("SM", 32, 48), v("W1", 15, 256, 16), 0.0, A.min, 4096.0, A.mult)
+        tt(v("W3"), ind(v("W1"), v("REP15")), v(ct), A.subtract)
+        tt(v("SM", 48, 64), v("SM", 32, 48), v("MN", 15, 256, 16), A.add)
+        tt(v("W4"), ind(v("SM", 48, 64), v("REP", 0, 16)), v("KEY"), A.is_equal)
+        tt(v("W5"), v("W3"), v("W4"), A.mult)
+        o = v("PK", 256, 512)
+        mm([(o, pos32, v(ct), True, False), (o, pos32, v("W5"), False, True)])
+        cp(v("CL%d" % t), o)
+
+    tk_gather(0, (0, 1), "a")
+    tk_gather(0, (2, 3), "v")
+    prep(0)
+    k_gather()
+    ts(col(21), col(0), 16.0, A.mult, -256.0, A.add)
+    ts(v("GC", p=p24), v("J16", p=p24), v("PC", 84, 85, p=p24), A.is_equal)
+    lists(0, 80, v("PD_", 0, 80))
+    lists(1, 48, v("PD_", 80, 128))
+    act(v("UL"), v("PD_", 0, 80), scale=1.0 / 256)
+    act(v("BGL"), v("PD_", 80, 128))
+    for h, bank in enumerate(("PR0", "PR1")):
+        mm([(v(bank, 0, 384), v("GC", p=p24), v("QF", 384 * h, 384 * h + 384, p=p24), True, True)])
+        ts(v("OH", 384 * h, 384 * h + 384), v(bank, 0, 384), col(1), A.is_equal)
+    ts(v("SEG"), v("KI"), 0.0, A.not_equal)
+    fill(v("LB"), 1.0e6)
+    fill(v("LBK"), 1.0e6)
+    ts(col(22), col(1), float(DUMPA), A.add)
+    ts(col(23), col(1), float(DUMPB), A.add)
+    ts(col(24), col(1), float(E), A.add)
+    prep2(0)
+    mm([(v("PD_", 0, 112), win("FM", a), v("YY", a, 1792, 16), a == 0, a == 15) for a in range(16)])
+    act(v("YU"), v("PD_", 0, 112))
+    mm([(v("PD_", 0, 112), roll32, v("YU"), True, True)])
+    cp(v("MSN"), v("YU", 56, 112))
+    ts(v("SIX"), v("JF", 0, 56), 16.0, A.mult, col(1), A.add)
+    ts(v("YT", 0, 56), v("PD_", 0, 56), float(GUN), A.is_ge)
+    ts(v("YT", 56, 112), v("PD_", 0, 56), float(GUN - NG), A.subtract)
+    ts(v("LST"), v("PD_", 56, 112), float(GUN - NG), A.subtract)
+    tt(v("YT", 112, 168), v("YT", 0, 56), v("YT", 56, 112), A.mult)
+    tt(v("YT", 0, 56), v("YT", 112, 168), v("SIX"), A.max)
+    cp(v("PRV"), v("YT", 0, 56))
+    be = v("BE", 0, 1)
+    ts(v("BT", 0, 1), be, -1.0 / 6, A.mult, 0.5, A.add)
+    ts(v("BT", 4, 5), v("BT", 0, 1), be, A.mult, -1.0, A.add)
+    ts(v("BT", 8, 9), v("BT", 4, 5), be, A.mult, 1.0, A.add)
+    act(v("SC", 0, 2048), v("AW", 0, E), AF.Identity, bias=v("BT", 8, 9), scale=0.0)
+    for c in range(0, 2048, 512):
+        scan(v("RG1", c, c + 512), v("SC", c, c + 512), v("SC", c, c + 512), v("RG1", c - 1, c) if c else 1.0, A.mult, A.min)
+    run("v", lambda: g.vector.reciprocal(T.BT[:, 12:13], T.RG1[:, 1023:1024]), v("BT", 12, 13), [v("RG1", 1023, 1024)], 12.0)
+    act(v("RT", 0, 2047), v("RG1", 0, 2047), scale=v("BT", 12, 13))
+    fill(v("RT", 2047, 2048), 0.0)
+    ts(v("REP15"), v("JF", 0, 16), 16.0, A.mult, 15.0, A.add)
+    ts(col(25), col(1), 256.0, A.mult, 15.0, A.add)
+    ts(v("LAML"), v("JF", 0, 16), 16.0, A.mult, col(25), A.add)
+    ts(v("DG"), v("KI"), col(1), A.is_equal)
+    act(v("KF"), v("KI"), scale=1.0 / 16)
+    ts(v("BSEG"), v("KI"), 0.0, A.is_equal, 1.0e6, A.mult)
+    ts(v("GO"), v("J16"), col(2), A.is_equal)
+    fill(v("LP", E, E + 16), -1)
+
+    act(v("INC", GHO, GHO + NG), v("HI"), scale=0.0)
+    own = v("AW", 0, GHO)
+    first_round = len(ops)
+    for t in range(R):
+        s = t % 3
+        for b0, b1 in PARTS:
+            weights(t, b0, b1)
+            c0, c1 = 16 * b0, 16 * b1
+            scan(v("CUM", c0, c1), v("SEG", c0, c1), v("PW", c0, c1), 0.0, A.mult, A.add)
+            tt(v("S1", b0, b1), v("CUM", c0 + 15, c1, 16), v("BGL", 16 * s + b0, 16 * s + b1), A.add)
+            tt(v("THR", b0, b1), v("S1", b0, b1), v("UL", 16 * t + b0, 16 * t + b1), A.mult)
+            tt(v("HIT", c0, c1), ind(v("THR", b0, b1), v("REP", 0, b1 - b0)), v("CUM", c0, c1), A.is_lt)
+            elect(0, "PD_", "", "XS", "LB", 1.0, col(22), c0, c1)
+            cp(v("L1", 2 * b0, 2 * b1, 2), v("OF", c0 + 15, c1, 16))
+            ts(v("L2C", b0, b1), v("OF", c0 + 15, c1, 16), col(23), A.min)
+            ts(v("L2", 2 * b0, 2 * b1, 2), v("OF", c0 + 15, c1, 16), col(23), A.min)
+            raised(own, "L2C", 256 * s, "NV", 15.0, b0, b1)
+        for b in range(15, -1, -1):
+            scatter(v("INC"), "L1", "OH", 256 * s, b)
+            scatter(own, "L2", "NV2", 0, b)
+        exchange("INC", GHO, "BUF", NG, -1, "h1")
+        act(v("XB"), ind(own, v("MSN")))
+        through("BUF", 0, [(roll, "XB", 0)])
+        for d in range(7):
+            c = NG + GH * d
+            tt(v("BUF", c, c + GH), ind(v("BUF", 0, c), v("PRV", 8 * d, 8 * d + 8)), v("BUF", c, c + GH), A.add)
+        if t < R - 1:
+            ts(v("GN", 0, 640), ind(v("BUF", 0, 2 * NG), v("LST", 0, 40)), 15.0, A.min)
+            act(v("XB", 640, NG), ind(v("BUF", 0, 2 * NG), v("LST", 40, 56)), AF.Relu, bias=col(28), scale=-1.0)
+            act(v("GN", 640, NG), v("XB", 640, NG), AF.Identity, bias=col(28), scale=-1.0)
+            exchange("GN", 0, "AW", GHO, 1, "h2")
+            through("AW", GUN, [(unroll, "GN", 0)])
+            tk_gather(t + 1, range(4), "a")
+            elect(256, "PW", "K", "XK", "LBK", 64.0, col(24))
+            cp(v("LKC"), v("OFK", 15, 256, 16))
+            cp(v("LK", 0, 32, 2), v("OFK", 15, 256, 16))
+            raised(v("KW"), "LKC", 256 * s, "NW", 7.0)
+            for b in range(15, -1, -1):
+                scatter(v("KW"), "LK", "NW2", 0, b)
+            prep(t + 1)
+            k_gather()
+            act(v("INC", GHO, GHO + NG), v("HI"), scale=0.0)
+            prep2(t + 1)
+        else:
+            for c in range(4):
+                bank = v("PR%d" % (c % 2), 0, 512)
+                mm([(bank, roll, v("AW", 512 * c, 512 * c + 512), True, True)])
+                act(v("BUF", 2 * NG + 512 * c, 2 * NG + 512 * c + 512), bank)
+            for c0, c1, eng in ((0, 640, "v"), (640, 1024, "a"), (1024, 1664, "v"), (1664, 2048, "a")):
+                o, src = v("RG1", c0, c1), ind(v("BUF"), v("MAPL", c0 // 16, c1 // 16))
+                if eng == "v":
+                    ts(o, src, 15.0, A.min)
+                else:
+                    act(v("RG1", E + c0, E + c1), src, AF.Relu, bias=col(28), scale=-1.0)
+                    act(o, v("RG1", E + c0, E + c1), AF.Identity, bias=col(28), scale=-1.0)
+                dma("s" if eng == "v" else "a", [(T.ya[0:112, c0:c1], v("RG1", c0, c1, p=slice(16, 128))), (T.ya[112:128, c0:c1], v("RG1", c0, c1, p=slice(0, 16)))])
+        if t < 2:
+            candidates(t)
+        r_gather(t)
+        lam(t)
+        if t == 2:
+            mm([(v("PD_", 0, 128), win("FM", a), v("TW", a, E, 16), a == 0, a == 15) for a in range(16)])
+            act(v("W1", 0, 128), v("PD_", 0, 128))
+            mm([(v("PD_", 0, 128), roll32, v("W1", 0, 128), True, True)])
+            ts(v("W2", 0, 128), v("PD_", 0, 128), float(GUN), A.is_lt, float(GUN + NG), A.mult)
+            tt(v("W3", 0, 128), v("W2", 0, 128), v("PD_", 0, 128), A.add)
+            ts(v("MAPL"), v("W3", 0, 128), float(GUN - NG), A.subtract)
+
+    n = len(ops)
+    succ = [[] for _ in range(n)]
+    for i, o in enumerate(ops):
+        if o["kind"] == "r":
+            o["deps"] = set([o["with"]])
+        for d in o["deps"]:
+            succ[d].append(i)
+
+    def gap(d, i):
+        return 0.0 if ops[i]["kind"] == "r" or ops[i]["q"] == ops[d]["q"] == "t" else ops[d]["lat"] + SYNC
+
+    level = [0.0] * n
+    for i in range(n - 1, -1, -1):
+        level[i] = ops[i]["cost"] + max([gap(i, j) + level[j] for j in succ[i]] + [ops[i]["lat"]])
+
+    def place(key, pred, succ, gap):
+        left, est, done, order, ends = [len(x) for x in pred], [0.0] * n, set(), [], [0.0] * n
+        ready, free = {q: [] for q in Q}, {q: 0.0 for q in Q}
+        byq = {q: sorted([i for i in range(n) if ops[i]["q"] == q], key=lambda j: (-key[j], -j)) for q in Q}
+
+        def release(i, end):
+            done.add(i)
+            order.append(i)
+            ends[i] = end
+            for j in succ[i]:
+                est[j] = max(est[j], end + gap(i, j))
+                left[j] -= 1
+                if left[j] == 0:
+                    if ops[j]["q"] is None:
+                        release(j, est[j])
+                    else:
+                        ready[ops[j]["q"]].append(j)
+
+        def early(j, now, memo):
+            if j not in memo:
+                e = max(est[j], now)
+                if left[j]:
+                    for d in pred[j]:
+                        if d not in done:
+                            e = max(e, max(early(d, now, memo), free.get(ops[d]["q"], 0.0)) + ops[d]["cost"] + gap(d, j))
+                memo[j] = e
+            return memo[j]
+
+        for i in range(n):
+            if not pred[i]:
+                ready[ops[i]["q"]].append(i)
+        while any(ready.values()):
+            now, q = min((max(free[x], min(est[j] for j in ready[x])), x) for x in Q if ready[x])
+            can = [j for j in ready[q] if est[j] <= now]
+            i = min(can, key=lambda j: (key[j], j))
+            while byq[q][-1] in done:
+                byq[q].pop()
+            memo, soon = {}, None
+            for j in byq[q][:-1 - DEPTH:-1]:
+                if j not in done and key[j] + (LEAD if j >= first_round else LEAD0) < key[i]:
+                    e = early(j, now, memo)
+                    if e < now + LOOK * ops[i]["cost"] and (soon is None or e < soon):
+                        soon = e
+            if soon is not None:
+                short = [j for j in can if ops[j]["cost"] <= soon - now + SHORT]
+                if not short:
+                    free[q] = max(soon, now + 20.0)
+                    continue
+                i = min(short, key=lambda j: (key[j], j))
+            ready[q].remove(i)
+            free[q] = max(now, est[i]) + ops[i]["cost"]
+            release(i, free[q])
+        return max(ends[i] + ops[i]["lat"] for i in range(n)), order, ends
+
+    if n not in ORDER:
+        pred = [sorted(o["deps"]) for o in ops]
+        key, best = [-x for x in level], None
+        for _ in range(PASSES):
+            fw = place(key, pred, succ, gap)
+            if best is None or fw[0] < best[0]:
+                best = fw
+            bw = place([-x for x in fw[2]], succ, pred, lambda d, i: gap(i, d))
+            key = [MIX * -bw[2][i] + (1 - MIX) * key[i] for i in range(n)]
+        ORDER[n] = best
+    order = ORDER[n][1]
+
+    ESEM = {"v": "ev", "a": "ea", "t": "et", "g": "eg"}
+    count = {x: 0 for x in SEMAPHORES}
+    known = {q: {} for q in Q}
+    token = {}
+
+    def wait(q, sem, val):
+        if known[q].get(sem, 0) < val:
+            Q[q].wait_ge(T.sem[sem], val)
+            known[q][sem] = val
+
+    for i in order:
+        o = ops[i]
+        q = o["q"]
+        if o["kind"] == "r":
+            count[o["sem"]] += o["n"]
+            token[i] = (o["sem"], count[o["sem"]])
+            continue
+        need = {}
+        for d in o["deps"]:
+            if q == ops[d]["q"] == "t":
+                continue
+            sem, val = token[d]
+            need[sem] = max(need.get(sem, 0), val)
+        for sem in sorted(need):
+            wait(q, sem, need[sem])
+        if o["kind"] == "x":
+            o["calls"][0]()
+            sem, k = "ls", o["n"]
+        elif o["kind"] == "d":
+            sem, k = o["sem"], 16 * len(o["calls"])
+            for c in o["calls"]:
+                c().then_inc(T.sem[sem], 16)
+        else:
+            sem, k = ESEM[q], 1
+            for c in o["calls"][:-1]:
+                c()
+            o["calls"][-1]().then_inc(T.sem[sem], 1)
+        count[sem] += k
+        token[i] = (sem, count[sem])
+    for sem in SEMAPHORES:
+        if count[sem]:
+            wait("g", sem, count[sem])

@@ -1,90 +1,75 @@
+import numpy as np
 from concourse.bass import DstId, RemoteDMATransfer
 from concourse.mybir import AluOpType, ActivationFunctionType
 
 N, E, GH, NG, R = 8, 2048, 128, 896, 5
-HOLE, GUN, DUMPB, GHO, DUMPA = 2048, 2064, 2960, 2976, 3872
+GUN, GHO, OWN = 0, 896, 1792
+HOLE, IGUN, IGH, DUMP, RWN = 2048, 2112, 3008, 3904, 3920
 F32, BF, I32, U16, F16 = "float32", "bfloat16", "int32", "uint16", "float16"
 SB = {
-    "AW": (3872, BF), "INC": (3888, BF), "TW": (2944, BF), "KW": (2064, BF), "BUF": (3840, BF), "GN": (NG, BF), "GT": (NG, BF),
-    "X0": (NG, BF), "VV": (NG, BF), "GS": (NG, BF), "SL": (NG, BF), "HI": (NG, BF), "LO": (NG, BF), "YY": (1792, BF), "XB": (NG, BF),
-    "XX": (4096, BF), "KG": (4096, BF), "PR0_": (4096, BF), "PR1_": (4096, BF), "RG0": (4096, F32), "RG1": (4096, F32), "SC": (4096, F32), "RT": (2048, F32),
-    "LP": (2064, I32), "CA": (768, I32), "CAL": (768, U16), "SN": (56, I32), "SNL": (56, U16), "SI": (256, I32), "S2": (640, I32), "S3": (640, BF),
-    "QI": (1280, I32), "QF": (1280, F32), "JF": (656, F32), "FQ": (656, F32), "KI": (256, F32), "J16": (128, F32), "PI": (8, I32), "PC": (128, F32),
-    "F0": (144, BF), "FT": (144, BF), "FK": (144, BF), "FM": (144, BF), "FC": (144, BF), "I2": (256, BF), "RLT": (128, BF), "D11": (128, BF), "D12": (128, BF), "AG": (2048, BF), "I32F": (384, F32),
-    "GO": (128, F32), "GC": (128, F32), "SH": (2048, BF), "DG": (256, F32), "KF": (256, F32), "SEG": (256, F32), "BSEG": (256, F32),
-    "REP": (48, U16), "REP15": (16, U16), "LAML": (16, U16), "PERM": (48, U16), "SIX": (56, F32), "T48": (48, F32),
-    "UL": (80, F32), "BGL": (48, F32), "NTV": (48, F32), "KV": (48, F32), "TVR": (768, F32), "KVR": (768, F32), "OH": (768, BF),
-    "YU": (112, F32), "YT": (168, F32), "PRV": (56, U16), "LST": (56, U16), "MSN": (56, U16), "MAPL": (128, U16), "BE": (8, F32), "BT": (16, F32),
-    "LAG": (256, F32), "YI": (256, BF), "SS": (256, F32), "MT": (256, F32), "CT0": (256, F32), "CT1": (256, F32), "CL0": (256, U16), "CL1": (256, U16),
+    "AW": (OWN + RWN, BF), "SW": (RWN, BF), "TW": (3456, BF), "KW": (2064, BF), "BUF": (3840, BF), "GN": (NG, BF), "XB": (384, BF),
+    "XX0": (4352, BF), "XX1": (4352, BF), "XX2": (4096, BF), "KG": (4096, BF), "PR0_": (4096, BF), "PR1_": (4096, BF), "AS": (3072, BF),
+    "RG0": (4096, F32), "RG1": (4096, F32), "SC": (4096, F32), "RT": (2048, F32),
+    "GT": (NG, BF), "GC": (NG, BF), "VV": (NG, BF), "YY": (1792, BF), "TR": (E, BF), "GS": (NG, BF), "SL": (448, BF), "HI": (448, BF), "LO": (448, BF), "AG": (1920, BF),
+    "CA": (768, I32), "CAL": (768, U16), "SN": (56, I32), "SNR": (56, I32), "SNL": (56, U16), "SRL": (56, U16),
+    "SI": (384, I32), "S2": (896, I32), "S3": (1024, BF),
+    "QI": (1280, I32), "QF": (1280, F32), "JF": (272, F32), "FQ": (272, F32), "KI": (256, F32), "J16": (128, F32), "PI": (16, I32), "PC": (192, F32),
+    "F0": (144, BF), "FT": (144, BF), "FK": (144, BF), "FM": (144, BF), "FC": (144, BF), "FR": (144, BF), "FL": (144, BF),
+    "I2": (256, BF), "D11": (128, BF), "D12": (128, BF), "K89": (128, BF), "P56": (128, BF), "I32F": (384, F32),
+    "GK": (128, F32), "SH": (2048, BF), "KF": (256, F32), "SEG": (256, F32), "BSEG": (256, F32),
+    "REP": (48, U16), "LAML": (16, U16), "PERM": (48, U16), "T48": (48, F32), "PB": (64, F32),
+    "UL": (80, F32), "BGL": (48, F32), "NTV": (48, F32), "KV": (48, F32), "TVR": (768, F32), "KVR": (768, F32), "OH": (768, BF), "CAPA": (768, BF), "CAPK": (768, BF),
+    "YU": (112, F32), "YT": (168, F32), "PRV": (56, U16), "LST": (56, U16), "MAPL": (128, U16), "BE": (8, F32), "BT": (24, F32),
+    "LAG": (256, F32), "YI": (256, BF), "SS": (256, F32), "MT": (256, F32), "CT0": (256, F32), "CT1": (256, F32),
     "ML": (256, U16), "BNL": (256, U16), "RL0": (256, U16), "RL1": (256, U16), "EL0": (16, U16), "EL1": (16, U16), "E150": (256, F32), "E151": (256, F32),
-    "CUM": (256, F32), "S1": (16, F32), "THR": (16, F32), "HIT": (256, F32), "PD": (256, F32), "PDK": (256, F32), "XS": (256, F16), "XK": (256, F16),
+    "CUM": (256, F32), "S1": (16, F32), "THR": (128, F32), "HIT": (256, F32), "PD": (256, F32), "PDK": (256, F32), "XS": (256, F16), "XK": (256, F16),
     "LB": (256, F32), "LBK": (256, F32), "EE": (256, F32), "EEK": (256, F32), "OF": (256, F32), "OFK": (256, F32),
-    "L1": (32, U16), "L2": (32, U16), "L2C": (16, U16), "LK": (32, U16), "LKC": (16, U16), "NV": (256, BF), "NW": (256, BF), "NV2": (256, BF), "NW2": (256, BF),
-    "LAM": (256, F32), "KEY": (256, F32), "MN": (256, F32), "W1": (256, F32), "W2": (256, F32), "W3": (256, F32), "W4": (256, F32), "W5": (256, F32),
-    "W6": (256, F32), "SM": (64, F32), "IX": (16, U16),
+    "L1": (32, U16), "L1C": (16, U16), "LK": (32, U16), "LKC": (16, U16), "NV": (256, BF), "NW": (256, BF), "NX": (256, BF), "NX1": (256, BF), "NX2": (256, BF),
+    "LAM": (256, F32), "KEY": (256, F32), "MN": (256, F32), "W1": (256, F32), "W2": (256, F32), "W3": (256, F32),
+    "SM": (96, F32), "MI": (32, I32), "IX1": (16, U16), "IX2": (16, U16), "PL": (16, U16), "NC": (16, U16),
 }
+ALIAS = {"GT": ("KG", 0), "GC": ("KG", NG), "YY": ("XX2", 0), "VV": ("XX2", 1792), "TR": ("PR0_", 0), "GS": ("PR0_", E), "SL": ("PR0_", E + NG),
+         "AG": ("PR1_", 0), "HI": ("PR1_", 1920), "LO": ("PR1_", 1920 + NG), "QF": ("RG0", 0)}
 PS = ["PW", "PD_", "PR0", "PR1", "PT", "PK", "PX", "PM"]
 POOL, _n = {}, 0
 for _k, (_c, _d) in SB.items():
     if _d == U16:
         POOL[_k] = _n
         _n += (_c + 15) // 16 * 16
-SCRATCH = {k: ("sbuf", [128, n], d) for k, (n, d) in SB.items() if k not in POOL}
+SCRATCH = {k: ("sbuf", [128, n], d) for k, (n, d) in SB.items() if k not in POOL and k not in ALIAS}
 SCRATCH["UP"] = ("sbuf", [128, _n], U16)
 for _k in PS:
     SCRATCH[_k] = ("psum", [128, 512], F32)
-SEMAPHORES = ["ev", "ea", "et", "eg", "ls", "h0t", "h1", "h2"] + ["hh%d" % _k for _k in range(1, 2 * R + 1)] + ["d%d" % _k for _k in range(40)]
+CALLS = ((1, 2, 3, 4), (5, 6), (7,))
+X1, X2 = CALLS, CALLS
+NX_ = (2 * R + 1) * len(CALLS)
+SEMAPHORES = ["ev", "ea", "et", "eg"] + ["l%d" % _k for _k in range(NX_)] + ["h%d" % _k for _k in range(NX_)] + ["d%d" % _k for _k in range(56)]
 SIZE = {F32: 4, I32: 4, BF: 2, U16: 2, F16: 2}
 A = AluOpType
 AF = ActivationFunctionType
-CYC, FIX, GATHER, SCATTER, PEC, SYNC, DMALAT, HOP = 1.04, 60.0, 1.56, 3.8, 0.55, 120.0, 2200.0, 7000.0
-LOOK, DEPTH, LEAD, LEAD0, SHORT, PASSES, MIX, ORDER = 0.8, 8, 2500.0, 2500.0, 250.0, 5, 0.6, {}
-
-
+CYC, FIX, GATHER, SCATTER, PEC, SYNC, DMALAT, ISSUE, HOP, ROW = 0.95, 50.0, 1.56, 3.8, 0.45, 100.0, 2200.0, 400.0, 1500.0, 35.0
+LOOK, DEPTH, LEAD, LEAD0, SHORT, MIX, ORDER = 0.8, 14, 2500.0, 2500.0, 50.0, 0.6, {}
+PASSES, SLIP, NOISE, PASS0, FIXS, ROWLAT, NOISE0 = 10, 1000.0, 0.0, 5, 20.0, 250.0, 0.0
+FINAL = ((0, 416, "v"), (416, 672, "a"), (672, 1088, "v"), (1088, 1344, "a"), (1344, 1792, "v"), (1792, 2048, "a"))
 PARTS = ((8, 16), (0, 8))
-HELP = True
-EXCHANGES = [("TW", E, 1, "h0t"), ("AW", GHO, 1, "h2")] + [("BUF", NG, -1, "h1"), ("AW", GHO, 1, "h2")] * (R - 1) + [("BUF", NG, -1, "h1")]
-
-
-def transfer(T, topo, core, peer, engines, sem, src, dst):
-    rid, pid, _ = topo.addr(peer)
-    mask = sum(1 << topo.engines(core, peer)[e] for e in engines)
-    return RemoteDMATransfer(dst_ids=[DstId(rid=rid, pnc=pid)], dma_engine_mask=mask, remote_sem=T.sem[sem], src=src, dst=dst)
-
-
-def helpers(T, topo, core):
-    return [c for c in topo.cores_of(core) if T.rank_of(c) is None and all(topo.may_write(c, x) for x in T.cores)][:3]
-
-
-def hand_on(g, core, T, topo):
-    boss = [c for c in topo.cores_of(core) if T.rank_of(c) is not None]
-    if not HELP or not boss or core not in helpers(T, topo, boss[0]):
-        return
-    rank, j = T.rank_of(boss[0]), helpers(T, topo, boss[0]).index(core)
-    for k in range(1, len(EXCHANGES)):
-        dst, d0, sign, sem = EXCHANGES[k]
-        g.wait_ge(T.sem["hh%d" % k], 4)
-        g.remote_dma_fused([transfer(T, topo, core, T.cores[(rank + sign * d) % N], range(4 * h, 4 * h + 4), sem,
-                                     T.XX[:, GH * (2 * k + h):GH * (2 * k + h + 1)], T[dst][:, d0 + GH * (d - 1):d0 + GH * d])
-                            for h, d in enumerate((2 * j + 1, 2 * j + 2))], local_sem=T.sem.ls)
-    g.wait_ge(T.sem.ls, 8 * (len(EXCHANGES) - 1))
+SPLIT = (0, 0, 4, 4, 4)
 
 
 def rank_program(g, core, T, topo):
     rank = T.rank_of(core)
     if rank is None:
-        hand_on(g, core, T, topo)
         return
     Q = {"v": g.vector, "a": g.scalar, "t": g.tensor, "g": g, "s": g.sync}
-    ops, hist, ndma = [], {}, [0]
+    ops, hist, ndma, nx = [], {}, [0], [0]
 
     def v(name, c0=0, c1=None, step=1, p=None):
         n, sz = (SB[name][0], SIZE[SB[name][1]]) if name in SB else (512, 4)
         c1 = n if c1 is None else c1
         rows = slice(None) if p is None else p
-        ten, b = (T.UP, POOL[name]) if name in POOL else (T[name], 0)
+        base, r0 = ALIAS.get(name, (name, 0))
+        ten, b = (T.UP, POOL[name]) if name in POOL else (T[base], r0)
         ap_ = ten[rows, b + c0:b + c1:step] if step != 1 else ten[rows, b + c0:b + c1]
-        return {"ap": ap_, "reg": [(name, (c0 * sz) // 16 * 16, (c1 * sz + 15) // 16 * 16)], "n": len(range(c0, c1, step)), "sz": sz, "ps": name in PS}
+        return {"ap": ap_, "reg": [(base, ((r0 + c0) * sz) // 16 * 16, ((r0 + c1) * sz + 15) // 16 * 16)], "n": len(range(c0, c1, step)), "sz": sz, "ps": name in PS}
 
     def ind(win, off):
         return {"ap": win["ap"].indirect(off["ap"]), "reg": win["reg"], "off": off["reg"], "n": 16 * off["n"], "sz": win["sz"], "ps": False}
@@ -95,7 +80,7 @@ def rank_program(g, core, T, topo):
     def ap(x):
         return x["ap"] if isinstance(x, dict) else x
 
-    def add(q, calls, rd, wr, cost, lat=0.0, kind="c", after=(), free=False):
+    def add(q, calls, rd, wr, cost, lat=0.0, kind="c", after=(), free=False, behind=()):
         me, deps = len(ops), set(after)
         if not free:
             for rs, w in ((rd, False), (wr, True)):
@@ -108,10 +93,10 @@ def rank_program(g, core, T, topo):
             hist[name] = keep + [(me, lo, hi, True)]
         for name, lo, hi in rd:
             hist.setdefault(name, []).append((me, lo, hi, False))
-        ops.append({"q": q, "calls": calls, "deps": deps, "cost": cost, "lat": lat, "kind": kind})
+        ops.append({"q": q, "calls": calls, "deps": deps | set(behind), "behind": set(behind) - deps, "cost": cost, "lat": lat, "kind": kind})
         return me
 
-    def run(q, call, o, ins, per, after=()):
+    def run(q, call, o, ins, per, behind=()):
         xs = [x for x in [o] + ins if isinstance(x, dict)]
         if "off" in o:
             per = SCATTER
@@ -119,81 +104,89 @@ def rank_program(g, core, T, topo):
             per = GATHER
         elif per == 0.5 and any(x["sz"] == 4 and x["n"] > 1 for x in xs):
             per = 1.0
-        return add(q, [call], regs(ins) + o.get("off", []), o["reg"], FIX + CYC * per * max(o["n"], 16), after=after)
+        cost = FIX + CYC * per * o["n"] if q != "v" or per in (GATHER, SCATTER) else FIXS + CYC * max(64, per * o["n"])
+        return add(q, [call], regs(ins) + o.get("off", []), o["reg"], cost, behind=behind)
 
     def tt(o, a, b, op):
-        run("v", lambda: g.vector.tensor_tensor(ap(o), ap(a), ap(b), op), o, [a, b], 1.0 if a["ps"] or b["ps"] else 2.0)
+        return run("v", lambda: g.vector.tensor_tensor(ap(o), ap(a), ap(b), op), o, [a, b], 1.0 if a["ps"] or b["ps"] else 2.0)
 
     def ts(o, a, s1, op0, s2=None, op1=None):
         if op1 is None:
-            run("v", lambda: g.vector.tensor_scalar(ap(o), ap(a), ap(s1), None, op0), o, [a, s1], 0.5)
-        else:
-            run("v", lambda: g.vector.tensor_scalar(ap(o), ap(a), ap(s1), ap(s2), op0, op1), o, [a, s1, s2], 0.5)
+            return run("v", lambda: g.vector.tensor_scalar(ap(o), ap(a), ap(s1), None, op0), o, [a, s1], 0.5)
+        return run("v", lambda: g.vector.tensor_scalar(ap(o), ap(a), ap(s1), ap(s2), op0, op1), o, [a, s1, s2], 0.5)
 
     def cp(o, a):
-        run("v", lambda: g.vector.tensor_copy(ap(o), ap(a)), o, [a], 0.5)
+        return run("v", lambda: g.vector.tensor_copy(ap(o), ap(a)), o, [a], 0.5)
 
     def scan(o, d0, d1, init, op0, op1):
-        run("v", lambda: g.vector.tensor_tensor_scan(ap(o), ap(d0), ap(d1), ap(init), op0, op1), o, [d0, d1, init], 0.5)
+        return run("v", lambda: g.vector.tensor_tensor_scan(ap(o), ap(d0), ap(d1), ap(init), op0, op1), o, [d0, d1, init], 0.5)
 
     def fill(o, c):
-        run("v", lambda: g.vector.memset(ap(o), c), o, [], 0.5)
+        return run("v", lambda: g.vector.memset(ap(o), c), o, [], 0.5)
 
     def act(o, a, f=AF.Copy, bias=None, scale=1.0):
         if bias is None:
-            run("a", lambda: g.scalar.activation(ap(o), ap(a), f, scale=ap(scale)), o, [a, scale], 1.0)
-        else:
-            run("a", lambda: g.scalar.activation(ap(o), ap(a), f, bias=ap(bias), scale=ap(scale)), o, [a, bias, scale], 1.0)
+            return run("a", lambda: g.scalar.activation(ap(o), ap(a), f, scale=ap(scale)), o, [a, scale], 1.0)
+        return run("a", lambda: g.scalar.activation(ap(o), ap(a), f, bias=ap(bias), scale=ap(scale)), o, [a, bias, scale], 1.0)
 
     def mm(items):
         def one(x):
             return lambda: g.tensor.matmul(ap(x[0]), ap(x[1]), ap(x[2]), x[3], x[4])
         cost = sum(max(64, x[2]["n"]) * (4 if x[2]["sz"] == 4 else 1) * PEC for x in items)
-        add("t", [one(x) for x in items], regs([y for x in items for y in x[1:3]]), list(set(regs([x[0] for x in items]))), cost, 150.0)
+        return add("t", [one(x) for x in items], regs([y for x in items for y in x[1:3]]), list(set(regs([x[0] for x in items]))), cost, 150.0)
 
-    def iota(o, pat, base, cm, small=True):
+    def iota(o, pat, base, cm, small=True, after=()):
         if small:
-            run("g", lambda: g.iota(ap(o), pat, base, cm, allow_small_or_imprecise_dtypes=True), o, [], 2.0)
-        else:
-            run("g", lambda: g.iota(ap(o), pat, base, cm), o, [], 2.0)
+            return run("g", lambda: g.iota(ap(o), pat, base, cm, allow_small_or_imprecise_dtypes=True), o, [], 2.0, after)
+        return run("g", lambda: g.iota(ap(o), pat, base, cm), o, [], 2.0, after)
 
     def sel(o, a, pat, op, fl, base, cm, after=()):
-        run("g", lambda: g.affine_select(ap(o), ap(a), pat, op, fl, base, cm), o, [a], 2.0, after)
+        return run("g", lambda: g.affine_select(ap(o), ap(a), pat, op, fl, base, cm), o, [a], 2.0, after)
 
-    def dma(q, pairs, other_rows=False):
+    def dma(q, pairs, other_rows=False, after=(), lat=DMALAT, behind=()):
         def one(o, a):
             return lambda: Q[q].dma_start(ap(o), ap(a))
         rd, wr = regs([a for o, a in pairs]), list(set(regs([o for o, a in pairs])))
-        me = add(q, [one(o, a) for o, a in pairs], rd, wr, 150.0 * len(pairs), DMALAT, "d")
+        me = add(q, [one(o, a) for o, a in pairs], rd, wr, 100.0 * len(pairs), lat, "d")
         if other_rows:
             ops[me]["deps"] = set(o for o in ops[me]["deps"] if ops[o]["kind"] != "d")
+        ops[me]["deps"].update(after)
+        ops[me]["behind"] = set(behind) - ops[me]["deps"]
+        ops[me]["deps"].update(behind)
         ops[me]["sem"] = "d%d" % ndma[0]
         ndma[0] += 1
         return me
 
-    last_send = []
+    sends = []
 
-    def exchange(src, s0, dst, d0, sign, sem):
-        k = len(last_send)
-        assert EXCHANGES[k] == (dst, d0, sign, sem)
-        handed = HELP and k > 0
+    def exchange(src, s0, dst, d0, sign, after=(), late=0.0, calls=None):
+        rows, mine, came = 0, [], []
+        for j, blocks in enumerate(calls or X2):
+            k = nx[0]
+            nx[0] += 1
+            engines = len(topo.engines(core, T.cores[(rank + 1) % N]))
+            m = engines // len(blocks)
 
-        def block(d, engines):
-            return transfer(T, topo, core, T.cores[(rank + sign * d) % N], engines, sem, T[src][:, s0 + GH * (d - 1):s0 + GH * d], T[dst][:, d0 + GH * (d - 1):d0 + GH * d])
-
-        def call():
-            if handed:
-                g.remote_dma_fused([transfer(T, topo, core, h, range(4 * j + 4, 4 * j + 8), "hh%d" % k, T[src][:, s0 + 2 * GH * j:s0 + 2 * GH * (j + 1)], T.XX[:, 2 * GH * k:2 * GH * (k + 1)])
-                                    for j, h in enumerate(helpers(T, topo, core))], local_sem=T.sem.ls)
-                g.remote_dma_fused([block(N - 1, range(4))], local_sem=T.sem.ls)
-            else:
-                g.remote_dma_fused([block(d, [d - 1]) for d in range(1, N)], local_sem=T.sem.ls)
-        me = add("g", [call], v(src, s0, s0 + NG)["reg"], [], 300.0, HOP - 1000.0, "x", after=last_send[-1:])
-        last_send.append(me)
-        arr = add(None, [], [], v(dst, d0, d0 + NG)["reg"], 0.0, HOP, "r", free=True)
-        ops[arr]["sem"], ops[arr]["with"] = sem, me
-        ops[me]["n"], ops[arr]["n"] = (16, 4 * (N - 1)) if handed else (N - 1, N - 1)
-        return me
+            def call(blocks=blocks, k=k, m=m):
+                out = []
+                for i, d in enumerate(blocks):
+                    peer = T.cores[(rank + sign * d) % N]
+                    rid, pid, _ = topo.addr(peer)
+                    mask = sum(1 << e for e in topo.engines(core, peer)[m * i:m * i + m])
+                    out.append(RemoteDMATransfer(dst_ids=[DstId(rid=rid, pnc=pid)], dma_engine_mask=mask, remote_sem=T.sem["h%d" % k],
+                                                 src=v(src, s0 + GH * (d - 1), s0 + GH * d)["ap"], dst=v(dst, d0 + GH * (d - 1), d0 + GH * d)["ap"]))
+                g.remote_dma_fused(out, local_sem=T.sem["l%d" % k])
+            c0, c1 = GH * (blocks[0] - 1), GH * blocks[-1]
+            rows += 128 // m
+            lat = late + HOP + ROW * rows - ISSUE * j
+            me = add("g", [call], v(src, s0 + c0, s0 + c1)["reg"], [], ISSUE, lat - 500.0, "x", after=after, behind=sends[-1:])
+            sends.append(me)
+            arr = add(None, [], [], v(dst, d0 + c0, d0 + c1)["reg"], 0.0, lat, "r", free=True)
+            ops[me]["sem"], ops[arr]["sem"], ops[arr]["with"] = "l%d" % k, "h%d" % k, me
+            ops[me]["n"] = ops[arr]["n"] = m * len(blocks)
+            mine.append(me)
+            came.append(arr)
+        return mine, came
 
     def col(j):
         return v("PC", 4 * j, 4 * j + 1)
@@ -201,44 +194,61 @@ def rank_program(g, core, T, topo):
     def win(name, a):
         return v(name, 15 - a, 143 - a)
 
-    dma("s", [(v("SI", 0, 128), T.ti[:])])
-    dma("s", [(v("S2", 512, 640), T.kd[:])])
-    dma("s", [(v("SN"), T.snd[:])])
-    dma("a", [(v("AW", 0, E), T.a0[:])])
-    dma("a", [(v("CA"), T.ca[:])])
-    dma("s", [(v("BE", 0, 1), T.be[:])])
-    dma("a", [(v("KW", 0, E), T.k0[:])])
+    up, down = slice(16, 128), slice(0, 16)
+    dma("s", [(v("SI", 0, 128, p=up), T.ti[0:7, :]), (v("SI", 0, 128, p=down), T.ti[7:8, :])])
+    dma("a", [(v("S2", 512, 640, p=up), T.kd[0:7, :]), (v("S2", 512, 640, p=down), T.kd[7:8, :])])
+    dma("s", [(v("SNR", p=up), T.snd[0:112, :]), (v("SNR", p=down), T.snd[112:128, :])])
+    dma("a", [(v("SN"), T.snd[:])])
+    dma("a", [(v("SI", 256, 384), T.lp[:])])
+    fill(v("TR"), 0.0)
     fill(v("TW", 0, E), 0.0)
-    fill(v("KW", E, E + 16), 0.0)
-    fill(v("AW", HOLE, GUN), 0.0)
-    fill(v("AW", DUMPB, GHO), 0.0)
-    iota(v("SI", 128, 256), [[1, 128]], 0, 128, False)
-    iota(v("PI", 0, 1), [[0, 1]], 0, 1, False)
-    iota(v("JF", 0, 144), [[1, 144]], 0, 0)
-    iota(v("JF", 144, 656), [[1, 512]], 144, 0)
-    iota(v("HI"), [[64, 14], [0, 64]], 0, 0)
-    iota(v("LO"), [[0, 14], [1, 64]], 0, 0)
+    fill(v("TW", 2944, 3456), 0.0)
+    g0 = iota(v("SI", 128, 256), [[1, 128]], 0, 128, False)
+    g0 = iota(v("PI", 0, 1), [[0, 1]], 0, 1, False, [g0])
+    g0 = iota(v("JF", 0, 144), [[1, 144]], 0, 0, True, [g0])
+    g0 = iota(v("HI"), [[64, 7], [0, 64]], 0, 0, True, [g0])
+    g0 = iota(v("LO"), [[0, 7], [1, 64]], 0, 0, True, [g0])
+    iota(v("JF", 144, 272), [[1, 128]], 144, 0)
+    iota(v("T48"), [[256, 3], [128, 2], [2, 8]], 0, 0)
     iota(v("KI"), [[0, 16], [1, 16]], 0, 0)
     iota(v("J16"), [[16, 8], [0, 16]], 0, 0)
-    iota(v("T48"), [[256, 3], [1, 16]], 0, 0)
-    for c0 in (128, 0):
+    iota(v("PB", 0, 16), [[2048, 2], [16, 8]], 0, 0)
+    for c0 in (0, 128):
         ts(v("S2", c0, c0 + 128), v("SI", c0, c0 + 128), 0x7C0, A.bitwise_and)
         ts(v("S2", c0 + 256, c0 + 384), v("SI", c0, c0 + 128), 63, A.bitwise_and)
         cp(v("S3", c0, c0 + 128), v("S2", c0, c0 + 128))
         cp(v("S3", c0 + 256, c0 + 384), v("S2", c0 + 256, c0 + 384))
     cp(v("S3", 512, 640), v("S2", 512, 640))
-    rows = [dma(q, [(v("TW", 0, E, p=slice(row, 128, 16)), v("S3", c, c + 128))], True)
-            for q, row, c in (("s", 3, 128), ("a", 4, 384), ("s", 5, 128), ("a", 6, 384), ("s", 0, 0), ("a", 1, 256), ("s", 2, 512))]
-    small = dma("s", [(v("QI", 0, n, p=slice(8 * j, 8 * j + 8)), src[:, 0:n]) for j, (src, n) in enumerate(((T.us, 1280), (T.bg, 768), (T.cl, 768), (T.ti, 768), (T.kd, 768)))])
-    ops[small]["deps"].update(rows)
-    last = dma("s", [(v("LP", 0, E, p=slice(p, 128, 16)), T.lp[:]) for p in range(16)])
-    ops[last]["deps"].add(small)
+    ts(v("S3", 640, 768), v("S3", 128, 256), float(OWN), A.add)
+    ts(v("S2", 640, 768), v("SI", 256, 384), 0xFC0, A.bitwise_and)
+    ts(v("S2", 768, 896), v("SI", 256, 384), 63, A.bitwise_and)
+    cp(v("S3", 768, 1024), v("S2", 640, 896))
+    line = {"s": [], "a": []}
+
+    def row_dma(q, pairs):
+        line[q].append(dma(q, pairs, True, behind=line[q][-1:], lat=DMALAT + ROWLAT * len(line[q])))
+
+    for q, row, c in (("s", 3, 640), ("a", 4, 384), ("s", 5, 128), ("a", 6, 384), ("s", 7, 128)):
+        row_dma(q, [(v("TW", 0, E, p=slice(row, 128, 16)), v("S3", c, c + 128))])
+    for q, row, c in (("s", 0, 0), ("a", 1, 256), ("s", 2, 512)):
+        row_dma(q, [(v("TR", p=slice(row, 128, 16)), v("S3", c, c + 128))])
+    for q, row, c in (("a", 0, 0), ("s", 1, 256), ("a", 2, 512)):
+        row_dma(q, [(v("TW", 0, E, p=slice(row, 112, 16)), v("S3", c, c + 128, p=up)), (v("TW", 0, E, p=slice(112 + row, 113 + row)), v("S3", c, c + 128, p=down))])
+    for q, row, c in (("s", 8, 768), ("a", 9, 896)):
+        row_dma(q, [(v("TW", 0, E, p=slice(row, 128, 16)), v("S3", c, c + 128))])
+    a0 = dma("a", [(v("AW", OWN, OWN + E), T.a0[:])], lat=5000.0, behind=line["a"][-1:])
+    dma("a", [(v("CA"), T.ca[:])], behind=[a0], lat=6000.0)
+    small = dma("s", [(v("QI", 0, n, p=slice(8 * j, 8 * j + 8)), src[:, 0:n]) for j, (src, n) in enumerate(((T.us, 1280), (T.bg, 768), (T.cl, 768)))], behind=line["s"][-1:], lat=5000.0)
+    dma("s", [(v("BE", 0, 1), T.be[:])], behind=[small])
+    cp(v("SRL"), v("SNR"))
     cp(v("SNL"), v("SN"))
-    fill(col(26), 1.0)
-    fill(col(27), -1.0)
+    fill(v("KW", E, E + 16), 0.0)
+    fill(v("AW", OWN + E, OWN + RWN), 0.0)
+    fill(v("SW", E, RWN), 0.0)
     fill(col(28), 15.0)
     fill(col(29), 160.0 - 15.5 / 32)
     fill(col(30), -160.0)
+    fill(col(31), 7.0)
     ts(v("PI", 4, 5), v("PI", 0, 1), 15, A.bitwise_and)
     cp(col(0), v("PI", 0, 1))
     cp(col(1), v("PI", 4, 5))
@@ -247,25 +257,29 @@ def rank_program(g, core, T, topo):
     ts(col(4), col(1), 4.0, A.is_equal)
     ts(col(5), col(1), 5.0, A.is_equal)
     ts(col(6), col(1), 6.0, A.is_equal)
-    tt(col(7), col(3), col(5), A.add)
+    ts(col(32), col(1), 7.0, A.is_equal)
+    tt(col(33), col(3), col(32), A.add)
+    tt(col(7), col(33), col(5), A.add)
     tt(col(8), col(4), col(6), A.add)
-    ts(col(9), col(3), float(GHO - E), A.mult)
-    ts(col(10), col(7), float(E), A.mult, col(9), A.add)
-    tt(col(11), col(3), col(4), A.add)
+    ts(col(39), col(1), 8.0, A.is_equal, 4032.0, A.mult)
+    ts(col(9), col(3), float(GHO), A.mult, col(39), A.add)
+    ts(col(34), col(5), float(E), A.mult, col(9), A.add)
+    ts(col(10), col(32), float(IGH), A.mult, col(34), A.add)
+    tt(col(11), col(33), col(4), A.add)
     ts(col(12), col(11), -1.0, A.mult, 1.0, A.add)
-    ts(col(13), col(3), float(GUN - GHO), A.mult)
-    ts(col(14), col(1), 2.5, A.is_lt)
+    ts(col(13), col(33), -float(NG), A.mult)
     ts(v("I2", 0, 128), v("JF", 0, 128), col(0), A.is_equal)
     act(v("I2", 128, 256), v("I2", 0, 128))
-    act(v("RLT"), v("I2", 112, 240), scale=col(14))
-    ts(v("GS"), v("HI"), col(7), A.mult, col(10), A.add)
+    ts(col(43), col(7), 448.0, A.mult, col(10), A.add)
+    ts(v("GS", 0, 448), v("HI"), col(7), A.mult, col(10), A.add)
+    ts(v("GS", 448, NG), v("HI"), col(7), A.mult, col(43), A.add)
     ts(v("SL"), v("LO"), col(8), A.mult)
     act(v("D11"), v("I2", 0, 128), scale=col(11))
     act(v("D12"), v("I2", 0, 128), scale=col(12))
     ident, roll, unroll = v("I2", 0, 128), v("I2", 112, 240), v("I2", 16, 144)
     pos32, roll32, neg32 = v("I32F", 0, 128), v("I32F", 112, 240), v("I32F", 256, 384)
 
-    def through(dst, d0, terms, bias=None, banks=("PR0", "PR1"), both=False):
+    def through(dst, d0, terms, bias=None, banks=("PR0", "PR1")):
         for h, bank in enumerate(banks):
             c = 448 * h
             for j, (lhs, src, s0) in enumerate(terms):
@@ -273,42 +287,63 @@ def rank_program(g, core, T, topo):
         for h, bank in enumerate(banks):
             o = v(dst, d0 + 448 * h, d0 + 448 * h + 448)
             if bias is not None:
-                ts(o, v(bank, 0, 448), bias, A.add)
+                act(o, v(bank, 0, 448), AF.Identity, bias)
             else:
-                (cp if both and h else act)(o, v(bank, 0, 448))
+                act(o, v(bank, 0, 448))
 
-    cp(v("X0"), ind(v("TW", 0, E), v("SNL")))
-    through("GT", 0, [(ident, "GS", 0), (ident, "SL", 0), (v("RLT"), "X0", 0)], both=True)
-    exchange("GT", 0, "TW", E, 1, "h0t")
-    through("VV", 0, [(v("D11"), "GS", 0), (v("D11"), "SL", 0), (v("D12"), "X0", 0)], col(13), ("PT", "PK"))
-    act(v("AW", GUN, GUN + NG), ind(v("AW", 0, E), v("SNL")))
+    for h, bank in enumerate(("PR0", "PR1")):
+        mm([(v(bank, 0, 448), ident, v("GS", 448 * h, 448 * h + 448), True, False), (v(bank, 0, 448), ident, v("SL"), False, True)])
+        (cp if h else act)(v("GC", 448 * h, 448 * h + 448), v(bank, 0, 448))
+    for c0, c1 in ((0, 512), (512, NG)):
+        tt(v("GT", c0, c1), ind(v("TR"), v("SRL", c0 // 16, c1 // 16)), v("GC", c0, c1), A.add)
+    first, came0 = exchange("GT", 0, "TW", E, 1, late=2500.0)
+    act(v("AW", GUN, GUN + NG), ind(v("AW", OWN, OWN + E), v("SNL")))
     through("GN", 0, [(roll, "AW", GUN)])
-    sent = exchange("GN", 0, "AW", GHO, 1, "h2")
-    act(v("YY", 0, GH), v("X0", 0, GH))
-    for d in range(7):
-        lst = v("SNL", 8 * d, 8 * d + 8)
-        if d:
-            act(v("YY", GH * d, GH * d + GH), ind(v("TW", 0, E), lst))
-        cp(ind(v("TW", 0, E), lst), v("VV", GH * d, GH * d + GH))
-    act(v("YY", NG, 2 * NG), ind(v("TW", 0, E), v("SNL")))
+    sent, came = exchange("GN", 0, "AW", GHO, 1, late=3000.0)
+    dma("a", [(v("KW", 0, E), T.k0[:])], after=first, lat=3000.0)
+    dma("s", [(v("SW", 0, E), T.a0[:])], after=sent, lat=3000.0)
     ts(col(15), col(2), 15.0, A.add)
     ts(v("F0"), v("JF", 0, 144), col(15), A.is_equal)
     ts(col(16), col(1), 1.5, A.is_lt)
     ts(col(17), col(1), 2.0, A.is_equal, 1.0 / 64, A.mult)
     tt(col(18), col(5), col(6), A.add)
+    tt(col(14), col(3), col(4), A.add)
+    tt(col(35), col(32), col(4), A.add)
     act(v("FT"), v("F0"), scale=col(16))
     act(v("FK"), v("F0"), scale=col(17))
-    act(v("FM"), v("F0"), scale=col(11))
+    act(v("FM"), v("F0"), scale=col(14))
     act(v("FC"), v("F0"), scale=col(18))
+    act(v("FR"), v("F0"), scale=col(35))
+    ts(col(40), col(1), 7.5, A.is_gt)
+    ts(col(41), col(1), 9.5, A.is_lt, col(40), A.mult)
+    ts(col(42), col(41), -1.0, A.mult, 1.0, A.add)
+    act(v("FL"), v("F0"), scale=col(41))
+    act(v("K89"), ident, scale=col(42))
+    act(v("P56"), v("I2", 125, 253), scale=col(18))
+    mm([(v("PX", 0, 48), win("FT", a), v("TW", a, 768, 16), a == 0, a == 15) for a in range(16)])
+    mm([(v("PX", 48, 96), win("FK", a), v("TW", a, 768, 16), a == 0, a == 15) for a in range(16)])
+    act(v("NTV"), v("PX", 0, 48), scale=-1.0)
+    act(v("KV"), v("PX", 48, 96), AF.Identity, bias=col(30), scale=8.0)
+    act(v("YY", 0, 448), ind(v("TW", 0, E), v("SNL", 0, 28)))
+    act(v("YY", 448, NG), ind(v("TW", 0, E), v("SNL", 28, 56)))
+    through("VV", 0, [(v("D11"), "GC", 0), (v("D12"), "YY", 0)], col(13), ("PT", "PK"))
+    for d in range(7):
+        lst = v("SNL", 8 * d, 8 * d + 8)
+        if d:
+            act(v("YY", GH * d, GH * d + GH), ind(v("TW", 0, E), lst))
+        cp(ind(v("TW", 0, E), lst), v("VV", GH * d, GH * d + GH))
+    dma("s", [(v("TW", 2944, 3456, p=slice(row, 128, 16)), v("TW", 0, 512, p=slice(row + 3, 128, 16))) for row in (5, 6)])
     ts(col(19), col(0), 16.0, A.mult, 15.0, A.add)
-    p40, p24 = slice(0, 40), slice(0, 24)
-    ts(v("FQ", p=p40), v("JF", p=p40), v("PC", 76, 77, p=p40), A.is_equal)
-    cp(v("QF", 0, 768, p=p40), v("QI", 0, 768, p=p40))
+    p16, p24 = slice(0, 16), slice(0, 24)
+    ts(v("FQ", p=p16), v("JF", p=p16), v("PC", 76, 77, p=p16), A.is_equal)
+    cp(v("QF", 0, 768, p=p24), v("QI", 0, 768, p=p24))
     cp(v("QF", 768, 1280, p=slice(0, 8)), v("QI", 768, 1280, p=slice(0, 8)))
     act(v("I32F", 0, 256), v("I2"))
     act(neg32, ident, scale=-1.0)
     cp(v("REP"), v("JF", 0, 48))
-    ts(col(20), col(1), 16.0, A.mult)
+    ts(v("PI", 8, 9), v("PI", 0, 1), 7, A.bitwise_and)
+    ts(col(36), col(1), 8.0, A.is_ge)
+    ts(col(20), v("PI", 8, 9), 16.0, A.mult, col(36), A.add)
     ts(v("PERM"), v("T48"), col(20), A.add)
     for s in range(3):
         cp(v("CAL", 256 * s, 256 * s + 256), ind(v("CA"), v("PERM", 16 * s, 16 * s + 16)))
@@ -317,69 +352,64 @@ def rank_program(g, core, T, topo):
         ps = slice(0, 8 * j + 8)
         mm([(o, v("FQ", 128 * j + 15 - a, 128 * j + 143 - a, p=ps), v("QF", a, 16 * n, 16, p=ps), a == 0, a == 15) for a in range(16)])
 
-    lists(3, 48, v("PX", 0, 48))
-    lists(4, 48, v("PX", 48, 96))
-    act(v("NTV"), v("PX", 0, 48), scale=-1.0)
-    act(v("KV"), v("PX", 48, 96), AF.Identity, bias=col(30), scale=0.125)
     for s in range(3):
         act(v("TVR", 256 * s, 256 * s + 256), ind(v("NTV"), v("REP", 16 * s, 16 * s + 16)))
         act(v("KVR", 256 * s, 256 * s + 256), ind(v("KV"), v("REP", 16 * s, 16 * s + 16)))
-    sha = v("AG", 0, 1920)
-    act(sha, v("KW", 0, 1920), AF.Identity, bias=col(26), scale=0.0)
+    fill(v("AG"), 1.0)
     fill(v("SH", 0, 128), 0.0)
-    sel(v("SH", 128, 2048), sha, [[-1, 15], [0, 8], [1, 16]], A.is_ge, 0.0, -1, 0, [sent])
-    sel(sha, v("SH", 128, 2048), [[1, 15], [-1, 128]], A.is_equal, 0.0, 1, 1)
-    sel(v("SH", 128, 2048), sha, [[0, 15], [-1, 128]], A.not_equal, -1.0, 0, 1)
+    sel(v("SH", 128, 2048), v("AG"), [[-1, 15], [0, 8], [1, 16]], A.is_ge, 0.0, -1, 0, sent)
+    sel(v("AG"), v("SH", 128, 2048), [[1, 15], [-1, 128]], A.is_equal, 0.0, 1, 1)
+    sel(v("SH", 128, 2048), v("AG"), [[0, 15], [-1, 128]], A.not_equal, -1.0, 0, 1)
 
-    def tk_gather(t, chunks, eng):
-        lst = ("CAL", 256 * t) if t < 3 else ("CL%d" % (t - 3), 0)
+    def tk_gather(s, chunks, eng):
         for c in chunks:
-            src = ind(v("TW"), v(lst[0], lst[1] + 64 * c, lst[1] + 64 * c + 64))
-            (cp if eng == "v" else act)(v("XX", 1024 * c, 1024 * c + 1024), src)
+            (cp if eng == "v" else act)(v("XX%d" % s, 1024 * c, 1024 * c + 1024), ind(v("TW", 0, 2944), v("CAL", 256 * s + 64 * c, 256 * s + 64 * c + 64)))
 
     def diff(bank, c0, src):
         o = v(bank, c0, c0 + 255)
         mm([(o, pos32, v(src, 0, 255), True, False), (o, neg32, v(src, 1, 256), False, True)])
 
-    def prep(t):
-        s = t % 3
+    def extract(t, halves, bank, b0, f, pre=None, close=True):
+        c0, c1 = 128 * min(halves), 128 * max(halves) + 128
+        if pre:
+            mm([(v(bank, b0 + c0, b0 + c1), pos32, v(pre, 256 * (t % 3) + c0, 256 * (t % 3) + c1), True, False)])
+        for h in halves:
+            for a0_ in (0, 8):
+                mm([(v(bank, b0 + 128 * h, b0 + 128 * h + 128), win(f, a), v("XX%d" % (t % 3), 2048 * h + 128 * a, 2048 * h + 128 * a + 128),
+                     a == 0 and not pre, a == 15 and close and (not pre or h == halves[-1])) for a in range(a0_, a0_ + 8)])
 
-        def extract(bank, c0, f, pre):
-            o = v(bank, c0, c0 + 256)
-            if pre:
-                mm([(o, pos32, v(pre, 256 * s, 256 * s + 256), True, False)])
-            for q4 in (0, 2, 1, 3):
-                mm([(o, win(f, a), v("XX", 256 * a, 256 * a + 256) if t < 3 else v("XX", a, 4096, 16), a == 0 and not pre, a == 15 and f != "FK") for a in range(4 * q4, 4 * q4 + 4)])
-
-        extract("PT", 0, "FT", "TVR")
-        extract("PK", 0, "FK", "KVR")
-        extract("PM", 0, "FM", None)
-        act(v("LAG"), v("PT", 0, 256), AF.Abs)
-        act(v("YI"), v("LAG"), AF.Identity, bias=col(29), scale=1.0 / 32)
-        mm([(v("PK", 0, 256), ident, v("YI"), False, True)])
-        ts(v("BNL"), v("PK", 0, 256), 64.0, A.mult)
-        act(v("SS"), v("PK", 0, 256))
-        cp(v("ML"), v("PM", 0, 256))
-        act(v("MT"), v("PM", 0, 256))
-        if t < 2:
-            extract("PM", 256, "FC", None)
-            act(v("CT%d" % t), v("PM", 256, 512))
-        rl = "RL%d" % (t % 2)
-        diff("PT", 256, "LAG")
-        ts(v(rl, 1, 256), v("PT", 256, 511), 1023.0, A.add)
-        fill(v(rl, 0, 256, 16), 2047)
-        ts(v("EL%d" % (t % 2)), v("LAG", 15, 256, 16), 1023.0, A.add)
+    def prep(t, halves=(1, 0), bt="PT", bk="PK", bm="PM"):
+        c0, c1 = 128 * min(halves), 128 * max(halves) + 128
+        extract(t, halves, bt, 0, "FT", "TVR")
+        extract(t, halves, bk, 0, "FK", "KVR", False)
+        act(v("LAG", c0, c1), v(bt, c0, c1), AF.Abs)
+        act(v("YI", c0, c1), v("LAG", c0, c1), AF.Identity, bias=col(29), scale=1.0 / 32)
+        extract(t, halves, bm, 0, "FM")
+        mm([(v(bk, c0, c1), ident, v("YI", c0, c1), False, True)])
+        ts(v("BNL", c0, c1), v(bk, c0, c1), 64.0, A.mult)
+        cp(v("ML", c0, c1), v(bm, c0, c1))
+        act(v("SS", c0, c1), v(bk, c0, c1))
 
     def prep2(t):
+        extract(t, (1, 0), "PM", 256, "FR")
+        act(v("MT"), v("PM", 256, 512))
         diff("PX", 0, "MT")
         if t < R - 1:
             diff("PX", 256, "SS")
         ts(v("PX", 15, 256, 16), v("MT", 15, 256, 16), float(HOLE), A.subtract)
         if t < R - 1:
             ts(v("PX", 271, 512, 16), v("SS", 15, 256, 16), E / 64.0, A.subtract)
+        rl = "RL%d" % (t % 2)
+        diff("PT", 256, "LAG")
+        ts(v(rl, 1, 256), v("PT", 256, 511), 1023.0, A.add)
+        fill(v(rl, 0, 256, 16), 2047)
+        ts(v("EL%d" % (t % 2)), v("LAG", 15, 256, 16), 1023.0, A.add)
+        if t < 2:
+            extract(t, (1, 0), "PT", 0, "FC")
+            act(v("CT%d" % t), v("PT", 0, 256))
 
-    def k_gather():
-        for c in range(3, -1, -1):
+    def k_gather(chunks=(3, 2, 1, 0)):
+        for c in chunks:
             act(v("KG", 1024 * c, 1024 * c + 1024), ind(v("KW"), v("BNL", 64 * c, 64 * c + 64)))
 
     def r_gather(t):
@@ -389,9 +419,16 @@ def rank_program(g, core, T, topo):
 
     def weights(t, b0, b1):
         pr = "PR%d_" % (t % 2)
-        for c0 in range(16 * b1 - 64, 16 * b0 - 1, -64):
-            c1 = c0 + 64
-            tt(v(pr, 16 * c0, 16 * c1), ind(v("AW"), v("ML", c0, c1)), v("KG", 16 * c0, 16 * c1), A.mult)
+        for c1 in range(16 * b1, 16 * b0, -64):
+            c0 = max(c1 - 64, 16 * b0)
+            cut = min(max(32 * SPLIT[t], c0), c1)
+            if cut < c1:
+                tt(v(pr, 16 * cut, 16 * c1), ind(v("AW", 0, OWN + E), v("ML", cut, c1)), v("KG", 16 * cut, 16 * c1), A.mult)
+            for c in range(cut - 32, c0 - 1, -32):
+                bank = v("PR%d" % (c // 32 % 2), 0, 512)
+                act(v("AS", 16 * c, 16 * c + 512), ind(v("AW", 0, OWN + E), v("ML", c, c + 32)))
+                mm([(bank, ident, v("AS", 16 * c, 16 * c + 512), True, True)])
+                tt(v(pr, 16 * c, 16 * c + 512), bank, v("KG", 16 * c, 16 * c + 512), A.mult)
             mm([(v("PW", c0, c1), win("F0", a), v(pr, 16 * c0 + a, 16 * c1, 16), a == 0, a == 15) for a in range(16)])
 
     def elect(px0, bank, sfx, xs, lb, scale, dump, c0=0, c1=256):
@@ -402,12 +439,8 @@ def rank_program(g, core, T, topo):
         ts(v("EE" + sfx, c0, c1), v(bank, px0 + c0, px0 + c1), 0.0, A.is_equal, dump, A.mult)
         scan(v("OF" + sfx, c0, c1), v("EE" + sfx, c0, c1), v(lb, c0, c1), 0.0, A.max, A.min)
 
-    def scatter(window, lst, val, c0, b):
-        cp(ind(window, v(lst, 2 * b, 2 * b + 1)), v(val, c0 + 16 * b, c0 + 16 * b + 16))
-
-    def raised(window, lc, oh, nv, cap, b0=0, b1=16):
-        tt(v(nv, 16 * b0, 16 * b1), ind(window, v(lc, b0, b1)), v("OH", oh + 16 * b0, oh + 16 * b1), A.add)
-        ts(v(nv + "2", 16 * b0, 16 * b1), v(nv, 16 * b0, 16 * b1), cap, A.min)
+    def scatter(window, lst, val, oh, b):
+        tt(ind(window, v(lst, 2 * b, 2 * b + 1)), v(val, 16 * b, 16 * b + 16), v("OH", oh + 16 * b, oh + 16 * b + 16), A.add)
 
     def lam(t):
         for a in range(16):
@@ -416,85 +449,95 @@ def rank_program(g, core, T, topo):
         dma("s", [(T.yl[:, 256 * t:256 * t + 256], v("LAM"))])
 
     def candidates(t):
-        ct, lp = "CT%d" % t, v("LP", 256 * t, 256 * t + 256)
+        ct, own = "CT%d" % t, v("TW", 256 * t, 256 * t + 256)
         tt(v("KEY"), v("PW", 0, 256), v("KF"), A.add)
         scan(v("MN"), v("BSEG"), v("KEY"), 0.0, A.add, A.min)
-        diff("PK", 256, ct)
-        ts(v("PK", 271, 512, 16), v(ct, 15, 256, 16), 1.0, A.add)
-        tt(v("W2"), v("HIT"), v("PK", 256, 512), A.mult)
+        diff("PD_", 256, ct)
+        ts(v("PD_", 271, 512, 16), v(ct, 15, 256, 16), 4096.0, A.subtract)
+        tt(v("W2"), v("HIT"), v("PD_", 256, 512), A.mult)
         scan(v("W1"), v("SEG"), v("W2"), 0.0, A.mult, A.add)
-        tt(v("W3"), ind(v("W1"), v("REP15")), v("DG"), A.mult)
-        mm([(v("PK", 256, 512), v("GO"), v("W3"), True, True)])
-        ts(v("SM", 0, 16), v("W1", 15, 256, 16), 0.0, A.is_equal, 4096.0, A.mult)
-        tt(v("SM", 16, 32), v("SM", 0, 16), v("W1", 15, 256, 16), A.add)
-        ts(v("IX"), v("SM", 16, 32), 1.0, A.subtract, float(E), A.min)
-        act(v("W4"), v("PK", 256, 512), AF.Relu, bias=col(26), scale=-1.0)
-        act(v("W5"), v("PK", 256, 512), AF.Relu, bias=col(27), scale=1.0)
-        tt(v("W6"), v("W4"), lp, A.mult)
-        tt(lp, v("W6"), v("W5"), A.add)
-        tt(v("W2"), ind(v("LP"), v("IX")), v("DG"), A.mult)
-        scan(v("W1"), v("SEG"), v("W2"), 0.0, A.mult, A.add)
-        ts(v("SM", 32, 48), v("W1", 15, 256, 16), 0.0, A.min, 4096.0, A.mult)
-        tt(v("W3"), ind(v("W1"), v("REP15")), v(ct), A.subtract)
-        tt(v("SM", 48, 64), v("SM", 32, 48), v("MN", 15, 256, 16), A.add)
-        tt(v("W4"), ind(v("SM", 48, 64), v("REP", 0, 16)), v("KEY"), A.is_equal)
-        tt(v("W5"), v("W3"), v("W4"), A.mult)
-        o = v("PK", 256, 512)
-        mm([(o, pos32, v(ct), True, False), (o, pos32, v("W5"), False, True)])
-        cp(v("CL%d" % t), o)
+        tt(v("SM", 0, 16), v("W1", 15, 256, 16), v("PB", 32 + 16 * t, 48 + 16 * t), A.min)
+        ts(v("IX1"), v("SM", 0, 16), 4096.0, A.add)
+        ts(v("IX2"), v("W1", 15, 256, 16), 4096.0, A.add, 2943.0, A.min)
+        act(v("NX1"), ind(v("TW"), v("IX1")))
+        mm([(v("PD_", 256, 512), v("K89"), own, True, False), (v("PD_", 256, 512), v("P56"), v("NX1"), False, True)])
+        act(own, v("PD_", 256, 512))
+        act(v("NX2"), ind(v("TW"), v("IX2")))
+        up_ = v("PD_", 256, 272)
+        mm([(up_, win("FL", a), v("NX2", a, 256, 16), a == 0, a == 15) for a in range(16)])
+        ts(v("MI", 0, 16), v("MN", 15, 256, 16), 16.0, A.mult)
+        ts(v("MI", 16, 32), v("MI", 0, 16), 15, A.bitwise_and)
+        tt(v("SM", 32, 48), v("MI", 16, 32), v("PB", 0, 16), A.add)
+        ts(v("SM", 48, 64), up_, 4000.0, A.is_gt, 8192.0, A.mult)
+        tt(v("SM", 64, 80), v("SM", 32, 48), v("SM", 48, 64), A.add)
+        tt(v("SM", 80, 96), v("SM", 64, 80), v("PB", 16, 32), A.min)
+        cp(v("PL"), v("SM", 80, 96))
+        ts(v("NC"), up_, 2943.0, A.min)
+        act(v("NX"), ind(v("TW"), v("NC")))
+        cp(ind(v("XX%d" % t), v("PL")), v("NX"))
 
-    tk_gather(0, (0, 1), "a")
-    tk_gather(0, (2, 3), "v")
-    prep(0)
-    k_gather()
+    tk_gather(0, (3,), "a")
+    tk_gather(0, (2,), "v")
+    tk_gather(0, (1,), "a")
+    tk_gather(0, (0,), "v")
+    prep(0, (1,))
+    k_gather((3, 2))
+    prep(0, (0,), "PR0", "PR1", "PD_")
+    k_gather((1, 0))
+    act(v("YY", NG, 2 * NG), ind(v("TW", 0, E), v("SNL")))
     ts(col(21), col(0), 16.0, A.mult, -256.0, A.add)
-    ts(v("GC", p=p24), v("J16", p=p24), v("PC", 84, 85, p=p24), A.is_equal)
-    lists(0, 80, v("PD_", 0, 80))
-    lists(1, 48, v("PD_", 80, 128))
-    act(v("UL"), v("PD_", 0, 80), scale=1.0 / 256)
-    act(v("BGL"), v("PD_", 80, 128))
-    for h, bank in enumerate(("PR0", "PR1")):
-        mm([(v(bank, 0, 384), v("GC", p=p24), v("QF", 384 * h, 384 * h + 384, p=p24), True, True)])
+    ts(v("GK", p=p24), v("J16", p=p24), v("PC", 84, 85, p=p24), A.is_equal)
+    lists(0, 80, v("PW", 0, 80))
+    lists(1, 48, v("PW", 80, 128))
+    act(v("UL"), v("PW", 0, 80), scale=1.0 / 256)
+    act(v("BGL"), v("PW", 80, 128))
+    for h, bank in enumerate(("PM", "PX")):
+        mm([(v(bank, 0, 384), v("GK", p=p24), v("QF", 384 * h, 384 * h + 384, p=p24), True, True)])
         ts(v("OH", 384 * h, 384 * h + 384), v(bank, 0, 384), col(1), A.is_equal)
+    act(v("CAPA"), v("OH"), AF.Identity, bias=col(28), scale=-1.0)
+    act(v("CAPK"), v("OH"), AF.Identity, bias=col(31), scale=-1.0)
     ts(v("SEG"), v("KI"), 0.0, A.not_equal)
     fill(v("LB"), 1.0e6)
     fill(v("LBK"), 1.0e6)
-    ts(col(22), col(1), float(DUMPA), A.add)
-    ts(col(23), col(1), float(DUMPB), A.add)
+    ts(col(22), col(1), float(DUMP), A.add)
     ts(col(24), col(1), float(E), A.add)
     prep2(0)
     mm([(v("PD_", 0, 112), win("FM", a), v("YY", a, 1792, 16), a == 0, a == 15) for a in range(16)])
     act(v("YU"), v("PD_", 0, 112))
     mm([(v("PD_", 0, 112), roll32, v("YU"), True, True)])
-    cp(v("MSN"), v("YU", 56, 112))
-    ts(v("SIX"), v("JF", 0, 56), 16.0, A.mult, col(1), A.add)
-    ts(v("YT", 0, 56), v("PD_", 0, 56), float(GUN), A.is_ge)
-    ts(v("YT", 56, 112), v("PD_", 0, 56), float(GUN - NG), A.subtract)
-    ts(v("LST"), v("PD_", 56, 112), float(GUN - NG), A.subtract)
+    ts(v("YT", 0, 56), v("PD_", 0, 56), float(NG), A.is_lt)
+    ts(v("YT", 56, 112), v("PD_", 0, 56), float(NG), A.add)
+    ts(v("LST"), v("PD_", 56, 112), float(NG), A.add)
     tt(v("YT", 112, 168), v("YT", 0, 56), v("YT", 56, 112), A.mult)
-    tt(v("YT", 0, 56), v("YT", 112, 168), v("SIX"), A.max)
+    tt(v("YT", 0, 56), v("YT", 112, 168), v("PD_", 56, 112), A.max)
     cp(v("PRV"), v("YT", 0, 56))
     be = v("BE", 0, 1)
     ts(v("BT", 0, 1), be, -1.0 / 6, A.mult, 0.5, A.add)
     ts(v("BT", 4, 5), v("BT", 0, 1), be, A.mult, -1.0, A.add)
     ts(v("BT", 8, 9), v("BT", 4, 5), be, A.mult, 1.0, A.add)
-    act(v("SC", 0, 2048), v("AW", 0, E), AF.Identity, bias=v("BT", 8, 9), scale=0.0)
-    for c in range(0, 2048, 512):
-        scan(v("RG1", c, c + 512), v("SC", c, c + 512), v("SC", c, c + 512), v("RG1", c - 1, c) if c else 1.0, A.mult, A.min)
-    run("v", lambda: g.vector.reciprocal(T.BT[:, 12:13], T.RG1[:, 1023:1024]), v("BT", 12, 13), [v("RG1", 1023, 1024)], 12.0)
-    act(v("RT", 0, 2047), v("RG1", 0, 2047), scale=v("BT", 12, 13))
+    act(v("SC", 0, 512), v("TVR", 0, 512), AF.Identity, bias=v("BT", 8, 9), scale=0.0)
+    mid = v("RT", 1024, 1536)
+    scan(mid, v("SC", 0, 512), v("SC", 0, 512), 1.0, A.mult, A.min)
+    run("v", lambda: g.vector.reciprocal(T.BT[:, 12:13], T.RT[:, 1535:1536]), v("BT", 12, 13), [v("RT", 1535, 1536)], 200.0)
+    tt(v("BT", 16, 17), v("BT", 12, 13), v("BT", 12, 13), A.mult)
+    act(v("RT", 0, 512), mid, scale=v("BT", 16, 17))
+    act(v("RT", 512, 1024), mid, scale=v("BT", 12, 13))
+    act(v("RT", 1536, 2048), mid, scale=v("RT", 1535, 1536))
     fill(v("RT", 2047, 2048), 0.0)
-    ts(v("REP15"), v("JF", 0, 16), 16.0, A.mult, 15.0, A.add)
     ts(col(25), col(1), 256.0, A.mult, 15.0, A.add)
     ts(v("LAML"), v("JF", 0, 16), 16.0, A.mult, col(25), A.add)
-    ts(v("DG"), v("KI"), col(1), A.is_equal)
+    ts(col(37), col(1), 128.0, A.mult)
+    ts(v("PB", 0, 16), v("PB", 0, 16), col(37), A.add)
+    ts(col(38), col(1), 4096.0, A.add)
+    ts(v("PB", 16, 32), v("JF", 0, 16), 16.0, A.mult, col(38), A.add)
+    for t in range(2):
+        ts(v("PB", 32 + 16 * t, 48 + 16 * t), v("PB", 16, 32), 2944.0 + 256 * t - 8192.0, A.add)
     act(v("KF"), v("KI"), scale=1.0 / 16)
     ts(v("BSEG"), v("KI"), 0.0, A.is_equal, 1.0e6, A.mult)
-    ts(v("GO"), v("J16"), col(2), A.is_equal)
-    fill(v("LP", E, E + 16), -1)
+    fill(v("XX0", 4096, 4352), 0.0)
+    fill(v("XX1", 4096, 4352), 0.0)
 
-    act(v("INC", GHO, GHO + NG), v("HI"), scale=0.0)
-    own = v("AW", 0, GHO)
+    raises = v("SW")
     first_round = len(ops)
     for t in range(R):
         s = t % 3
@@ -503,63 +546,64 @@ def rank_program(g, core, T, topo):
             c0, c1 = 16 * b0, 16 * b1
             scan(v("CUM", c0, c1), v("SEG", c0, c1), v("PW", c0, c1), 0.0, A.mult, A.add)
             tt(v("S1", b0, b1), v("CUM", c0 + 15, c1, 16), v("BGL", 16 * s + b0, 16 * s + b1), A.add)
-            tt(v("THR", b0, b1), v("S1", b0, b1), v("UL", 16 * t + b0, 16 * t + b1), A.mult)
-            tt(v("HIT", c0, c1), ind(v("THR", b0, b1), v("REP", 0, b1 - b0)), v("CUM", c0, c1), A.is_lt)
+            tt(v("THR", 8 * b0, 7 * b0 + b1), v("S1", b0, b1), v("UL", 16 * t + b0, 16 * t + b1), A.mult)
+            tt(v("HIT", c0, c1), ind(v("THR", 8 * b0, 7 * b0 + b1), v("REP", 0, b1 - b0)), v("CUM", c0, c1), A.is_lt)
             elect(0, "PD_", "", "XS", "LB", 1.0, col(22), c0, c1)
+            ts(v("L1C", b0, b1), v("XS", c0 + 15, c1, 16), float(HOLE), A.add)
             cp(v("L1", 2 * b0, 2 * b1, 2), v("OF", c0 + 15, c1, 16))
-            ts(v("L2C", b0, b1), v("OF", c0 + 15, c1, 16), col(23), A.min)
-            ts(v("L2", 2 * b0, 2 * b1, 2), v("OF", c0 + 15, c1, 16), col(23), A.min)
-            raised(own, "L2C", 256 * s, "NV", 15.0, b0, b1)
-        for b in range(15, -1, -1):
-            scatter(v("INC"), "L1", "OH", 256 * s, b)
-            scatter(own, "L2", "NV2", 0, b)
-        exchange("INC", GHO, "BUF", NG, -1, "h1")
-        act(v("XB"), ind(own, v("MSN")))
-        through("BUF", 0, [(roll, "XB", 0)])
+            tt(v("NV", c0, c1), ind(v("AW", OWN, OWN + RWN), v("L1C", b0, b1)), v("CAPA", 256 * s + c0, 256 * s + c1), A.min)
+            for b in range(b1 - 1, b0 - 1, -1):
+                scatter(raises, "L1", "NV", 256 * s, b)
+        sent, came = exchange("SW", IGH, "BUF", NG, -1, calls=X1)
+        through("BUF", 0, [(ident, "GN", 0), (roll, "SW", IGUN)])
+        if t < R - 1:
+            dma("s", [(v("AW", OWN, OWN + E), v("SW", 0, E))], after=sent, lat=3000.0)
         for d in range(7):
             c = NG + GH * d
             tt(v("BUF", c, c + GH), ind(v("BUF", 0, c), v("PRV", 8 * d, 8 * d + 8)), v("BUF", c, c + GH), A.add)
         if t < R - 1:
-            ts(v("GN", 0, 640), ind(v("BUF", 0, 2 * NG), v("LST", 0, 40)), 15.0, A.min)
-            act(v("XB", 640, NG), ind(v("BUF", 0, 2 * NG), v("LST", 40, 56)), AF.Relu, bias=col(28), scale=-1.0)
-            act(v("GN", 640, NG), v("XB", 640, NG), AF.Identity, bias=col(28), scale=-1.0)
-            exchange("GN", 0, "AW", GHO, 1, "h2")
+            ts(v("GN", 0, 512), ind(v("BUF", 0, 2 * NG), v("LST", 0, 32)), 15.0, A.min)
+            last = act(v("XB"), ind(v("BUF", 0, 2 * NG), v("LST", 32, 56)), AF.Relu, bias=col(28), scale=-1.0)
+            act(v("GN", 512, NG), v("XB"), AF.Identity, bias=col(28), scale=-1.0)
+            sent, came = exchange("GN", 0, "AW", GHO, 1, after=[last])
             through("AW", GUN, [(unroll, "GN", 0)])
-            tk_gather(t + 1, range(4), "a")
+            iota(v("SW", IGUN, DUMP), [[0, 2 * NG]], 0, 0, after=sent[-1:])
             elect(256, "PW", "K", "XK", "LBK", 64.0, col(24))
-            cp(v("LKC"), v("OFK", 15, 256, 16))
+            ts(v("LKC"), v("XK", 15, 256, 16), 64.0, A.mult, float(E), A.add)
             cp(v("LK", 0, 32, 2), v("OFK", 15, 256, 16))
-            raised(v("KW"), "LKC", 256 * s, "NW", 7.0)
+            tt(v("NW"), ind(v("KW"), v("LKC")), v("CAPK", 256 * s, 256 * s + 256), A.min)
             for b in range(15, -1, -1):
-                scatter(v("KW"), "LK", "NW2", 0, b)
+                scatter(v("KW"), "LK", "NW", 256 * s, b)
+            if t < 2:
+                tk_gather(t + 1, range(4), "a")
             prep(t + 1)
             k_gather()
-            act(v("INC", GHO, GHO + NG), v("HI"), scale=0.0)
+            if t < 2:
+                candidates(t)
+            r_gather(t)
             prep2(t + 1)
         else:
+            r_gather(t)
             for c in range(4):
                 bank = v("PR%d" % (c % 2), 0, 512)
-                mm([(bank, roll, v("AW", 512 * c, 512 * c + 512), True, True)])
+                mm([(bank, roll, v("SW", 512 * c, 512 * c + 512), True, True)])
                 act(v("BUF", 2 * NG + 512 * c, 2 * NG + 512 * c + 512), bank)
-            for c0, c1, eng in ((0, 640, "v"), (640, 1024, "a"), (1024, 1664, "v"), (1664, 2048, "a")):
+            for c0, c1, eng in FINAL:
                 o, src = v("RG1", c0, c1), ind(v("BUF"), v("MAPL", c0 // 16, c1 // 16))
                 if eng == "v":
                     ts(o, src, 15.0, A.min)
                 else:
                     act(v("RG1", E + c0, E + c1), src, AF.Relu, bias=col(28), scale=-1.0)
                     act(o, v("RG1", E + c0, E + c1), AF.Identity, bias=col(28), scale=-1.0)
-                dma("s" if eng == "v" else "a", [(T.ya[0:112, c0:c1], v("RG1", c0, c1, p=slice(16, 128))), (T.ya[112:128, c0:c1], v("RG1", c0, c1, p=slice(0, 16)))])
-        if t < 2:
-            candidates(t)
-        r_gather(t)
+                dma("s" if eng == "v" else "a", [(T.ya[0:112, c0:c1], v("RG1", c0, c1, p=up)), (T.ya[112:128, c0:c1], v("RG1", c0, c1, p=down))])
         lam(t)
         if t == 2:
             mm([(v("PD_", 0, 128), win("FM", a), v("TW", a, E, 16), a == 0, a == 15) for a in range(16)])
             act(v("W1", 0, 128), v("PD_", 0, 128))
             mm([(v("PD_", 0, 128), roll32, v("W1", 0, 128), True, True)])
-            ts(v("W2", 0, 128), v("PD_", 0, 128), float(GUN), A.is_lt, float(GUN + NG), A.mult)
+            ts(v("W2", 0, 128), v("PD_", 0, 128), float(NG), A.is_lt, float(NG), A.mult)
             tt(v("W3", 0, 128), v("W2", 0, 128), v("PD_", 0, 128), A.add)
-            ts(v("MAPL"), v("W3", 0, 128), float(GUN - NG), A.subtract)
+            cp(v("MAPL"), v("W3", 0, 128))
 
     n = len(ops)
     succ = [[] for _ in range(n)]
@@ -570,7 +614,9 @@ def rank_program(g, core, T, topo):
             succ[d].append(i)
 
     def gap(d, i):
-        return 0.0 if ops[i]["kind"] == "r" or ops[i]["q"] == ops[d]["q"] == "t" else ops[d]["lat"] + SYNC
+        if ops[i]["kind"] == "r" or ops[i]["q"] == ops[d]["q"] == "t" or d in ops[i]["behind"]:
+            return 0.0
+        return ops[d]["lat"] + SYNC
 
     level = [0.0] * n
     for i in range(n - 1, -1, -1):
@@ -632,13 +678,56 @@ def rank_program(g, core, T, topo):
 
     if n not in ORDER:
         pred = [sorted(o["deps"]) for o in ops]
-        key, best = [-x for x in level], None
-        for _ in range(PASSES):
+        fgap = [[(j, gap(i, j)) for j in succ[i]] for i in range(n)]
+        bgap = [[(d, gap(d, i)) for d in pred[i]] for i in range(n)]
+
+        def fit(key, npred, out, head):
+            left, est, start, busy = list(npred), list(head), [0.0] * n, {q: [] for q in Q}
+            ready = [i for i in range(n) if not left[i]]
+            while ready:
+                i = min(ready, key=lambda j: key[j])
+                ready.remove(i)
+                t0, c, q = est[i], ops[i]["cost"], ops[i]["q"]
+                if q is not None:
+                    line_ = busy[q]
+                    lo, hi = 0, len(line_)
+                    while lo < hi:
+                        mid_ = (lo + hi) // 2
+                        if line_[mid_][1] <= t0:
+                            lo = mid_ + 1
+                        else:
+                            hi = mid_
+                    while lo < len(line_) and line_[lo][0] < t0 + c:
+                        t0 = max(t0, line_[lo][1])
+                        lo += 1
+                    line_.insert(lo, (t0, t0 + c))
+                start[i] = t0
+                for j, w in out[i]:
+                    est[j] = max(est[j], t0 + c + w)
+                    left[j] -= 1
+                    if not left[j]:
+                        ready.append(j)
+            return start
+
+        key, best, rng = [-x for x in level], None, np.random.default_rng(1)
+        for _ in range(PASS0):
             fw = place(key, pred, succ, gap)
             if best is None or fw[0] < best[0]:
-                best = fw
+                best = (fw[0], fw[1], [fw[2][i] - ops[i]["cost"] for i in range(n)])
             bw = place([-x for x in fw[2]], succ, pred, lambda d, i: gap(i, d))
-            key = [MIX * -bw[2][i] + (1 - MIX) * key[i] for i in range(n)]
+            noise = rng.random(n) * NOISE0
+            key = [MIX * -bw[2][i] + (1 - MIX) * key[i] + float(noise[i]) for i in range(n)]
+        if best:
+            key = best[2]
+        for it in range(PASSES):
+            fw = fit(key, [len(x) for x in pred], fgap, [0.0] * n)
+            span = max(fw[i] + ops[i]["cost"] + ops[i]["lat"] for i in range(n))
+            if best is None or span < best[0]:
+                best = (span, sorted(range(n), key=lambda i: (fw[i], i)), fw)
+            base = fw if span <= best[0] + SLIP else best[2]
+            bw = fit([-(base[i] + ops[i]["cost"]) for i in range(n)], [len(x) for x in succ], bgap, [ops[i]["lat"] if not succ[i] else 0.0 for i in range(n)])
+            noise = rng.random(n) * NOISE
+            key = [-(bw[i] + ops[i]["cost"]) + float(noise[i]) for i in range(n)]
         ORDER[n] = best
     order = ORDER[n][1]
 
@@ -661,7 +750,7 @@ def rank_program(g, core, T, topo):
             continue
         need = {}
         for d in o["deps"]:
-            if q == ops[d]["q"] == "t":
+            if q == ops[d]["q"] == "t" or d in o["behind"]:
                 continue
             sem, val = token[d]
             need[sem] = max(need.get(sem, 0), val)
@@ -669,7 +758,7 @@ def rank_program(g, core, T, topo):
             wait(q, sem, need[sem])
         if o["kind"] == "x":
             o["calls"][0]()
-            sem, k = "ls", o["n"]
+            sem, k = o["sem"], o["n"]
         elif o["kind"] == "d":
             sem, k = o["sem"], 16 * len(o["calls"])
             for c in o["calls"]:

@@ -7,29 +7,30 @@ GUN, GHO, OWN = 0, 896, 1792
 HOLE, IGUN, IGH, DUMP, RWN = 2048, 2112, 3008, 3904, 3920
 F32, BF, I32, U16, F16 = "float32", "bfloat16", "int32", "uint16", "float16"
 SB = {
-    "AW": (OWN + RWN, BF), "SW": (RWN, BF), "TW": (3456, BF), "KW": (2064, BF), "BUF": (3840, BF), "GN": (NG, BF), "XB": (384, BF),
-    "XX0": (4352, BF), "XX1": (4352, BF), "XX2": (4096, BF), "KG": (4096, BF), "PR0_": (4096, BF), "PR1_": (4096, BF), "AS": (3072, BF),
+    "AW": (OWN + E + 16, BF), "SW": (RWN, BF), "TW": (3456, BF), "KW": (2064, BF), "KS": (2064, BF), "BUF": (3840, BF), "GN": (NG, BF), "XB": (384, BF),
+    "XX0": (4352, BF), "XX1": (4352, BF), "XX2": (4096, BF), "KG": (4096, BF), "PR0_": (4096, BF), "PR1_": (4096, BF), "PR2_": (4096, BF), "AS": (3072, BF),
     "RG0": (4096, F32), "RG1": (4096, F32), "SC": (4096, F32), "RT": (2048, F32),
     "GT": (NG, BF), "GC": (NG, BF), "VV": (NG, BF), "YY": (1792, BF), "TR": (E, BF), "GS": (NG, BF), "SL": (448, BF), "HI": (448, BF), "LO": (448, BF), "AG": (1920, BF),
     "CA": (768, I32), "CAL": (768, U16), "SN": (56, I32), "SNR": (56, I32), "SNL": (56, U16), "SRL": (56, U16),
     "SI": (384, I32), "S2": (896, I32), "S3": (1024, BF),
-    "QI": (1280, I32), "QF": (1280, F32), "JF": (272, F32), "FQ": (272, F32), "KI": (256, F32), "J16": (128, F32), "PI": (16, I32), "PC": (192, F32),
+    "QI": (1280, I32), "QF": (1280, F16), "JF": (272, F32), "FQ": (272, BF), "KI": (256, F32), "J16": (128, F32), "PI": (16, I32), "PC": (192, F32),
     "F0": (144, BF), "FT": (144, BF), "FK": (144, BF), "FM": (144, BF), "FC": (144, BF), "FR": (144, BF), "FL": (144, BF),
     "I2": (256, BF), "D11": (128, BF), "D12": (128, BF), "K89": (128, BF), "P56": (128, BF), "I32F": (384, F32),
-    "GK": (128, F32), "SH": (2048, BF), "KF": (256, F32), "SEG": (256, F32), "BSEG": (256, F32),
-    "REP": (48, U16), "LAML": (16, U16), "PERM": (48, U16), "T48": (48, F32), "PB": (64, F32),
-    "UL": (80, F32), "BGL": (48, F32), "NTV": (48, F32), "KV": (48, F32), "TVR": (768, F32), "KVR": (768, F32), "OH": (768, BF), "CAPA": (768, BF), "CAPK": (768, BF),
+    "GK": (128, BF), "SH": (2048, BF), "KF": (256, F32), "SEG": (256, F32), "BSEG": (256, F32),
+    "REP": (48, U16), "REP3": (16, U16), "LAML": (16, U16), "PERM": (48, U16), "T48": (48, F32), "PB": (64, F32),
+    "UL": (240, F32), "BGL": (48, F32), "NTV": (48, F32), "KV": (48, F32), "TVR": (768, F32), "KVR": (768, F32), "OH": (768, BF), "CAPA": (768, BF), "CAPK": (768, BF),
     "YU": (112, F32), "YT": (168, F32), "PRV": (56, U16), "LST": (56, U16), "MAPL": (128, U16), "BE": (8, F32), "BT": (24, F32),
     "LAG": (256, F32), "YI": (256, BF), "SS": (256, F32), "MT": (256, F32), "CT0": (256, F32), "CT1": (256, F32),
-    "ML": (256, U16), "BNL": (256, U16), "RL0": (256, U16), "RL1": (256, U16), "EL0": (16, U16), "EL1": (16, U16), "E150": (256, F32), "E151": (256, F32),
-    "CUM": (256, F32), "S1": (16, F32), "THR": (128, F32), "HIT": (256, F32), "PD": (256, F32), "PDK": (256, F32), "XS": (256, F16), "XK": (256, F16),
+    "ML": (256, U16), "BNL": (256, U16), "RL0": (256, U16), "RL1": (256, U16), "RL2": (256, U16), "EL0": (16, U16), "EL1": (16, U16), "EL2": (16, U16),
+    "E150": (256, F32), "E151": (256, F32),
+    "CUM": (768, F32), "THR": (128, F32), "HIT": (256, F32), "PD": (256, F32), "PDK": (256, F32), "XS": (256, F16), "XK": (256, F16),
     "LB": (256, F32), "LBK": (256, F32), "EE": (256, F32), "EEK": (256, F32), "OF": (256, F32), "OFK": (256, F32),
     "L1": (32, U16), "L1C": (16, U16), "LK": (32, U16), "LKC": (16, U16), "NV": (256, BF), "NW": (256, BF), "NX": (256, BF), "NX1": (256, BF), "NX2": (256, BF),
     "LAM": (256, F32), "KEY": (256, F32), "MN": (256, F32), "W1": (256, F32), "W2": (256, F32), "W3": (256, F32),
     "SM": (96, F32), "MI": (32, I32), "IX1": (16, U16), "IX2": (16, U16), "PL": (16, U16), "NC": (16, U16),
 }
 ALIAS = {"GT": ("KG", 0), "GC": ("KG", NG), "YY": ("XX2", 0), "VV": ("XX2", 1792), "TR": ("PR0_", 0), "GS": ("PR0_", E), "SL": ("PR0_", E + NG),
-         "AG": ("PR1_", 0), "HI": ("PR1_", 1920), "LO": ("PR1_", 1920 + NG), "QF": ("RG0", 0)}
+         "SI": ("QI", 0), "S2": ("QI", 384), "AG": ("PR1_", 0), "HI": ("PR1_", 1920), "LO": ("PR1_", 1920 + NG)}
 PS = ["PW", "PD_", "PR0", "PR1", "PT", "PK", "PX", "PM"]
 POOL, _n = {}, 0
 for _k, (_c, _d) in SB.items():
@@ -40,19 +41,24 @@ SCRATCH = {k: ("sbuf", [128, n], d) for k, (n, d) in SB.items() if k not in POOL
 SCRATCH["UP"] = ("sbuf", [128, _n], U16)
 for _k in PS:
     SCRATCH[_k] = ("psum", [128, 512], F32)
-CALLS = ((1, 2, 3, 4), (5, 6), (7,))
-X1, X2 = CALLS, CALLS
-NX_ = (2 * R + 1) * len(CALLS)
-SEMAPHORES = ["ev", "ea", "et", "eg"] + ["l%d" % _k for _k in range(NX_)] + ["h%d" % _k for _k in range(NX_)] + ["d%d" % _k for _k in range(56)]
+X1 = ((((1, 2), 0, 4),), (((3, 4), 0, 4),), (((5, 6), 0, 4),), (((7,), 0, 8),))
+X2 = ((((1, 2, 3, 4), 0, 2),), (((5, 6), 0, 4),), (((7,), 0, 8),))
+SEMAPHORES = ["ev", "ea", "et", "eg"] + ["l%d" % _k for _k in range(40)] + ["h%d" % _k for _k in range(44)] + ["d%d" % _k for _k in range(46)]
 SIZE = {F32: 4, I32: 4, BF: 2, U16: 2, F16: 2}
 A = AluOpType
 AF = ActivationFunctionType
-CYC, FIX, GATHER, SCATTER, PEC, SYNC, DMALAT, ISSUE, HOP, ROW = 0.95, 50.0, 1.56, 3.8, 0.45, 100.0, 2200.0, 400.0, 1500.0, 35.0
-LOOK, DEPTH, LEAD, LEAD0, SHORT, MIX, ORDER = 0.8, 14, 2500.0, 2500.0, 50.0, 0.6, {}
-PASSES, SLIP, NOISE, PASS0, FIXS, ROWLAT, NOISE0 = 10, 1000.0, 0.0, 5, 20.0, 250.0, 0.0
+CYC, FIX, FIXS, GATHER, SCATTER, PEC, SYNC, DMALAT, ROWLAT, ISSUE, HOP, ROW = 0.87, 50.0, 5.0, 1.8, 3.8, 0.43, 250.0, 2200.0, 250.0, 400.0, 1500.0, 35.0
+PASSES, SLIP, NOISE, MOVES, REACH, FAR, JITTER, TENURE, ORDER = 15, 1000.0, 0.0, 400, 5, 80, 100.0, 60, {}
+PARTS = ((12, 16), (8, 12), (4, 8), (0, 4))
+KPARTS = ((8, 16), (0, 8))
+SPLIT = (0, 0, 2, 2, 2)
+BANKS, WCH, LATE, CH0 = ("PD_", "PM"), 64, 500.0, 8
+FIRST = (("va", (3,)), ("va", (2,)), ("a", (1,)), ("v", (0,)))
+B0 = (("PT", "PK", "PM"), ("PR0", "PR1", "PD_"), ("PT", "PK", "PM"), ("PR0", "PR1", "PD_"))
+VIEWS, SLACK = ((1.56, 250.0), (2.08, 250.0), (1.56, 120.0)), 150.0
+CUT = 512
+SECOND = {1: (3, 2), 3: (1, 0)}
 FINAL = ((0, 416, "v"), (416, 672, "a"), (672, 1088, "v"), (1088, 1344, "a"), (1344, 1792, "v"), (1792, 2048, "a"))
-PARTS = ((8, 16), (0, 8))
-SPLIT = (0, 0, 4, 4, 4)
 
 
 def rank_program(g, core, T, topo):
@@ -60,7 +66,7 @@ def rank_program(g, core, T, topo):
     if rank is None:
         return
     Q = {"v": g.vector, "a": g.scalar, "t": g.tensor, "g": g, "s": g.sync}
-    ops, hist, ndma, nx = [], {}, [0], [0]
+    ops, hist, ndma, nx = [], {}, [0], [0, 0]
 
     def v(name, c0=0, c1=None, step=1, p=None):
         n, sz = (SB[name][0], SIZE[SB[name][1]]) if name in SB else (512, 4)
@@ -105,7 +111,9 @@ def rank_program(g, core, T, topo):
         elif per == 0.5 and any(x["sz"] == 4 and x["n"] > 1 for x in xs):
             per = 1.0
         cost = FIX + CYC * per * o["n"] if q != "v" or per in (GATHER, SCATTER) else FIXS + CYC * max(64, per * o["n"])
-        return add(q, [call], regs(ins) + o.get("off", []), o["reg"], cost, behind=behind)
+        me = add(q, [call], regs(ins) + o.get("off", []), o["reg"], cost, behind=behind)
+        ops[me]["picked"] = CYC * o["n"] if per == GATHER else 0.0
+        return me
 
     def tt(o, a, b, op):
         return run("v", lambda: g.vector.tensor_tensor(ap(o), ap(a), ap(b), op), o, [a, b], 1.0 if a["ps"] or b["ps"] else 2.0)
@@ -115,14 +123,14 @@ def rank_program(g, core, T, topo):
             return run("v", lambda: g.vector.tensor_scalar(ap(o), ap(a), ap(s1), None, op0), o, [a, s1], 0.5)
         return run("v", lambda: g.vector.tensor_scalar(ap(o), ap(a), ap(s1), ap(s2), op0, op1), o, [a, s1, s2], 0.5)
 
-    def cp(o, a):
-        return run("v", lambda: g.vector.tensor_copy(ap(o), ap(a)), o, [a], 0.5)
+    def cp(o, a, behind=()):
+        return run("v", lambda: g.vector.tensor_copy(ap(o), ap(a)), o, [a], 0.5, behind)
 
     def scan(o, d0, d1, init, op0, op1):
         return run("v", lambda: g.vector.tensor_tensor_scan(ap(o), ap(d0), ap(d1), ap(init), op0, op1), o, [d0, d1, init], 0.5)
 
-    def fill(o, c):
-        return run("v", lambda: g.vector.memset(ap(o), c), o, [], 0.5)
+    def fill(o, c, behind=()):
+        return run("v", lambda: g.vector.memset(ap(o), c), o, [], 0.5, behind)
 
     def act(o, a, f=AF.Copy, bias=None, scale=1.0):
         if bias is None:
@@ -135,13 +143,13 @@ def rank_program(g, core, T, topo):
         cost = sum(max(64, x[2]["n"]) * (4 if x[2]["sz"] == 4 else 1) * PEC for x in items)
         return add("t", [one(x) for x in items], regs([y for x in items for y in x[1:3]]), list(set(regs([x[0] for x in items]))), cost, 150.0)
 
-    def iota(o, pat, base, cm, small=True, after=()):
+    def iota(o, pat, base, cm, small=True, behind=()):
         if small:
-            return run("g", lambda: g.iota(ap(o), pat, base, cm, allow_small_or_imprecise_dtypes=True), o, [], 2.0, after)
-        return run("g", lambda: g.iota(ap(o), pat, base, cm), o, [], 2.0, after)
+            return run("g", lambda: g.iota(ap(o), pat, base, cm, allow_small_or_imprecise_dtypes=True), o, [], 2.0, behind)
+        return run("g", lambda: g.iota(ap(o), pat, base, cm), o, [], 2.0, behind)
 
-    def sel(o, a, pat, op, fl, base, cm, after=()):
-        return run("g", lambda: g.affine_select(ap(o), ap(a), pat, op, fl, base, cm), o, [a], 2.0, after)
+    def sel(o, a, pat, op, fl, base, cm, behind=()):
+        return run("g", lambda: g.affine_select(ap(o), ap(a), pat, op, fl, base, cm), o, [a], 2.0, behind)
 
     def dma(q, pairs, other_rows=False, after=(), lat=DMALAT, behind=()):
         def one(o, a):
@@ -160,32 +168,37 @@ def rank_program(g, core, T, topo):
     sends = []
 
     def exchange(src, s0, dst, d0, sign, after=(), late=0.0, calls=None):
-        rows, mine, came = 0, [], []
-        for j, blocks in enumerate(calls or X2):
-            k = nx[0]
+        mine, came, busy = [], [], {}
+        for j, call_ in enumerate(calls or X2):
+            k, lands = nx[0], []
             nx[0] += 1
-            engines = len(topo.engines(core, T.cores[(rank + 1) % N]))
-            m = engines // len(blocks)
+            for blocks, e0, m in call_:
+                used = range(e0, e0 + m * len(blocks))
+                end = max(busy.get(e, 0.0) for e in used)
+                end = max(end, ISSUE * j) + ROW * 128 // m
+                busy.update({e: end for e in used})
+                lands.append((blocks, e0, m, nx[1], end))
+                nx[1] += 1
 
-            def call(blocks=blocks, k=k, m=m):
+            def call(lands=lands, k=k):
                 out = []
-                for i, d in enumerate(blocks):
-                    peer = T.cores[(rank + sign * d) % N]
-                    rid, pid, _ = topo.addr(peer)
-                    mask = sum(1 << e for e in topo.engines(core, peer)[m * i:m * i + m])
-                    out.append(RemoteDMATransfer(dst_ids=[DstId(rid=rid, pnc=pid)], dma_engine_mask=mask, remote_sem=T.sem["h%d" % k],
-                                                 src=v(src, s0 + GH * (d - 1), s0 + GH * d)["ap"], dst=v(dst, d0 + GH * (d - 1), d0 + GH * d)["ap"]))
+                for blocks, e0, m, h, end in lands:
+                    for i, d in enumerate(blocks):
+                        peer = T.cores[(rank + sign * d) % N]
+                        rid, pid, _ = topo.addr(peer)
+                        mask = sum(1 << e for e in topo.engines(core, peer)[e0 + m * i:e0 + m * i + m])
+                        out.append(RemoteDMATransfer(dst_ids=[DstId(rid=rid, pnc=pid)], dma_engine_mask=mask, remote_sem=T.sem["h%d" % h],
+                                                     src=v(src, s0 + GH * (d - 1), s0 + GH * d)["ap"], dst=v(dst, d0 + GH * (d - 1), d0 + GH * d)["ap"]))
                 g.remote_dma_fused(out, local_sem=T.sem["l%d" % k])
-            c0, c1 = GH * (blocks[0] - 1), GH * blocks[-1]
-            rows += 128 // m
-            lat = late + HOP + ROW * rows - ISSUE * j
-            me = add("g", [call], v(src, s0 + c0, s0 + c1)["reg"], [], ISSUE, lat - 500.0, "x", after=after, behind=sends[-1:])
+            c0, c1 = GH * (lands[0][0][0] - 1), GH * lands[-1][0][-1]
+            me = add("g", [call], v(src, s0 + c0, s0 + c1)["reg"], [], ISSUE, late + HOP + max(x[4] for x in lands) - ISSUE * j - 500.0, "x", after=after, behind=sends[-1:])
             sends.append(me)
-            arr = add(None, [], [], v(dst, d0 + c0, d0 + c1)["reg"], 0.0, lat, "r", free=True)
-            ops[me]["sem"], ops[arr]["sem"], ops[arr]["with"] = "l%d" % k, "h%d" % k, me
-            ops[me]["n"] = ops[arr]["n"] = m * len(blocks)
+            ops[me]["sem"], ops[me]["n"] = "l%d" % k, sum(m * len(blocks) for blocks, e0, m, h, end in lands)
             mine.append(me)
-            came.append(arr)
+            for blocks, e0, m, h, end in lands:
+                arr = add(None, [], [], v(dst, d0 + GH * (blocks[0] - 1), d0 + GH * blocks[-1])["reg"], 0.0, late + HOP + end - ISSUE * j, "r", free=True)
+                ops[arr]["sem"], ops[arr]["with"], ops[arr]["n"] = "h%d" % h, me, m * len(blocks)
+                came.append(arr)
         return mine, came
 
     def col(j):
@@ -201,24 +214,23 @@ def rank_program(g, core, T, topo):
     dma("a", [(v("SN"), T.snd[:])])
     dma("a", [(v("SI", 256, 384), T.lp[:])])
     fill(v("TR"), 0.0)
-    fill(v("TW", 0, E), 0.0)
-    fill(v("TW", 2944, 3456), 0.0)
+    ones = fill(v("AG"), 1.0, [fill(v("TW", 0, E), 0.0)])
     g0 = iota(v("SI", 128, 256), [[1, 128]], 0, 128, False)
     g0 = iota(v("PI", 0, 1), [[0, 1]], 0, 1, False, [g0])
     g0 = iota(v("JF", 0, 144), [[1, 144]], 0, 0, True, [g0])
     g0 = iota(v("HI"), [[64, 7], [0, 64]], 0, 0, True, [g0])
     g0 = iota(v("LO"), [[0, 7], [1, 64]], 0, 0, True, [g0])
     iota(v("JF", 144, 272), [[1, 128]], 144, 0)
-    iota(v("T48"), [[256, 3], [128, 2], [2, 8]], 0, 0)
+    iota(v("T48"), [[256, 3], [64, 4], [4, 4]], 0, 0)
     iota(v("KI"), [[0, 16], [1, 16]], 0, 0)
     iota(v("J16"), [[16, 8], [0, 16]], 0, 0)
-    iota(v("PB", 0, 16), [[2048, 2], [16, 8]], 0, 0)
+    iota(v("PB", 0, 16), [[1024, 4], [16, 4]], 0, 0)
     for c0 in (0, 128):
         ts(v("S2", c0, c0 + 128), v("SI", c0, c0 + 128), 0x7C0, A.bitwise_and)
         ts(v("S2", c0 + 256, c0 + 384), v("SI", c0, c0 + 128), 63, A.bitwise_and)
         cp(v("S3", c0, c0 + 128), v("S2", c0, c0 + 128))
         cp(v("S3", c0 + 256, c0 + 384), v("S2", c0 + 256, c0 + 384))
-    cp(v("S3", 512, 640), v("S2", 512, 640))
+    cp(v("S3", 512, 640), v("S2", 512, 640), [ones])
     ts(v("S3", 640, 768), v("S3", 128, 256), float(OWN), A.add)
     ts(v("S2", 640, 768), v("SI", 256, 384), 0xFC0, A.bitwise_and)
     ts(v("S2", 768, 896), v("SI", 256, 384), 63, A.bitwise_and)
@@ -243,8 +255,10 @@ def rank_program(g, core, T, topo):
     cp(v("SRL"), v("SNR"))
     cp(v("SNL"), v("SN"))
     fill(v("KW", E, E + 16), 0.0)
-    fill(v("AW", OWN + E, OWN + RWN), 0.0)
-    fill(v("SW", E, RWN), 0.0)
+    fill(v("KS", E, E + 16), 0.0)
+    fill(v("AW", OWN + E, OWN + E + 16), 0.0)
+    iota(v("SW", E, IGH), [[0, IGH - E]], 0, 0, True, [g0])
+    iota(v("SW", IGH, RWN), [[0, RWN - IGH]], 0, 0, True, [g0])
     fill(col(28), 15.0)
     fill(col(29), 160.0 - 15.5 / 32)
     fill(col(30), -160.0)
@@ -279,29 +293,27 @@ def rank_program(g, core, T, topo):
     ident, roll, unroll = v("I2", 0, 128), v("I2", 112, 240), v("I2", 16, 144)
     pos32, roll32, neg32 = v("I32F", 0, 128), v("I32F", 112, 240), v("I32F", 256, 384)
 
-    def through(dst, d0, terms, bias=None, banks=("PR0", "PR1")):
-        for h, bank in enumerate(banks):
+    def through(dst, d0, terms, both=False):
+        for h, bank in enumerate(("PR0", "PR1")):
             c = 448 * h
             for j, (lhs, src, s0) in enumerate(terms):
                 mm([(v(bank, 0, 448), lhs, v(src, s0 + c, s0 + c + 448), j == 0, j == len(terms) - 1)])
-        for h, bank in enumerate(banks):
-            o = v(dst, d0 + 448 * h, d0 + 448 * h + 448)
-            if bias is not None:
-                act(o, v(bank, 0, 448), AF.Identity, bias)
-            else:
-                act(o, v(bank, 0, 448))
+        for h, bank in enumerate(("PR0", "PR1")):
+            (cp if both and h else act)(v(dst, d0 + 448 * h, d0 + 448 * h + 448), v(bank, 0, 448))
 
     for h, bank in enumerate(("PR0", "PR1")):
         mm([(v(bank, 0, 448), ident, v("GS", 448 * h, 448 * h + 448), True, False), (v(bank, 0, 448), ident, v("SL"), False, True)])
         (cp if h else act)(v("GC", 448 * h, 448 * h + 448), v(bank, 0, 448))
     for c0, c1 in ((0, 512), (512, NG)):
         tt(v("GT", c0, c1), ind(v("TR"), v("SRL", c0 // 16, c1 // 16)), v("GC", c0, c1), A.add)
-    first, came0 = exchange("GT", 0, "TW", E, 1, late=2500.0)
-    act(v("AW", GUN, GUN + NG), ind(v("AW", OWN, OWN + E), v("SNL")))
+    first, came = exchange("GT", 0, "TW", E, 1, late=2500.0)
+    for c in (0, 448):
+        act(v("AW", GUN + c, GUN + c + 448), ind(v("AW", OWN, OWN + E), v("SNL", c // 16, c // 16 + 28)))
     through("GN", 0, [(roll, "AW", GUN)])
-    sent, came = exchange("GN", 0, "AW", GHO, 1, late=3000.0)
+    sent, came = exchange("GN", 0, "AW", GHO, 1, late=LATE)
     dma("a", [(v("KW", 0, E), T.k0[:])], after=first, lat=3000.0)
     dma("s", [(v("SW", 0, E), T.a0[:])], after=sent, lat=3000.0)
+    dma("s", [(v("KS", 0, E), T.k0[:])], after=sent, lat=4000.0)
     ts(col(15), col(2), 15.0, A.add)
     ts(v("F0"), v("JF", 0, 144), col(15), A.is_equal)
     ts(col(16), col(1), 1.5, A.is_lt)
@@ -324,25 +336,34 @@ def rank_program(g, core, T, topo):
     mm([(v("PX", 48, 96), win("FK", a), v("TW", a, 768, 16), a == 0, a == 15) for a in range(16)])
     act(v("NTV"), v("PX", 0, 48), scale=-1.0)
     act(v("KV"), v("PX", 48, 96), AF.Identity, bias=col(30), scale=8.0)
-    act(v("YY", 0, 448), ind(v("TW", 0, E), v("SNL", 0, 28)))
-    act(v("YY", 448, NG), ind(v("TW", 0, E), v("SNL", 28, 56)))
-    through("VV", 0, [(v("D11"), "GC", 0), (v("D12"), "YY", 0)], col(13), ("PT", "PK"))
+    for c0, c1, bank in ((0, 128, "PT"), (128, 512, "PK"), (512, NG, "PM")):
+        (cp if c0 == 512 else act)(v("YY", c0, c1), ind(v("TW", 0, E), v("SNL", c0 // 16, c1 // 16)))
+        mm([(v(bank, 0, c1 - c0), v("D11"), v("GC", c0, c1), True, False), (v(bank, 0, c1 - c0), v("D12"), v("YY", c0, c1), False, True)])
+        if c0 == 128:
+            act(v("VV", c0, c1), v(bank, 0, c1 - c0), AF.Identity, col(13))
+        else:
+            ts(v("VV", c0, c1), v(bank, 0, c1 - c0), col(13), A.add)
     for d in range(7):
         lst = v("SNL", 8 * d, 8 * d + 8)
         if d:
             act(v("YY", GH * d, GH * d + GH), ind(v("TW", 0, E), lst))
         cp(ind(v("TW", 0, E), lst), v("VV", GH * d, GH * d + GH))
+    dma("s", [(v("TW", 2944, 3456), v("TW", 0, 512))])
     dma("s", [(v("TW", 2944, 3456, p=slice(row, 128, 16)), v("TW", 0, 512, p=slice(row + 3, 128, 16))) for row in (5, 6)])
     ts(col(19), col(0), 16.0, A.mult, 15.0, A.add)
     p16, p24 = slice(0, 16), slice(0, 24)
     ts(v("FQ", p=p16), v("JF", p=p16), v("PC", 76, 77, p=p16), A.is_equal)
-    cp(v("QF", 0, 768, p=p24), v("QI", 0, 768, p=p24))
+    ts(col(44), col(0), 7.5, A.is_gt, 2048.0, A.mult)
+    ts(col(45), col(0), 15.5, A.is_lt, col(44), A.mult)
+    fill(col(46), 2048.0)
+    ts(v("QF", 0, 768, p=p24), v("QI", 0, 768, p=p24), v("PC", 180, 181, p=p24), A.subtract)
     cp(v("QF", 768, 1280, p=slice(0, 8)), v("QI", 768, 1280, p=slice(0, 8)))
     act(v("I32F", 0, 256), v("I2"))
     act(neg32, ident, scale=-1.0)
     cp(v("REP"), v("JF", 0, 48))
-    ts(v("PI", 8, 9), v("PI", 0, 1), 7, A.bitwise_and)
-    ts(col(36), col(1), 8.0, A.is_ge)
+    ts(v("PI", 8, 9), v("PI", 0, 1), 3, A.bitwise_and)
+    ts(v("PI", 12, 13), v("PI", 4, 5), 2, A.arith_shift_right)
+    cp(col(36), v("PI", 12, 13))
     ts(col(20), v("PI", 8, 9), 16.0, A.mult, col(36), A.add)
     ts(v("PERM"), v("T48"), col(20), A.add)
     for s in range(3):
@@ -355,57 +376,55 @@ def rank_program(g, core, T, topo):
     for s in range(3):
         act(v("TVR", 256 * s, 256 * s + 256), ind(v("NTV"), v("REP", 16 * s, 16 * s + 16)))
         act(v("KVR", 256 * s, 256 * s + 256), ind(v("KV"), v("REP", 16 * s, 16 * s + 16)))
-    fill(v("AG"), 1.0)
     fill(v("SH", 0, 128), 0.0)
-    sel(v("SH", 128, 2048), v("AG"), [[-1, 15], [0, 8], [1, 16]], A.is_ge, 0.0, -1, 0, sent)
+    sel(v("SH", 128, 2048), v("AG"), [[-1, 15], [0, 8], [1, 16]], A.is_ge, 0.0, -1, 0, first)
     sel(v("AG"), v("SH", 128, 2048), [[1, 15], [-1, 128]], A.is_equal, 0.0, 1, 1)
     sel(v("SH", 128, 2048), v("AG"), [[0, 15], [-1, 128]], A.not_equal, -1.0, 0, 1)
 
-    def tk_gather(s, chunks, eng):
-        for c in chunks:
-            (cp if eng == "v" else act)(v("XX%d" % s, 1024 * c, 1024 * c + 1024), ind(v("TW", 0, 2944), v("CAL", 256 * s + 64 * c, 256 * s + 64 * c + 64)))
+    def diff(bank, c0, src, lo=0, hi=256):
+        o = v(bank, c0 + lo, c0 + hi - 1)
+        mm([(o, pos32, v(src, lo, hi - 1), True, False), (o, neg32, v(src, lo + 1, hi), False, True)])
 
-    def diff(bank, c0, src):
-        o = v(bank, c0, c0 + 255)
-        mm([(o, pos32, v(src, 0, 255), True, False), (o, neg32, v(src, 1, 256), False, True)])
-
-    def extract(t, halves, bank, b0, f, pre=None, close=True):
-        c0, c1 = 128 * min(halves), 128 * max(halves) + 128
+    def extract(t, qs, bank, b0, f, pre=None, close=True):
+        c0, c1 = 64 * min(qs), 64 * max(qs) + 64
         if pre:
             mm([(v(bank, b0 + c0, b0 + c1), pos32, v(pre, 256 * (t % 3) + c0, 256 * (t % 3) + c1), True, False)])
-        for h in halves:
-            for a0_ in (0, 8):
-                mm([(v(bank, b0 + 128 * h, b0 + 128 * h + 128), win(f, a), v("XX%d" % (t % 3), 2048 * h + 128 * a, 2048 * h + 128 * a + 128),
-                     a == 0 and not pre, a == 15 and close and (not pre or h == halves[-1])) for a in range(a0_, a0_ + 8)])
+        for h in qs:
+            mm([(v(bank, b0 + 64 * h, b0 + 64 * h + 64), win(f, a), v("XX%d" % (t % 3), 1024 * h + 64 * a, 1024 * h + 64 * a + 64),
+                 a == 0 and not pre, a == 15 and close and (not pre or h == qs[-1])) for a in range(16)])
 
-    def prep(t, halves=(1, 0), bt="PT", bk="PK", bm="PM"):
-        c0, c1 = 128 * min(halves), 128 * max(halves) + 128
-        extract(t, halves, bt, 0, "FT", "TVR")
-        extract(t, halves, bk, 0, "FK", "KVR", False)
+    def prep(t, qs=(3, 2, 1, 0), bt="PT", bk="PK", bm="PM"):
+        c0, c1 = 64 * min(qs), 64 * max(qs) + 64
+        extract(t, qs, bt, 0, "FT", "TVR")
+        extract(t, qs, bk, 0, "FK", "KVR", False)
         act(v("LAG", c0, c1), v(bt, c0, c1), AF.Abs)
         act(v("YI", c0, c1), v("LAG", c0, c1), AF.Identity, bias=col(29), scale=1.0 / 32)
-        extract(t, halves, bm, 0, "FM")
+        extract(t, qs, bm, 0, "FM")
         mm([(v(bk, c0, c1), ident, v("YI", c0, c1), False, True)])
         ts(v("BNL", c0, c1), v(bk, c0, c1), 64.0, A.mult)
         cp(v("ML", c0, c1), v(bm, c0, c1))
         act(v("SS", c0, c1), v(bk, c0, c1))
 
+    def steps(t, qs=(3, 2, 1, 0), bm="PM"):
+        c0, c1 = 64 * min(qs), 64 * max(qs) + 64
+        extract(t, qs, bm, 256, "FR")
+        act(v("MT", c0, c1), v(bm, 256 + c0, 256 + c1))
+        diff("PX", 0, "MT", c0, c1)
+        ts(v("PX", c0 + 15, c1, 16), v("MT", c0 + 15, c1, 16), float(HOLE), A.subtract)
+        if t < R - 1:
+            diff("PX", 256, "SS", c0, c1)
+            ts(v("PX", 271 + c0, 256 + c1, 16), v("SS", c0 + 15, c1, 16), E / 64.0, A.subtract)
+
     def prep2(t):
-        extract(t, (1, 0), "PM", 256, "FR")
-        act(v("MT"), v("PM", 256, 512))
-        diff("PX", 0, "MT")
-        if t < R - 1:
-            diff("PX", 256, "SS")
-        ts(v("PX", 15, 256, 16), v("MT", 15, 256, 16), float(HOLE), A.subtract)
-        if t < R - 1:
-            ts(v("PX", 271, 512, 16), v("SS", 15, 256, 16), E / 64.0, A.subtract)
-        rl = "RL%d" % (t % 2)
+        if t:
+            steps(t)
+        rl = "RL%d" % (t % 3)
         diff("PT", 256, "LAG")
         ts(v(rl, 1, 256), v("PT", 256, 511), 1023.0, A.add)
         fill(v(rl, 0, 256, 16), 2047)
-        ts(v("EL%d" % (t % 2)), v("LAG", 15, 256, 16), 1023.0, A.add)
+        ts(v("EL%d" % (t % 3)), v("LAG", 15, 256, 16), 1023.0, A.add)
         if t < 2:
-            extract(t, (1, 0), "PT", 0, "FC")
+            extract(t, (3, 2, 1, 0), "PT", 0, "FC")
             act(v("CT%d" % t), v("PT", 0, 256))
 
     def k_gather(chunks=(3, 2, 1, 0)):
@@ -414,16 +433,17 @@ def rank_program(g, core, T, topo):
 
     def r_gather(t):
         for c in range(4):
-            act(v("RG%d" % (t % 2), 1024 * c, 1024 * c + 1024), ind(v("RT"), v("RL%d" % (t % 2), 64 * c, 64 * c + 64)))
-        act(v("E15%d" % (t % 2)), ind(v("RT"), v("EL%d" % (t % 2))))
+            act(v("RG%d" % (t % 2), 1024 * c, 1024 * c + 1024), ind(v("RT"), v("RL%d" % (t % 3), 64 * c, 64 * c + 64)))
+        act(v("E15%d" % (t % 2)), ind(v("RT"), v("EL%d" % (t % 3))))
 
     def weights(t, b0, b1):
-        pr = "PR%d_" % (t % 2)
+        pr = "PR%d_" % (t % 3)
         for c1 in range(16 * b1, 16 * b0, -64):
             c0 = max(c1 - 64, 16 * b0)
             cut = min(max(32 * SPLIT[t], c0), c1)
-            if cut < c1:
-                tt(v(pr, 16 * cut, 16 * c1), ind(v("AW", 0, OWN + E), v("ML", cut, c1)), v("KG", 16 * cut, 16 * c1), A.mult)
+            for c in range(c1, cut, -WCH):
+                cl = max(cut, c - WCH)
+                tt(v(pr, 16 * cl, 16 * c), ind(v("AW", 0, OWN + E), v("ML", cl, c)), v("KG", 16 * cl, 16 * c), A.mult)
             for c in range(cut - 32, c0 - 1, -32):
                 bank = v("PR%d" % (c // 32 % 2), 0, 512)
                 act(v("AS", 16 * c, 16 * c + 512), ind(v("AW", 0, OWN + E), v("ML", c, c + 32)))
@@ -431,7 +451,7 @@ def rank_program(g, core, T, topo):
                 tt(v(pr, 16 * c, 16 * c + 512), bank, v("KG", 16 * c, 16 * c + 512), A.mult)
             mm([(v("PW", c0, c1), win("F0", a), v(pr, 16 * c0 + a, 16 * c1, 16), a == 0, a == 15) for a in range(16)])
 
-    def elect(px0, bank, sfx, xs, lb, scale, dump, c0=0, c1=256):
+    def elect(px0, bank, sfx, xs, lb, scale, dump, c0, c1):
         tt(v("PD" + sfx, c0, c1), v("HIT", c0, c1), v("PX", px0 + c0, px0 + c1), A.mult)
         scan(v(xs, c0, c1), v("SEG", c0, c1), v("PD" + sfx, c0, c1), 0.0, A.mult, A.add)
         mm([(v(bank, px0 + c0 + dl, px0 + c1, 16), v("SH", 128 * dl, 128 * dl + 128), v(xs, c0 + 15, c1, 16), True, True) for dl in range(16)])
@@ -444,7 +464,7 @@ def rank_program(g, core, T, topo):
 
     def lam(t):
         for a in range(16):
-            scan(v("SC", 256 * a, 256 * a + 256), v("RG%d" % (t % 2), a, 4096, 16), v("PR%d_" % (t % 2), a, 4096, 16), 0.0, A.mult, A.add)
+            scan(v("SC", 256 * a, 256 * a + 256), v("RG%d" % (t % 2), a, 4096, 16), v("PR%d_" % (t % 3), a, 4096, 16), 0.0, A.mult, A.add)
         tt(v("LAM"), ind(v("SC"), v("LAML")), v("E15%d" % (t % 2)), A.mult)
         dma("s", [(T.yl[:, 256 * t:256 * t + 256], v("LAM"))])
 
@@ -476,41 +496,38 @@ def rank_program(g, core, T, topo):
         act(v("NX"), ind(v("TW"), v("NC")))
         cp(ind(v("XX%d" % t), v("PL")), v("NX"))
 
-    tk_gather(0, (3,), "a")
-    tk_gather(0, (2,), "v")
-    tk_gather(0, (1,), "a")
-    tk_gather(0, (0,), "v")
-    prep(0, (1,))
-    k_gather((3, 2))
-    prep(0, (0,), "PR0", "PR1", "PD_")
-    k_gather((1, 0))
-    act(v("YY", NG, 2 * NG), ind(v("TW", 0, E), v("SNL")))
     ts(col(21), col(0), 16.0, A.mult, -256.0, A.add)
     ts(v("GK", p=p24), v("J16", p=p24), v("PC", 84, 85, p=p24), A.is_equal)
     lists(0, 80, v("PW", 0, 80))
     lists(1, 48, v("PW", 80, 128))
-    act(v("UL"), v("PW", 0, 80), scale=1.0 / 256)
-    act(v("BGL"), v("PW", 80, 128))
-    for h, bank in enumerate(("PM", "PX")):
+    iota(v("UL"), [[0, 80], [1, 3]], 0, 0, True, [g0])
+    iota(v("CUM"), [[0, 768]], 0, 0, True, first)
+    act(v("UL", 2, 240, 3), v("PW", 0, 80), scale=1.0 / 256)
+    ts(v("REP3"), v("JF", 0, 16), 3.0, A.mult, 2.0, A.add)
+    act(v("BGL"), v("PW", 80, 128), AF.Identity, bias=col(46))
+    for h, bank in enumerate(("PD_", "PX")):
         mm([(v(bank, 0, 384), v("GK", p=p24), v("QF", 384 * h, 384 * h + 384, p=p24), True, True)])
         ts(v("OH", 384 * h, 384 * h + 384), v(bank, 0, 384), col(1), A.is_equal)
+    for c, (who, qs) in enumerate(FIRST):
+        for q_ in qs:
+            for h, eng in enumerate(who):
+                n_ = 64 // len(who)
+                c0 = 64 * q_ + n_ * h
+                (cp if eng == "v" else act)(v("XX0", 16 * c0, 16 * (c0 + n_)), ind(v("TW", 0, 2944), v("CAL", c0, c0 + n_)))
+        prep(0, qs, *B0[c])
+        k_gather(qs)
+        if c in SECOND:
+            steps(0, SECOND[c], ("PM", "PM", "PD_", "PD_")[c])
+    for c in (0, 448):
+        act(v("YY", NG + c, NG + c + 448), ind(v("TW", 0, E), v("SNL", c // 16, c // 16 + 28)))
     act(v("CAPA"), v("OH"), AF.Identity, bias=col(28), scale=-1.0)
     act(v("CAPK"), v("OH"), AF.Identity, bias=col(31), scale=-1.0)
     ts(v("SEG"), v("KI"), 0.0, A.not_equal)
-    fill(v("LB"), 1.0e6)
-    fill(v("LBK"), 1.0e6)
+    iota(v("LB"), [[0, 256]], 1000000, 0, True, first)
+    iota(v("LBK"), [[0, 256]], 1000000, 0, True, first)
     ts(col(22), col(1), float(DUMP), A.add)
     ts(col(24), col(1), float(E), A.add)
     prep2(0)
-    mm([(v("PD_", 0, 112), win("FM", a), v("YY", a, 1792, 16), a == 0, a == 15) for a in range(16)])
-    act(v("YU"), v("PD_", 0, 112))
-    mm([(v("PD_", 0, 112), roll32, v("YU"), True, True)])
-    ts(v("YT", 0, 56), v("PD_", 0, 56), float(NG), A.is_lt)
-    ts(v("YT", 56, 112), v("PD_", 0, 56), float(NG), A.add)
-    ts(v("LST"), v("PD_", 56, 112), float(NG), A.add)
-    tt(v("YT", 112, 168), v("YT", 0, 56), v("YT", 56, 112), A.mult)
-    tt(v("YT", 0, 56), v("YT", 112, 168), v("PD_", 56, 112), A.max)
-    cp(v("PRV"), v("YT", 0, 56))
     be = v("BE", 0, 1)
     ts(v("BT", 0, 1), be, -1.0 / 6, A.mult, 0.5, A.add)
     ts(v("BT", 4, 5), v("BT", 0, 1), be, A.mult, -1.0, A.add)
@@ -526,7 +543,7 @@ def rank_program(g, core, T, topo):
     fill(v("RT", 2047, 2048), 0.0)
     ts(col(25), col(1), 256.0, A.mult, 15.0, A.add)
     ts(v("LAML"), v("JF", 0, 16), 16.0, A.mult, col(25), A.add)
-    ts(col(37), col(1), 128.0, A.mult)
+    ts(col(37), col(1), 64.0, A.mult)
     ts(v("PB", 0, 16), v("PB", 0, 16), col(37), A.add)
     ts(col(38), col(1), 4096.0, A.add)
     ts(v("PB", 16, 32), v("JF", 0, 16), 16.0, A.mult, col(38), A.add)
@@ -534,48 +551,64 @@ def rank_program(g, core, T, topo):
         ts(v("PB", 32 + 16 * t, 48 + 16 * t), v("PB", 16, 32), 2944.0 + 256 * t - 8192.0, A.add)
     act(v("KF"), v("KI"), scale=1.0 / 16)
     ts(v("BSEG"), v("KI"), 0.0, A.is_equal, 1.0e6, A.mult)
-    fill(v("XX0", 4096, 4352), 0.0)
-    fill(v("XX1", 4096, 4352), 0.0)
 
-    raises = v("SW")
-    first_round = len(ops)
+    def chains():
+        mm([(v("PT", 0, 112), win("FM", a), v("YY", a, 1792, 16), a == 0, a == 15) for a in range(16)])
+        act(v("YU"), v("PT", 0, 112))
+        mm([(v("PT", 0, 112), roll32, v("YU"), True, True)])
+        ts(v("YT", 0, 56), v("PT", 0, 56), float(NG), A.is_lt)
+        ts(v("YT", 56, 112), v("PT", 0, 56), float(NG), A.add)
+        ts(v("LST"), v("PT", 56, 112), float(NG), A.add)
+        tt(v("YT", 112, 168), v("YT", 0, 56), v("YT", 56, 112), A.mult)
+        tt(v("YT", 0, 56), v("YT", 112, 168), v("PT", 56, 112), A.max)
+        cp(v("PRV"), v("YT", 0, 56))
+
     for t in range(R):
         s = t % 3
-        for b0, b1 in PARTS:
+        cp(v("CUM", 29, 768, 48), v("BGL", 16 * s, 16 * s + 16))
+        for j, (b0, b1) in enumerate(PARTS):
             weights(t, b0, b1)
             c0, c1 = 16 * b0, 16 * b1
-            scan(v("CUM", c0, c1), v("SEG", c0, c1), v("PW", c0, c1), 0.0, A.mult, A.add)
-            tt(v("S1", b0, b1), v("CUM", c0 + 15, c1, 16), v("BGL", 16 * s + b0, 16 * s + b1), A.add)
-            tt(v("THR", 8 * b0, 7 * b0 + b1), v("S1", b0, b1), v("UL", 16 * t + b0, 16 * t + b1), A.mult)
-            tt(v("HIT", c0, c1), ind(v("THR", 8 * b0, 7 * b0 + b1), v("REP", 0, b1 - b0)), v("CUM", c0, c1), A.is_lt)
-            elect(0, "PD_", "", "XS", "LB", 1.0, col(22), c0, c1)
-            ts(v("L1C", b0, b1), v("XS", c0 + 15, c1, 16), float(HOLE), A.add)
+            cum, thr = v("CUM", 3 * c0, 3 * c1, 3), v("THR", 8 * b0, 5 * b0 + 3 * b1)
+            scan(cum, v("SEG", c0, c1), v("PW", c0, c1), 0.0, A.mult, A.add)
+            scan(thr, v("CUM", 3 * c0 + 13, 3 * c1, 16), v("UL", 48 * t + 3 * b0, 48 * t + 3 * b1), 0.0, A.add, A.mult)
+            tt(v("HIT", c0, c1), ind(thr, v("REP3", 0, b1 - b0)), cum, A.is_lt)
+            elect(0, BANKS[j % len(BANKS)], "", "XS", "LB", 1.0, col(22), c0, c1)
+            ts(v("L1C", b0, b1), v("XS", c0 + 15, c1, 16), float(HOLE), A.add, float(HOLE), A.min)
             cp(v("L1", 2 * b0, 2 * b1, 2), v("OF", c0 + 15, c1, 16))
-            tt(v("NV", c0, c1), ind(v("AW", OWN, OWN + RWN), v("L1C", b0, b1)), v("CAPA", 256 * s + c0, 256 * s + c1), A.min)
+            tt(v("NV", c0, c1), ind(v("AW", OWN, OWN + E + 16), v("L1C", b0, b1)), v("CAPA", 256 * s + c0, 256 * s + c1), A.min)
             for b in range(b1 - 1, b0 - 1, -1):
-                scatter(raises, "L1", "NV", 256 * s, b)
+                scatter(v("SW"), "L1", "NV", 256 * s, b)
+            for k0, k1 in KPARTS:
+                if k0 == b0 and t < R - 1:
+                    c0, c1 = 16 * k0, 16 * k1
+                    elect(256, "PK", "K", "XK", "LBK", 64.0, col(24), c0, c1)
+                    ts(v("LKC", k0, k1), v("XK", c0 + 15, c1, 16), 64.0, A.mult, float(E), A.add)
+                    cp(v("LK", 2 * k0, 2 * k1, 2), v("OFK", c0 + 15, c1, 16))
+                    tt(v("NW", c0, c1), ind(v("KS"), v("LKC", k0, k1)), v("CAPK", 256 * s + c0, 256 * s + c1), A.min)
+                    for b in range(k1 - 1, k0 - 1, -1):
+                        scatter(v("KW"), "LK", "NW", 256 * s, b)
+            if t == 0 and b0 == CH0:
+                chains()
         sent, came = exchange("SW", IGH, "BUF", NG, -1, calls=X1)
-        through("BUF", 0, [(ident, "GN", 0), (roll, "SW", IGUN)])
+        through("BUF", 0, [(ident, "GN", 0), (roll, "SW", IGUN)], both=True)
         if t < R - 1:
             dma("s", [(v("AW", OWN, OWN + E), v("SW", 0, E))], after=sent, lat=3000.0)
         for d in range(7):
             c = NG + GH * d
             tt(v("BUF", c, c + GH), ind(v("BUF", 0, c), v("PRV", 8 * d, 8 * d + 8)), v("BUF", c, c + GH), A.add)
         if t < R - 1:
-            ts(v("GN", 0, 512), ind(v("BUF", 0, 2 * NG), v("LST", 0, 32)), 15.0, A.min)
-            last = act(v("XB"), ind(v("BUF", 0, 2 * NG), v("LST", 32, 56)), AF.Relu, bias=col(28), scale=-1.0)
-            act(v("GN", 512, NG), v("XB"), AF.Identity, bias=col(28), scale=-1.0)
+            ts(v("GN", 0, CUT), ind(v("BUF", 0, 2 * NG), v("LST", 0, CUT // 16)), 15.0, A.min)
+            last = act(v("XB", 0, NG - CUT), ind(v("BUF", 0, 2 * NG), v("LST", CUT // 16, 56)), AF.Relu, bias=col(28), scale=-1.0)
+            act(v("GN", CUT, NG), v("XB", 0, NG - CUT), AF.Identity, bias=col(28), scale=-1.0)
             sent, came = exchange("GN", 0, "AW", GHO, 1, after=[last])
             through("AW", GUN, [(unroll, "GN", 0)])
-            iota(v("SW", IGUN, DUMP), [[0, 2 * NG]], 0, 0, after=sent[-1:])
-            elect(256, "PW", "K", "XK", "LBK", 64.0, col(24))
-            ts(v("LKC"), v("XK", 15, 256, 16), 64.0, A.mult, float(E), A.add)
-            cp(v("LK", 0, 32, 2), v("OFK", 15, 256, 16))
-            tt(v("NW"), ind(v("KW"), v("LKC")), v("CAPK", 256 * s, 256 * s + 256), A.min)
-            for b in range(15, -1, -1):
-                scatter(v("KW"), "LK", "NW", 256 * s, b)
+            iota(v("SW", IGUN, DUMP), [[0, 2 * NG]], 0, 0, True, sent[-1:])
+            if t < R - 2:
+                dma("s", [(v("KS", 0, E), v("KW", 0, E))], after=came, lat=3000.0)
             if t < 2:
-                tk_gather(t + 1, range(4), "a")
+                for c in range(4):
+                    act(v("XX%d" % (t + 1), 1024 * c, 1024 * c + 1024), ind(v("TW", 0, 2944), v("CAL", 256 * t + 256 + 64 * c, 256 * t + 320 + 64 * c)))
             prep(t + 1)
             k_gather()
             if t < 2:
@@ -618,65 +651,10 @@ def rank_program(g, core, T, topo):
             return 0.0
         return ops[d]["lat"] + SYNC
 
-    level = [0.0] * n
-    for i in range(n - 1, -1, -1):
-        level[i] = ops[i]["cost"] + max([gap(i, j) + level[j] for j in succ[i]] + [ops[i]["lat"]])
-
-    def place(key, pred, succ, gap):
-        left, est, done, order, ends = [len(x) for x in pred], [0.0] * n, set(), [], [0.0] * n
-        ready, free = {q: [] for q in Q}, {q: 0.0 for q in Q}
-        byq = {q: sorted([i for i in range(n) if ops[i]["q"] == q], key=lambda j: (-key[j], -j)) for q in Q}
-
-        def release(i, end):
-            done.add(i)
-            order.append(i)
-            ends[i] = end
-            for j in succ[i]:
-                est[j] = max(est[j], end + gap(i, j))
-                left[j] -= 1
-                if left[j] == 0:
-                    if ops[j]["q"] is None:
-                        release(j, est[j])
-                    else:
-                        ready[ops[j]["q"]].append(j)
-
-        def early(j, now, memo):
-            if j not in memo:
-                e = max(est[j], now)
-                if left[j]:
-                    for d in pred[j]:
-                        if d not in done:
-                            e = max(e, max(early(d, now, memo), free.get(ops[d]["q"], 0.0)) + ops[d]["cost"] + gap(d, j))
-                memo[j] = e
-            return memo[j]
-
-        for i in range(n):
-            if not pred[i]:
-                ready[ops[i]["q"]].append(i)
-        while any(ready.values()):
-            now, q = min((max(free[x], min(est[j] for j in ready[x])), x) for x in Q if ready[x])
-            can = [j for j in ready[q] if est[j] <= now]
-            i = min(can, key=lambda j: (key[j], j))
-            while byq[q][-1] in done:
-                byq[q].pop()
-            memo, soon = {}, None
-            for j in byq[q][:-1 - DEPTH:-1]:
-                if j not in done and key[j] + (LEAD if j >= first_round else LEAD0) < key[i]:
-                    e = early(j, now, memo)
-                    if e < now + LOOK * ops[i]["cost"] and (soon is None or e < soon):
-                        soon = e
-            if soon is not None:
-                short = [j for j in can if ops[j]["cost"] <= soon - now + SHORT]
-                if not short:
-                    free[q] = max(soon, now + 20.0)
-                    continue
-                i = min(short, key=lambda j: (key[j], j))
-            ready[q].remove(i)
-            free[q] = max(now, est[i]) + ops[i]["cost"]
-            release(i, free[q])
-        return max(ends[i] + ops[i]["lat"] for i in range(n)), order, ends
-
     if n not in ORDER:
+        level = [0.0] * n
+        for i in range(n - 1, -1, -1):
+            level[i] = ops[i]["cost"] + max([gap(i, j) + level[j] for j in succ[i]] + [ops[i]["lat"]])
         pred = [sorted(o["deps"]) for o in ops]
         fgap = [[(j, gap(i, j)) for j in succ[i]] for i in range(n)]
         bgap = [[(d, gap(d, i)) for d in pred[i]] for i in range(n)]
@@ -710,15 +688,6 @@ def rank_program(g, core, T, topo):
             return start
 
         key, best, rng = [-x for x in level], None, np.random.default_rng(1)
-        for _ in range(PASS0):
-            fw = place(key, pred, succ, gap)
-            if best is None or fw[0] < best[0]:
-                best = (fw[0], fw[1], [fw[2][i] - ops[i]["cost"] for i in range(n)])
-            bw = place([-x for x in fw[2]], succ, pred, lambda d, i: gap(i, d))
-            noise = rng.random(n) * NOISE0
-            key = [MIX * -bw[2][i] + (1 - MIX) * key[i] + float(noise[i]) for i in range(n)]
-        if best:
-            key = best[2]
         for it in range(PASSES):
             fw = fit(key, [len(x) for x in pred], fgap, [0.0] * n)
             span = max(fw[i] + ops[i]["cost"] + ops[i]["lat"] for i in range(n))
@@ -728,6 +697,118 @@ def rank_program(g, core, T, topo):
             bw = fit([-(base[i] + ops[i]["cost"]) for i in range(n)], [len(x) for x in succ], bgap, [ops[i]["lat"] if not succ[i] else 0.0 for i in range(n)])
             noise = rng.random(n) * NOISE
             key = [-(bw[i] + ops[i]["cost"]) + float(noise[i]) for i in range(n)]
+        anc, fp = [0] * n, []
+        for i in range(n):
+            m_ = 0
+            for d in pred[i]:
+                m_ |= anc[d]
+            fp.append([(d, w) for d, w in bgap[i] if ops[d]["lat"] > 150.0 or not (m_ >> d) & 1])
+            for d in pred[i]:
+                m_ |= 1 << d
+            anc[i] = m_
+        lat, views = [o["lat"] for o in ops], []
+        for per, sync in VIEWS:
+            cost = [o["cost"] + o.get("picked", 0.0) * (per - GATHER) for o in ops]
+            into = [[(d, cost[d] + (w - SYNC + sync if w else 0.0)) for d, w in fp[i]] for i in range(n)]
+            out = [[] for _ in range(n)]
+            for i in range(n):
+                for d, w in into[i]:
+                    out[d].append((i, w))
+            views.append((cost, into, out))
+        seq = {q: [i for i in best[1] if ops[i]["q"] == q] for q in Q}
+
+        def times(cost, fp, fs):
+            before, after_ = [-1] * n, [-1] * n
+            for x in seq.values():
+                for a_, b_ in zip(x, x[1:]):
+                    before[b_], after_[a_] = a_, b_
+            left = [len(fp[i]) + (before[i] >= 0) for i in range(n)]
+            todo, r = [i for i in range(n) if not left[i]], [0.0] * n
+            for i in todo:
+                for j, w in fs[i] + ([(after_[i], cost[i])] if after_[i] >= 0 else []):
+                    if r[i] + w > r[j]:
+                        r[j] = r[i] + w
+                    left[j] -= 1
+                    if not left[j]:
+                        todo.append(j)
+            tail = [0.0] * n
+            for i in reversed(todo):
+                x = cost[i] + max(lat[i], tail[after_[i]] if after_[i] >= 0 else 0.0)
+                for j, w in fs[i]:
+                    if w + tail[j] > x:
+                        x = w + tail[j]
+                tail[i] = x
+            return r, tail, before, after_, todo
+
+        def guess(new, first_, last_, r, tail, cost, fp, fs):
+            t0, head = (r[first_] + cost[first_] if first_ >= 0 else 0.0), []
+            for i in new:
+                for d, w in fp[i]:
+                    if r[d] + w > t0:
+                        t0 = r[d] + w
+                head.append(t0)
+                t0 += cost[i]
+            t1, worst = (tail[last_] if last_ >= 0 else 0.0), 0.0
+            for i, h in zip(reversed(new), reversed(head)):
+                t1 = max(t1 + cost[i], cost[i] + lat[i])
+                for j, w in fs[i]:
+                    if w + tail[j] > t1:
+                        t1 = w + tail[j]
+                worst = max(worst, h + t1)
+            return worst
+
+        tabu, best, now, undo = {}, None, None, None
+        for it in range(MOVES):
+            got = [times(*x) for x in views]
+            total = sum(max(x[1]) for x in got)
+            if now is not None and total > now[0] + SLACK:
+                seq[undo[0]] = undo[1]
+                total, got = now
+            now = (total, got)
+            if best is None or total < best[0] - 1.0:
+                best = (total, got[0][4], got[0][0])
+            cost, fp, fs = views[it % len(views)]
+            r, tail, before, after_, todo = got[it % len(views)]
+            span = max(tail)
+            crit = [i for i in todo if r[i] + tail[i] > span - 0.01]
+            on, moves = set(crit), []
+            for u in crit:
+                w_ = after_[u]
+                if w_ < 0 or w_ not in on or r[w_] > r[u] + cost[u] + 0.01:
+                    continue
+                run_, x = [u], before[u]
+                for k_ in range(FAR):
+                    f = run_[0]
+                    if any(d == f or r[d] + cost[d] > r[f] + cost[f] for d, w in fp[w_]):
+                        break
+                    if tabu.get((w_, f), -1) < it and (k_ < REACH or x < 0 or r[f] - r[x] - cost[x] > 0.6 * cost[w_]):
+                        moves.append((guess([w_] + run_, before[f], after_[w_], r, tail, cost, fp, fs), w_, f, 0, run_[:]))
+                    if x < 0:
+                        break
+                    run_.insert(0, x)
+                    x = before[x]
+                run_, x = [w_], after_[w_]
+                for k_ in range(FAR):
+                    f = run_[-1]
+                    if any(j == f or tail[j] > tail[f] for j, w in fs[u]):
+                        break
+                    if tabu.get((f, u), -1) < it and (k_ < REACH or x < 0 or r[x] - r[f] - cost[f] > 0.6 * cost[u]):
+                        moves.append((guess(run_ + [u], before[u], after_[f], r, tail, cost, fp, fs), u, f, 1, run_[:]))
+                    if x < 0:
+                        break
+                    run_.append(x)
+                    x = after_[x]
+            if not moves:
+                tabu = {}
+                continue
+            e_, x, f, side, run_ = min(moves, key=lambda m_: m_[0] + float(rng.random()) * JITTER)
+            line_ = seq[ops[x]["q"]]
+            undo = (ops[x]["q"], line_[:])
+            line_.remove(x)
+            line_.insert(line_.index(f) + side, x)
+            tabu[(x, f) if side == 0 else (f, x)] = it + TENURE
+            for y in run_:
+                tabu[(y, x) if side == 0 else (x, y)] = it + TENURE
         ORDER[n] = best
     order = ORDER[n][1]
 

@@ -3,34 +3,36 @@ from concourse.bass import DstId, RemoteDMATransfer
 from concourse.mybir import AluOpType, ActivationFunctionType
 
 N, E, GH, NG, R = 8, 2048, 128, 896, 5
-GUN, GHO, OWN = 0, 896, 1792
-HOLE, IGUN, IGH, DUMP, RWN = 2048, 2112, 3008, 3904, 3920
+GUN, GHO, PAD, HOLE, OWN, DUMP, KB, KH, RWN = 0, 896, 1792, 1807, 1808, 3856, 3872, 5920, 5952
 F32, BF, I32, U16, F16 = "float32", "bfloat16", "int32", "uint16", "float16"
+HALF = F16
 SB = {
-    "AW": (OWN + E + 16, BF), "SW": (RWN, BF), "TW": (3456, BF), "KW": (2064, BF), "KS": (2064, BF), "BUF": (3840, BF), "GN": (NG, BF), "XB": (384, BF),
-    "XX0": (4352, BF), "XX1": (4352, BF), "XX2": (4096, BF), "KG": (4096, BF), "PR0_": (4096, BF), "PR1_": (4096, BF), "PR2_": (4096, BF), "AS": (3072, BF),
-    "RG0": (4096, F32), "RG1": (4096, F32), "SC": (4096, F32), "RT": (2048, F32),
-    "GT": (NG, BF), "GC": (NG, BF), "VV": (NG, BF), "YY": (1792, BF), "TR": (E, BF), "GS": (NG, BF), "SL": (448, BF), "HI": (448, BF), "LO": (448, BF), "AG": (1920, BF),
-    "CA": (768, I32), "CAL": (768, U16), "SN": (56, I32), "SNR": (56, I32), "SNL": (56, U16), "SRL": (56, U16),
+    "AW": (KH + 16, BF), "SW": (RWN, BF), "TW": (3456, BF), "BUF": (DUMP, BF), "GN": (NG, BF), "BUG": (2 * NG, BF),
+    "XX0": (4352, BF), "XX1": (4352, BF), "XX2": (4096, BF), "KG": (4096, BF), "PR0_": (4096, BF), "PR1_": (4096, BF), "PR2_": (4096, BF), "AS": (4096, BF),
+    "RG0": (4096, F32), "RG1": (4096, F32), "BC": (2048, BF), "FN": (144, BF), "NI": (128, BF), "LH": (256, F16), "DL0": (256, F16), "DL1": (256, F16), "DL2": (256, F16),
+    "GT": (NG, BF), "VV": (NG, BF), "YY": (1792, BF), "GS": (NG, BF), "SL": (512, BF), "HI": (448, BF), "LO": (512, BF), "AG": (2048, BF),
+    "CA": (768, I32), "CAL": (768, U16), "SN": (56, I32), "SNL": (56, U16), "EQ": (48, F32), "RM": (128, BF),
     "SI": (384, I32), "S2": (896, I32), "S3": (1024, BF),
-    "QI": (1280, I32), "QF": (1280, F16), "JF": (272, F32), "FQ": (272, BF), "KI": (256, F32), "J16": (128, F32), "PI": (16, I32), "PC": (192, F32),
-    "F0": (144, BF), "FT": (144, BF), "FK": (144, BF), "FM": (144, BF), "FC": (144, BF), "FR": (144, BF), "FL": (144, BF),
+    "QI": (176, I32), "QH": (176, F16), "QF": (1280, F16), "JF": (272, F32), "FQ": (272, BF), "KI": (256, F32), "J16": (128, F32), "PI": (16, I32), "PC": (192, F32),
+    "F0": (144, BF), "FT": (144, BF), "FK": (144, BF), "FM": (144, BF), "FC": (144, BF), "FL": (144, BF),
     "I2": (256, BF), "D11": (128, BF), "D12": (128, BF), "K89": (128, BF), "P56": (128, BF), "I32F": (384, F32),
-    "GK": (128, BF), "SH": (2048, BF), "KF": (256, F32), "SEG": (256, F32), "BSEG": (256, F32),
-    "REP": (48, U16), "REP3": (16, U16), "LAML": (16, U16), "PERM": (48, U16), "T48": (48, F32), "PB": (64, F32),
-    "UL": (240, F32), "BGL": (48, F32), "NTV": (48, F32), "KV": (48, F32), "TVR": (768, F32), "KVR": (768, F32), "OH": (768, BF), "CAPA": (768, BF), "CAPK": (768, BF),
-    "YU": (112, F32), "YT": (168, F32), "PRV": (56, U16), "LST": (56, U16), "MAPL": (128, U16), "BE": (8, F32), "BT": (24, F32),
-    "LAG": (256, F32), "YI": (256, BF), "SS": (256, F32), "MT": (256, F32), "CT0": (256, F32), "CT1": (256, F32),
-    "ML": (256, U16), "BNL": (256, U16), "RL0": (256, U16), "RL1": (256, U16), "RL2": (256, U16), "EL0": (16, U16), "EL1": (16, U16), "EL2": (16, U16),
-    "E150": (256, F32), "E151": (256, F32),
-    "CUM": (768, F32), "THR": (128, F32), "HIT": (256, F32), "PD": (256, F32), "PDK": (256, F32), "XS": (256, F16), "XK": (256, F16),
-    "LB": (256, F32), "LBK": (256, F32), "EE": (256, F32), "EEK": (256, F32), "OF": (256, F32), "OFK": (256, F32),
-    "L1": (32, U16), "L1C": (16, U16), "LK": (32, U16), "LKC": (16, U16), "NV": (256, BF), "NW": (256, BF), "NX": (256, BF), "NX1": (256, BF), "NX2": (256, BF),
-    "LAM": (256, F32), "KEY": (256, F32), "MN": (256, F32), "W1": (256, F32), "W2": (256, F32), "W3": (256, F32),
+    "GK": (128, BF), "SH": (2048, BF), "SEG": (256, F32), "BSEG": (256, F32),
+    "REP": (48, U16), "REP3": (16, U16), "PERM": (48, U16), "T48": (48, F32), "PB": (64, F32),
+    "UL": (240, F32), "BGL": (48, F32), "NTV": (48, F32), "KV": (48, F32), "TVR": (768, HALF), "KVR": (768, HALF), "OH": (768, BF), "CAP": (1536, BF),
+    "YU": (112, F32), "YT": (168, F32), "PRV": (56, U16), "LST": (56, U16), "MAPL": (128, U16), "BE": (8, F32), "BT": (4, F32),
+    "YI": (256, BF), "SS": (256, HALF), "MT": (256, HALF), "CT0": (256, F32), "CT1": (256, F32),
+    "ML": (256, U16), "BNL": (256, U16),
+    "CUM": (768, F32), "THR": (128, F32), "HIT": (256, F32), "PD": (512, F32), "XS": (512, F16), "LB": (512, F32), "EE": (512, F32), "OF": (512, F32),
+    "L1": (64, U16), "L1C": (32, U16), "NV": (512, BF), "NX": (256, BF), "NX1": (256, BF), "NX2": (256, BF),
+    "LAM": (256, F32), "MN": (256, F32), "W1": (256, F32), "W2": (256, F32), "W3": (256, F32),
     "SM": (96, F32), "MI": (32, I32), "IX1": (16, U16), "IX2": (16, U16), "PL": (16, U16), "NC": (16, U16),
 }
-ALIAS = {"GT": ("KG", 0), "GC": ("KG", NG), "YY": ("XX2", 0), "VV": ("XX2", 1792), "TR": ("PR0_", 0), "GS": ("PR0_", E), "SL": ("PR0_", E + NG),
-         "SI": ("QI", 0), "S2": ("QI", 384), "AG": ("PR1_", 0), "HI": ("PR1_", 1920), "LO": ("PR1_", 1920 + NG)}
+DROP = 24.0
+EXP = True
+if not EXP:
+    SB.update({"RT": (2048, F32), "SD": (4096, F32), "E150": (256, F32), "E151": (256, F32), "LAML": (16, U16), "BT": (24, F32), "BC": (16, BF),
+               "RL0": (256, U16), "RL1": (256, U16), "RL2": (256, U16), "EL0": (16, U16), "EL1": (16, U16), "EL2": (16, U16)})
+ALIAS = {"GT": ("KG", 0), "YY": ("PR2_", 0), "VV": ("PR2_", 1792), "GS": ("PR0_", E), "SL": ("PR0_", E + NG), "AG": ("PR1_", 0), "HI": ("PR1_", 2048), "LO": ("PR1_", 2048 + NG)}
 PS = ["PW", "PD_", "PR0", "PR1", "PT", "PK", "PX", "PM"]
 POOL, _n = {}, 0
 for _k, (_c, _d) in SB.items():
@@ -39,24 +41,37 @@ for _k, (_c, _d) in SB.items():
         _n += (_c + 15) // 16 * 16
 SCRATCH = {k: ("sbuf", [128, n], d) for k, (n, d) in SB.items() if k not in POOL and k not in ALIAS}
 SCRATCH["UP"] = ("sbuf", [128, _n], U16)
+if EXP:
+    SCRATCH["SC"] = ("sbuf", [128, 256, 16], F32)
 for _k in PS:
     SCRATCH[_k] = ("psum", [128, 512], F32)
 X1 = ((((1, 2), 0, 4),), (((3, 4), 0, 4),), (((5, 6), 0, 4),), (((7,), 0, 8),))
-X2 = ((((1, 2, 3, 4), 0, 2),), (((5, 6), 0, 4),), (((7,), 0, 8),))
-SEMAPHORES = ["ev", "ea", "et", "eg"] + ["l%d" % _k for _k in range(40)] + ["h%d" % _k for _k in range(44)] + ["d%d" % _k for _k in range(46)]
+X0 = ((((1, 2, 3, 4), 0, 2),), (((5, 6), 0, 4),), (((7,), 0, 8),))
+X2 = ((((1,), 0, 8),), (((2, 3), 0, 4),), (((4, 5, 6, 7), 0, 2),))
+SEMAPHORES = ["ev", "ea", "et", "eg"] + ["l%d" % _k for _k in range(40)] + ["h%d" % _k for _k in range(44)] + ["d%d" % _k for _k in range(56)]
 SIZE = {F32: 4, I32: 4, BF: 2, U16: 2, F16: 2}
 A = AluOpType
 AF = ActivationFunctionType
-CYC, FIX, FIXS, GATHER, SCATTER, PEC, SYNC, DMALAT, ROWLAT, ISSUE, HOP, ROW = 0.87, 50.0, 5.0, 1.8, 3.8, 0.43, 250.0, 2200.0, 250.0, 400.0, 1500.0, 35.0
-PASSES, SLIP, NOISE, MOVES, REACH, FAR, JITTER, TENURE, ORDER = 15, 1000.0, 0.0, 400, 5, 80, 100.0, 60, {}
+CYC, FIX, FIXS, GATHER, SCATTER, PEC, SYNC, DMALAT, ROWLAT, ISSUE, HOP, ROW = 0.87, 50.0, 5.0, 1.8, 3.8, 0.43, 250.0, 2200.0, 100.0, 400.0, 1500.0, 35.0
+PASSES, SLIP, NOISE, MOVES, REACH, FAR, JITTER, TENURE, ORDER = 15, 1000.0, 0.0, 60, 5, 80, 100.0, 20, {}
+SWEEPS, STRETCH = 12, (150,)
 PARTS = ((12, 16), (8, 12), (4, 8), (0, 4))
-KPARTS = ((8, 16), (0, 8))
-SPLIT = (0, 0, 2, 2, 2)
+SPLIT = ((0, 0, 0, 32), (32, 32, 32, 32), (32, 48, 48, 48), (32, 48, 48, 48), (32, 48, 48, 48))
+LATER = ("vaaa", "vaaa")
+DB, SBK = ("PR0", "PR1"), ("PR0", "PR1")
+WHO, K0 = "vvvaa", "aaaa"
+DUE = (70000.0, 50000.0, 35000.0, 15000.0, 0.0)
+ONS = ((False, True),) * 5
+KPARTS, KV = ((8, 16), (0, 8)), ("aaaa", "aaaa", "vaaa", "vaaa", "vaaa")
+BOOST = (1000.0, 500.0, 0.0)
+KFIRST = 0
+HALVES = (2, 2, 2, 2, 2)
 BANKS, WCH, LATE, CH0 = ("PD_", "PM"), 64, 500.0, 8
-FIRST = (("va", (3,)), ("va", (2,)), ("a", (1,)), ("v", (0,)))
-B0 = (("PT", "PK", "PM"), ("PR0", "PR1", "PD_"), ("PT", "PK", "PM"), ("PR0", "PR1", "PD_"))
-VIEWS, SLACK = ((1.56, 250.0), (2.08, 250.0), (1.56, 120.0)), 150.0
-CUT = 512
+FIRST = (("va", (3,)), ("v", (2,)), ("a", (1,)), ("v", (0,)))
+B0 = (("PT", "PK"), ("PR0", "PR1"), ("PT", "PK"), ("PR0", "PR1"))
+VIEWS, SLACK = ((1.56, 250.0, 1.0), (2.08, 250.0, 1.0), (1.56, 120.0, 1.0), (1.2, 150.0, 1.2), (1.8, 150.0, 1.35)), 150.0
+PICK = ((0, 128), (128, 384), (384, NG))
+BOTH, URGE = (False, False, False, False, False), 5000.0
 SECOND = {1: (3, 2), 3: (1, 0)}
 FINAL = ((0, 416, "v"), (416, 672, "a"), (672, 1088, "v"), (1088, 1344, "a"), (1344, 1792, "v"), (1792, 2048, "a"))
 
@@ -66,7 +81,7 @@ def rank_program(g, core, T, topo):
     if rank is None:
         return
     Q = {"v": g.vector, "a": g.scalar, "t": g.tensor, "g": g, "s": g.sync}
-    ops, hist, ndma, nx = [], {}, [0], [0, 0]
+    ops, hist, ndma, nx, tag = [], {}, [0], [0, 0], [1]
 
     def v(name, c0=0, c1=None, step=1, p=None):
         n, sz = (SB[name][0], SIZE[SB[name][1]]) if name in SB else (512, 4)
@@ -99,7 +114,7 @@ def rank_program(g, core, T, topo):
             hist[name] = keep + [(me, lo, hi, True)]
         for name, lo, hi in rd:
             hist.setdefault(name, []).append((me, lo, hi, False))
-        ops.append({"q": q, "calls": calls, "deps": deps | set(behind), "behind": set(behind) - deps, "cost": cost, "lat": lat, "kind": kind})
+        ops.append({"q": q, "calls": calls, "deps": deps | set(behind), "behind": set(behind) - deps, "cost": cost, "lat": lat, "rank": BOOST[tag[0]], "kind": kind})
         return me
 
     def run(q, call, o, ins, per, behind=()):
@@ -132,10 +147,10 @@ def rank_program(g, core, T, topo):
     def fill(o, c, behind=()):
         return run("v", lambda: g.vector.memset(ap(o), c), o, [], 0.5, behind)
 
-    def act(o, a, f=AF.Copy, bias=None, scale=1.0):
+    def act(o, a, f=AF.Copy, bias=None, scale=1.0, behind=()):
         if bias is None:
-            return run("a", lambda: g.scalar.activation(ap(o), ap(a), f, scale=ap(scale)), o, [a, scale], 1.0)
-        return run("a", lambda: g.scalar.activation(ap(o), ap(a), f, bias=ap(bias), scale=ap(scale)), o, [a, bias, scale], 1.0)
+            return run("a", lambda: g.scalar.activation(ap(o), ap(a), f, scale=ap(scale)), o, [a, scale], 1.0, behind)
+        return run("a", lambda: g.scalar.activation(ap(o), ap(a), f, bias=ap(bias), scale=ap(scale)), o, [a, bias, scale], 1.0, behind)
 
     def mm(items):
         def one(x):
@@ -169,7 +184,7 @@ def rank_program(g, core, T, topo):
 
     def exchange(src, s0, dst, d0, sign, after=(), late=0.0, calls=None):
         mine, came, busy = [], [], {}
-        for j, call_ in enumerate(calls or X2):
+        for j, call_ in enumerate(calls or X0):
             k, lands = nx[0], []
             nx[0] += 1
             for blocks, e0, m in call_:
@@ -196,8 +211,9 @@ def rank_program(g, core, T, topo):
             ops[me]["sem"], ops[me]["n"] = "l%d" % k, sum(m * len(blocks) for blocks, e0, m, h, end in lands)
             mine.append(me)
             for blocks, e0, m, h, end in lands:
-                arr = add(None, [], [], v(dst, d0 + GH * (blocks[0] - 1), d0 + GH * blocks[-1])["reg"], 0.0, late + HOP + end - ISSUE * j, "r", free=True)
-                ops[arr]["sem"], ops[arr]["with"], ops[arr]["n"] = "h%d" % h, me, m * len(blocks)
+                arr = add(None, [], [], v(dst, d0 + GH * (blocks[0] - 1), d0 + GH * blocks[-1])["reg"], 0.0, 0.0, "r", free=True)
+                ops[arr]["sem"], ops[arr]["n"] = "h%d" % h, m * len(blocks)
+                ops[arr]["gaps"] = dict([(me, late + HOP + ROW * 128 // m)] + [(x, ROW * 128 // m) for x in came[-1:]])
                 came.append(arr)
         return mine, came
 
@@ -208,156 +224,135 @@ def rank_program(g, core, T, topo):
         return v(name, 15 - a, 143 - a)
 
     up, down = slice(16, 128), slice(0, 16)
-    dma("s", [(v("SI", 0, 128, p=up), T.ti[0:7, :]), (v("SI", 0, 128, p=down), T.ti[7:8, :])])
-    dma("a", [(v("S2", 512, 640, p=up), T.kd[0:7, :]), (v("S2", 512, 640, p=down), T.kd[7:8, :])])
-    dma("s", [(v("SNR", p=up), T.snd[0:112, :]), (v("SNR", p=down), T.snd[112:128, :])])
-    dma("a", [(v("SN"), T.snd[:])])
+    dma("s", [(v("SI", 0, 128), T.ti[:])])
     dma("a", [(v("SI", 256, 384), T.lp[:])])
-    fill(v("TR"), 0.0)
-    ones = fill(v("AG"), 1.0, [fill(v("TW", 0, E), 0.0)])
+    dma("s", [(v("S2", 768, 896), T.kd[:])])
+    dma("a", [(v("SN"), T.snd[:])])
+    fill(v("TW", 0, E), 0.0)
     g0 = iota(v("SI", 128, 256), [[1, 128]], 0, 128, False)
     g0 = iota(v("PI", 0, 1), [[0, 1]], 0, 1, False, [g0])
     g0 = iota(v("JF", 0, 144), [[1, 144]], 0, 0, True, [g0])
     g0 = iota(v("HI"), [[64, 7], [0, 64]], 0, 0, True, [g0])
-    g0 = iota(v("LO"), [[0, 7], [1, 64]], 0, 0, True, [g0])
+    g0 = iota(v("LO"), [[0, 8], [1, 64]], 0, 0, True, [g0])
     iota(v("JF", 144, 272), [[1, 128]], 144, 0)
     iota(v("T48"), [[256, 3], [64, 4], [4, 4]], 0, 0)
     iota(v("KI"), [[0, 16], [1, 16]], 0, 0)
     iota(v("J16"), [[16, 8], [0, 16]], 0, 0)
     iota(v("PB", 0, 16), [[1024, 4], [16, 4]], 0, 0)
-    for c0 in (0, 128):
-        ts(v("S2", c0, c0 + 128), v("SI", c0, c0 + 128), 0x7C0, A.bitwise_and)
-        ts(v("S2", c0 + 256, c0 + 384), v("SI", c0, c0 + 128), 63, A.bitwise_and)
+    cp(v("S3", 0, 128), v("SI", 0, 128))
+    tt(v("S3", 384, 512), v("SI", 0, 128), v("S3", 0, 128), A.subtract)
+    for c0 in (128, 256):
+        ts(v("S2", c0, c0 + 128), v("SI", c0, c0 + 128), 0xFC0 if c0 == 256 else 0x7C0, A.bitwise_and)
+        ts(v("S2", c0 + 384, c0 + 512), v("SI", c0, c0 + 128), 63, A.bitwise_and)
         cp(v("S3", c0, c0 + 128), v("S2", c0, c0 + 128))
-        cp(v("S3", c0 + 256, c0 + 384), v("S2", c0 + 256, c0 + 384))
-    cp(v("S3", 512, 640), v("S2", 512, 640), [ones])
-    ts(v("S3", 640, 768), v("S3", 128, 256), float(OWN), A.add)
-    ts(v("S2", 640, 768), v("SI", 256, 384), 0xFC0, A.bitwise_and)
-    ts(v("S2", 768, 896), v("SI", 256, 384), 63, A.bitwise_and)
-    cp(v("S3", 768, 1024), v("S2", 640, 896))
+        cp(v("S3", c0 + 384, c0 + 512), v("S2", c0 + 384, c0 + 512))
+    cp(v("S3", 768, 896), v("S2", 768, 896))
+    act(v("S3", 896, 1024), v("S3", 128, 256), AF.Identity, bias=float(OWN))
     line = {"s": [], "a": []}
-
-    def row_dma(q, pairs):
-        line[q].append(dma(q, pairs, True, behind=line[q][-1:], lat=DMALAT + ROWLAT * len(line[q])))
-
-    for q, row, c in (("s", 3, 640), ("a", 4, 384), ("s", 5, 128), ("a", 6, 384), ("s", 7, 128)):
-        row_dma(q, [(v("TW", 0, E, p=slice(row, 128, 16)), v("S3", c, c + 128))])
-    for q, row, c in (("s", 0, 0), ("a", 1, 256), ("s", 2, 512)):
-        row_dma(q, [(v("TR", p=slice(row, 128, 16)), v("S3", c, c + 128))])
-    for q, row, c in (("a", 0, 0), ("s", 1, 256), ("a", 2, 512)):
-        row_dma(q, [(v("TW", 0, E, p=slice(row, 112, 16)), v("S3", c, c + 128, p=up)), (v("TW", 0, E, p=slice(112 + row, 113 + row)), v("S3", c, c + 128, p=down))])
-    for q, row, c in (("s", 8, 768), ("a", 9, 896)):
-        row_dma(q, [(v("TW", 0, E, p=slice(row, 128, 16)), v("S3", c, c + 128))])
+    for q, row, c in (("s", 5, 128), ("a", 4, 512), ("s", 6, 512), ("a", 3, 896), ("s", 11, 768), ("a", 0, 0), ("s", 7, 384)):
+        line[q].append(dma(q, [(v("TW", 0, E, p=slice(row, 128, 16)), v("S3", c, c + 128))], True, behind=line[q][-1:], lat=DMALAT + ROWLAT * len(line[q])))
     a0 = dma("a", [(v("AW", OWN, OWN + E), T.a0[:])], lat=5000.0, behind=line["a"][-1:])
-    dma("a", [(v("CA"), T.ca[:])], behind=[a0], lat=6000.0)
-    small = dma("s", [(v("QI", 0, n, p=slice(8 * j, 8 * j + 8)), src[:, 0:n]) for j, (src, n) in enumerate(((T.us, 1280), (T.bg, 768), (T.cl, 768)))], behind=line["s"][-1:], lat=5000.0)
-    dma("s", [(v("BE", 0, 1), T.be[:])], behind=[small])
-    cp(v("SRL"), v("SNR"))
+    small = dma("s", [(v("QI", 0, 80), T.us[:]), (v("QI", 80, 128), T.bg[:]), (v("QI", 128, 176), T.cl[:])], behind=line["s"][-1:], lat=3000.0)
+    ca = dma("s", [(v("CA"), T.ca[:])], behind=[small], lat=5000.0)
+    dma("s", [(v("BE", 0, 1), T.be[:])], behind=[ca])
     cp(v("SNL"), v("SN"))
-    fill(v("KW", E, E + 16), 0.0)
-    fill(v("KS", E, E + 16), 0.0)
-    fill(v("AW", OWN + E, OWN + E + 16), 0.0)
-    iota(v("SW", E, IGH), [[0, IGH - E]], 0, 0, True, [g0])
-    iota(v("SW", IGH, RWN), [[0, RWN - IGH]], 0, 0, True, [g0])
-    fill(col(28), 15.0)
-    fill(col(29), 160.0 - 15.5 / 32)
-    fill(col(30), -160.0)
-    fill(col(31), 7.0)
+    fill(v("AW", KH, KH + 16), 0.0)
+    fill(v("SW", DUMP, KB), 0.0)
+    fill(v("AW", PAD, OWN), 0.0)
+    fill(v("BUF", PAD, OWN), 0.0)
+    fill(v("SW", KH, RWN), 0.0)
+    iota(v("SW", 0, GHO), [[0, GHO]], 0, 0, True, [g0])
+    iota(v("SW", GHO, OWN), [[0, OWN - GHO]], 0, 0, True, [g0])
+    def lin(o, a, scale, bias):
+        return act(o, a, AF.Identity, bias=bias, scale=scale)
+
+    def row(j):
+        return v("EQ", j, j + 1)
+
+    def two(j):
+        return v("EQ", 16 + j, 17 + j)
+
     ts(v("PI", 4, 5), v("PI", 0, 1), 15, A.bitwise_and)
     cp(col(0), v("PI", 0, 1))
     cp(col(1), v("PI", 4, 5))
     tt(col(2), col(0), col(1), A.subtract)
-    ts(col(3), col(1), 3.0, A.is_equal)
-    ts(col(4), col(1), 4.0, A.is_equal)
-    ts(col(5), col(1), 5.0, A.is_equal)
-    ts(col(6), col(1), 6.0, A.is_equal)
-    ts(col(32), col(1), 7.0, A.is_equal)
-    tt(col(33), col(3), col(32), A.add)
-    tt(col(7), col(33), col(5), A.add)
-    tt(col(8), col(4), col(6), A.add)
-    ts(col(39), col(1), 8.0, A.is_equal, 4032.0, A.mult)
-    ts(col(9), col(3), float(GHO), A.mult, col(39), A.add)
-    ts(col(34), col(5), float(E), A.mult, col(9), A.add)
-    ts(col(10), col(32), float(IGH), A.mult, col(34), A.add)
-    tt(col(11), col(33), col(4), A.add)
-    ts(col(12), col(11), -1.0, A.mult, 1.0, A.add)
-    ts(col(13), col(33), -float(NG), A.mult)
+    ts(v("EQ", 0, 16), v("JF", 0, 16), col(1), A.is_equal)
+    tt(v("EQ", 16, 28), v("EQ", 0, 12), v("EQ", 1, 13), A.add)
+    tt(v("EQ", 32, 34), v("EQ", 3, 5), v("EQ", 5, 7), A.add)
+    high, low = v("EQ", 32, 33), v("EQ", 33, 34)
+    act(col(39), row(8), scale=4032.0)
+    lin(col(9), row(3), float(GHO), col(39))
+    lin(col(10), row(5), float(E), col(9))
+    lin(col(43), high, 448.0, col(10))
+    lin(col(12), two(3), -1.0, 1.0)
+    act(col(13), row(3), scale=-float(NG))
+    lin(col(16), row(7), 1.0, row(0))
+    lin(col(3), row(11), 1.0, col(16))
     ts(v("I2", 0, 128), v("JF", 0, 128), col(0), A.is_equal)
     act(v("I2", 128, 256), v("I2", 0, 128))
-    ts(col(43), col(7), 448.0, A.mult, col(10), A.add)
-    ts(v("GS", 0, 448), v("HI"), col(7), A.mult, col(10), A.add)
-    ts(v("GS", 448, NG), v("HI"), col(7), A.mult, col(43), A.add)
-    ts(v("SL"), v("LO"), col(8), A.mult)
-    act(v("D11"), v("I2", 0, 128), scale=col(11))
+    lin(v("GS", 0, 448), v("HI"), high, col(10))
+    lin(v("GS", 448, NG), v("HI"), high, col(43))
+    act(v("SL"), v("LO"), scale=low)
+    act(v("D11"), v("I2", 0, 128), scale=two(3))
     act(v("D12"), v("I2", 0, 128), scale=col(12))
+    act(v("RM"), v("I2", 112, 240), scale=col(3))
+    for c in (0, 1024):
+        fill(v("AG", c, c + 1024), 1.0)
     ident, roll, unroll = v("I2", 0, 128), v("I2", 112, 240), v("I2", 16, 144)
     pos32, roll32, neg32 = v("I32F", 0, 128), v("I32F", 112, 240), v("I32F", 256, 384)
 
     def through(dst, d0, terms, both=False):
-        for h, bank in enumerate(("PR0", "PR1")):
+        for h, bank in enumerate(BANKS):
             c = 448 * h
             for j, (lhs, src, s0) in enumerate(terms):
                 mm([(v(bank, 0, 448), lhs, v(src, s0 + c, s0 + c + 448), j == 0, j == len(terms) - 1)])
-        for h, bank in enumerate(("PR0", "PR1")):
+        for h, bank in enumerate(BANKS):
             (cp if both and h else act)(v(dst, d0 + 448 * h, d0 + 448 * h + 448), v(bank, 0, 448))
 
-    for h, bank in enumerate(("PR0", "PR1")):
-        mm([(v(bank, 0, 448), ident, v("GS", 448 * h, 448 * h + 448), True, False), (v(bank, 0, 448), ident, v("SL"), False, True)])
-        (cp if h else act)(v("GC", 448 * h, 448 * h + 448), v(bank, 0, 448))
-    for c0, c1 in ((0, 512), (512, NG)):
-        tt(v("GT", c0, c1), ind(v("TR"), v("SRL", c0 // 16, c1 // 16)), v("GC", c0, c1), A.add)
-    first, came = exchange("GT", 0, "TW", E, 1, late=2500.0)
+    for c0, c1, bank, pick, out in ((0, 384, "PR0", cp, cp), (384, NG, "PR1", act, act)):
+        mm([(v(bank, 0, c1 - c0), ident, v("GS", c0, c1), True, False), (v(bank, 0, c1 - c0), ident, v("SL", 0, c1 - c0), False, False)])
+        pick(v("YY", c0, c1), ind(v("TW", 0, E), v("SNL", c0 // 16, c1 // 16)))
+        mm([(v(bank, 0, c1 - c0), v("RM"), v("YY", c0, c1), False, True)])
+        out(v("GT", c0, c1), v(bank, 0, c1 - c0))
+    first, came = exchange("GT", 0, "TW", E, 1, late=2500.0, calls=X2)
     for c in (0, 448):
         act(v("AW", GUN + c, GUN + c + 448), ind(v("AW", OWN, OWN + E), v("SNL", c // 16, c // 16 + 28)))
     through("GN", 0, [(roll, "AW", GUN)])
     sent, came = exchange("GN", 0, "AW", GHO, 1, late=LATE)
-    dma("a", [(v("KW", 0, E), T.k0[:])], after=first, lat=3000.0)
-    dma("s", [(v("SW", 0, E), T.a0[:])], after=sent, lat=3000.0)
-    dma("s", [(v("KS", 0, E), T.k0[:])], after=sent, lat=4000.0)
-    ts(col(15), col(2), 15.0, A.add)
-    ts(v("F0"), v("JF", 0, 144), col(15), A.is_equal)
-    ts(col(16), col(1), 1.5, A.is_lt)
-    ts(col(17), col(1), 2.0, A.is_equal, 1.0 / 64, A.mult)
-    tt(col(18), col(5), col(6), A.add)
-    tt(col(14), col(3), col(4), A.add)
-    tt(col(35), col(32), col(4), A.add)
+    dma("a", [(v("SW", KB, KH), T.k0[:])], after=first, lat=3000.0)
+    dma("s", [(v("SW", OWN, OWN + E), T.a0[:])], after=sent, lat=3000.0)
+    dma("s", [(v("AW", KB, KH), T.k0[:])], after=sent, lat=4000.0)
+    ts(v("F0"), v("JF", 0, 144), -15.0, A.add, col(2), A.is_equal)
+    act(col(17), row(11), scale=1.0 / 64)
     act(v("FT"), v("F0"), scale=col(16))
     act(v("FK"), v("F0"), scale=col(17))
-    act(v("FM"), v("F0"), scale=col(14))
-    act(v("FC"), v("F0"), scale=col(18))
-    act(v("FR"), v("F0"), scale=col(35))
-    ts(col(40), col(1), 7.5, A.is_gt)
-    ts(col(41), col(1), 9.5, A.is_lt, col(40), A.mult)
-    ts(col(42), col(41), -1.0, A.mult, 1.0, A.add)
-    act(v("FL"), v("F0"), scale=col(41))
+    act(v("FM"), v("F0"), scale=two(3))
+    act(v("FC"), v("F0"), scale=two(5))
+    act(v("FN"), v("F0"), scale=-1.0)
+    act(v("NI"), ident, scale=-1.0)
+    lin(col(42), two(8), -1.0, 1.0)
+    act(v("FL"), v("F0"), scale=two(8))
     act(v("K89"), ident, scale=col(42))
-    act(v("P56"), v("I2", 125, 253), scale=col(18))
+    act(v("P56"), v("I2", 125, 253), scale=two(5))
     mm([(v("PX", 0, 48), win("FT", a), v("TW", a, 768, 16), a == 0, a == 15) for a in range(16)])
     mm([(v("PX", 48, 96), win("FK", a), v("TW", a, 768, 16), a == 0, a == 15) for a in range(16)])
     act(v("NTV"), v("PX", 0, 48), scale=-1.0)
-    act(v("KV"), v("PX", 48, 96), AF.Identity, bias=col(30), scale=8.0)
+    lin(v("KV"), v("PX", 48, 96), 8.0, -160.0)
     for c0, c1, bank in ((0, 128, "PT"), (128, 512, "PK"), (512, NG, "PM")):
-        (cp if c0 == 512 else act)(v("YY", c0, c1), ind(v("TW", 0, E), v("SNL", c0 // 16, c1 // 16)))
-        mm([(v(bank, 0, c1 - c0), v("D11"), v("GC", c0, c1), True, False), (v(bank, 0, c1 - c0), v("D12"), v("YY", c0, c1), False, True)])
-        if c0 == 128:
-            act(v("VV", c0, c1), v(bank, 0, c1 - c0), AF.Identity, col(13))
-        else:
-            ts(v("VV", c0, c1), v(bank, 0, c1 - c0), col(13), A.add)
+        o = v(bank, 0, c1 - c0)
+        mm([(o, v("D11"), v("GS", c0, c1), True, False), (o, v("D11"), v("SL", 0, c1 - c0), False, False), (o, v("D12"), v("YY", c0, c1), False, True)])
+        ts(v("VV", c0, c1), o, col(13), A.add)
     for d in range(7):
         lst = v("SNL", 8 * d, 8 * d + 8)
         if d:
             act(v("YY", GH * d, GH * d + GH), ind(v("TW", 0, E), lst))
         cp(ind(v("TW", 0, E), lst), v("VV", GH * d, GH * d + GH))
-    dma("s", [(v("TW", 2944, 3456), v("TW", 0, 512))])
-    dma("s", [(v("TW", 2944, 3456, p=slice(row, 128, 16)), v("TW", 0, 512, p=slice(row + 3, 128, 16))) for row in (5, 6)])
-    ts(col(19), col(0), 16.0, A.mult, 15.0, A.add)
+    lin(col(19), col(0), 16.0, 15.0)
     p16, p24 = slice(0, 16), slice(0, 24)
     ts(v("FQ", p=p16), v("JF", p=p16), v("PC", 76, 77, p=p16), A.is_equal)
-    ts(col(44), col(0), 7.5, A.is_gt, 2048.0, A.mult)
-    ts(col(45), col(0), 15.5, A.is_lt, col(44), A.mult)
-    fill(col(46), 2048.0)
-    ts(v("QF", 0, 768, p=p24), v("QI", 0, 768, p=p24), v("PC", 180, 181, p=p24), A.subtract)
-    cp(v("QF", 768, 1280, p=slice(0, 8)), v("QI", 768, 1280, p=slice(0, 8)))
+    cp(v("QH"), v("QI", 0, 176))
+    ts(v("QH", 80, 128), v("QI", 80, 128), -2048.0, A.add)
+    dma("s", [(v("QF", 0, 16 * (c1 - c0), p=slice(8 * j, 8 * j + 8)), v("QH", c0, c1)) for j, (c0, c1) in enumerate(((0, 80), (80, 128), (128, 176)))])
     act(v("I32F", 0, 256), v("I2"))
     act(neg32, ident, scale=-1.0)
     cp(v("REP"), v("JF", 0, 48))
@@ -374,106 +369,147 @@ def rank_program(g, core, T, topo):
         mm([(o, v("FQ", 128 * j + 15 - a, 128 * j + 143 - a, p=ps), v("QF", a, 16 * n, 16, p=ps), a == 0, a == 15) for a in range(16)])
 
     for s in range(3):
-        act(v("TVR", 256 * s, 256 * s + 256), ind(v("NTV"), v("REP", 16 * s, 16 * s + 16)))
-        act(v("KVR", 256 * s, 256 * s + 256), ind(v("KV"), v("REP", 16 * s, 16 * s + 16)))
+        (cp if WHO[2 + s] == "v" else act)(v("TVR", 256 * s, 256 * s + 256), ind(v("NTV"), v("REP", 16 * s, 16 * s + 16)))
+        (cp if WHO[2 + s] == "v" else act)(v("KVR", 256 * s, 256 * s + 256), ind(v("KV"), v("REP", 16 * s, 16 * s + 16)))
     fill(v("SH", 0, 128), 0.0)
-    sel(v("SH", 128, 2048), v("AG"), [[-1, 15], [0, 8], [1, 16]], A.is_ge, 0.0, -1, 0, first)
-    sel(v("AG"), v("SH", 128, 2048), [[1, 15], [-1, 128]], A.is_equal, 0.0, 1, 1)
-    sel(v("SH", 128, 2048), v("AG"), [[0, 15], [-1, 128]], A.not_equal, -1.0, 0, 1)
+    sel(v("SH", 128, 2048), v("AG", 0, 1920), [[-1, 15], [0, 8], [1, 16]], A.is_ge, 0.0, -1, 0, first)
+    sel(v("XX2", 0, 1920), v("SH", 128, 2048), [[1, 15], [-1, 128]], A.is_equal, 0.0, 1, 1)
+    sh = sel(v("SH", 128, 2048), v("XX2", 0, 1920), [[0, 15], [-1, 128]], A.not_equal, -1.0, 0, 1)
+    if EXP:
+        sel(v("BC"), v("AG"), [[-1, 16], [-16, 8], [0, 16]], A.is_equal, 0.0, 0, 1, [sh])
 
-    def diff(bank, c0, src, lo=0, hi=256):
-        o = v(bank, c0 + lo, c0 + hi - 1)
-        mm([(o, pos32, v(src, lo, hi - 1), True, False), (o, neg32, v(src, lo + 1, hi), False, True)])
+    def diff(bank, c0, src, lo=0, hi=256, run_=16):
+        pos, neg = (pos32, neg32) if SB[src][1] == F32 else (ident, v("NI"))
+        mm([(v(bank, c0 + lo, c0 + hi), pos, v(src, lo, hi), True, False), (v(bank, c0 + lo, c0 + hi - 1), neg, v(src, lo + 1, hi), False, False),
+            (v(bank, c0 + lo + run_ - 1, c0 + hi - 1, run_), pos, v(src, lo + run_, hi, run_), False, True)])
 
     def extract(t, qs, bank, b0, f, pre=None, close=True):
         c0, c1 = 64 * min(qs), 64 * max(qs) + 64
         if pre:
-            mm([(v(bank, b0 + c0, b0 + c1), pos32, v(pre, 256 * (t % 3) + c0, 256 * (t % 3) + c1), True, False)])
+            mm([(v(bank, b0 + c0, b0 + c1), pos32 if HALF == F32 else ident, v(pre, 256 * (t % 3) + c0, 256 * (t % 3) + c1), True, False)])
         for h in qs:
             mm([(v(bank, b0 + 64 * h, b0 + 64 * h + 64), win(f, a), v("XX%d" % (t % 3), 1024 * h + 64 * a, 1024 * h + 64 * a + 64),
                  a == 0 and not pre, a == 15 and close and (not pre or h == qs[-1])) for a in range(16)])
 
-    def prep(t, qs=(3, 2, 1, 0), bt="PT", bk="PK", bm="PM"):
+    def prep(t, qs=(3, 2, 1, 0), bt="PT", bk="PK"):
         c0, c1 = 64 * min(qs), 64 * max(qs) + 64
         extract(t, qs, bt, 0, "FT", "TVR")
         extract(t, qs, bk, 0, "FK", "KVR", False)
-        act(v("LAG", c0, c1), v(bt, c0, c1), AF.Abs)
-        act(v("YI", c0, c1), v("LAG", c0, c1), AF.Identity, bias=col(29), scale=1.0 / 32)
-        extract(t, qs, bm, 0, "FM")
+        act(v("LH", c0, c1), v(bt, c0, c1), AF.Abs)
+        act(v("YI", c0, c1), v("LH", c0, c1), AF.Identity, bias=160.0 - 15.5 / 32, scale=1.0 / 32)
+        extract(t, qs, bt, 256, "FM")
         mm([(v(bk, c0, c1), ident, v("YI", c0, c1), False, True)])
         ts(v("BNL", c0, c1), v(bk, c0, c1), 64.0, A.mult)
-        cp(v("ML", c0, c1), v(bm, c0, c1))
-        act(v("SS", c0, c1), v(bk, c0, c1))
+        cp(v("ML", c0, c1), v(bt, 256 + c0, 256 + c1))
+        if t < R - 1:
+            lin(v("SS", c0, c1), v(bk, c0, c1), 64.0, -float(E))
+        lin(v("MT", c0, c1), v(bt, 256 + c0, 256 + c1), 1.0, -float(HOLE))
 
-    def steps(t, qs=(3, 2, 1, 0), bm="PM"):
+    def steps(t, qs=(3, 2, 1, 0)):
         c0, c1 = 64 * min(qs), 64 * max(qs) + 64
-        extract(t, qs, bm, 256, "FR")
-        act(v("MT", c0, c1), v(bm, 256 + c0, 256 + c1))
         diff("PX", 0, "MT", c0, c1)
-        ts(v("PX", c0 + 15, c1, 16), v("MT", c0 + 15, c1, 16), float(HOLE), A.subtract)
         if t < R - 1:
             diff("PX", 256, "SS", c0, c1)
-            ts(v("PX", 271 + c0, 256 + c1, 16), v("SS", c0 + 15, c1, 16), E / 64.0, A.subtract)
 
     def prep2(t):
         if t:
             steps(t)
-        rl = "RL%d" % (t % 3)
-        diff("PT", 256, "LAG")
-        ts(v(rl, 1, 256), v("PT", 256, 511), 1023.0, A.add)
-        fill(v(rl, 0, 256, 16), 2047)
-        ts(v("EL%d" % (t % 3)), v("LAG", 15, 256, 16), 1023.0, A.add)
+        if EXP:
+            diff("PT", 0, "LH", run_=4)
+            act(v("DL%d" % (t % 3)), v("PT", 0, 256))
+        if not EXP:
+            rl, lh = "RL%d" % (t % 3), "LH"
+            mm([(v("PT", 0, 255), ident, v(lh, 0, 255), True, False), (v("PT", 0, 255), v("NI"), v(lh, 1, 256), False, True)])
+            ts(v(rl, 1, 256), v("PT", 0, 255), 1023.0, A.add)
+            fill(v(rl, 0, 256, 16), 2047)
+            ts(v("EL%d" % (t % 3)), v(lh, 15, 256, 16), 1023.0, A.add)
         if t < 2:
             extract(t, (3, 2, 1, 0), "PT", 0, "FC")
-            act(v("CT%d" % t), v("PT", 0, 256))
+            lin(v("CT%d" % t), v("PT", 0, 256), 1.0, -4096.0)
 
-    def k_gather(chunks=(3, 2, 1, 0)):
+    kg = []
+
+    def k_gather(t, chunks=(3, 2, 1, 0)):
+        kg[:] = []
         for c in chunks:
-            act(v("KG", 1024 * c, 1024 * c + 1024), ind(v("KW"), v("BNL", 64 * c, 64 * c + 64)))
+            o, src = v("KG", 1024 * c, 1024 * c + 1024), ind(v("SW", KB, KH), v("BNL", 64 * c, 64 * c + 64))
+            me = ts(o, src, -1.0, A.mult) if KV[t][c] == "v" else act(o, src, scale=-1.0)
+            if t:
+                ops[me]["urge"] = URGE
+            if KV[t][c] == "a":
+                kg.append(me)
 
-    def r_gather(t):
-        for c in range(4):
-            act(v("RG%d" % (t % 2), 1024 * c, 1024 * c + 1024), ind(v("RT"), v("RL%d" % (t % 3), 64 * c, 64 * c + 64)))
-        act(v("E15%d" % (t % 2)), ind(v("RT"), v("EL%d" % (t % 3))))
+    def decay(t):
+        if not EXP:
+            for c in range(4):
+                act(v("RG%d" % (t % 2), 1024 * c, 1024 * c + 1024), ind(v("RT"), v("RL%d" % (t % 3), 64 * c, 64 * c + 64)))
+            act(v("E15%d" % (t % 2)), ind(v("RT"), v("EL%d" % (t % 3))), scale=-1.0)
+            return
+        for c in range(8):
+            bank, h, r = DB[c % 2], c // 4, c % 4
+            mm([(v(bank, 64 * a, 64 * a + 64), v("BC", 128 * (8 * h + a), 128 * (8 * h + a + 1)), v("DL%d" % (t % 3), r, 256, 4), True, True) for a in range(8)])
+            o = dict(v("RG%d" % (t % 2), 2048 * h + r, 2048 * h + 2048, 4), reg=[("RG%d" % (t % 2), 2048 * c, 2048 * c + 2048)])
+            act(o, v(bank), AF.Exp, bias=-DROP if r == 3 else None, scale=v("BT", 0, 1))
 
-    def weights(t, b0, b1):
-        pr = "PR%d_" % (t % 3)
-        for c1 in range(16 * b1, 16 * b0, -64):
-            c0 = max(c1 - 64, 16 * b0)
-            cut = min(max(32 * SPLIT[t], c0), c1)
-            for c in range(c1, cut, -WCH):
-                cl = max(cut, c - WCH)
-                tt(v(pr, 16 * cl, 16 * c), ind(v("AW", 0, OWN + E), v("ML", cl, c)), v("KG", 16 * cl, 16 * c), A.mult)
-            for c in range(cut - 32, c0 - 1, -32):
-                bank = v("PR%d" % (c // 32 % 2), 0, 512)
-                act(v("AS", 16 * c, 16 * c + 512), ind(v("AW", 0, OWN + E), v("ML", c, c + 32)))
-                mm([(bank, ident, v("AS", 16 * c, 16 * c + 512), True, True)])
-                tt(v(pr, 16 * c, 16 * c + 512), bank, v("KG", 16 * c, 16 * c + 512), A.mult)
-            mm([(v("PW", c0, c1), win("F0", a), v(pr, 16 * c0 + a, 16 * c1, 16), a == 0, a == 15) for a in range(16)])
+    def weights(t, j, b0, b1):
+        pr, c0, c1 = "PR%d_" % (t % 3), 16 * b0, 16 * b1
+        cut = c0 + SPLIT[t][j]
+        if cut < c1:
+            tt(v(pr, 16 * cut, 16 * c1), ind(v("AW", 0, DUMP), v("ML", cut, c1)), v("KG", 16 * cut, 16 * c1), A.mult)
+        for c in range(c0, cut, WCH):
+            ce = min(cut, c + WCH)
+            act(v("AS", 16 * c, 16 * ce), ind(v("AW", 0, DUMP), v("ML", c, ce)), behind=kg[:KFIRST] if t else ())
+            scan(v(pr, 16 * c, 16 * ce), v("AS", 16 * c, 16 * ce), v("KG", 16 * c, 16 * ce), 0.0, A.max, A.mult)
+        mm([(v("PW", c0, c1), win("FN", a), v(pr, 16 * c0 + a, 16 * c1, 16), a == 0, a == 15) for a in range(16)])
 
-    def elect(px0, bank, sfx, xs, lb, scale, dump, c0, c1):
-        tt(v("PD" + sfx, c0, c1), v("HIT", c0, c1), v("PX", px0 + c0, px0 + c1), A.mult)
-        scan(v(xs, c0, c1), v("SEG", c0, c1), v("PD" + sfx, c0, c1), 0.0, A.mult, A.add)
-        mm([(v(bank, px0 + c0 + dl, px0 + c1, 16), v("SH", 128 * dl, 128 * dl + 128), v(xs, c0 + 15, c1, 16), True, True) for dl in range(16)])
-        ts(v(lb, c0, c1, 16), v(xs, c0 + 15, c1, 16), scale, A.mult, float(HOLE), A.add)
-        ts(v("EE" + sfx, c0, c1), v(bank, px0 + c0, px0 + c1), 0.0, A.is_equal, dump, A.mult)
-        scan(v("OF" + sfx, c0, c1), v("EE" + sfx, c0, c1), v(lb, c0, c1), 0.0, A.max, A.min)
-
-    def scatter(window, lst, val, oh, b):
-        tt(ind(window, v(lst, 2 * b, 2 * b + 1)), v(val, 16 * b, 16 * b + 16), v("OH", oh + 16 * b, oh + 16 * b + 16), A.add)
+    def raise_(t, bank, b0, b1, h):
+        s, q0, q1 = 256 * (t % 3), 256 * h + 16 * b0, 256 * h + 16 * b1
+        tt(v("PD", q0, q1), v("HIT", 16 * b0, 16 * b1), v("PX", q0, q1), A.mult)
+        scan(v("XS", q0, q1), v("SEG", 0, q1 - q0), v("PD", q0, q1), 0.0, A.mult, A.add)
+        xs = v("XS", q0 + 15, q1, 16)
+        mm([(v(bank, q0 + dl, q1, 16), v("SH", 128 * dl, 128 * dl + 128), xs, True, True) for dl in range(16)])
+        if ONS[t][h]:
+            lin(v("LB", q0, q1, 16), xs, -1.0, col(24 + h))
+            act(v("EE", q0, q1), v(bank, q0, q1), AF.Square, scale=128.0)
+        else:
+            ts(v("LB", q0, q1, 16), xs, -1.0, A.mult, col(24 + h), A.add)
+            ts(v("EE", q0, q1), v(bank, q0, q1), 0.0, A.not_equal, 16384.0, A.mult)
+        scan(v("OF", q0, q1), v("EE", q0, q1), v("LB", q0, q1), 0.0, A.min, A.max)
+        old = v("L1C", q0 // 16, q1 // 16)
+        if h:
+            ts(old, xs, float(E), A.add)
+        else:
+            ts(old, xs, 0.0, A.max, float(HOLE - PAD), A.add)
+        ts(v("L1", q0 // 8, q1 // 8, 2), v("OF", q0 + 15, q1, 16), -1.0, A.mult, col(22 + h), A.add)
+        tt(v("NV", q0, q1), ind(v("AW", KB, KH + 16) if h else v("AW", PAD, DUMP), old), v("CAP", 768 * h + s + 16 * b0, 768 * h + s + 16 * b1), A.min)
+        for b in range(b1 - 1, b0 - 1, -1):
+            c = 256 * h + 16 * b
+            tt(ind(v("SW", KB, RWN) if h else v("SW", 0, KB), v("L1", c // 8, c // 8 + 1)), v("NV", c, c + 16), v("OH", s + 16 * b, s + 16 * b + 16), A.add)
 
     def lam(t):
-        for a in range(16):
-            scan(v("SC", 256 * a, 256 * a + 256), v("RG%d" % (t % 2), a, 4096, 16), v("PR%d_" % (t % 3), a, 4096, 16), 0.0, A.mult, A.add)
-        tt(v("LAM"), ind(v("SC"), v("LAML")), v("E15%d" % (t % 2)), A.mult)
-        dma("s", [(T.yl[:, 256 * t:256 * t + 256], v("LAM"))])
+        if not EXP:
+            for a in range(16):
+                scan(v("SD", 256 * a, 256 * a + 256), v("RG%d" % (t % 2), a, 4096, 16), v("PR%d_" % (t % 3), a, 4096, 16), 0.0, A.mult, A.add)
+            tt(v("LAM"), ind(v("SD"), v("LAML")), v("E15%d" % (t % 2)), A.mult)
+            dma("s", [(T.yl[:, 256 * t:256 * t + 256], v("LAM"))])
+            return
+        w = 256 // HALVES[t]
+        for h in range(HALVES[t] - 1, -1, -1):
+            c0, c1, bank = w * h, w * h + w, SBK[h % 2]
+            for a in range(16):
+                o = {"ap": T.SC[:, c0:c1, a], "reg": [("SC", 1024 * a + 4 * c0, 1024 * a + 4 * c1)], "n": w, "sz": 4, "ps": False}
+                q = dict(v("RG%d" % (t % 2), 256 * a + c0, 256 * a + c1), reg=[("RG%d" % (t % 2), 8192 * (a // 8), 8192 * (a // 8) + 8192)])
+                scan(o, v("PR%d_" % (t % 3), 16 * c0 + a, 16 * c1, 16), q, 0.0, A.add, A.mult)
+            for k in (3, 7, 11, 15):
+                x = {"ap": T.SC[:, c0 + k:c1:16, :], "reg": [("SC", 1024 * a + 4 * c0, 1024 * a + 4 * c1) for a in range(16)], "n": w, "sz": 4, "ps": False}
+                mm([(v(bank, c0, c1), pos32, x, k == 3, k == 15)])
+            act(v("LAM", c0, c1), v(bank, c0, c1), scale=-float(np.exp(DROP)))
+            ops[dma("s", [(T.yl[:, 256 * t + c0:256 * t + c1], v("LAM", c0, c1))])]["due"] = DUE[t]
 
     def candidates(t):
         ct, own = "CT%d" % t, v("TW", 256 * t, 256 * t + 256)
-        tt(v("KEY"), v("PW", 0, 256), v("KF"), A.add)
-        scan(v("MN"), v("BSEG"), v("KEY"), 0.0, A.add, A.min)
+        scan(v("MN"), v("BSEG"), v("PW", 0, 256), 0.0, A.add, A.min)
         diff("PD_", 256, ct)
-        ts(v("PD_", 271, 512, 16), v(ct, 15, 256, 16), 4096.0, A.subtract)
         tt(v("W2"), v("HIT"), v("PD_", 256, 512), A.mult)
         scan(v("W1"), v("SEG"), v("W2"), 0.0, A.mult, A.add)
         tt(v("SM", 0, 16), v("W1", 15, 256, 16), v("PB", 32 + 16 * t, 48 + 16 * t), A.min)
@@ -485,7 +521,7 @@ def rank_program(g, core, T, topo):
         act(v("NX2"), ind(v("TW"), v("IX2")))
         up_ = v("PD_", 256, 272)
         mm([(up_, win("FL", a), v("NX2", a, 256, 16), a == 0, a == 15) for a in range(16)])
-        ts(v("MI", 0, 16), v("MN", 15, 256, 16), 16.0, A.mult)
+        ts(v("MI", 0, 16), v("MN", 15, 256, 16), 16.0, A.mult, 15.0, A.add)
         ts(v("MI", 16, 32), v("MI", 0, 16), 15, A.bitwise_and)
         tt(v("SM", 32, 48), v("MI", 16, 32), v("PB", 0, 16), A.add)
         ts(v("SM", 48, 64), up_, 4000.0, A.is_gt, 8192.0, A.mult)
@@ -496,7 +532,7 @@ def rank_program(g, core, T, topo):
         act(v("NX"), ind(v("TW"), v("NC")))
         cp(ind(v("XX%d" % t), v("PL")), v("NX"))
 
-    ts(col(21), col(0), 16.0, A.mult, -256.0, A.add)
+    lin(col(21), col(0), 16.0, -256.0)
     ts(v("GK", p=p24), v("J16", p=p24), v("PC", 84, 85, p=p24), A.is_equal)
     lists(0, 80, v("PW", 0, 80))
     lists(1, 48, v("PW", 80, 128))
@@ -504,10 +540,12 @@ def rank_program(g, core, T, topo):
     iota(v("CUM"), [[0, 768]], 0, 0, True, first)
     act(v("UL", 2, 240, 3), v("PW", 0, 80), scale=1.0 / 256)
     ts(v("REP3"), v("JF", 0, 16), 3.0, A.mult, 2.0, A.add)
-    act(v("BGL"), v("PW", 80, 128), AF.Identity, bias=col(46))
-    for h, bank in enumerate(("PD_", "PX")):
+    lin(v("BGL"), v("PW", 80, 128), 1.0, 2048.0)
+    for h, bank in enumerate(("PT", "PK")):
         mm([(v(bank, 0, 384), v("GK", p=p24), v("QF", 384 * h, 384 * h + 384, p=p24), True, True)])
         ts(v("OH", 384 * h, 384 * h + 384), v(bank, 0, 384), col(1), A.is_equal)
+    ts(v("CAP", 0, 768), v("OH"), -1.0, A.mult, 15.0, A.add)
+    ts(v("CAP", 768, 1536), v("OH"), -1.0, A.mult, 7.0, A.add)
     for c, (who, qs) in enumerate(FIRST):
         for q_ in qs:
             for h, eng in enumerate(who):
@@ -515,42 +553,46 @@ def rank_program(g, core, T, topo):
                 c0 = 64 * q_ + n_ * h
                 (cp if eng == "v" else act)(v("XX0", 16 * c0, 16 * (c0 + n_)), ind(v("TW", 0, 2944), v("CAL", c0, c0 + n_)))
         prep(0, qs, *B0[c])
-        k_gather(qs)
+        k_gather(0, qs)
         if c in SECOND:
-            steps(0, SECOND[c], ("PM", "PM", "PD_", "PD_")[c])
+            steps(0, SECOND[c])
+    dma("s", [(v("TW", 0, E, p=slice(row, 128, 16)), v("S3", c, c + 128)) for row, c in ((8, 256), (9, 640))])
+    fill(v("TW", 2944, 3456), 0.0)
+    dma("s", [(v("TW", 2944, 3456, p=slice(row, 128, 16)), v("TW", 0, 512, p=slice(row + 3, 128, 16))) for row in (5, 6)])
     for c in (0, 448):
-        act(v("YY", NG + c, NG + c + 448), ind(v("TW", 0, E), v("SNL", c // 16, c // 16 + 28)))
-    act(v("CAPA"), v("OH"), AF.Identity, bias=col(28), scale=-1.0)
-    act(v("CAPK"), v("OH"), AF.Identity, bias=col(31), scale=-1.0)
-    ts(v("SEG"), v("KI"), 0.0, A.not_equal)
-    iota(v("LB"), [[0, 256]], 1000000, 0, True, first)
-    iota(v("LBK"), [[0, 256]], 1000000, 0, True, first)
-    ts(col(22), col(1), float(DUMP), A.add)
-    ts(col(24), col(1), float(E), A.add)
+        (cp if WHO[c // 448] == "v" else act)(v("YY", NG + c, NG + c + 448), ind(v("TW", 0, E), v("SNL", c // 16, c // 16 + 28)))
+    act(v("SEG"), v("KI"), AF.Sign)
+    iota(v("LB"), [[0, 512]], 0, 0, True, first)
+    lin(col(22), col(1), 1.0, float(DUMP))
+    lin(col(23), col(1), 1.0, float(E + 16))
+    lin(col(24), col(1), 1.0, float(DUMP - HOLE))
+    lin(col(25), col(1), 1.0, 16.0)
     prep2(0)
-    be = v("BE", 0, 1)
-    ts(v("BT", 0, 1), be, -1.0 / 6, A.mult, 0.5, A.add)
-    ts(v("BT", 4, 5), v("BT", 0, 1), be, A.mult, -1.0, A.add)
-    ts(v("BT", 8, 9), v("BT", 4, 5), be, A.mult, 1.0, A.add)
-    act(v("SC", 0, 512), v("TVR", 0, 512), AF.Identity, bias=v("BT", 8, 9), scale=0.0)
-    mid = v("RT", 1024, 1536)
-    scan(mid, v("SC", 0, 512), v("SC", 0, 512), 1.0, A.mult, A.min)
-    run("v", lambda: g.vector.reciprocal(T.BT[:, 12:13], T.RT[:, 1535:1536]), v("BT", 12, 13), [v("RT", 1535, 1536)], 200.0)
-    tt(v("BT", 16, 17), v("BT", 12, 13), v("BT", 12, 13), A.mult)
-    act(v("RT", 0, 512), mid, scale=v("BT", 16, 17))
-    act(v("RT", 512, 1024), mid, scale=v("BT", 12, 13))
-    act(v("RT", 1536, 2048), mid, scale=v("RT", 1535, 1536))
-    fill(v("RT", 2047, 2048), 0.0)
-    ts(col(25), col(1), 256.0, A.mult, 15.0, A.add)
-    ts(v("LAML"), v("JF", 0, 16), 16.0, A.mult, col(25), A.add)
-    ts(col(37), col(1), 64.0, A.mult)
-    ts(v("PB", 0, 16), v("PB", 0, 16), col(37), A.add)
-    ts(col(38), col(1), 4096.0, A.add)
-    ts(v("PB", 16, 32), v("JF", 0, 16), 16.0, A.mult, col(38), A.add)
+    if EXP:
+        act(v("BT", 0, 1), v("BE", 0, 1), scale=-1.0)
+    else:
+        be = v("BE", 0, 1)
+        ts(v("BT", 0, 1), be, -1.0 / 6, A.mult, 0.5, A.add)
+        ts(v("BT", 4, 5), v("BT", 0, 1), be, A.mult, -1.0, A.add)
+        ts(v("BT", 8, 9), v("BT", 4, 5), be, A.mult, 1.0, A.add)
+        act(v("SD", 0, 512), v("OH", 0, 512), AF.Identity, bias=v("BT", 8, 9), scale=0.0)
+        mid = v("RT", 1024, 1536)
+        scan(mid, v("SD", 0, 512), v("SD", 0, 512), 1.0, A.mult, A.min)
+        run("v", lambda: g.vector.reciprocal(T.BT[:, 12:13], T.RT[:, 1535:1536]), v("BT", 12, 13), [v("RT", 1535, 1536)], 200.0)
+        tt(v("BT", 16, 17), v("BT", 12, 13), v("BT", 12, 13), A.mult)
+        act(v("RT", 0, 512), mid, scale=v("BT", 16, 17))
+        act(v("RT", 512, 1024), mid, scale=v("BT", 12, 13))
+        act(v("RT", 1536, 2048), mid, scale=v("RT", 1535, 1536))
+        fill(v("RT", 2047, 2048), 0.0)
+        ts(col(25), col(1), 256.0, A.mult, 15.0, A.add)
+        ts(v("LAML"), v("JF", 0, 16), 16.0, A.mult, col(25), A.add)
+    act(col(37), col(1), scale=64.0)
+    lin(v("PB", 0, 16), v("PB", 0, 16), 1.0, col(37))
+    lin(col(38), col(1), 1.0, 4096.0)
+    lin(v("PB", 16, 32), v("JF", 0, 16), 16.0, col(38))
     for t in range(2):
-        ts(v("PB", 32 + 16 * t, 48 + 16 * t), v("PB", 16, 32), 2944.0 + 256 * t - 8192.0, A.add)
-    act(v("KF"), v("KI"), scale=1.0 / 16)
-    ts(v("BSEG"), v("KI"), 0.0, A.is_equal, 1.0e6, A.mult)
+        lin(v("PB", 32 + 16 * t, 48 + 16 * t), v("PB", 16, 32), 1.0, 2944.0 + 256 * t - 8192.0)
+    lin(v("BSEG"), v("SEG"), -4096.0625, 4096.0)
 
     def chains():
         mm([(v("PT", 0, 112), win("FM", a), v("YY", a, 1792, 16), a == 0, a == 15) for a in range(16)])
@@ -565,71 +607,67 @@ def rank_program(g, core, T, topo):
 
     for t in range(R):
         s = t % 3
-        cp(v("CUM", 29, 768, 48), v("BGL", 16 * s, 16 * s + 16))
+        act(v("CUM", 29, 768, 48), v("BGL", 16 * s, 16 * s + 16))
         for j, (b0, b1) in enumerate(PARTS):
-            weights(t, b0, b1)
+            tag[0] = 0
+            weights(t, j, b0, b1)
             c0, c1 = 16 * b0, 16 * b1
             cum, thr = v("CUM", 3 * c0, 3 * c1, 3), v("THR", 8 * b0, 5 * b0 + 3 * b1)
             scan(cum, v("SEG", c0, c1), v("PW", c0, c1), 0.0, A.mult, A.add)
             scan(thr, v("CUM", 3 * c0 + 13, 3 * c1, 16), v("UL", 48 * t + 3 * b0, 48 * t + 3 * b1), 0.0, A.add, A.mult)
             tt(v("HIT", c0, c1), ind(thr, v("REP3", 0, b1 - b0)), cum, A.is_lt)
-            elect(0, BANKS[j % len(BANKS)], "", "XS", "LB", 1.0, col(22), c0, c1)
-            ts(v("L1C", b0, b1), v("XS", c0 + 15, c1, 16), float(HOLE), A.add, float(HOLE), A.min)
-            cp(v("L1", 2 * b0, 2 * b1, 2), v("OF", c0 + 15, c1, 16))
-            tt(v("NV", c0, c1), ind(v("AW", OWN, OWN + E + 16), v("L1C", b0, b1)), v("CAPA", 256 * s + c0, 256 * s + c1), A.min)
-            for b in range(b1 - 1, b0 - 1, -1):
-                scatter(v("SW"), "L1", "NV", 256 * s, b)
-            for k0, k1 in KPARTS:
-                if k0 == b0 and t < R - 1:
-                    c0, c1 = 16 * k0, 16 * k1
-                    elect(256, "PK", "K", "XK", "LBK", 64.0, col(24), c0, c1)
-                    ts(v("LKC", k0, k1), v("XK", c0 + 15, c1, 16), 64.0, A.mult, float(E), A.add)
-                    cp(v("LK", 2 * k0, 2 * k1, 2), v("OFK", c0 + 15, c1, 16))
-                    tt(v("NW", c0, c1), ind(v("KS"), v("LKC", k0, k1)), v("CAPK", 256 * s + c0, 256 * s + c1), A.min)
-                    for b in range(k1 - 1, k0 - 1, -1):
-                        scatter(v("KW"), "LK", "NW", 256 * s, b)
+            raise_(t, BANKS[j % len(BANKS)], b0, b1, 0)
+            tag[0] = 1
+            for k0, k1 in KPARTS if b0 == 0 and t < R - 1 else ():
+                raise_(t, "PX", k0, k1, 1)
             if t == 0 and b0 == CH0:
                 chains()
-        sent, came = exchange("SW", IGH, "BUF", NG, -1, calls=X1)
-        through("BUF", 0, [(ident, "GN", 0), (roll, "SW", IGUN)], both=True)
+        tag[0] = 0
+        buf = "BUF" if t % 2 == 0 else "BUG"
+        sent, came = exchange("SW", GHO, buf, NG, -1, calls=X1)
+        through(buf, 0, [(ident, "GN", 0), (roll, "SW", GUN)], both=BOTH[t])
         if t < R - 1:
-            dma("s", [(v("AW", OWN, OWN + E), v("SW", 0, E))], after=sent, lat=3000.0)
+            dma("s", [(v("AW", OWN, OWN + E), v("SW", OWN, OWN + E))], after=sent, lat=3000.0)
         for d in range(7):
             c = NG + GH * d
-            tt(v("BUF", c, c + GH), ind(v("BUF", 0, c), v("PRV", 8 * d, 8 * d + 8)), v("BUF", c, c + GH), A.add)
+            tt(v(buf, c, c + GH), ind(v(buf, 0, c), v("PRV", 8 * d, 8 * d + 8)), v(buf, c, c + GH), A.add)
         if t < R - 1:
-            ts(v("GN", 0, CUT), ind(v("BUF", 0, 2 * NG), v("LST", 0, CUT // 16)), 15.0, A.min)
-            last = act(v("XB", 0, NG - CUT), ind(v("BUF", 0, 2 * NG), v("LST", CUT // 16, 56)), AF.Relu, bias=col(28), scale=-1.0)
-            act(v("GN", CUT, NG), v("XB", 0, NG - CUT), AF.Identity, bias=col(28), scale=-1.0)
-            sent, came = exchange("GN", 0, "AW", GHO, 1, after=[last])
+            for c0, c1 in PICK:
+                ts(v("GN", c0, c1), ind(v(buf, 0, 2 * NG), v("LST", c0 // 16, c1 // 16)), 15.0, A.min)
+            sent, came = exchange("GN", 0, "AW", GHO, 1, calls=X2)
             through("AW", GUN, [(unroll, "GN", 0)])
-            iota(v("SW", IGUN, DUMP), [[0, 2 * NG]], 0, 0, True, sent[-1:])
+            tag[0] = 1
+            iota(v("SW", GUN, PAD), [[0, 2 * NG]], 0, 0, True, sent[-1:])
             if t < R - 2:
-                dma("s", [(v("KS", 0, E), v("KW", 0, E))], after=came, lat=3000.0)
+                dma("s", [(v("AW", KB, KH), v("SW", KB, KH))], after=came, lat=3000.0)
             if t < 2:
                 for c in range(4):
-                    act(v("XX%d" % (t + 1), 1024 * c, 1024 * c + 1024), ind(v("TW", 0, 2944), v("CAL", 256 * t + 256 + 64 * c, 256 * t + 320 + 64 * c)))
+                    (cp if LATER[t][c] == "v" else act)(v("XX%d" % (t + 1), 1024 * c, 1024 * c + 1024), ind(v("TW", 0, 2944), v("CAL", 256 * t + 256 + 64 * c, 256 * t + 320 + 64 * c)))
             prep(t + 1)
-            k_gather()
+            k_gather(t + 1)
             if t < 2:
                 candidates(t)
-            r_gather(t)
             prep2(t + 1)
+            tag[0] = 2
+            if t == 0:
+                decay(0)
+            decay(t + 1)
         else:
-            r_gather(t)
             for c in range(4):
-                bank = v("PR%d" % (c % 2), 0, 512)
-                mm([(bank, roll, v("SW", 512 * c, 512 * c + 512), True, True)])
-                act(v("BUF", 2 * NG + 512 * c, 2 * NG + 512 * c + 512), bank)
+                bank = v(BANKS[c % 2], 0, 512)
+                mm([(bank, roll, v("SW", OWN + 512 * c, OWN + 512 * c + 512), True, True)])
+                act(v("BUF", OWN + 512 * c, OWN + 512 * c + 512), bank)
             for c0, c1, eng in FINAL:
                 o, src = v("RG1", c0, c1), ind(v("BUF"), v("MAPL", c0 // 16, c1 // 16))
                 if eng == "v":
                     ts(o, src, 15.0, A.min)
                 else:
-                    act(v("RG1", E + c0, E + c1), src, AF.Relu, bias=col(28), scale=-1.0)
-                    act(o, v("RG1", E + c0, E + c1), AF.Identity, bias=col(28), scale=-1.0)
+                    act(v("RG1", E + c0, E + c1), src, AF.Relu, bias=15.0, scale=-1.0)
+                    lin(o, v("RG1", E + c0, E + c1), -1.0, 15.0)
                 dma("s" if eng == "v" else "a", [(T.ya[0:112, c0:c1], v("RG1", c0, c1, p=up)), (T.ya[112:128, c0:c1], v("RG1", c0, c1, p=down))])
+        tag[0] = 2
         lam(t)
+        tag[0] = 1
         if t == 2:
             mm([(v("PD_", 0, 128), win("FM", a), v("TW", a, E, 16), a == 0, a == 15) for a in range(16)])
             act(v("W1", 0, 128), v("PD_", 0, 128))
@@ -642,28 +680,30 @@ def rank_program(g, core, T, topo):
     succ = [[] for _ in range(n)]
     for i, o in enumerate(ops):
         if o["kind"] == "r":
-            o["deps"] = set([o["with"]])
+            o["deps"] = set(o["gaps"])
         for d in o["deps"]:
             succ[d].append(i)
 
     def gap(d, i):
-        if ops[i]["kind"] == "r" or ops[i]["q"] == ops[d]["q"] == "t" or d in ops[i]["behind"]:
+        if ops[i]["kind"] == "r":
+            return ops[i]["gaps"][d]
+        if ops[i]["q"] == ops[d]["q"] == "t" or d in ops[i]["behind"]:
             return 0.0
         return ops[d]["lat"] + SYNC
 
     if n not in ORDER:
         level = [0.0] * n
         for i in range(n - 1, -1, -1):
-            level[i] = ops[i]["cost"] + max([gap(i, j) + level[j] for j in succ[i]] + [ops[i]["lat"]])
+            level[i] = ops[i]["cost"] + max([gap(i, j) + ops[i].get("urge", 0.0) + level[j] for j in succ[i]] + [ops[i]["lat"] + ops[i].get("due", 0.0)])
         pred = [sorted(o["deps"]) for o in ops]
-        fgap = [[(j, gap(i, j)) for j in succ[i]] for i in range(n)]
-        bgap = [[(d, gap(d, i)) for d in pred[i]] for i in range(n)]
+        fgap = [[(j, gap(i, j) + ops[i].get("urge", 0.0)) for j in succ[i]] for i in range(n)]
+        bgap = [[(d, gap(d, i) + ops[d].get("urge", 0.0)) for d in pred[i]] for i in range(n)]
 
-        def fit(key, npred, out, head):
+        def fit(key, npred, out, head, sign=1.0):
             left, est, start, busy = list(npred), list(head), [0.0] * n, {q: [] for q in Q}
             ready = [i for i in range(n) if not left[i]]
             while ready:
-                i = min(ready, key=lambda j: key[j])
+                i = min(ready, key=lambda j: key[j] - sign * ops[j]["rank"])
                 ready.remove(i)
                 t0, c, q = est[i], ops[i]["cost"], ops[i]["q"]
                 if q is not None:
@@ -694,7 +734,7 @@ def rank_program(g, core, T, topo):
             if best is None or span < best[0]:
                 best = (span, sorted(range(n), key=lambda i: (fw[i], i)), fw)
             base = fw if span <= best[0] + SLIP else best[2]
-            bw = fit([-(base[i] + ops[i]["cost"]) for i in range(n)], [len(x) for x in succ], bgap, [ops[i]["lat"] if not succ[i] else 0.0 for i in range(n)])
+            bw = fit([-(base[i] + ops[i]["cost"]) for i in range(n)], [len(x) for x in succ], bgap, [(ops[i]["lat"] if not succ[i] else 0.0) + ops[i].get("due", 0.0) for i in range(n)])
             noise = rng.random(n) * NOISE
             key = [-(bw[i] + ops[i]["cost"]) + float(noise[i]) for i in range(n)]
         anc, fp = [0] * n, []
@@ -702,14 +742,14 @@ def rank_program(g, core, T, topo):
             m_ = 0
             for d in pred[i]:
                 m_ |= anc[d]
-            fp.append([(d, w) for d, w in bgap[i] if ops[d]["lat"] > 150.0 or not (m_ >> d) & 1])
+            fp.append([(d, gap(d, i)) for d in pred[i] if ops[d]["lat"] > 150.0 or ops[i]["kind"] == "r" or not (m_ >> d) & 1])
             for d in pred[i]:
                 m_ |= 1 << d
             anc[i] = m_
         lat, views = [o["lat"] for o in ops], []
-        for per, sync in VIEWS:
-            cost = [o["cost"] + o.get("picked", 0.0) * (per - GATHER) for o in ops]
-            into = [[(d, cost[d] + (w - SYNC + sync if w else 0.0)) for d, w in fp[i]] for i in range(n)]
+        for per, sync, slow in VIEWS:
+            cost = [(o["cost"] + o.get("picked", 0.0) * (per - GATHER)) * (slow if o["kind"] == "c" else 1.0) for o in ops]
+            into = [[(d, cost[d] + (w - SYNC + sync if w and ops[i]["kind"] != "r" else w)) for d, w in fp[i]] for i in range(n)]
             out = [[] for _ in range(n)]
             for i in range(n):
                 for d, w in into[i]:
@@ -717,28 +757,51 @@ def rank_program(g, core, T, topo):
             views.append((cost, into, out))
         seq = {q: [i for i in best[1] if ops[i]["q"] == q] for q in Q}
 
-        def times(cost, fp, fs):
-            before, after_ = [-1] * n, [-1] * n
-            for x in seq.values():
-                for a_, b_ in zip(x, x[1:]):
-                    before[b_], after_[a_] = a_, b_
-            left = [len(fp[i]) + (before[i] >= 0) for i in range(n)]
-            todo, r = [i for i in range(n) if not left[i]], [0.0] * n
+        before, after_ = [-1] * n, [-1] * n
+
+        def link(x, first_=-1, last_=-1):
+            for a_, b_ in zip([first_] + x, x + [last_]):
+                if a_ >= 0:
+                    after_[a_] = b_
+                if b_ >= 0:
+                    before[b_] = a_
+
+        def sort(part, inside, fs):
+            left = {i: npre[i] + (before[i] in inside) for i in part}
+            todo = [i for i in part if not left[i]]
             for i in todo:
-                for j, w in fs[i] + ([(after_[i], cost[i])] if after_[i] >= 0 else []):
-                    if r[i] + w > r[j]:
-                        r[j] = r[i] + w
+                for j, w in fs[i]:
+                    if j in inside:
+                        left[j] -= 1
+                        if not left[j]:
+                            todo.append(j)
+                j = after_[i]
+                if j in inside:
                     left[j] -= 1
                     if not left[j]:
                         todo.append(j)
-            tail = [0.0] * n
+            return todo
+
+        def times(todo, view, r, tail):
+            cost, fp, fs = view
+            for i in todo:
+                d = before[i]
+                x = r[d] + cost[d] if d >= 0 else 0.0
+                for d, w in fp[i]:
+                    if r[d] + w > x:
+                        x = r[d] + w
+                r[i] = x
+            span = 0.0
             for i in reversed(todo):
-                x = cost[i] + max(lat[i], tail[after_[i]] if after_[i] >= 0 else 0.0)
+                j = after_[i]
+                x = cost[i] + (tail[j] if j >= 0 and tail[j] > lat[i] else lat[i])
                 for j, w in fs[i]:
                     if w + tail[j] > x:
                         x = w + tail[j]
                 tail[i] = x
-            return r, tail, before, after_, todo
+                if r[i] + x > span:
+                    span = r[i] + x
+            return span
 
         def guess(new, first_, last_, r, tail, cost, fp, fs):
             t0, head = (r[first_] + cost[first_] if first_ >= 0 else 0.0), []
@@ -757,59 +820,81 @@ def rank_program(g, core, T, topo):
                 worst = max(worst, h + t1)
             return worst
 
-        tabu, best, now, undo = {}, None, None, None
-        for it in range(MOVES):
-            got = [times(*x) for x in views]
-            total = sum(max(x[1]) for x in got)
-            if now is not None and total > now[0] + SLACK:
-                seq[undo[0]] = undo[1]
-                total, got = now
-            now = (total, got)
-            if best is None or total < best[0] - 1.0:
-                best = (total, got[0][4], got[0][0])
-            cost, fp, fs = views[it % len(views)]
-            r, tail, before, after_, todo = got[it % len(views)]
-            span = max(tail)
-            crit = [i for i in todo if r[i] + tail[i] > span - 0.01]
-            on, moves = set(crit), []
-            for u in crit:
-                w_ = after_[u]
-                if w_ < 0 or w_ not in on or r[w_] > r[u] + cost[u] + 0.01:
-                    continue
-                run_, x = [u], before[u]
-                for k_ in range(FAR):
-                    f = run_[0]
-                    if any(d == f or r[d] + cost[d] > r[f] + cost[f] for d, w in fp[w_]):
-                        break
-                    if tabu.get((w_, f), -1) < it and (k_ < REACH or x < 0 or r[f] - r[x] - cost[x] > 0.6 * cost[w_]):
-                        moves.append((guess([w_] + run_, before[f], after_[w_], r, tail, cost, fp, fs), w_, f, 0, run_[:]))
-                    if x < 0:
-                        break
-                    run_.insert(0, x)
-                    x = before[x]
-                run_, x = [w_], after_[w_]
-                for k_ in range(FAR):
-                    f = run_[-1]
-                    if any(j == f or tail[j] > tail[f] for j, w in fs[u]):
-                        break
-                    if tabu.get((f, u), -1) < it and (k_ < REACH or x < 0 or r[x] - r[f] - cost[f] > 0.6 * cost[u]):
-                        moves.append((guess(run_ + [u], before[u], after_[f], r, tail, cost, fp, fs), u, f, 1, run_[:]))
-                    if x < 0:
-                        break
-                    run_.append(x)
-                    x = after_[x]
-            if not moves:
-                tabu = {}
-                continue
-            e_, x, f, side, run_ = min(moves, key=lambda m_: m_[0] + float(rng.random()) * JITTER)
-            line_ = seq[ops[x]["q"]]
-            undo = (ops[x]["q"], line_[:])
-            line_.remove(x)
-            line_.insert(line_.index(f) + side, x)
-            tabu[(x, f) if side == 0 else (f, x)] = it + TENURE
-            for y in run_:
-                tabu[(y, x) if side == 0 else (x, y)] = it + TENURE
-        ORDER[n] = best
+        for x in seq.values():
+            link(x)
+        every, order_ = set(range(n)), best[1]
+        heads, tails = [[0.0] * n for x in views], [[0.0] * n for x in views]
+        for sweep in range(SWEEPS):
+            size = STRETCH[sweep % len(STRETCH)]
+            for p0 in range(-(sweep % 2) * size // 4, n - size // 2, size // 2):
+                npre = [len(x) for x in fp]
+                order_ = sort(order_, every, views[0][2])
+                for x, r, tail in zip(views, heads, tails):
+                    times(order_, x, r, tail)
+                order_.sort(key=lambda i: heads[0][i] + heads[-1][i])
+                part = order_[max(p0, 0):p0 + size]
+                inside = set(part)
+                npre = {i: sum(d in inside for d, w in fp[i]) for i in part}
+                lines = {q: [i for i in part if ops[i]["q"] == q] for q in Q}
+                ends = {q: (before[x[0]], after_[x[-1]]) for q, x in lines.items() if x}
+                tabu, best_, now, undo = {}, None, None, None
+                for it in range(MOVES):
+                    todo = sort(part, inside, views[0][2])
+                    total = sum(times(todo, x, r, tail) for x, r, tail in zip(views, heads, tails)) if len(todo) == len(part) else 1e18
+                    if now is not None and total > now + SLACK:
+                        lines[undo[0]] = undo[1]
+                        link(undo[1], *ends[undo[0]])
+                        todo = sort(part, inside, views[0][2])
+                        total = sum(times(todo, x, r, tail) for x, r, tail in zip(views, heads, tails))
+                    now = total
+                    if best_ is None or total < best_[0] - 1.0:
+                        best_ = (total, {q: x[:] for q, x in lines.items()})
+                    (cost, fp_, fs), r, tail = views[it % len(views)], heads[it % len(views)], tails[it % len(views)]
+                    span = max(r[i] + tail[i] for i in part)
+                    on, moves = set(i for i in part if r[i] + tail[i] > span - 0.01), []
+                    for u in sorted(on):
+                        w_ = after_[u]
+                        if w_ not in on or r[w_] > r[u] + cost[u] + 0.01:
+                            continue
+                        run_, x = [u], before[u]
+                        for k_ in range(FAR):
+                            f = run_[0]
+                            if any(d == f or r[d] + cost[d] > r[f] + cost[f] for d, w in fp_[w_]):
+                                break
+                            if tabu.get((w_, f), -1) < it and (k_ < REACH or x < 0 or r[f] - r[x] - cost[x] > 0.6 * cost[w_]):
+                                moves.append((guess([w_] + run_, before[f], after_[w_], r, tail, cost, fp_, fs), w_, f, 0, run_[:]))
+                            if x not in inside:
+                                break
+                            run_.insert(0, x)
+                            x = before[x]
+                        run_, x = [w_], after_[w_]
+                        for k_ in range(FAR):
+                            f = run_[-1]
+                            if any(j == f or tail[j] > tail[f] for j, w in fs[u]):
+                                break
+                            if tabu.get((f, u), -1) < it and (k_ < REACH or x < 0 or r[x] - r[f] - cost[f] > 0.6 * cost[u]):
+                                moves.append((guess(run_ + [u], before[u], after_[f], r, tail, cost, fp_, fs), u, f, 1, run_[:]))
+                            if x not in inside:
+                                break
+                            run_.append(x)
+                            x = after_[x]
+                    if not moves:
+                        tabu, now = {}, None
+                        continue
+                    e_, x, f, side, run_ = min(moves, key=lambda m_: m_[0] + float(rng.random()) * JITTER)
+                    q = ops[x]["q"]
+                    undo = (q, lines[q][:])
+                    lines[q].remove(x)
+                    lines[q].insert(lines[q].index(f) + side, x)
+                    link(lines[q], *ends[q])
+                    tabu[(x, f) if side == 0 else (f, x)] = it + TENURE
+                    for y in run_:
+                        tabu[(y, x) if side == 0 else (x, y)] = it + TENURE
+                for q, x in best_[1].items():
+                    if x:
+                        link(x, *ends[q])
+        npre = [len(x) for x in fp]
+        ORDER[n] = (0.0, sort(order_, every, views[0][2]))
     order = ORDER[n][1]
 
     ESEM = {"v": "ev", "a": "ea", "t": "et", "g": "eg"}

@@ -3,36 +3,31 @@ from concourse.bass import DstId, RemoteDMATransfer
 from concourse.mybir import AluOpType, ActivationFunctionType
 
 N, E, GH, NG, R = 8, 2048, 128, 896, 5
-GUN, GHO, PAD, HOLE, OWN, DUMP, KB, KH, RWN = 0, 896, 1792, 1807, 1808, 3856, 3872, 5920, 5952
+GUN, GHO, PAD, HOLE, OWN, DUMP, KB, KH, RWN = 0, 896, 1792, 1807, 1808, 3856, 3920, 5968, 6048
 F32, BF, I32, U16, F16 = "float32", "bfloat16", "int32", "uint16", "float16"
-HALF = F16
+SEGW = 66
 SB = {
-    "AW": (KH + 16, BF), "SW": (RWN, BF), "TW": (3456, BF), "BUF": (DUMP, BF), "GN": (NG, BF), "BUG": (2 * NG, BF),
+    "AW": (RWN, BF), "SW": (RWN, BF), "TW": (3456, BF), "BUF": (DUMP, BF), "GN": (NG, BF), "BUG": (2 * NG, BF),
     "XX0": (4352, BF), "XX1": (4352, BF), "XX2": (4096, BF), "KG": (4096, BF), "PR0_": (4096, BF), "PR1_": (4096, BF), "PR2_": (4096, BF), "AS": (4096, BF),
-    "RG0": (4096, F32), "RG1": (4096, F32), "BC": (2048, BF), "FN": (144, BF), "NI": (128, BF), "LH": (256, F16), "DL0": (256, F16), "DL1": (256, F16), "DL2": (256, F16),
-    "GT": (NG, BF), "VV": (NG, BF), "YY": (1792, BF), "GS": (NG, BF), "SL": (512, BF), "HI": (448, BF), "LO": (512, BF), "AG": (2048, BF),
+    "RG0": (4096, F32), "RG1": (4096, F32), "SC": (4096, F32), "BC": (2048, BF), "FN": (144, BF), "LH0": (256, F16), "LH1": (256, F16), "LH2": (256, F16),
+    "GT": (NG, BF), "VV": (NG, BF), "YY": (1792, BF), "GS": (NG, BF), "SL": (512, BF), "HI": (448, BF), "LO": (512, BF), "AG": (512, BF),
     "CA": (768, I32), "CAL": (768, U16), "SN": (56, I32), "SNL": (56, U16), "EQ": (48, F32), "RM": (128, BF),
-    "SI": (384, I32), "S2": (896, I32), "S3": (1024, BF),
-    "QI": (176, I32), "QH": (176, F16), "QF": (1280, F16), "JF": (272, F32), "FQ": (272, BF), "KI": (256, F32), "J16": (128, F32), "PI": (16, I32), "PC": (192, F32),
-    "F0": (144, BF), "FT": (144, BF), "FK": (144, BF), "FM": (144, BF), "FC": (144, BF), "FL": (144, BF),
-    "I2": (256, BF), "D11": (128, BF), "D12": (128, BF), "K89": (128, BF), "P56": (128, BF), "I32F": (384, F32),
-    "GK": (128, BF), "SH": (2048, BF), "SEG": (256, F32), "BSEG": (256, F32),
-    "REP": (48, U16), "REP3": (16, U16), "PERM": (48, U16), "T48": (48, F32), "PB": (64, F32),
-    "UL": (240, F32), "BGL": (48, F32), "NTV": (48, F32), "KV": (48, F32), "TVR": (768, HALF), "KVR": (768, HALF), "OH": (768, BF), "CAP": (1536, BF),
+    "SI": (384, I32), "S2": (896, I32), "S3": (1024, BF), "UR": (1280, I32),
+    "QI": (144, I32), "QH": (144, BF), "QF": (768, BF), "JF": (144, F32), "KI": (256, F32), "J16": (128, F32), "J8": (128, F32), "PI": (32, I32), "PC": (224, F32),
+    "F0": (144, BF), "FT": (144, BF), "FK": (144, BF), "FM": (144, BF), "FL": (144, BF), "F15": (144, BF),
+    "I2": (256, BF), "D11": (128, BF), "D12": (128, BF), "K89": (128, BF), "P56": (128, BF), "I32F": (256, F32),
+    "GK": (128, BF), "GM": (128, BF), "NT": (128, BF), "KV": (128, BF), "WC": (248, BF), "WB": (128, BF), "W0": (128, BF), "FH": (384, BF),
+    "TRI": (160, BF), "RST": (8 * SEGW, F16), "SEG": (256, BF), "BSEG": (256, F32), "PB": (64, F32), "OH": (768, BF), "CAP": (768, BF),
     "YU": (112, F32), "YT": (168, F32), "PRV": (56, U16), "LST": (56, U16), "MAPL": (128, U16), "BE": (8, F32), "BT": (4, F32),
-    "YI": (256, BF), "SS": (256, HALF), "MT": (256, HALF), "CT0": (256, F32), "CT1": (256, F32),
-    "ML": (256, U16), "BNL": (256, U16),
-    "CUM": (768, F32), "THR": (128, F32), "HIT": (256, F32), "PD": (512, F32), "XS": (512, F16), "LB": (512, F32), "EE": (512, F32), "OF": (512, F32),
-    "L1": (64, U16), "L1C": (32, U16), "NV": (512, BF), "NX": (256, BF), "NX1": (256, BF), "NX2": (256, BF),
-    "LAM": (256, F32), "MN": (256, F32), "W1": (256, F32), "W2": (256, F32), "W3": (256, F32),
+    "YI": (256, BF), "SS": (512, F16), "MT": (512, F16), "CT": (512, F16), "ML": (512, U16), "BNL": (512, U16), "XL": (512, F32), "DG": (128, BF), "RS": (128, F32),
+    "THR": (256, F32), "HIT": (256, BF), "PD": (768, F16), "EE": (32 * SEGW, F16), "OF": (32 * SEGW, F16),
+    "SH": (2048, BF), "XK": (256, F16), "LK": (256, F32), "EK": (256, F32), "OK": (256, F32), "L2": (32, U16), "ONE": (512, BF), "WS": (256, F16),
+    "L1": (32, U16), "L1C": (32, U16), "NV": (512, BF), "NX": (256, BF), "NX1": (256, BF), "NX2": (256, BF),
+    "LAM": (256, F32), "MN": (256, F32), "W1": (128, F32), "W2": (128, F32), "W3": (128, F32),
     "SM": (96, F32), "MI": (32, I32), "IX1": (16, U16), "IX2": (16, U16), "PL": (16, U16), "NC": (16, U16),
 }
 DROP = 24.0
-EXP = True
-if not EXP:
-    SB.update({"RT": (2048, F32), "SD": (4096, F32), "E150": (256, F32), "E151": (256, F32), "LAML": (16, U16), "BT": (24, F32), "BC": (16, BF),
-               "RL0": (256, U16), "RL1": (256, U16), "RL2": (256, U16), "EL0": (16, U16), "EL1": (16, U16), "EL2": (16, U16)})
-ALIAS = {"GT": ("KG", 0), "YY": ("PR2_", 0), "VV": ("PR2_", 1792), "GS": ("PR0_", E), "SL": ("PR0_", E + NG), "AG": ("PR1_", 0), "HI": ("PR1_", 2048), "LO": ("PR1_", 2048 + NG)}
+ALIAS = {"GT": ("KG", 0), "YY": ("PR2_", 0), "VV": ("PR2_", 1792), "GS": ("PR0_", E), "SL": ("PR0_", E + NG), "AG": ("ONE", 0), "HI": ("PR1_", 2048), "LO": ("PR1_", 2048 + NG)}
 PS = ["PW", "PD_", "PR0", "PR1", "PT", "PK", "PX", "PM"]
 POOL, _n = {}, 0
 for _k, (_c, _d) in SB.items():
@@ -41,8 +36,6 @@ for _k, (_c, _d) in SB.items():
         _n += (_c + 15) // 16 * 16
 SCRATCH = {k: ("sbuf", [128, n], d) for k, (n, d) in SB.items() if k not in POOL and k not in ALIAS}
 SCRATCH["UP"] = ("sbuf", [128, _n], U16)
-if EXP:
-    SCRATCH["SC"] = ("sbuf", [128, 256, 16], F32)
 for _k in PS:
     SCRATCH[_k] = ("psum", [128, 512], F32)
 X1 = ((((1, 2), 0, 4),), (((3, 4), 0, 4),), (((5, 6), 0, 4),), (((7,), 0, 8),))
@@ -53,35 +46,47 @@ SIZE = {F32: 4, I32: 4, BF: 2, U16: 2, F16: 2}
 A = AluOpType
 AF = ActivationFunctionType
 CYC, FIX, FIXS, GATHER, SCATTER, PEC, SYNC, DMALAT, ROWLAT, ISSUE, HOP, ROW = 0.87, 50.0, 5.0, 1.8, 3.8, 0.43, 250.0, 2200.0, 100.0, 400.0, 1500.0, 35.0
-PASSES, SLIP, NOISE, MOVES, REACH, FAR, JITTER, TENURE, ORDER = 15, 1000.0, 0.0, 60, 5, 80, 100.0, 20, {}
-SWEEPS, STRETCH = 12, (150,)
-PARTS = ((12, 16), (8, 12), (4, 8), (0, 4))
-SPLIT = ((0, 0, 0, 32), (32, 32, 32, 32), (32, 48, 48, 48), (32, 48, 48, 48), (32, 48, 48, 48))
-LATER = ("vaaa", "vaaa")
-DB, SBK = ("PR0", "PR1"), ("PR0", "PR1")
-WHO, K0 = "vvvaa", "aaaa"
-DUE = (70000.0, 50000.0, 35000.0, 15000.0, 0.0)
-ONS = ((False, True),) * 5
-KPARTS, KV = ((8, 16), (0, 8)), ("aaaa", "aaaa", "vaaa", "vaaa", "vaaa")
-BOOST = (1000.0, 500.0, 0.0)
-KFIRST = 0
-HALVES = (2, 2, 2, 2, 2)
+PASSES, SLIP, NOISE, MOVES, REACH, FAR, JITTER, TENURE, ORDER = 15, 3000.0, 600.0, 60, 5, 80, 300.0, 20, {}
+SEED, STARTS, BUILD, WEIGHT = 6, 9, (0, 2, 4), (1.0, 1.0, 1.0, 1.0, 1.0)
+LAG, COVER, AHEAD, KBOOST, SHADOW = 0, True, (0.0, 0.0, 0.0, 0.0, 0.0), 700.0, 3
+KOLD, RUNS, WSV = False, 16, ("vvvv",) * 5
+SOON, RBANK = (0.0, 0.0, 0.0, 0.0, 0.0), "PR1"
+SETUP, PICKS0, FIRSTLATE = (50000.0, 100000.0), 50000.0, 2000.0
+PHASED, PH = False, {"chain": 0.1, "prep": (0.15, 0.15, 0.15, 0.15, 0.15), "raise": 0.2, "gather": 0.3, "parents": 0.4, "replace": 0.5, "decay": (1.6, 1.6, 1.6, 1.05, 0.05), "lam": (1.7, 1.7, 1.7, 1.06, 0.2)}
+STEPS, NEAR, WIDE, PUSH = 0, 300.0, 6000.0, 1500.0
+SWEEPS, STRETCH = 20, (150, 110, 200)
+EARLY, LBA = (2100.0, 1400.0, 700.0, 0.0), ("aa",) * 5
+PARTS = ((((12, 16),), ((8, 12),), ((4, 8),), ((0, 4),)),) * 5
+SPLIT = ((0, 0, 16, 48), (32, 32, 32, 32), (32, 48, 48, 48), (32, 48, 48, 48), (32, 48, 48, 48))
+LATER = ("vvaaaaaa", "vvaaaaaa")
+DB, SBK = ("PR0", "PR0"), ("PR1", "PR1")
+WHO = "va"
+DUE = (80000.0, 58000.0, 39000.0, 19000.0, 0.0)
+KBANKS, CBANKS = ("PW", "PX"), ("PT", "PK")
+KV = ("aaaaaaaa", "aaaaaaaa", "vvaaaaaa", "vaaaaaaa", "vaaaaaaa")
+BOOST = (1500.0, 500.0, 0.0)
+PIECE = 128
 BANKS, WCH, LATE, CH0 = ("PD_", "PM"), 64, 500.0, 8
-FIRST = (("va", (3,)), ("v", (2,)), ("a", (1,)), ("v", (0,)))
-B0 = (("PT", "PK"), ("PR0", "PR1"), ("PT", "PK"), ("PR0", "PR1"))
-VIEWS, SLACK = ((1.56, 250.0, 1.0), (2.08, 250.0, 1.0), (1.56, 120.0, 1.0), (1.2, 150.0, 1.2), (1.8, 150.0, 1.35)), 150.0
-PICK = ((0, 128), (128, 384), (384, NG))
-BOTH, URGE = (False, False, False, False, False), 5000.0
-SECOND = {1: (3, 2), 3: (1, 0)}
-FINAL = ((0, 416, "v"), (416, 672, "a"), (672, 1088, "v"), (1088, 1344, "a"), (1344, 1792, "v"), (1792, 2048, "a"))
+FIRST = (("va", (3,)), ("va", (2,)), ("v", (1,)), ("v", (0,)))
+B0 = (("PT", "PK"), ("PR0", "PR1"), ("PD_", "PM"), ("PW", "PX"))
+VIEWS, SLACK = ((1.56, 3.8, 80.0, 1.0, 0.0, 1.0), (2.0, 4.5, 120.0, 1.3, 0.0, 1.0), (1.2, 3.0, 100.0, 1.2, 0.0, 1.2), (1.8, 3.8, 150.0, 1.45, 10.0, 1.0), (1.56, 3.8, 200.0, 1.1, 0.0, 1.0)), 500.0
+NVK = "a"
+PICK, PICKS = ((0, 128), (128, 384), (384, 768), (768, NG)), ("vvvv",) * 4
+BOTH, URGE = (False, False, False, False, False), (0.0, 5000.0, 5000.0, 5000.0, 5000.0)
+HALFLISTS = (False, True, True, True, True)
+FINAL = ((0, 448, "v"), (448, 896, "a"), (896, 1248, "v"), (1248, 1600, "a"), (1600, 1824, "v"), (1824, 2048, "a"))
+ABANKS, PB1 = (("PK", "PR1", "PM", "PX"),) + (("PW", "PX", "PD_", "PM"),) * 4, False
+XLV, XLK = (True, True, True, True), True
+RENUM = "a"
 
 
 def rank_program(g, core, T, topo):
     rank = T.rank_of(core)
     if rank is None:
         return
+    phase = [0.0]
     Q = {"v": g.vector, "a": g.scalar, "t": g.tensor, "g": g, "s": g.sync}
-    ops, hist, ndma, nx, tag = [], {}, [0], [0, 0], [1]
+    ops, hist, ndma, nx, tag, extra = [], {}, [0], [0, 0], [1], [0.0]
 
     def v(name, c0=0, c1=None, step=1, p=None):
         n, sz = (SB[name][0], SIZE[SB[name][1]]) if name in SB else (512, 4)
@@ -91,6 +96,14 @@ def rank_program(g, core, T, topo):
         ten, b = (T.UP, POOL[name]) if name in POOL else (T[base], r0)
         ap_ = ten[rows, b + c0:b + c1:step] if step != 1 else ten[rows, b + c0:b + c1]
         return {"ap": ap_, "reg": [(base, ((r0 + c0) * sz) // 16 * 16, ((r0 + c1) * sz + 15) // 16 * 16)], "n": len(range(c0, c1, step)), "sz": sz, "ps": name in PS}
+
+    def spots(name, c0, c1, step):
+        x = v(name, c0, c1, step)
+        return dict(x, reg=[(name, c * x["sz"], (c + 1) * x["sz"]) for c in range(c0, c1, step)])
+
+    def exact(name, c0, c1):
+        x = v(name, c0, c1)
+        return dict(x, reg=[(name, c0 * x["sz"], c1 * x["sz"])])
 
     def ind(win, off):
         return {"ap": win["ap"].indirect(off["ap"]), "reg": win["reg"], "off": off["reg"], "n": 16 * off["n"], "sz": win["sz"], "ps": False}
@@ -114,7 +127,7 @@ def rank_program(g, core, T, topo):
             hist[name] = keep + [(me, lo, hi, True)]
         for name, lo, hi in rd:
             hist.setdefault(name, []).append((me, lo, hi, False))
-        ops.append({"q": q, "calls": calls, "deps": deps | set(behind), "behind": set(behind) - deps, "cost": cost, "lat": lat, "rank": BOOST[tag[0]], "kind": kind})
+        ops.append({"q": q, "calls": calls, "deps": deps | set(behind), "behind": set(behind) - deps, "cost": cost, "lat": lat, "rank": BOOST[tag[0]] + extra[0], "phase": phase[0], "kind": kind})
         return me
 
     def run(q, call, o, ins, per, behind=()):
@@ -127,7 +140,7 @@ def rank_program(g, core, T, topo):
             per = 1.0
         cost = FIX + CYC * per * o["n"] if q != "v" or per in (GATHER, SCATTER) else FIXS + CYC * max(64, per * o["n"])
         me = add(q, [call], regs(ins) + o.get("off", []), o["reg"], cost, behind=behind)
-        ops[me]["picked"] = CYC * o["n"] if per == GATHER else 0.0
+        ops[me]["picked"], ops[me]["put"] = CYC * o["n"] * (per == GATHER), CYC * o["n"] * (per == SCATTER)
         return me
 
     def tt(o, a, b, op):
@@ -217,52 +230,15 @@ def rank_program(g, core, T, topo):
                 came.append(arr)
         return mine, came
 
-    def col(j):
-        return v("PC", 4 * j, 4 * j + 1)
+    def col(j, p=None):
+        return v("PC", 4 * j, 4 * j + 1, p=p)
+
+    def pint(j):
+        return v("PI", 4 * j, 4 * j + 1)
 
     def win(name, a):
         return v(name, 15 - a, 143 - a)
 
-    up, down = slice(16, 128), slice(0, 16)
-    dma("s", [(v("SI", 0, 128), T.ti[:])])
-    dma("a", [(v("SI", 256, 384), T.lp[:])])
-    dma("s", [(v("S2", 768, 896), T.kd[:])])
-    dma("a", [(v("SN"), T.snd[:])])
-    fill(v("TW", 0, E), 0.0)
-    g0 = iota(v("SI", 128, 256), [[1, 128]], 0, 128, False)
-    g0 = iota(v("PI", 0, 1), [[0, 1]], 0, 1, False, [g0])
-    g0 = iota(v("JF", 0, 144), [[1, 144]], 0, 0, True, [g0])
-    g0 = iota(v("HI"), [[64, 7], [0, 64]], 0, 0, True, [g0])
-    g0 = iota(v("LO"), [[0, 8], [1, 64]], 0, 0, True, [g0])
-    iota(v("JF", 144, 272), [[1, 128]], 144, 0)
-    iota(v("T48"), [[256, 3], [64, 4], [4, 4]], 0, 0)
-    iota(v("KI"), [[0, 16], [1, 16]], 0, 0)
-    iota(v("J16"), [[16, 8], [0, 16]], 0, 0)
-    iota(v("PB", 0, 16), [[1024, 4], [16, 4]], 0, 0)
-    cp(v("S3", 0, 128), v("SI", 0, 128))
-    tt(v("S3", 384, 512), v("SI", 0, 128), v("S3", 0, 128), A.subtract)
-    for c0 in (128, 256):
-        ts(v("S2", c0, c0 + 128), v("SI", c0, c0 + 128), 0xFC0 if c0 == 256 else 0x7C0, A.bitwise_and)
-        ts(v("S2", c0 + 384, c0 + 512), v("SI", c0, c0 + 128), 63, A.bitwise_and)
-        cp(v("S3", c0, c0 + 128), v("S2", c0, c0 + 128))
-        cp(v("S3", c0 + 384, c0 + 512), v("S2", c0 + 384, c0 + 512))
-    cp(v("S3", 768, 896), v("S2", 768, 896))
-    act(v("S3", 896, 1024), v("S3", 128, 256), AF.Identity, bias=float(OWN))
-    line = {"s": [], "a": []}
-    for q, row, c in (("s", 5, 128), ("a", 4, 512), ("s", 6, 512), ("a", 3, 896), ("s", 11, 768), ("a", 0, 0), ("s", 7, 384)):
-        line[q].append(dma(q, [(v("TW", 0, E, p=slice(row, 128, 16)), v("S3", c, c + 128))], True, behind=line[q][-1:], lat=DMALAT + ROWLAT * len(line[q])))
-    a0 = dma("a", [(v("AW", OWN, OWN + E), T.a0[:])], lat=5000.0, behind=line["a"][-1:])
-    small = dma("s", [(v("QI", 0, 80), T.us[:]), (v("QI", 80, 128), T.bg[:]), (v("QI", 128, 176), T.cl[:])], behind=line["s"][-1:], lat=3000.0)
-    ca = dma("s", [(v("CA"), T.ca[:])], behind=[small], lat=5000.0)
-    dma("s", [(v("BE", 0, 1), T.be[:])], behind=[ca])
-    cp(v("SNL"), v("SN"))
-    fill(v("AW", KH, KH + 16), 0.0)
-    fill(v("SW", DUMP, KB), 0.0)
-    fill(v("AW", PAD, OWN), 0.0)
-    fill(v("BUF", PAD, OWN), 0.0)
-    fill(v("SW", KH, RWN), 0.0)
-    iota(v("SW", 0, GHO), [[0, GHO]], 0, 0, True, [g0])
-    iota(v("SW", GHO, OWN), [[0, OWN - GHO]], 0, 0, True, [g0])
     def lin(o, a, scale, bias):
         return act(o, a, AF.Identity, bias=bias, scale=scale)
 
@@ -272,9 +248,49 @@ def rank_program(g, core, T, topo):
     def two(j):
         return v("EQ", 16 + j, 17 + j)
 
-    ts(v("PI", 4, 5), v("PI", 0, 1), 15, A.bitwise_and)
-    cp(col(0), v("PI", 0, 1))
-    cp(col(1), v("PI", 4, 5))
+    up, down = slice(16, 128), slice(0, 16)
+    p8, p16, p24 = slice(0, 8), slice(0, 16), slice(0, 24)
+    extra[0] = SETUP[0]
+    x = dma("s", [(v("SI", 0, 128), T.ti[:])])
+    dma("s", [(v("SN"), T.snd[:])], behind=[x])
+    dma("a", [(v("S2", 768, 896), T.kd[:])])
+    fill(v("TW", 0, E), 0.0)
+    g0 = iota(v("SI", 128, 256), [[1, 128]], 0, 128, False)
+    g0 = iota(pint(0), [[0, 1]], 0, 1, False, [g0])
+    g0 = iota(v("JF"), [[1, 144]], 0, 0, True, [g0])
+    g0 = iota(v("HI"), [[64, 7], [0, 64]], 0, 0, True, [g0])
+    g0 = iota(v("LO"), [[0, 8], [1, 64]], 0, 0, True, [g0])
+    iota(v("KI"), [[0, 16], [1, 16]], 0, 0)
+    iota(v("J16"), [[16, 8], [0, 16]], 0, 0)
+    iota(v("J8"), [[0, 16], [1, 8]], 0, 0)
+    cp(v("S3", 0, 128), v("SI", 0, 128))
+    tt(v("S3", 384, 512), v("SI", 0, 128), v("S3", 0, 128), A.subtract)
+    def halves(c0):
+        ts(v("S2", c0, c0 + 128), v("SI", c0, c0 + 128), 0xFC0 if c0 == 256 else 0x7C0, A.bitwise_and)
+        ts(v("S2", c0 + 384, c0 + 512), v("SI", c0, c0 + 128), 63, A.bitwise_and)
+        cp(v("S3", c0, c0 + 128), v("S2", c0, c0 + 128))
+        cp(v("S3", c0 + 384, c0 + 512), v("S2", c0 + 384, c0 + 512))
+
+    halves(128)
+    cp(v("S3", 768, 896), v("S2", 768, 896))
+    act(v("S3", 896, 1024), v("S3", 128, 256), AF.Identity, bias=float(OWN))
+    line = {"s": [], "a": []}
+    for q, row_, c in (("s", 5, 128), ("a", 4, 512), ("s", 6, 512), ("a", 3, 896), ("s", 11, 768), ("a", 0, 0), ("s", 7, 384)):
+        line[q].append(dma(q, [(v("TW", 0, E, p=slice(row_, 128, 16)), v("S3", c, c + 128))], True, behind=line[q][-1:], lat=DMALAT + ROWLAT * len(line[q])))
+    a0 = dma("a", [(v("AW", OWN, OWN + E), T.a0[:])], lat=5000.0, behind=line["a"][-1:])
+    small = dma("s", [(v("QI", 48, 96), T.bg[:]), (v("QI", 96, 144), T.cl[:])], behind=line["s"][-1:], lat=3000.0)
+    ca = dma("s", [(v("CA"), T.ca[:])], behind=[small], lat=5000.0)
+    x = dma("s", [(v("BE", 0, 1), T.be[:])], behind=[ca], lat=5000.0)
+    k0 = dma("s", [(v("AW", KB, KH), T.k0[:])], behind=[x], lat=6000.0)
+    snl = cp(v("SNL"), v("SN"))
+    for name, c0, c1, x in (("AW", KH, RWN, 0), ("SW", DUMP, KB, 0), ("AW", PAD, OWN, 0), ("BUF", PAD, OWN, 0), ("SW", KH, RWN, 0), ("AG", 0, 512, 1), ("WC", 0, 248, 0),
+                            ("TRI", 0, 160, 0), ("TW", 2944, 3456, 0)):
+        iota(v(name, c0, c1), [[0, c1 - c0]], x, 0, True, [g0])
+    iota(v("SW", 0, GHO), [[0, GHO]], 0, 0, True, [g0])
+    iota(v("SW", GHO, OWN), [[0, OWN - GHO]], 0, 0, True, [g0])
+    ts(pint(1), pint(0), 15, A.bitwise_and)
+    cp(col(0), pint(0))
+    cp(col(1), pint(1))
     tt(col(2), col(0), col(1), A.subtract)
     ts(v("EQ", 0, 16), v("JF", 0, 16), col(1), A.is_equal)
     tt(v("EQ", 16, 28), v("EQ", 0, 12), v("EQ", 1, 13), A.add)
@@ -296,231 +312,260 @@ def rank_program(g, core, T, topo):
     act(v("D11"), v("I2", 0, 128), scale=two(3))
     act(v("D12"), v("I2", 0, 128), scale=col(12))
     act(v("RM"), v("I2", 112, 240), scale=col(3))
-    for c in (0, 1024):
-        fill(v("AG", c, c + 1024), 1.0)
     ident, roll, unroll = v("I2", 0, 128), v("I2", 112, 240), v("I2", 16, 144)
-    pos32, roll32, neg32 = v("I32F", 0, 128), v("I32F", 112, 240), v("I32F", 256, 384)
+    pos32, roll32 = v("I32F", 0, 128), v("I32F", 112, 240)
 
-    def through(dst, d0, terms, both=False):
+    def through(dst, d0, terms, both=False, plus=0.0):
         for h, bank in enumerate(BANKS):
             c = 448 * h
             for j, (lhs, src, s0) in enumerate(terms):
                 mm([(v(bank, 0, 448), lhs, v(src, s0 + c, s0 + c + 448), j == 0, j == len(terms) - 1)])
         for h, bank in enumerate(BANKS):
-            (cp if both and h else act)(v(dst, d0 + 448 * h, d0 + 448 * h + 448), v(bank, 0, 448))
+            o = v(dst, d0 + 448 * h, d0 + 448 * h + 448)
+            if both and h:
+                ts(o, v(bank, 0, 448), plus, A.add)
+            else:
+                lin(o, v(bank, 0, 448), 1.0, plus)
 
     for c0, c1, bank, pick, out in ((0, 384, "PR0", cp, cp), (384, NG, "PR1", act, act)):
         mm([(v(bank, 0, c1 - c0), ident, v("GS", c0, c1), True, False), (v(bank, 0, c1 - c0), ident, v("SL", 0, c1 - c0), False, False)])
         pick(v("YY", c0, c1), ind(v("TW", 0, E), v("SNL", c0 // 16, c1 // 16)))
         mm([(v(bank, 0, c1 - c0), v("RM"), v("YY", c0, c1), False, True)])
         out(v("GT", c0, c1), v(bank, 0, c1 - c0))
-    first, came = exchange("GT", 0, "TW", E, 1, late=2500.0, calls=X2)
+    extra[0] = SETUP[1]
+    first, came = exchange("GT", 0, "TW", E, 1, late=FIRSTLATE, calls=X2)
+    extra[0] = SETUP[0]
     for c in (0, 448):
         act(v("AW", GUN + c, GUN + c + 448), ind(v("AW", OWN, OWN + E), v("SNL", c // 16, c // 16 + 28)))
     through("GN", 0, [(roll, "AW", GUN)])
     sent, came = exchange("GN", 0, "AW", GHO, 1, late=LATE)
-    dma("a", [(v("SW", KB, KH), T.k0[:])], after=first, lat=3000.0)
-    dma("s", [(v("SW", OWN, OWN + E), T.a0[:])], after=sent, lat=3000.0)
-    dma("s", [(v("AW", KB, KH), T.k0[:])], after=sent, lat=4000.0)
-    ts(v("F0"), v("JF", 0, 144), -15.0, A.add, col(2), A.is_equal)
+    for c in (KB, KB + 1024):
+        ts(v("SW", c, c + 1024), v("AW", c, c + 1024), 249.0, A.add)
+    dma("s", [(v("UR", 0, 256, p=slice(8 * k, 8 * k + 8)), T.us[:, 0:256]) for k in range(16)], behind=[k0], lat=5000.0)
+    x = dma("s", [(v("SW", OWN, OWN + E), T.a0[:])], after=sent, lat=3000.0)
+    x = dma("s", [(v("AW", KB, KH), v("SW", KB, KH))], after=sent, lat=4000.0, behind=[x])
+    dma("s", [(v("UR", 256, 1280, p=slice(8 * k, 8 * k + 8)), T.us[:, 256:1280]) for k in range(16)], behind=[x], lat=5000.0)
+    dma("s", [(v("SI", 256, 384), T.lp[:])], behind=[x], lat=5000.0)
+    late_ = len(ops)
+    halves(256)
+    for o in ops[late_ - 5:]:
+        o["rank"] = 0.0
+    ts(v("F0"), v("JF"), -15.0, A.add, col(2), A.is_equal)
     act(col(17), row(11), scale=1.0 / 64)
     act(v("FT"), v("F0"), scale=col(16))
     act(v("FK"), v("F0"), scale=col(17))
     act(v("FM"), v("F0"), scale=two(3))
-    act(v("FC"), v("F0"), scale=two(5))
     act(v("FN"), v("F0"), scale=-1.0)
-    act(v("NI"), ident, scale=-1.0)
     lin(col(42), two(8), -1.0, 1.0)
     act(v("FL"), v("F0"), scale=two(8))
     act(v("K89"), ident, scale=col(42))
     act(v("P56"), v("I2", 125, 253), scale=two(5))
-    mm([(v("PX", 0, 48), win("FT", a), v("TW", a, 768, 16), a == 0, a == 15) for a in range(16)])
-    mm([(v("PX", 48, 96), win("FK", a), v("TW", a, 768, 16), a == 0, a == 15) for a in range(16)])
-    act(v("NTV"), v("PX", 0, 48), scale=-1.0)
-    lin(v("KV"), v("PX", 48, 96), 8.0, -160.0)
-    for c0, c1, bank in ((0, 128, "PT"), (128, 512, "PK"), (512, NG, "PM")):
+    ts(v("GM"), v("J16"), col(2), A.is_equal)
+    act(col(18), col(16), scale=-1.0)
+    act(col(19), row(11), scale=1.0 / 8)
+    act(v("NT"), v("GM"), scale=col(18))
+    act(v("KV"), v("GM"), scale=col(19))
+    for c0, c1, bank in ((0, 128, "PT"), (128, 512, "PK"), (512, NG, "PX")):
         o = v(bank, 0, c1 - c0)
         mm([(o, v("D11"), v("GS", c0, c1), True, False), (o, v("D11"), v("SL", 0, c1 - c0), False, False), (o, v("D12"), v("YY", c0, c1), False, True)])
         ts(v("VV", c0, c1), o, col(13), A.add)
+    extra[0] = SETUP[1]
     for d in range(7):
         lst = v("SNL", 8 * d, 8 * d + 8)
         if d:
-            act(v("YY", GH * d, GH * d + GH), ind(v("TW", 0, E), lst))
+            (cp if RENUM == "v" else act)(v("YY", GH * d, GH * d + GH), ind(v("TW", 0, E), lst))
         cp(ind(v("TW", 0, E), lst), v("VV", GH * d, GH * d + GH))
-    lin(col(19), col(0), 16.0, 15.0)
-    p16, p24 = slice(0, 16), slice(0, 24)
-    ts(v("FQ", p=p16), v("JF", p=p16), v("PC", 76, 77, p=p16), A.is_equal)
-    cp(v("QH"), v("QI", 0, 176))
-    ts(v("QH", 80, 128), v("QI", 80, 128), -2048.0, A.add)
-    dma("s", [(v("QF", 0, 16 * (c1 - c0), p=slice(8 * j, 8 * j + 8)), v("QH", c0, c1)) for j, (c0, c1) in enumerate(((0, 80), (80, 128), (128, 176)))])
-    act(v("I32F", 0, 256), v("I2"))
-    act(neg32, ident, scale=-1.0)
-    cp(v("REP"), v("JF", 0, 48))
-    ts(v("PI", 8, 9), v("PI", 0, 1), 3, A.bitwise_and)
-    ts(v("PI", 12, 13), v("PI", 4, 5), 2, A.arith_shift_right)
-    cp(col(36), v("PI", 12, 13))
-    ts(col(20), v("PI", 8, 9), 16.0, A.mult, col(36), A.add)
-    ts(v("PERM"), v("T48"), col(20), A.add)
+    extra[0] = SETUP[0]
+    ts(v("QI", 0, 48), v("QI", 48, 96), 63, A.bitwise_and)
+    ts(v("QI", 48, 96), v("QI", 48, 96), 0xFC0, A.bitwise_and)
+    cp(v("QH"), v("QI"))
+    dma("s", [(v("QF", p=slice(8 * j, 8 * j + 8)), v("QH", 48 * j, 48 * j + 48)) for j in range(3)])
+    act(v("I32F"), v("I2"))
     for s in range(3):
-        cp(v("CAL", 256 * s, 256 * s + 256), ind(v("CA"), v("PERM", 16 * s, 16 * s + 16)))
-
-    def lists(j, n, o):
-        ps = slice(0, 8 * j + 8)
-        mm([(o, v("FQ", 128 * j + 15 - a, 128 * j + 143 - a, p=ps), v("QF", a, 16 * n, 16, p=ps), a == 0, a == 15) for a in range(16)])
-
-    for s in range(3):
-        (cp if WHO[2 + s] == "v" else act)(v("TVR", 256 * s, 256 * s + 256), ind(v("NTV"), v("REP", 16 * s, 16 * s + 16)))
-        (cp if WHO[2 + s] == "v" else act)(v("KVR", 256 * s, 256 * s + 256), ind(v("KV"), v("REP", 16 * s, 16 * s + 16)))
-    fill(v("SH", 0, 128), 0.0)
-    sel(v("SH", 128, 2048), v("AG", 0, 1920), [[-1, 15], [0, 8], [1, 16]], A.is_ge, 0.0, -1, 0, first)
-    sel(v("XX2", 0, 1920), v("SH", 128, 2048), [[1, 15], [-1, 128]], A.is_equal, 0.0, 1, 1)
-    sh = sel(v("SH", 128, 2048), v("XX2", 0, 1920), [[0, 15], [-1, 128]], A.not_equal, -1.0, 0, 1)
-    if EXP:
-        sel(v("BC"), v("AG"), [[-1, 16], [-16, 8], [0, 16]], A.is_equal, 0.0, 0, 1, [sh])
-
-    def diff(bank, c0, src, lo=0, hi=256, run_=16):
-        pos, neg = (pos32, neg32) if SB[src][1] == F32 else (ident, v("NI"))
-        mm([(v(bank, c0 + lo, c0 + hi), pos, v(src, lo, hi), True, False), (v(bank, c0 + lo, c0 + hi - 1), neg, v(src, lo + 1, hi), False, False),
-            (v(bank, c0 + lo + run_ - 1, c0 + hi - 1, run_), pos, v(src, lo + run_, hi, run_), False, True)])
+        cp(v("CAL", 256 * s, 256 * s + 256), v("CA", 256 * s, 256 * s + 256))
+    act(col(20), col(2), scale=1.0 / 16)
+    ts(exact("WC", 120, 128), v("J8", 0, 8), col(20), A.is_equal, -1.0, A.mult)
+    ts(pint(2), pint(0), 7, A.bitwise_and)
+    cp(col(32), pint(2))
+    ts(v("WB"), v("J8"), col(32), A.is_equal, 1.0 / 256, A.mult)
+    act(v("W0"), v("WB"), scale=256.0)
+    sel(v("W0"), v("W0"), [[1, 128]], A.is_ge, 0.0, 0, -1, first)
+    ts(pint(3), pint(0), 3, A.arith_shift_right)
+    cp(col(27), pint(3))
+    ts(col(28), pint(2), 16.0, A.mult, col(27), A.add)
+    ts(col(29), col(27), 15.0, A.is_equal, 1000.0, A.mult)
+    ts(col(30), col(28), 1.0, A.add, col(29), A.add)
+    ts(col(31), col(28), 1000.0, A.add, col(29), A.subtract)
+    ts(v("FH", 128, 256), v("JF", 0, 128), col(28), A.is_equal)
+    ts(v("FH", 256, 384), v("JF", 0, 128), col(30), A.is_equal)
+    tt(v("FH", 0, 128), v("FH", 128, 256), v("FH", 256, 384), A.subtract)
+    ts(v("F15"), v("JF"), col(31), A.is_equal, -3072.0, A.mult)
+    for q in range(4):
+        x = sel(v("BC", 512 * q, 512 * q + 512), v("AG"), [[-1, 4], [-16, 8], [0, 16]], A.is_equal, 0.0, -4 * q, 1, first)
+        sel(v("BC", 512 * q, 512 * q + 384), v("BC", 512 * q, 512 * q + 384), [[-1, 3], [-16, 8], [0, 16]], A.not_equal, -1.0, -4 * q - 1, 1)
 
     def extract(t, qs, bank, b0, f, pre=None, close=True):
         c0, c1 = 64 * min(qs), 64 * max(qs) + 64
         if pre:
-            mm([(v(bank, b0 + c0, b0 + c1), pos32 if HALF == F32 else ident, v(pre, 256 * (t % 3) + c0, 256 * (t % 3) + c1), True, False)])
+            mm([(v(bank, b0 + c0, b0 + c1), v(pre), v("TW", 256 * (t % 3) + c0, 256 * (t % 3) + c1), True, False)])
         for h in qs:
-            mm([(v(bank, b0 + 64 * h, b0 + 64 * h + 64), win(f, a), v("XX%d" % (t % 3), 1024 * h + 64 * a, 1024 * h + 64 * a + 64),
-                 a == 0 and not pre, a == 15 and close and (not pre or h == qs[-1])) for a in range(16)])
+            for k0_ in range(0, 16, RUNS if t else 16):
+                mm([(v(bank, b0 + 64 * h, b0 + 64 * h + 64), win(f, k), v("XX%d" % (t % 3), 1024 * h + k, 1024 * h + 1024, 16),
+                     k == 0 and not pre, k == 15 and close and (not pre or h == qs[-1])) for k in range(k0_, k0_ + (RUNS if t else 16))])
 
     def prep(t, qs=(3, 2, 1, 0), bt="PT", bk="PK"):
-        c0, c1 = 64 * min(qs), 64 * max(qs) + 64
-        extract(t, qs, bt, 0, "FT", "TVR")
-        extract(t, qs, bk, 0, "FK", "KVR", False)
-        act(v("LH", c0, c1), v(bt, c0, c1), AF.Abs)
-        act(v("YI", c0, c1), v("LH", c0, c1), AF.Identity, bias=160.0 - 15.5 / 32, scale=1.0 / 32)
-        extract(t, qs, bt, 256, "FM")
+        c0, c1, lh = 64 * min(qs), 64 * max(qs) + 64, "LH%d" % (t % 3)
+        extract(t, qs, bt, 0, "FT", "NT")
+        if bk != bt:
+            extract(t, qs, bk, 0, "FK", "KV", False)
+        else:
+            extract(t, qs, bt, 256, "FM")
+        act(v(lh, c0, c1), v(bt, c0, c1), AF.Abs)
+        act(v("YI", c0, c1), v(lh, c0, c1), AF.Identity, bias=160.0 - 15.5 / 32, scale=1.0 / 32)
+        if bk != bt:
+            extract(t, qs, bt, 256, "FM")
+        else:
+            extract(t, qs, bk, 0, "FK", "KV", False)
         mm([(v(bk, c0, c1), ident, v("YI", c0, c1), False, True)])
-        ts(v("BNL", c0, c1), v(bk, c0, c1), 64.0, A.mult)
-        cp(v("ML", c0, c1), v(bt, 256 + c0, 256 + c1))
+        half, (bnl, ml, ss, mt) = HALFLISTS[t], [v(x, 256 * (t % 2) + c0, 256 * (t % 2) + c1) for x in ("BNL", "ML", "SS", "MT")]
+        if t == R - 1 or not half:
+            ts(bnl, v(bk, c0, c1), 64.0, A.mult, -10240.0, A.add)
+        if not half:
+            cp(ml, v(bt, 256 + c0, 256 + c1))
+            ts(mt, ml, -float(HOLE), A.add)
+            if c0 % 128 == 0:
+                ts(v("SS", c0, c0 + 128), v("BNL", c0, c0 + 128), -float(E), A.add)
+            return
         if t < R - 1:
-            lin(v("SS", c0, c1), v(bk, c0, c1), 64.0, -float(E))
-        lin(v("MT", c0, c1), v(bt, 256 + c0, 256 + c1), 1.0, -float(HOLE))
-
-    def steps(t, qs=(3, 2, 1, 0)):
-        c0, c1 = 64 * min(qs), 64 * max(qs) + 64
-        diff("PX", 0, "MT", c0, c1)
-        if t < R - 1:
-            diff("PX", 256, "SS", c0, c1)
-
-    def prep2(t):
-        if t:
-            steps(t)
-        if EXP:
-            diff("PT", 0, "LH", run_=4)
-            act(v("DL%d" % (t % 3)), v("PT", 0, 256))
-        if not EXP:
-            rl, lh = "RL%d" % (t % 3), "LH"
-            mm([(v("PT", 0, 255), ident, v(lh, 0, 255), True, False), (v("PT", 0, 255), v("NI"), v(lh, 1, 256), False, True)])
-            ts(v(rl, 1, 256), v("PT", 0, 255), 1023.0, A.add)
-            fill(v(rl, 0, 256, 16), 2047)
-            ts(v("EL%d" % (t % 3)), v(lh, 15, 256, 16), 1023.0, A.add)
-        if t < 2:
-            extract(t, (3, 2, 1, 0), "PT", 0, "FC")
-            lin(v("CT%d" % t), v("PT", 0, 256), 1.0, -4096.0)
-
-    kg = []
+            lin(ss, v(bk, c0, c1), 64.0, -10240.0 - E)
+        lin(mt, v(bt, 256 + c0, 256 + c1), 1.0, -float(HOLE))
+        if half:
+            if t < R - 1:
+                ts(bnl, ss, float(E), A.add)
+            ts(ml, mt, float(HOLE), A.add)
+        for o in ops[-4:] if t else ():
+            o["urge"] = AHEAD[t]
 
     def k_gather(t, chunks=(3, 2, 1, 0)):
-        kg[:] = []
-        for c in chunks:
-            o, src = v("KG", 1024 * c, 1024 * c + 1024), ind(v("SW", KB, KH), v("BNL", 64 * c, 64 * c + 64))
-            me = ts(o, src, -1.0, A.mult) if KV[t][c] == "v" else act(o, src, scale=-1.0)
+        w = 256 // len(KV[t])
+        for c in [x for q in chunks for x in range(64 * q + 64 - w, 64 * q - 1, -w)]:
+            o, src = v("KG", 16 * c, 16 * (c + w)), ind(v("SW", KB, KH), v("BNL", 256 * (t % 2) + c, 256 * (t % 2) + c + w))
+            me = ts(o, src, -1.0, A.mult, 249.0, A.add) if KV[t][c // w] == "v" else lin(o, src, -1.0, 249.0)
             if t:
-                ops[me]["urge"] = URGE
-            if KV[t][c] == "a":
-                kg.append(me)
+                ops[me]["urge"] = URGE[t]
 
     def decay(t):
-        if not EXP:
-            for c in range(4):
-                act(v("RG%d" % (t % 2), 1024 * c, 1024 * c + 1024), ind(v("RT"), v("RL%d" % (t % 3), 64 * c, 64 * c + 64)))
-            act(v("E15%d" % (t % 2)), ind(v("RT"), v("EL%d" % (t % 3))), scale=-1.0)
-            return
+        rg = "RG%d" % (t % 2)
         for c in range(8):
-            bank, h, r = DB[c % 2], c // 4, c % 4
-            mm([(v(bank, 64 * a, 64 * a + 64), v("BC", 128 * (8 * h + a), 128 * (8 * h + a + 1)), v("DL%d" % (t % 3), r, 256, 4), True, True) for a in range(8)])
-            o = dict(v("RG%d" % (t % 2), 2048 * h + r, 2048 * h + 2048, 4), reg=[("RG%d" % (t % 2), 2048 * c, 2048 * c + 2048)])
+            bank, h, r = DB[c % 2], 1 - c // 4, c % 4
+            mm([(v(bank, q, 512, 4), v("BC", 128 * (4 * q + r), 128 * (4 * q + r + 1)), v("LH%d" % (t % 3), 128 * h, 128 * h + 128), True, True) for q in range(4)])
+            o = dict(v(rg, 2048 * h + r, 2048 * h + 2048, 4), reg=[(rg, 8192 * h + 2048 * r, 8192 * h + 2048 * r + 2048)])
             act(o, v(bank), AF.Exp, bias=-DROP if r == 3 else None, scale=v("BT", 0, 1))
 
-    def weights(t, j, b0, b1):
-        pr, c0, c1 = "PR%d_" % (t % 3), 16 * b0, 16 * b1
-        cut = c0 + SPLIT[t][j]
+    def elect(t, j, b0, b1):
+        pr, c0, c1, s = "PR%d_" % (t % 3), 16 * b0, 16 * b1, 256 * (t % 3)
+        cut, m0 = c0 + SPLIT[t][j], 256 * (t % 2)
         if cut < c1:
-            tt(v(pr, 16 * cut, 16 * c1), ind(v("AW", 0, DUMP), v("ML", cut, c1)), v("KG", 16 * cut, 16 * c1), A.mult)
+            tt(v(pr, 16 * cut, 16 * c1), ind(v("AW", 0, DUMP), v("ML", m0 + cut, m0 + c1)), v("KG", 16 * cut, 16 * c1), A.mult)
         for c in range(c0, cut, WCH):
             ce = min(cut, c + WCH)
-            act(v("AS", 16 * c, 16 * ce), ind(v("AW", 0, DUMP), v("ML", c, ce)), behind=kg[:KFIRST] if t else ())
+            act(v("AS", 16 * c, 16 * ce), ind(v("AW", 0, DUMP), v("ML", m0 + c, m0 + ce)))
             scan(v(pr, 16 * c, 16 * ce), v("AS", 16 * c, 16 * ce), v("KG", 16 * c, 16 * ce), 0.0, A.max, A.mult)
-        mm([(v("PW", c0, c1), win("FN", a), v(pr, 16 * c0 + a, 16 * c1, 16), a == 0, a == 15) for a in range(16)])
+        tot, cum = v(ABANKS[t][j], 256, 256 + c1 - c0), v(ABANKS[t][j], 0, c1 - c0)
+        mm([(cum, v("WC", 120 - 8 * k, 248 - 8 * k), v(pr, 16 * c0 + k, 16 * c1, 16), k == 0, k == 15) for k in range(16)])
+        (cp if WSV[t][j] == "v" else act)(v("WS", c0, c1), cum)
+        mm([(tot, v("WB", p=p16), v("QF", s + c0, s + c1, p=p16), True, False), (tot, v("WB"), v("WS", c0, c1), False, True), (cum, v("W0"), v("WS", c0, c1), True, True)])
+        tt(v("THR", c0, c1), tot, v("UR", 256 * t + c0, 256 * t + c1), A.mult)
+        tt(v("HIT", c0, c1), cum, v("THR", c0, c1), A.is_gt)
 
-    def raise_(t, bank, b0, b1, h):
-        s, q0, q1 = 256 * (t % 3), 256 * h + 16 * b0, 256 * h + 16 * b1
-        tt(v("PD", q0, q1), v("HIT", 16 * b0, 16 * b1), v("PX", q0, q1), A.mult)
-        scan(v("XS", q0, q1), v("SEG", 0, q1 - q0), v("PD", q0, q1), 0.0, A.mult, A.add)
-        xs = v("XS", q0 + 15, q1, 16)
-        mm([(v(bank, q0 + dl, q1, 16), v("SH", 128 * dl, 128 * dl + 128), xs, True, True) for dl in range(16)])
-        if ONS[t][h]:
-            lin(v("LB", q0, q1, 16), xs, -1.0, col(24 + h))
-            act(v("EE", q0, q1), v(bank, q0, q1), AF.Square, scale=128.0)
+    def elected(t, bank, hs, c0, c1):
+        one = v(bank, 384, 384 + c1 - c0)
+        mm([(one, v("FH", 0, 128), v("HIT", c0, c1), True, True)])
+        for h in hs:
+            tt(v("PD", 256 * h + c0, 256 * h + c1), one, v(("MT", "SS", "CT")[h], 256 * (t % 2) + c0, 256 * (t % 2) + c1), A.mult)
+
+    def raise_(t, bank, parts, h, byscan):
+        s, lo, hi = 256 * (t % 3), min(x[0] for x in parts), max(x[1] for x in parts)
+        n, q0 = hi - lo, 256 * h
+        if byscan:
+            mm([(v(bank, 0, 16 * n), ident, v("DG", 0, 16 * n), True, False), (v(bank, 0, 16 * n), v("GM"), v("PD", q0 + 16 * lo, q0 + 16 * hi), False, True)])
+            xs, x1 = v("XL", q0 + 16 * lo + 15, q0 + 16 * hi, 16), lambda b: v("XL", q0 + 16 * b + 15, q0 + 16 * b + 16)
         else:
-            ts(v("LB", q0, q1, 16), xs, -1.0, A.mult, col(24 + h), A.add)
-            ts(v("EE", q0, q1), v(bank, q0, q1), 0.0, A.not_equal, 16384.0, A.mult)
-        scan(v("OF", q0, q1), v("EE", q0, q1), v("LB", q0, q1), 0.0, A.min, A.max)
-        old = v("L1C", q0 // 16, q1 // 16)
-        if h:
-            ts(old, xs, float(E), A.add)
+            xs, x1 = v(bank, 0, n), lambda b: v(bank, b - lo, b - lo + 1)
+            mm([(xs, win("F0", a), v("PD", q0 + 16 * lo + a, q0 + 16 * hi, 16), a == 0, a == 15) for a in range(16)])
+        seg = SEGW * (16 * h + lo)
+        for j, (b0, b1) in enumerate(parts):
+            y0, m = 128 + 160 * j, b1 - b0
+            mm([(v(bank, y0, y0 + 8 * m * (m + 1)), ident, v("TRI", 0, 8 * m * (m + 1)), True, False)] +
+               [(v(bank, y0 + 8 * i * (i + 1), y0 + 8 * (i + 1) * (i + 2)), v("GM"), v("PD", q0 + 16 * b0, q0 + 16 * (b0 + i + 1)), False, i == m - 1) for i in range(m)])
+        if byscan:
+            scan(v("XL", q0 + 16 * lo, q0 + 16 * hi), v("RS", 0, 16 * n), v(bank, 0, 16 * n), 0.0, A.min, A.max)
+        if LBA[t][h] == "a":
+            lin(spots("EE", seg + SEGW - 1, seg + SEGW * n, SEGW), xs, -1.0 / 4096, col(24 + h))
         else:
+            ts(spots("EE", seg + SEGW - 1, seg + SEGW * n, SEGW), xs, -1.0 / 4096, A.mult, col(24 + h), A.add)
+        old = exact("L1C", 16 * h + lo, 16 * h + hi)
+        if not h:
             ts(old, xs, 0.0, A.max, float(HOLE - PAD), A.add)
-        ts(v("L1", q0 // 8, q1 // 8, 2), v("OF", q0 + 15, q1, 16), -1.0, A.mult, col(22 + h), A.add)
-        tt(v("NV", q0, q1), ind(v("AW", KB, KH + 16) if h else v("AW", PAD, DUMP), old), v("CAP", 768 * h + s + 16 * b0, 768 * h + s + 16 * b1), A.min)
-        for b in range(b1 - 1, b0 - 1, -1):
-            c = 256 * h + 16 * b
-            tt(ind(v("SW", KB, RWN) if h else v("SW", 0, KB), v("L1", c // 8, c // 8 + 1)), v("NV", c, c + 16), v("OH", s + 16 * b, s + 16 * b + 16), A.add)
+        for j, (b0, b1) in enumerate(parts):
+            for i in range(b1 - b0):
+                e, y = SEGW * (16 * h + b0 + i + 1) - 1, 128 + 160 * j + 8 * i * (i + 1)
+                ts(exact("EE", e - 16 * (i + 1), e), v(bank, y, y + 16 * (i + 1)), x1(b0 + i), A.not_equal, -0.5, A.add)
+        scan(exact("OF", seg + SEGW - 18, seg + SEGW * n), exact("EE", seg + SEGW - 18, seg + SEGW * n), v("RST", SEGW - 18, SEGW * n), 0.0, A.min, A.max)
+        ts(exact("L1", 16 * h + lo, 16 * h + hi), spots("OF", seg + SEGW - 1, seg + SEGW * n, SEGW), -4096.0, A.mult, col(22 + h), A.add)
+        if h:
+            (cp if NVK == "v" else act)(v("NV", q0 + 16 * lo, q0 + 16 * hi), ind(v("AW", KB, RWN), exact("L1", 16 + lo, 16 + hi)))
+        else:
+            tt(v("NV", 16 * lo, 16 * hi), ind(v("AW", PAD, DUMP), old), v("CAP", s + 16 * lo, s + 16 * hi), A.min)
+        for b0, b1 in parts:
+            tt(ind(v("SW", KB, RWN) if h else v("SW", 0, KB), exact("L1", 16 * h + b0, 16 * h + b1)), v("NV", q0 + 16 * b0, q0 + 16 * b1), v("OH", s + 16 * b0, s + 16 * b1), A.add)
+
+    def raise_k(t, bank, lo, hi):
+        s, c0, c1 = 256 * (t % 3), 16 * lo, 16 * hi
+        mm([(v(bank, 0, c1 - c0), ident, v("DG", 0, c1 - c0), True, False), (v(bank, 0, c1 - c0), v("GM"), v("PD", 256 + c0, 256 + c1), False, True)])
+        scan(v("XK", c0, c1), v("RS", 0, c1 - c0), v(bank, 0, c1 - c0), 0.0, A.min, A.max)
+        xs = v("XK", c0 + 15, c1, 16)
+        mm([(v(bank, dl, c1 - c0, 16), v("SH", 128 * dl, 128 * dl + 128), xs, True, True) for dl in range(16)])
+        lin(v("LK", c0, c1, 16), xs, -1.0, col(25))
+        act(v("EK", c0, c1), v(bank, 0, c1 - c0), AF.Square, scale=128.0)
+        scan(v("OK", c0, c1), v("EK", c0, c1), v("LK", c0, c1), 0.0, A.min, A.max)
+        ts(v("L2", 2 * lo, 2 * hi, 2), v("OK", c0 + 15, c1, 16), -1.0, A.mult, col(23), A.add)
+        ts(v("L1", 16 + lo, 16 + hi), xs, float(E), A.add)
+        act(v("NV", 256 + c0, 256 + c1), ind(v("AW", KB, RWN), v("L1", 16 + lo, 16 + hi)))
+        for b in range(hi - 1, lo - 1, -1):
+            tt(ind(v("SW", KB, RWN), v("L2", 2 * b, 2 * b + 1)), v("NV", 256 + 16 * b, 272 + 16 * b), v("OH", s + 16 * b, s + 16 * b + 16), A.add)
 
     def lam(t):
-        if not EXP:
-            for a in range(16):
-                scan(v("SD", 256 * a, 256 * a + 256), v("RG%d" % (t % 2), a, 4096, 16), v("PR%d_" % (t % 3), a, 4096, 16), 0.0, A.mult, A.add)
-            tt(v("LAM"), ind(v("SD"), v("LAML")), v("E15%d" % (t % 2)), A.mult)
-            dma("s", [(T.yl[:, 256 * t:256 * t + 256], v("LAM"))])
-            return
-        w = 256 // HALVES[t]
-        for h in range(HALVES[t] - 1, -1, -1):
-            c0, c1, bank = w * h, w * h + w, SBK[h % 2]
-            for a in range(16):
-                o = {"ap": T.SC[:, c0:c1, a], "reg": [("SC", 1024 * a + 4 * c0, 1024 * a + 4 * c1)], "n": w, "sz": 4, "ps": False}
-                q = dict(v("RG%d" % (t % 2), 256 * a + c0, 256 * a + c1), reg=[("RG%d" % (t % 2), 8192 * (a // 8), 8192 * (a // 8) + 8192)])
-                scan(o, v("PR%d_" % (t % 3), 16 * c0 + a, 16 * c1, 16), q, 0.0, A.add, A.mult)
+        rg = "RG%d" % (t % 2)
+        for h in (1, 0):
+            c0, c1, bank = 128 * h, 128 * h + 128, SBK[h % 2]
+            for c in range(16 * c0, 16 * c1, PIECE):
+                scan(v("SC", c, c + PIECE), v("PR%d_" % (t % 3), c, c + PIECE), dict(v(rg, c, c + PIECE), reg=[(rg, 8192 * h, 8192 * h + 8192)]), 0.0, A.add, A.mult)
             for k in (3, 7, 11, 15):
-                x = {"ap": T.SC[:, c0 + k:c1:16, :], "reg": [("SC", 1024 * a + 4 * c0, 1024 * a + 4 * c1) for a in range(16)], "n": w, "sz": 4, "ps": False}
-                mm([(v(bank, c0, c1), pos32, x, k == 3, k == 15)])
+                mm([(v(bank, c0, c1), pos32, v("SC", 16 * c0 + k, 16 * c1, 16), k == 3, k == 15)])
             act(v("LAM", c0, c1), v(bank, c0, c1), scale=-float(np.exp(DROP)))
             ops[dma("s", [(T.yl[:, 256 * t + c0:256 * t + c1], v("LAM", c0, c1))])]["due"] = DUE[t]
 
     def candidates(t):
-        ct, own = "CT%d" % t, v("TW", 256 * t, 256 * t + 256)
-        scan(v("MN"), v("BSEG"), v("PW", 0, 256), 0.0, A.add, A.min)
-        diff("PD_", 256, ct)
-        tt(v("W2"), v("HIT"), v("PD_", 256, 512), A.mult)
-        scan(v("W1"), v("SEG"), v("W2"), 0.0, A.mult, A.add)
-        tt(v("SM", 0, 16), v("W1", 15, 256, 16), v("PB", 32 + 16 * t, 48 + 16 * t), A.min)
+        own, (b1, b2) = v("TW", 256 * t, 256 * t + 256), CBANKS
+        par = v(b1, 256, 272)
+        mm([(par, win("F0", a), v("PD", 512 + a, 768, 16), a == 0, False) for a in range(16)])
+        mm([(par, win("F15", a), v("HIT", a, 256, 16), False, a == 15) for a in range(16)])
+        tt(v("SM", 0, 16), par, v("PB", 32 + 16 * t, 48 + 16 * t), A.min)
         ts(v("IX1"), v("SM", 0, 16), 4096.0, A.add)
-        ts(v("IX2"), v("W1", 15, 256, 16), 4096.0, A.add, 2943.0, A.min)
+        ts(v("IX2"), par, 4096.0, A.add, 2943.0, A.min)
+        for c in range(4):
+            mm([(v(b2, 0, 256), win("FN", b), v("PR%d_" % t, 256 * b, 256 * b + 256), b == 0, b == 15) for b in range(4 * c, 4 * c + 4)])
+        scan(v("MN"), v("BSEG"), v(b2, 0, 256), 0.0, A.add, A.min)
+
+    def replace(t):
+        own, b1 = v("TW", 256 * t, 256 * t + 256), RBANK or CBANKS[0]
         act(v("NX1"), ind(v("TW"), v("IX1")))
-        mm([(v("PD_", 256, 512), v("K89"), own, True, False), (v("PD_", 256, 512), v("P56"), v("NX1"), False, True)])
-        act(own, v("PD_", 256, 512))
+        mm([(v(b1, 256, 512), v("K89"), own, True, False), (v(b1, 256, 512), v("P56"), v("NX1"), False, True)])
+        act(own, v(b1, 256, 512))
         act(v("NX2"), ind(v("TW"), v("IX2")))
-        up_ = v("PD_", 256, 272)
-        mm([(up_, win("FL", a), v("NX2", a, 256, 16), a == 0, a == 15) for a in range(16)])
+        up_ = v(b1, 256, 272)
+        mm([(up_, win("FL", b), v("NX2", 16 * b, 16 * b + 16), b == 0, b == 15) for b in range(16)])
         ts(v("MI", 0, 16), v("MN", 15, 256, 16), 16.0, A.mult, 15.0, A.add)
         ts(v("MI", 16, 32), v("MI", 0, 16), 15, A.bitwise_and)
         tt(v("SM", 32, 48), v("MI", 16, 32), v("PB", 0, 16), A.add)
@@ -532,20 +577,51 @@ def rank_program(g, core, T, topo):
         act(v("NX"), ind(v("TW"), v("NC")))
         cp(ind(v("XX%d" % t), v("PL")), v("NX"))
 
-    lin(col(21), col(0), 16.0, -256.0)
-    ts(v("GK", p=p24), v("J16", p=p24), v("PC", 84, 85, p=p24), A.is_equal)
-    lists(0, 80, v("PW", 0, 80))
-    lists(1, 48, v("PW", 80, 128))
-    iota(v("UL"), [[0, 80], [1, 3]], 0, 0, True, [g0])
-    iota(v("CUM"), [[0, 768]], 0, 0, True, first)
-    act(v("UL", 2, 240, 3), v("PW", 0, 80), scale=1.0 / 256)
-    ts(v("REP3"), v("JF", 0, 16), 3.0, A.mult, 2.0, A.add)
-    lin(v("BGL"), v("PW", 80, 128), 1.0, 2048.0)
-    for h, bank in enumerate(("PT", "PK")):
+    lin(col(21, p24), col(0, p24), 16.0, -256.0)
+    ts(v("GK", p=p24), v("J16", p=p24), col(21, p24), A.is_equal)
+    for h, bank in enumerate(("PW", "PX")):
         mm([(v(bank, 0, 384), v("GK", p=p24), v("QF", 384 * h, 384 * h + 384, p=p24), True, True)])
         ts(v("OH", 384 * h, 384 * h + 384), v(bank, 0, 384), col(1), A.is_equal)
-    ts(v("CAP", 0, 768), v("OH"), -1.0, A.mult, 15.0, A.add)
-    ts(v("CAP", 768, 1536), v("OH"), -1.0, A.mult, 7.0, A.add)
+    ts(v("CAP", 0, 256), v("OH", 0, 256), -1.0, A.mult, 15.0, A.add)
+    ts(v("CAP", 256, 768), v("OH", 256, 768), -1.0, A.mult, 15.0, A.add)
+    for i in range(4):
+        ts(exact("TRI", 8 * i * (i + 3), 8 * i * (i + 3) + 16), v("JF", 0, 16), col(1), A.is_ge, 8192.0, A.mult)
+    x = act(v("SEG"), v("KI"), AF.Exp, scale=-100.0)
+    ops[x]["cost"] += 1300.0
+    ts(v("DG"), v("KI", 0, 128), col(1), A.not_equal, -8192.0, A.mult)
+    lin(v("RS"), v("SEG", 0, 128), -32768.0, 16384.0)
+    fill(v("RST"), -1.0)
+    for i in range(4):
+        fill(spots("RST", SEGW * (i + 1) - 18 - 16 * i, 8 * SEGW, 4 * SEGW), 0.5)
+        fill(spots("RST", SEGW * (i + 1) - 1, 8 * SEGW, 4 * SEGW), (i - 2048.0) / 4096)
+    dma("s", [(v("EE", 8 * SEGW * c, 8 * SEGW * (c + 1)), v("RST")) for c in range(4)], after=sent, lat=3500.0)
+    lin(col(22), col(1), 4.0, float(DUMP + 3 - 2048))
+    lin(col(23), col(1), 1.0, float(E + 16)) if KOLD else lin(col(23), col(1), 4.0, 19.0)
+    lin(col(24), col(1), 4.0 / 4096, (DUMP + 3 - HOLE - 2048) / 4096.0)
+    lin(col(25), col(1), 1.0, 16.0) if KOLD else lin(col(25), col(1), 4.0 / 4096, (19 - 2048) / 4096.0)
+    if KOLD:
+        iota(v("LK"), [[0, 256]], 0, 0, True, first)
+        fill(v("SH", 0, 128), 0.0)
+    extra[0] = 0.0
+    for d0, d1 in ((1, 4), (4, 8), (8, 12), (12, 16)) if KOLD else ():
+        o, m = v("SH", 128 * d0, 128 * d1), d1 - d0
+        sel(o, v("AG", 0, 128 * m), [[-1, m], [0, 8], [1, 16]], A.is_ge, 0.0, -d0, 0, sent)
+        sel(o, o, [[1, m], [-1, 128]], A.is_equal, 0.0, d0, 1)
+        sel(o, o, [[0, m], [-1, 128]], A.not_equal, -1.0, 0, 1)
+    extra[0] = SETUP[0]
+    ts(v("CT"), v("CAL", 0, 512), -1024.0, A.add)
+    act(v("BT", 0, 1), v("BE", 0, 1), scale=-1.0)
+    act(col(37), col(1), scale=256.0)
+    lin(v("PB", 0, 16), v("JF", 0, 16), 16.0, col(37))
+    lin(col(38), col(1), 1.0, 4096.0)
+    lin(v("PB", 16, 32), v("JF", 0, 16), 16.0, col(38))
+    for t in range(2):
+        lin(v("PB", 32 + 16 * t, 48 + 16 * t), v("PB", 16, 32), 1.0, 2944.0 + 256 * t - 8192.0)
+    lin(v("BSEG"), v("SEG"), 4096.0625, -0.0625)
+    extra[0] = PICKS0
+    for c in (0, 448):
+        (cp if WHO[c // 448] == "v" else act)(v("YY", NG + c, NG + c + 448), ind(v("TW", 0, E), v("SNL", c // 16, c // 16 + 28)))
+    extra[0] = 0.0
     for c, (who, qs) in enumerate(FIRST):
         for q_ in qs:
             for h, eng in enumerate(who):
@@ -554,45 +630,6 @@ def rank_program(g, core, T, topo):
                 (cp if eng == "v" else act)(v("XX0", 16 * c0, 16 * (c0 + n_)), ind(v("TW", 0, 2944), v("CAL", c0, c0 + n_)))
         prep(0, qs, *B0[c])
         k_gather(0, qs)
-        if c in SECOND:
-            steps(0, SECOND[c])
-    dma("s", [(v("TW", 0, E, p=slice(row, 128, 16)), v("S3", c, c + 128)) for row, c in ((8, 256), (9, 640))])
-    fill(v("TW", 2944, 3456), 0.0)
-    dma("s", [(v("TW", 2944, 3456, p=slice(row, 128, 16)), v("TW", 0, 512, p=slice(row + 3, 128, 16))) for row in (5, 6)])
-    for c in (0, 448):
-        (cp if WHO[c // 448] == "v" else act)(v("YY", NG + c, NG + c + 448), ind(v("TW", 0, E), v("SNL", c // 16, c // 16 + 28)))
-    act(v("SEG"), v("KI"), AF.Sign)
-    iota(v("LB"), [[0, 512]], 0, 0, True, first)
-    lin(col(22), col(1), 1.0, float(DUMP))
-    lin(col(23), col(1), 1.0, float(E + 16))
-    lin(col(24), col(1), 1.0, float(DUMP - HOLE))
-    lin(col(25), col(1), 1.0, 16.0)
-    prep2(0)
-    if EXP:
-        act(v("BT", 0, 1), v("BE", 0, 1), scale=-1.0)
-    else:
-        be = v("BE", 0, 1)
-        ts(v("BT", 0, 1), be, -1.0 / 6, A.mult, 0.5, A.add)
-        ts(v("BT", 4, 5), v("BT", 0, 1), be, A.mult, -1.0, A.add)
-        ts(v("BT", 8, 9), v("BT", 4, 5), be, A.mult, 1.0, A.add)
-        act(v("SD", 0, 512), v("OH", 0, 512), AF.Identity, bias=v("BT", 8, 9), scale=0.0)
-        mid = v("RT", 1024, 1536)
-        scan(mid, v("SD", 0, 512), v("SD", 0, 512), 1.0, A.mult, A.min)
-        run("v", lambda: g.vector.reciprocal(T.BT[:, 12:13], T.RT[:, 1535:1536]), v("BT", 12, 13), [v("RT", 1535, 1536)], 200.0)
-        tt(v("BT", 16, 17), v("BT", 12, 13), v("BT", 12, 13), A.mult)
-        act(v("RT", 0, 512), mid, scale=v("BT", 16, 17))
-        act(v("RT", 512, 1024), mid, scale=v("BT", 12, 13))
-        act(v("RT", 1536, 2048), mid, scale=v("RT", 1535, 1536))
-        fill(v("RT", 2047, 2048), 0.0)
-        ts(col(25), col(1), 256.0, A.mult, 15.0, A.add)
-        ts(v("LAML"), v("JF", 0, 16), 16.0, A.mult, col(25), A.add)
-    act(col(37), col(1), scale=64.0)
-    lin(v("PB", 0, 16), v("PB", 0, 16), 1.0, col(37))
-    lin(col(38), col(1), 1.0, 4096.0)
-    lin(v("PB", 16, 32), v("JF", 0, 16), 16.0, col(38))
-    for t in range(2):
-        lin(v("PB", 32 + 16 * t, 48 + 16 * t), v("PB", 16, 32), 1.0, 2944.0 + 256 * t - 8192.0)
-    lin(v("BSEG"), v("SEG"), -4096.0625, 4096.0)
 
     def chains():
         mm([(v("PT", 0, 112), win("FM", a), v("YY", a, 1792, 16), a == 0, a == 15) for a in range(16)])
@@ -606,75 +643,90 @@ def rank_program(g, core, T, topo):
         cp(v("PRV"), v("YT", 0, 56))
 
     for t in range(R):
-        s = t % 3
-        act(v("CUM", 29, 768, 48), v("BGL", 16 * s, 16 * s + 16))
-        for j, (b0, b1) in enumerate(PARTS):
-            tag[0] = 0
-            weights(t, j, b0, b1)
-            c0, c1 = 16 * b0, 16 * b1
-            cum, thr = v("CUM", 3 * c0, 3 * c1, 3), v("THR", 8 * b0, 5 * b0 + 3 * b1)
-            scan(cum, v("SEG", c0, c1), v("PW", c0, c1), 0.0, A.mult, A.add)
-            scan(thr, v("CUM", 3 * c0 + 13, 3 * c1, 16), v("UL", 48 * t + 3 * b0, 48 * t + 3 * b1), 0.0, A.add, A.mult)
-            tt(v("HIT", c0, c1), ind(thr, v("REP3", 0, b1 - b0)), cum, A.is_lt)
-            raise_(t, BANKS[j % len(BANKS)], b0, b1, 0)
-            tag[0] = 1
-            for k0, k1 in KPARTS if b0 == 0 and t < R - 1 else ():
-                raise_(t, "PX", k0, k1, 1)
-            if t == 0 and b0 == CH0:
-                chains()
-        tag[0] = 0
+        tag[0], phase[0] = 1, t + PH["prep"][t]
+        if t < 2:
+            w = 256 // len(LATER[t])
+            for c in range(256 - w, -1, -w):
+                (cp if LATER[t][c // w] == "v" else act)(v("XX%d" % (t + 1), 16 * c, 16 * (c + w)), ind(v("TW", 0, 2944), v("CAL", 256 * t + 256 + c, 256 * t + 256 + c + w)))
+        extra[0] = SOON[t]
+        if 0 < t < R - 1:
+            prep(t + 1, bk="PT" if PB1 else "PK")
+        extra[0] = SOON[t + 2] if t < 3 else 0.0
+        phase[0] = t + PH["replace"]
+        if t == 1:
+            dma("s", [(v("TW", 0, E, p=slice(row_, 128, 16)), v("S3", c, c + 128)) for row_, c in ((8, 256), (9, 640))])
+            dma("s", [(v("TW", 2944, 3456, p=slice(row_, 128, 16)), v("TW", 0, 512, p=slice(row_ + 3, 128, 16))) for row_ in (5, 6)])
+        if t in (1, 2) and not RBANK:
+            replace(t - 1)
+        extra[0] = 0.0
+        if t == 3:
+            mm([(v("PT", 0, 128), win("FM", a), v("TW", a, E, 16), a == 0, a == 15) for a in range(16)])
+            act(v("W1"), v("PT", 0, 128))
+            mm([(v("PT", 0, 128), roll32, v("W1"), True, True)])
+            ts(v("W2"), v("PT", 0, 128), float(NG), A.is_lt, float(NG), A.mult)
+            tt(v("W3"), v("W2"), v("PT", 0, 128), A.add)
+            cp(v("MAPL"), v("W3"))
+        for j, parts in enumerate(PARTS[t]):
+            tag[0], extra[0], b0, b1, phase[0] = 0, EARLY[j], parts[-1][0], parts[0][1], float(t)
+            elect(t, j, b0, b1)
+            elected(t, ABANKS[t][j], (0,), 16 * b0, 16 * b1)
+            raise_(t, ABANKS[t][j], parts, 0, XLV[j])
+        tag[0], extra[0] = 1, 0.0
+        if t == 0:
+            chains()
+            prep(1)
+        tag[0], extra[0], phase[0] = 1, KBOOST, t + PH["raise"]
+        for bank, b in zip(KBANKS, (8, 0)) if t < R - 1 else ():
+            elected(t, bank, (1, 2) if t < 2 else (1,), 16 * b, 16 * b + 128)
+            if KOLD:
+                raise_k(t, bank, b, b + 8)
+            else:
+                raise_(t, bank, [(b + 4, b + 8), (b, b + 4)], 1, XLK)
+        if t in (1, 2) and RBANK:
+            extra[0] = SOON[t + 2]
+            replace(t - 1)
+        if t == 1 and RBANK:
+            candidates(t)
+        tag[0], extra[0], phase[0] = 0, 0.0, t + PH["chain"]
         buf = "BUF" if t % 2 == 0 else "BUG"
         sent, came = exchange("SW", GHO, buf, NG, -1, calls=X1)
-        through(buf, 0, [(ident, "GN", 0), (roll, "SW", GUN)], both=BOTH[t])
+        through(buf, 0, [(ident, "GN", 0), (roll, "SW", GUN)], both=BOTH[t], plus=241.0)
         if t < R - 1:
-            dma("s", [(v("AW", OWN, OWN + E), v("SW", OWN, OWN + E))], after=sent, lat=3000.0)
+            dma("s", [(v("AW", OWN, OWN + E), v("SW", OWN, OWN + E))], after=sent[:SHADOW], lat=3000.0)
         for d in range(7):
             c = NG + GH * d
             tt(v(buf, c, c + GH), ind(v(buf, 0, c), v("PRV", 8 * d, 8 * d + 8)), v(buf, c, c + GH), A.add)
         if t < R - 1:
-            for c0, c1 in PICK:
-                ts(v("GN", c0, c1), ind(v(buf, 0, 2 * NG), v("LST", c0 // 16, c1 // 16)), 15.0, A.min)
+            for (c0, c1), eng in zip(PICK, PICKS[t]):
+                o, src = v("GN", c0, c1), ind(v(buf, 0, 2 * NG), v("LST", c0 // 16, c1 // 16)) if c0 < NG - GH else v(buf, NG + c0, NG + c1)
+                ts(o, src, -241.0, A.add) if eng == "v" else lin(o, src, 1.0, -241.0)
             sent, came = exchange("GN", 0, "AW", GHO, 1, calls=X2)
             through("AW", GUN, [(unroll, "GN", 0)])
             tag[0] = 1
             iota(v("SW", GUN, PAD), [[0, 2 * NG]], 0, 0, True, sent[-1:])
             if t < R - 2:
                 dma("s", [(v("AW", KB, KH), v("SW", KB, KH))], after=came, lat=3000.0)
-            if t < 2:
-                for c in range(4):
-                    (cp if LATER[t][c] == "v" else act)(v("XX%d" % (t + 1), 1024 * c, 1024 * c + 1024), ind(v("TW", 0, 2944), v("CAL", 256 * t + 256 + 64 * c, 256 * t + 320 + 64 * c)))
-            prep(t + 1)
+            phase[0] = t + PH["gather"]
             k_gather(t + 1)
-            if t < 2:
+            phase[0] = t + PH["parents"]
+            if t < (1 if RBANK else 2):
                 candidates(t)
-            prep2(t + 1)
-            tag[0] = 2
-            if t == 0:
-                decay(0)
-            decay(t + 1)
+            tag[0], phase[0] = 2, t + PH["decay"][t]
+            decay(t)
         else:
+            phase[0] = t + PH["decay"][t]
+            decay(t)
+            phase[0] = t + PH["chain"]
             for c in range(4):
                 bank = v(BANKS[c % 2], 0, 512)
                 mm([(bank, roll, v("SW", OWN + 512 * c, OWN + 512 * c + 512), True, True)])
-                act(v("BUF", OWN + 512 * c, OWN + 512 * c + 512), bank)
+                lin(v("BUF", OWN + 512 * c, OWN + 512 * c + 512), bank, 1.0, 241.0)
             for c0, c1, eng in FINAL:
                 o, src = v("RG1", c0, c1), ind(v("BUF"), v("MAPL", c0 // 16, c1 // 16))
-                if eng == "v":
-                    ts(o, src, 15.0, A.min)
-                else:
-                    act(v("RG1", E + c0, E + c1), src, AF.Relu, bias=15.0, scale=-1.0)
-                    lin(o, v("RG1", E + c0, E + c1), -1.0, 15.0)
+                ts(o, src, -241.0, A.add) if eng == "v" else lin(o, src, 1.0, -241.0)
                 dma("s" if eng == "v" else "a", [(T.ya[0:112, c0:c1], v("RG1", c0, c1, p=up)), (T.ya[112:128, c0:c1], v("RG1", c0, c1, p=down))])
-        tag[0] = 2
+        tag[0], phase[0] = 2, t + PH["lam"][t]
         lam(t)
-        tag[0] = 1
-        if t == 2:
-            mm([(v("PD_", 0, 128), win("FM", a), v("TW", a, E, 16), a == 0, a == 15) for a in range(16)])
-            act(v("W1", 0, 128), v("PD_", 0, 128))
-            mm([(v("PD_", 0, 128), roll32, v("W1", 0, 128), True, True)])
-            ts(v("W2", 0, 128), v("PD_", 0, 128), float(NG), A.is_lt, float(NG), A.mult)
-            tt(v("W3", 0, 128), v("W2", 0, 128), v("PD_", 0, 128), A.add)
-            cp(v("MAPL"), v("W3", 0, 128))
 
     n = len(ops)
     succ = [[] for _ in range(n)]
@@ -692,51 +744,7 @@ def rank_program(g, core, T, topo):
         return ops[d]["lat"] + SYNC
 
     if n not in ORDER:
-        level = [0.0] * n
-        for i in range(n - 1, -1, -1):
-            level[i] = ops[i]["cost"] + max([gap(i, j) + ops[i].get("urge", 0.0) + level[j] for j in succ[i]] + [ops[i]["lat"] + ops[i].get("due", 0.0)])
-        pred = [sorted(o["deps"]) for o in ops]
-        fgap = [[(j, gap(i, j) + ops[i].get("urge", 0.0)) for j in succ[i]] for i in range(n)]
-        bgap = [[(d, gap(d, i) + ops[d].get("urge", 0.0)) for d in pred[i]] for i in range(n)]
-
-        def fit(key, npred, out, head, sign=1.0):
-            left, est, start, busy = list(npred), list(head), [0.0] * n, {q: [] for q in Q}
-            ready = [i for i in range(n) if not left[i]]
-            while ready:
-                i = min(ready, key=lambda j: key[j] - sign * ops[j]["rank"])
-                ready.remove(i)
-                t0, c, q = est[i], ops[i]["cost"], ops[i]["q"]
-                if q is not None:
-                    line_ = busy[q]
-                    lo, hi = 0, len(line_)
-                    while lo < hi:
-                        mid_ = (lo + hi) // 2
-                        if line_[mid_][1] <= t0:
-                            lo = mid_ + 1
-                        else:
-                            hi = mid_
-                    while lo < len(line_) and line_[lo][0] < t0 + c:
-                        t0 = max(t0, line_[lo][1])
-                        lo += 1
-                    line_.insert(lo, (t0, t0 + c))
-                start[i] = t0
-                for j, w in out[i]:
-                    est[j] = max(est[j], t0 + c + w)
-                    left[j] -= 1
-                    if not left[j]:
-                        ready.append(j)
-            return start
-
-        key, best, rng = [-x for x in level], None, np.random.default_rng(1)
-        for it in range(PASSES):
-            fw = fit(key, [len(x) for x in pred], fgap, [0.0] * n)
-            span = max(fw[i] + ops[i]["cost"] + ops[i]["lat"] for i in range(n))
-            if best is None or span < best[0]:
-                best = (span, sorted(range(n), key=lambda i: (fw[i], i)), fw)
-            base = fw if span <= best[0] + SLIP else best[2]
-            bw = fit([-(base[i] + ops[i]["cost"]) for i in range(n)], [len(x) for x in succ], bgap, [(ops[i]["lat"] if not succ[i] else 0.0) + ops[i].get("due", 0.0) for i in range(n)])
-            noise = rng.random(n) * NOISE
-            key = [-(bw[i] + ops[i]["cost"]) + float(noise[i]) for i in range(n)]
+        pred, rng = [sorted(o["deps"]) for o in ops], np.random.default_rng(SEED)
         anc, fp = [0] * n, []
         for i in range(n):
             m_ = 0
@@ -747,17 +755,52 @@ def rank_program(g, core, T, topo):
                 m_ |= 1 << d
             anc[i] = m_
         lat, views = [o["lat"] for o in ops], []
-        for per, sync, slow in VIEWS:
-            cost = [(o["cost"] + o.get("picked", 0.0) * (per - GATHER)) * (slow if o["kind"] == "c" else 1.0) for o in ops]
+        for per, put, sync, slow, fix, pe in VIEWS:
+            cost = [(o["cost"] + o.get("picked", 0.0) * (per - GATHER) + o.get("put", 0.0) * (put - SCATTER) + (fix if o["q"] == "v" else 0.0)) * (slow if o["kind"] == "c" else 1.0)
+                    * (pe if o["q"] == "t" else 1.0) for o in ops]
             into = [[(d, cost[d] + (w - SYNC + sync if w and ops[i]["kind"] != "r" else w)) for d, w in fp[i]] for i in range(n)]
             out = [[] for _ in range(n)]
             for i in range(n):
                 for d, w in into[i]:
                     out[d].append((i, w))
             views.append((cost, into, out))
-        seq = {q: [i for i in best[1] if ops[i]["q"] == q] for q in Q}
-
         before, after_ = [-1] * n, [-1] * n
+
+        def fit(key, cost, out, npred, head):
+            left, est, start, busy = list(npred), list(head), [0.0] * n, {q: ([], []) for q in Q}
+            place = [0] * n
+            for x, i in enumerate(sorted(range(n), key=lambda j: key[j])):
+                place[i] = x
+            ready = sorted((-place[i], i) for i in range(n) if not left[i])
+            while ready:
+                i = ready.pop()[1]
+                t0, c, q = est[i], cost[i], ops[i]["q"]
+                if q is not None:
+                    begins, stops = busy[q]
+                    lo, hi = 0, len(stops)
+                    while lo < hi:
+                        mid_ = (lo + hi) // 2
+                        if stops[mid_] <= t0:
+                            lo = mid_ + 1
+                        else:
+                            hi = mid_
+                    while lo < len(stops) and begins[lo] < t0 + c:
+                        t0 = max(t0, stops[lo])
+                        lo += 1
+                    begins.insert(lo, t0)
+                    stops.insert(lo, t0 + c)
+                start[i] = t0
+                fresh = False
+                for j, w in out[i]:
+                    if t0 + w > est[j]:
+                        est[j] = t0 + w
+                    left[j] -= 1
+                    if not left[j]:
+                        ready.append((-place[j], j))
+                        fresh = True
+                if fresh:
+                    ready.sort()
+            return start
 
         def link(x, first_=-1, last_=-1):
             for a_, b_ in zip([first_] + x, x + [last_]):
@@ -820,10 +863,62 @@ def rank_program(g, core, T, topo):
                 worst = max(worst, h + t1)
             return worst
 
-        for x in seq.values():
-            link(x)
-        every, order_ = set(range(n)), best[1]
         heads, tails = [[0.0] * n for x in views], [[0.0] * n for x in views]
+        best, nin, nout = None, [len(x) for x in fp], [len(x) for x in views[0][2]]
+        urge, due, boost = [o.get("urge", 0.0) for o in ops], [o.get("due", 0.0) for o in ops], [o["rank"] for o in ops]
+        for i in range(n - 1, -1, -1):
+            boost[i] = max([boost[i]] + [boost[j] for j, w in views[0][2][i] if boost[j] > SETUP[0] > 0])
+        for start_ in range(STARTS):
+            cost, into, out = views[BUILD[start_ % len(BUILD)]]
+            fore = [[(j, w + urge[i]) for j, w in out[i]] for i in range(n)]
+            back = [[(d, w - cost[d] + cost[i] + urge[d]) for d, w in into[i]] for i in range(n)]
+            level = [0.0] * n
+            for i in range(n - 1, -1, -1):
+                level[i] = max([w + level[j] for j, w in fore[i]] + [cost[i] + lat[i] + due[i]])
+            key, mine = [-x for x in level], None
+            if PHASED:
+                turn = [o["phase"] for o in ops]
+                for i in range(n - 1, -1, -1):
+                    turn[i] = min([turn[i]] + [turn[j] for j, w in out[i]])
+                key = [1e7 * turn[i] - level[i] for i in range(n)]
+            for it in range(PASSES):
+                noise = rng.random(n) * (NOISE if start_ >= len(BUILD) or it else 0.0)
+                fw = fit([key[i] - boost[i] + float(noise[i]) for i in range(n)], cost, fore, nin, [0.0] * n)
+                order_ = sorted(range(n), key=lambda i: (fw[i], i))
+                for q in Q:
+                    link([i for i in order_ if ops[i]["q"] == q])
+                total = sum(times(order_, x, r, tail) * w for x, r, tail, w in zip(views, heads, tails, WEIGHT))
+                if mine is None or total < mine[0]:
+                    mine = (total, order_, fw)
+                base = fw if total <= mine[0] + SLIP else mine[2]
+                bw = fit([-(base[i] + cost[i]) - boost[i] for i in range(n)], cost, back, nout, [(lat[i] if not out[i] else 0.0) + due[i] for i in range(n)])
+                key = [-(bw[i] + cost[i]) for i in range(n)]
+            if best is None or mine[0] < best[0]:
+                best = mine + (BUILD[start_ % len(BUILD)],)
+        cost, into, out = views[best[3]]
+        key, now_ = list(best[2]), best[0]
+        for it in range(STEPS):
+            for q in Q:
+                link([i for i in best[1] if ops[i]["q"] == q])
+            j = it % len(views)
+            span = times(best[1], views[j], heads[j], tails[j])
+            on = [i for i in range(n) if heads[j][i] + tails[j][i] > span - NEAR]
+            mid = best[2][on[int(rng.integers(len(on)))]]
+            wide, push = float(rng.random()) * WIDE, float(rng.random()) * PUSH
+            key = list(best[2])
+            for i in on:
+                if abs(best[2][i] - mid) < wide:
+                    key[i] -= push
+            fw = fit(key, cost, out, nin, [0.0] * n)
+            order_ = sorted(range(n), key=lambda i: (fw[i], i))
+            for q in Q:
+                link([i for i in order_ if ops[i]["q"] == q])
+            total = sum(times(order_, x, r, tail) * w for x, r, tail, w in zip(views, heads, tails, WEIGHT))
+            if total <= best[0]:
+                best = (total, order_, fw, best[3])
+        for q in Q:
+            link([i for i in best[1] if ops[i]["q"] == q])
+        every, order_ = set(range(n)), best[1]
         for sweep in range(SWEEPS):
             size = STRETCH[sweep % len(STRETCH)]
             for p0 in range(-(sweep % 2) * size // 4, n - size // 2, size // 2):
@@ -837,16 +932,16 @@ def rank_program(g, core, T, topo):
                 npre = {i: sum(d in inside for d, w in fp[i]) for i in part}
                 lines = {q: [i for i in part if ops[i]["q"] == q] for q in Q}
                 ends = {q: (before[x[0]], after_[x[-1]]) for q, x in lines.items() if x}
-                tabu, best_, now, undo = {}, None, None, None
+                tabu, best_, now_, undo = {}, None, None, None
                 for it in range(MOVES):
                     todo = sort(part, inside, views[0][2])
-                    total = sum(times(todo, x, r, tail) for x, r, tail in zip(views, heads, tails)) if len(todo) == len(part) else 1e18
-                    if now is not None and total > now + SLACK:
+                    total = sum(times(todo, x, r, tail) * w for x, r, tail, w in zip(views, heads, tails, WEIGHT)) if len(todo) == len(part) else 1e18
+                    if now_ is not None and total > now_ + SLACK:
                         lines[undo[0]] = undo[1]
                         link(undo[1], *ends[undo[0]])
                         todo = sort(part, inside, views[0][2])
-                        total = sum(times(todo, x, r, tail) for x, r, tail in zip(views, heads, tails))
-                    now = total
+                        total = sum(times(todo, x, r, tail) * w for x, r, tail, w in zip(views, heads, tails, WEIGHT))
+                    now_ = total
                     if best_ is None or total < best_[0] - 1.0:
                         best_ = (total, {q: x[:] for q, x in lines.items()})
                     (cost, fp_, fs), r, tail = views[it % len(views)], heads[it % len(views)], tails[it % len(views)]
@@ -879,7 +974,7 @@ def rank_program(g, core, T, topo):
                             run_.append(x)
                             x = after_[x]
                     if not moves:
-                        tabu, now = {}, None
+                        tabu, now_ = {}, None
                         continue
                     e_, x, f, side, run_ = min(moves, key=lambda m_: m_[0] + float(rng.random()) * JITTER)
                     q = ops[x]["q"]
@@ -894,18 +989,24 @@ def rank_program(g, core, T, topo):
                     if x:
                         link(x, *ends[q])
         npre = [len(x) for x in fp]
-        ORDER[n] = (0.0, sort(order_, every, views[0][2]))
+        order_ = sort(order_, every, views[0][2])
+        ORDER[n] = ([times(order_, x, r, tail) for x, r, tail in zip(views, heads, tails)], order_)
     order = ORDER[n][1]
+    place = {i: x for x, i in enumerate(order)}
 
     ESEM = {"v": "ev", "a": "ea", "t": "et", "g": "eg"}
     count = {x: 0 for x in SEMAPHORES}
-    known = {q: {} for q in Q}
-    token = {}
+    known, waited = {q: {} for q in Q}, {}
+    token, seen = {}, {}
 
-    def wait(q, sem, val):
+    def wait(q, sem, val, also=()):
         if known[q].get(sem, 0) < val:
             Q[q].wait_ge(T.sem[sem], val)
             known[q][sem] = val
+            if q == "g":
+                waited[sem] = val
+        for s_ in also:
+            known[q][s_] = max(known[q].get(s_, 0), also[s_])
 
     for i in order:
         o = ops[i]
@@ -919,9 +1020,11 @@ def rank_program(g, core, T, topo):
             if q == ops[d]["q"] == "t" or d in o["behind"]:
                 continue
             sem, val = token[d]
-            need[sem] = max(need.get(sem, 0), val)
-        for sem in sorted(need):
-            wait(q, sem, need[sem])
+            if val > need.get(sem, (0, 0))[0]:
+                need[sem] = (val, d)
+        for sem in sorted(need, key=lambda s_: -place[need[s_][1]]):
+            wait(q, sem, need[sem][0], seen.get(need[sem][1], ()) if COVER else ())
+        seen[i] = dict(known[q])
         if o["kind"] == "x":
             o["calls"][0]()
             sem, k = o["sem"], o["n"]
@@ -936,6 +1039,7 @@ def rank_program(g, core, T, topo):
             o["calls"][-1]().then_inc(T.sem[sem], 1)
         count[sem] += k
         token[i] = (sem, count[sem])
-    for sem in SEMAPHORES:
-        if count[sem]:
-            wait("g", sem, count[sem])
+    last = {token[i][0]: x for x, i in enumerate(order)}
+    for sem in sorted(last, key=lambda s_: last[s_]):
+        if waited.get(sem, 0) < count[sem]:
+            g.wait_ge(T.sem[sem], count[sem])

import numpy as np
from concourse.bass import DstId, RemoteDMATransfer
from concourse.mybir import AluOpType, ActivationFunctionType

N, E, GH, NG, R = 8, 2048, 128, 896, 5
GUN, GHO, PAD, HOLE, OWN, DUMP, KB, KH, RWN = 0, 896, 1792, 1807, 1808, 3856, 3920, 5968, 6048
F32, BF, I32, U16, F16 = "float32", "bfloat16", "int32", "uint16", "float16"
SEGW = 66
SB = {
    "AW": (RWN, BF), "SW": (RWN, BF), "TW": (3456, BF), "BUF": (DUMP, BF), "GN": (NG, BF), "BUG": (2 * NG, BF),
    "XX0": (4352, BF), "XX1": (4352, BF), "XX2": (4096, BF), "KG": (4096, BF), "PR0_": (4096, BF), "PR1_": (4096, BF), "PR2_": (4096, BF), "AS": (4096, BF),
    "RG0": (4096, F32), "RG1": (4096, F32), "SC": (4096, F32), "BC": (2048, BF), "FN": (144, BF), "LH0": (256, F16), "LH1": (256, F16), "LH2": (256, F16),
    "GT": (NG, BF), "VV": (NG, BF), "YY": (1792, BF), "GS": (NG, BF), "SL": (512, BF), "HI": (448, BF), "LO": (512, BF), "AG": (512, BF),
    "CA": (768, I32), "CAL": (768, U16), "SN": (56, I32), "SNL": (56, U16), "EQ": (48, F32), "RM": (128, BF),
    "SI": (384, I32), "S2": (896, I32), "S3": (1024, BF), "UR": (1280, I32),
    "QI": (144, I32), "QH": (144, BF), "QF": (768, BF), "JF": (144, F32), "KI": (256, F32), "J16": (128, F32), "J8": (128, F32), "PI": (32, I32), "PC": (224, F32),
    "F0": (144, BF), "FT": (144, BF), "FK": (144, BF), "FM": (144, BF), "FL": (144, BF), "F15": (144, BF),
    "I2": (256, BF), "D11": (128, BF), "D12": (128, BF), "K89": (128, BF), "P56": (128, BF), "I32F": (256, F32),
    "GK": (128, BF), "GM": (128, BF), "NT": (128, BF), "KV": (128, BF), "WC": (248, BF), "WB": (128, BF), "W0": (128, BF), "FH": (384, BF),
    "TRI": (160, BF), "RST": (8 * SEGW, F16), "SEG": (256, BF), "BSEG": (256, F32), "PB": (64, F32), "OH": (768, BF), "CAP": (768, BF),
    "YU": (112, F32), "YT": (168, F32), "PRV": (56, U16), "LST": (56, U16), "MAPL": (128, U16), "BE": (8, F32), "BT": (4, F32),
    "YI": (256, BF), "SS": (512, F16), "MT": (512, F16), "CT": (512, F16), "ML": (512, U16), "BNL": (512, U16), "XL": (512, F32), "DG": (128, BF), "RS": (128, F32),
    "THR": (256, F32), "HIT": (256, BF), "PD": (768, F16), "EE": (32 * SEGW, F16), "OF": (32 * SEGW, F16),
    "SH": (2048, BF), "XK": (256, F16), "LK": (256, F32), "EK": (256, F32), "OK": (256, F32), "L2": (32, U16), "ONE": (512, BF), "WS": (256, F16),
    "L1": (32, U16), "L1C": (32, U16), "NV": (512, BF), "NX": (256, BF), "NX1": (256, BF), "NX2": (256, BF),
    "LAM": (256, F32), "MN": (256, F32), "W1": (128, F32), "W2": (128, F32), "W3": (128, F32),
    "SM": (96, F32), "MI": (32, I32), "IX1": (16, U16), "IX2": (16, U16), "PL": (16, U16), "NC": (16, U16),
}
DROP = 24.0
ALIAS = {"GT": ("KG", 0), "YY": ("PR2_", 0), "VV": ("PR2_", 1792), "GS": ("PR0_", E), "SL": ("PR0_", E + NG), "AG": ("ONE", 0), "HI": ("PR1_", 2048), "LO": ("PR1_", 2048 + NG)}
PS = ["PW", "PD_", "PR0", "PR1", "PT", "PK", "PX", "PM"]
POOL, _n = {}, 0
for _k, (_c, _d) in SB.items():
    if _d == U16:
        POOL[_k] = _n
        _n += (_c + 15) // 16 * 16
SCRATCH = {k: ("sbuf", [128, n], d) for k, (n, d) in SB.items() if k not in POOL and k not in ALIAS}
SCRATCH["UP"] = ("sbuf", [128, _n], U16)
for _k in PS:
    SCRATCH[_k] = ("psum", [128, 512], F32)
X1 = ((((1, 2), 0, 4),), (((3, 4), 0, 4),), (((5, 6), 0, 4),), (((7,), 0, 8),))
X0 = ((((1, 2, 3, 4), 0, 2),), (((5, 6), 0, 4),), (((7,), 0, 8),))
X2 = ((((1,), 0, 8),), (((2, 3), 0, 4),), (((4, 5, 6, 7), 0, 2),))
SEMAPHORES = ["ev", "ea", "et", "eg"] + ["l%d" % _k for _k in range(40)] + ["h%d" % _k for _k in range(44)] + ["d%d" % _k for _k in range(56)]
SIZE = {F32: 4, I32: 4, BF: 2, U16: 2, F16: 2}
A = AluOpType
AF = ActivationFunctionType
CYC, FIX, FIXS, GATHER, SCATTER, PEC, SYNC, DMALAT, ROWLAT, ISSUE, HOP, ROW = 0.87, 50.0, 5.0, 1.8, 3.8, 0.43, 250.0, 2200.0, 100.0, 400.0, 1500.0, 35.0
PASSES, SLIP, NOISE, MOVES, REACH, FAR, JITTER, TENURE, ORDER = 15, 3000.0, 600.0, 60, 5, 80, 300.0, 20, {}
SEED, STARTS, BUILD, WEIGHT = 6, 9, (0, 2, 4), (1.0, 1.0, 1.0, 1.0, 1.0)
LAG, COVER, AHEAD, KBOOST, SHADOW = 0, True, (0.0, 0.0, 0.0, 0.0, 0.0), 700.0, 3
KOLD, RUNS, WSV = False, 16, ("vvvv",) * 5
SOON, RBANK = (0.0, 0.0, 0.0, 0.0, 0.0), "PR1"
SETUP, PICKS0, FIRSTLATE = (50000.0, 100000.0), 50000.0, 2000.0
PHASED, PH = False, {"chain": 0.1, "prep": (0.15, 0.15, 0.15, 0.15, 0.15), "raise": 0.2, "gather": 0.3, "parents": 0.4, "replace": 0.5, "decay": (1.6, 1.6, 1.6, 1.05, 0.05), "lam": (1.7, 1.7, 1.7, 1.06, 0.2)}
STEPS, NEAR, WIDE, PUSH = 0, 300.0, 6000.0, 1500.0
SWEEPS, STRETCH = 20, (150, 110, 200)
EARLY, LBA = (2100.0, 1400.0, 700.0, 0.0), ("aa",) * 5
PARTS = ((((12, 16),), ((8, 12),), ((4, 8),), ((0, 4),)),) * 5
SPLIT = ((0, 0, 16, 48), (32, 32, 32, 32), (32, 48, 48, 48), (32, 48, 48, 48), (32, 48, 48, 48))
LATER = ("vvaaaaaa", "vvaaaaaa")
DB, SBK = ("PR0", "PR0"), ("PR1", "PR1")
WHO = "va"
DUE = (80000.0, 58000.0, 39000.0, 19000.0, 0.0)
KBANKS, CBANKS = ("PW", "PX"), ("PT", "PK")
KV = ("aaaaaaaa", "aaaaaaaa", "vvaaaaaa", "vaaaaaaa", "vaaaaaaa")
BOOST = (1500.0, 500.0, 0.0)
PIECE = 128
BANKS, WCH, LATE, CH0 = ("PD_", "PM"), 64, 500.0, 8
FIRST = (("va", (3,)), ("va", (2,)), ("v", (1,)), ("v", (0,)))
B0 = (("PT", "PK"), ("PR0", "PR1"), ("PD_", "PM"), ("PW", "PX"))
VIEWS, SLACK = ((1.56, 3.8, 80.0, 1.0, 0.0, 1.0), (2.0, 4.5, 120.0, 1.3, 0.0, 1.0), (1.2, 3.0, 100.0, 1.2, 0.0, 1.2), (1.8, 3.8, 150.0, 1.45, 10.0, 1.0), (1.56, 3.8, 200.0, 1.1, 0.0, 1.0)), 500.0
NVK = "a"
PICK, PICKS = ((0, 128), (128, 384), (384, 768), (768, NG)), ("vvvv",) * 4
BOTH, URGE = (False, False, False, False, False), (0.0, 5000.0, 5000.0, 5000.0, 5000.0)
HALFLISTS = (False, True, True, True, True)
FINAL = ((0, 448, "v"), (448, 896, "a"), (896, 1248, "v"), (1248, 1600, "a"), (1600, 1824, "v"), (1824, 2048, "a"))
ABANKS, PB1 = (("PK", "PR1", "PM", "PX"),) + (("PW", "PX", "PD_", "PM"),) * 4, False
XLV, XLK = (True, True, True, True), True
RENUM = "a"


def rank_program(g, core, T, topo):
    rank = T.rank_of(core)
    if rank is None:
        return
    phase = [0.0]
    Q = {"v": g.vector, "a": g.scalar, "t": g.tensor, "g": g, "s": g.sync}
    ops, hist, ndma, nx, tag, extra = [], {}, [0], [0, 0], [1], [0.0]

    def v(name, c0=0, c1=None, step=1, p=None):
        n, sz = (SB[name][0], SIZE[SB[name][1]]) if name in SB else (512, 4)
        c1 = n if c1 is None else c1
        rows = slice(None) if p is None else p
        base, r0 = ALIAS.get(name, (name, 0))
        ten, b = (T.UP, POOL[name]) if name in POOL else (T[base], r0)
        ap_ = ten[rows, b + c0:b + c1:step] if step != 1 else ten[rows, b + c0:b + c1]
        return {"ap": ap_, "reg": [(base, ((r0 + c0) * sz) // 16 * 16, ((r0 + c1) * sz + 15) // 16 * 16)], "n": len(range(c0, c1, step)), "sz": sz, "ps": name in PS}

    def spots(name, c0, c1, step):
        x = v(name, c0, c1, step)
        return dict(x, reg=[(name, c * x["sz"], (c + 1) * x["sz"]) for c in range(c0, c1, step)])

    def exact(name, c0, c1):
        x = v(name, c0, c1)
        return dict(x, reg=[(name, c0 * x["sz"], c1 * x["sz"])])

    def ind(win, off):
        return {"ap": win["ap"].indirect(off["ap"]), "reg": win["reg"], "off": off["reg"], "n": 16 * off["n"], "sz": win["sz"], "ps": False}

    def regs(xs):
        return [r for x in xs if isinstance(x, dict) for r in x["reg"] + x.get("off", [])]

    def ap(x):
        return x["ap"] if isinstance(x, dict) else x

    def add(q, calls, rd, wr, cost, lat=0.0, kind="c", after=(), free=False, behind=()):
        me, deps = len(ops), set(after)
        if not free:
            for rs, w in ((rd, False), (wr, True)):
                for name, lo, hi in rs:
                    for (o, l2, h2, w2) in hist.get(name, []):
                        if (name in PS and (ops[o]["q"] != q or q == "t")) or (l2 < hi and lo < h2 and (w or w2)):
                            deps.add(o)
        for name, lo, hi in wr:
            keep = [r for r in hist.get(name, []) if kind == "d" or name in PS or not (lo <= r[1] and r[2] <= hi)]
            hist[name] = keep + [(me, lo, hi, True)]
        for name, lo, hi in rd:
            hist.setdefault(name, []).append((me, lo, hi, False))
        ops.append({"q": q, "calls": calls, "deps": deps | set(behind), "behind": set(behind) - deps, "cost": cost, "lat": lat, "rank": BOOST[tag[0]] + extra[0], "phase": phase[0], "kind": kind})
        return me

    def run(q, call, o, ins, per, behind=()):
        xs = [x for x in [o] + ins if isinstance(x, dict)]
        if "off" in o:
            per = SCATTER
        elif any("off" in x for x in xs):
            per = GATHER
        elif per == 0.5 and any(x["sz"] == 4 and x["n"] > 1 for x in xs):
            per = 1.0
        cost = FIX + CYC * per * o["n"] if q != "v" or per in (GATHER, SCATTER) else FIXS + CYC * max(64, per * o["n"])
        me = add(q, [call], regs(ins) + o.get("off", []), o["reg"], cost, behind=behind)
        ops[me]["picked"], ops[me]["put"] = CYC * o["n"] * (per == GATHER), CYC * o["n"] * (per == SCATTER)
        return me

    def tt(o, a, b, op):
        return run("v", lambda: g.vector.tensor_tensor(ap(o), ap(a), ap(b), op), o, [a, b], 1.0 if a["ps"] or b["ps"] else 2.0)

    def ts(o, a, s1, op0, s2=None, op1=None):
        if op1 is None:
            return run("v", lambda: g.vector.tensor_scalar(ap(o), ap(a), ap(s1), None, op0), o, [a, s1], 0.5)
        return run("v", lambda: g.vector.tensor_scalar(ap(o), ap(a), ap(s1), ap(s2), op0, op1), o, [a, s1, s2], 0.5)

    def cp(o, a, behind=()):
        return run("v", lambda: g.vector.tensor_copy(ap(o), ap(a)), o, [a], 0.5, behind)

    def scan(o, d0, d1, init, op0, op1):
        return run("v", lambda: g.vector.tensor_tensor_scan(ap(o), ap(d0), ap(d1), ap(init), op0, op1), o, [d0, d1, init], 0.5)

    def fill(o, c, behind=()):
        return run("v", lambda: g.vector.memset(ap(o), c), o, [], 0.5, behind)

    def act(o, a, f=AF.Copy, bias=None, scale=1.0, behind=()):
        if bias is None:
            return run("a", lambda: g.scalar.activation(ap(o), ap(a), f, scale=ap(scale)), o, [a, scale], 1.0, behind)
        return run("a", lambda: g.scalar.activation(ap(o), ap(a), f, bias=ap(bias), scale=ap(scale)), o, [a, bias, scale], 1.0, behind)

    def mm(items):
        def one(x):
            return lambda: g.tensor.matmul(ap(x[0]), ap(x[1]), ap(x[2]), x[3], x[4])
        cost = sum(max(64, x[2]["n"]) * (4 if x[2]["sz"] == 4 else 1) * PEC for x in items)
        return add("t", [one(x) for x in items], regs([y for x in items for y in x[1:3]]), list(set(regs([x[0] for x in items]))), cost, 150.0)

    def iota(o, pat, base, cm, small=True, behind=()):
        if small:
            return run("g", lambda: g.iota(ap(o), pat, base, cm, allow_small_or_imprecise_dtypes=True), o, [], 2.0, behind)
        return run("g", lambda: g.iota(ap(o), pat, base, cm), o, [], 2.0, behind)

    def sel(o, a, pat, op, fl, base, cm, behind=()):
        return run("g", lambda: g.affine_select(ap(o), ap(a), pat, op, fl, base, cm), o, [a], 2.0, behind)

    def dma(q, pairs, other_rows=False, after=(), lat=DMALAT, behind=()):
        def one(o, a):
            return lambda: Q[q].dma_start(ap(o), ap(a))
        rd, wr = regs([a for o, a in pairs]), list(set(regs([o for o, a in pairs])))
        me = add(q, [one(o, a) for o, a in pairs], rd, wr, 100.0 * len(pairs), lat, "d")
        if other_rows:
            ops[me]["deps"] = set(o for o in ops[me]["deps"] if ops[o]["kind"] != "d")
        ops[me]["deps"].update(after)
        ops[me]["behind"] = set(behind) - ops[me]["deps"]
        ops[me]["deps"].update(behind)
        ops[me]["sem"] = "d%d" % ndma[0]
        ndma[0] += 1
        return me

    sends = []

    def exchange(src, s0, dst, d0, sign, after=(), late=0.0, calls=None):
        mine, came, busy = [], [], {}
        for j, call_ in enumerate(calls or X0):
            k, lands = nx[0], []
            nx[0] += 1
            for blocks, e0, m in call_:
                used = range(e0, e0 + m * len(blocks))
                end = max(busy.get(e, 0.0) for e in used)
                end = max(end, ISSUE * j) + ROW * 128 // m
                busy.update({e: end for e in used})
                lands.append((blocks, e0, m, nx[1], end))
                nx[1] += 1

            def call(lands=lands, k=k):
                out = []
                for blocks, e0, m, h, end in lands:
                    for i, d in enumerate(blocks):
                        peer = T.cores[(rank + sign * d) % N]
                        rid, pid, _ = topo.addr(peer)
                        mask = sum(1 << e for e in topo.engines(core, peer)[e0 + m * i:e0 + m * i + m])
                        out.append(RemoteDMATransfer(dst_ids=[DstId(rid=rid, pnc=pid)], dma_engine_mask=mask, remote_sem=T.sem["h%d" % h],
                                                     src=v(src, s0 + GH * (d - 1), s0 + GH * d)["ap"], dst=v(dst, d0 + GH * (d - 1), d0 + GH * d)["ap"]))
                g.remote_dma_fused(out, local_sem=T.sem["l%d" % k])
            c0, c1 = GH * (lands[0][0][0] - 1), GH * lands[-1][0][-1]
            me = add("g", [call], v(src, s0 + c0, s0 + c1)["reg"], [], ISSUE, late + HOP + max(x[4] for x in lands) - ISSUE * j - 500.0, "x", after=after, behind=sends[-1:])
            sends.append(me)
            ops[me]["sem"], ops[me]["n"] = "l%d" % k, sum(m * len(blocks) for blocks, e0, m, h, end in lands)
            mine.append(me)
            for blocks, e0, m, h, end in lands:
                arr = add(None, [], [], v(dst, d0 + GH * (blocks[0] - 1), d0 + GH * blocks[-1])["reg"], 0.0, 0.0, "r", free=True)
                ops[arr]["sem"], ops[arr]["n"] = "h%d" % h, m * len(blocks)
                ops[arr]["gaps"] = dict([(me, late + HOP + ROW * 128 // m)] + [(x, ROW * 128 // m) for x in came[-1:]])
                came.append(arr)
        return mine, came

    def col(j, p=None):
        return v("PC", 4 * j, 4 * j + 1, p=p)

    def pint(j):
        return v("PI", 4 * j, 4 * j + 1)

    def win(name, a):
        return v(name, 15 - a, 143 - a)

    def lin(o, a, scale, bias):
        return act(o, a, AF.Identity, bias=bias, scale=scale)

    def row(j):
        return v("EQ", j, j + 1)

    def two(j):
        return v("EQ", 16 + j, 17 + j)

    up, down = slice(16, 128), slice(0, 16)
    p8, p16, p24 = slice(0, 8), slice(0, 16), slice(0, 24)
    extra[0] = SETUP[0]
    x = dma("s", [(v("SI", 0, 128), T.ti[:])])
    dma("s", [(v("SN"), T.snd[:])], behind=[x])
    dma("a", [(v("S2", 768, 896), T.kd[:])])
    fill(v("TW", 0, E), 0.0)
    g0 = iota(v("SI", 128, 256), [[1, 128]], 0, 128, False)
    g0 = iota(pint(0), [[0, 1]], 0, 1, False, [g0])
    g0 = iota(v("JF"), [[1, 144]], 0, 0, True, [g0])
    g0 = iota(v("HI"), [[64, 7], [0, 64]], 0, 0, True, [g0])
    g0 = iota(v("LO"), [[0, 8], [1, 64]], 0, 0, True, [g0])
    iota(v("KI"), [[0, 16], [1, 16]], 0, 0)
    iota(v("J16"), [[16, 8], [0, 16]], 0, 0)
    iota(v("J8"), [[0, 16], [1, 8]], 0, 0)
    cp(v("S3", 0, 128), v("SI", 0, 128))
    tt(v("S3", 384, 512), v("SI", 0, 128), v("S3", 0, 128), A.subtract)
    def halves(c0):
        ts(v("S2", c0, c0 + 128), v("SI", c0, c0 + 128), 0xFC0 if c0 == 256 else 0x7C0, A.bitwise_and)
        ts(v("S2", c0 + 384, c0 + 512), v("SI", c0, c0 + 128), 63, A.bitwise_and)
        cp(v("S3", c0, c0 + 128), v("S2", c0, c0 + 128))
        cp(v("S3", c0 + 384, c0 + 512), v("S2", c0 + 384, c0 + 512))

    halves(128)
    cp(v("S3", 768, 896), v("S2", 768, 896))
    act(v("S3", 896, 1024), v("S3", 128, 256), AF.Identity, bias=float(OWN))
    line = {"s": [], "a": []}
    for q, row_, c in (("s", 5, 128), ("a", 4, 512), ("s", 6, 512), ("a", 3, 896), ("s", 11, 768), ("a", 0, 0), ("s", 7, 384)):
        line[q].append(dma(q, [(v("TW", 0, E, p=slice(row_, 128, 16)), v("S3", c, c + 128))], True, behind=line[q][-1:], lat=DMALAT + ROWLAT * len(line[q])))
    a0 = dma("a", [(v("AW", OWN, OWN + E), T.a0[:])], lat=5000.0, behind=line["a"][-1:])
    small = dma("s", [(v("QI", 48, 96), T.bg[:]), (v("QI", 96, 144), T.cl[:])], behind=line["s"][-1:], lat=3000.0)
    ca = dma("s", [(v("CA"), T.ca[:])], behind=[small], lat=5000.0)
    x = dma("s", [(v("BE", 0, 1), T.be[:])], behind=[ca], lat=5000.0)
    k0 = dma("s", [(v("AW", KB, KH), T.k0[:])], behind=[x], lat=6000.0)
    snl = cp(v("SNL"), v("SN"))
    for name, c0, c1, x in (("AW", KH, RWN, 0), ("SW", DUMP, KB, 0), ("AW", PAD, OWN, 0), ("BUF", PAD, OWN, 0), ("SW", KH, RWN, 0), ("AG", 0, 512, 1), ("WC", 0, 248, 0),
                            ("TRI", 0, 160, 0), ("TW", 2944, 3456, 0)):
        iota(v(name, c0, c1), [[0, c1 - c0]], x, 0, True, [g0])
    iota(v("SW", 0, GHO), [[0, GHO]], 0, 0, True, [g0])
    iota(v("SW", GHO, OWN), [[0, OWN - GHO]], 0, 0, True, [g0])
    ts(pint(1), pint(0), 15, A.bitwise_and)
    cp(col(0), pint(0))
    cp(col(1), pint(1))
    tt(col(2), col(0), col(1), A.subtract)
    ts(v("EQ", 0, 16), v("JF", 0, 16), col(1), A.is_equal)
    tt(v("EQ", 16, 28), v("EQ", 0, 12), v("EQ", 1, 13), A.add)
    tt(v("EQ", 32, 34), v("EQ", 3, 5), v("EQ", 5, 7), A.add)
    high, low = v("EQ", 32, 33), v("EQ", 33, 34)
    act(col(39), row(8), scale=4032.0)
    lin(col(9), row(3), float(GHO), col(39))
    lin(col(10), row(5), float(E), col(9))
    lin(col(43), high, 448.0, col(10))
    lin(col(12), two(3), -1.0, 1.0)
    act(col(13), row(3), scale=-float(NG))
    lin(col(16), row(7), 1.0, row(0))
    lin(col(3), row(11), 1.0, col(16))
    ts(v("I2", 0, 128), v("JF", 0, 128), col(0), A.is_equal)
    act(v("I2", 128, 256), v("I2", 0, 128))
    lin(v("GS", 0, 448), v("HI"), high, col(10))
    lin(v("GS", 448, NG), v("HI"), high, col(43))
    act(v("SL"), v("LO"), scale=low)
    act(v("D11"), v("I2", 0, 128), scale=two(3))
    act(v("D12"), v("I2", 0, 128), scale=col(12))
    act(v("RM"), v("I2", 112, 240), scale=col(3))
    ident, roll, unroll = v("I2", 0, 128), v("I2", 112, 240), v("I2", 16, 144)
    pos32, roll32 = v("I32F", 0, 128), v("I32F", 112, 240)

    def through(dst, d0, terms, both=False, plus=0.0):
        for h, bank in enumerate(BANKS):
            c = 448 * h
            for j, (lhs, src, s0) in enumerate(terms):
                mm([(v(bank, 0, 448), lhs, v(src, s0 + c, s0 + c + 448), j == 0, j == len(terms) - 1)])
        for h, bank in enumerate(BANKS):
            o = v(dst, d0 + 448 * h, d0 + 448 * h + 448)
            if both and h:
                ts(o, v(bank, 0, 448), plus, A.add)
            else:
                lin(o, v(bank, 0, 448), 1.0, plus)

    for c0, c1, bank, pick, out in ((0, 384, "PR0", cp, cp), (384, NG, "PR1", act, act)):
        mm([(v(bank, 0, c1 - c0), ident, v("GS", c0, c1), True, False), (v(bank, 0, c1 - c0), ident, v("SL", 0, c1 - c0), False, False)])
        pick(v("YY", c0, c1), ind(v("TW", 0, E), v("SNL", c0 // 16, c1 // 16)))
        mm([(v(bank, 0, c1 - c0), v("RM"), v("YY", c0, c1), False, True)])
        out(v("GT", c0, c1), v(bank, 0, c1 - c0))
    extra[0] = SETUP[1]
    first, came = exchange("GT", 0, "TW", E, 1, late=FIRSTLATE, calls=X2)
    extra[0] = SETUP[0]
    for c in (0, 448):
        act(v("AW", GUN + c, GUN + c + 448), ind(v("AW", OWN, OWN + E), v("SNL", c // 16, c // 16 + 28)))
    through("GN", 0, [(roll, "AW", GUN)])
    sent, came = exchange("GN", 0, "AW", GHO, 1, late=LATE)
    for c in (KB, KB + 1024):
        ts(v("SW", c, c + 1024), v("AW", c, c + 1024), 249.0, A.add)
    dma("s", [(v("UR", 0, 256, p=slice(8 * k, 8 * k + 8)), T.us[:, 0:256]) for k in range(16)], behind=[k0], lat=5000.0)
    x = dma("s", [(v("SW", OWN, OWN + E), T.a0[:])], after=sent, lat=3000.0)
    x = dma("s", [(v("AW", KB, KH), v("SW", KB, KH))], after=sent, lat=4000.0, behind=[x])
    dma("s", [(v("UR", 256, 1280, p=slice(8 * k, 8 * k + 8)), T.us[:, 256:1280]) for k in range(16)], behind=[x], lat=5000.0)
    dma("s", [(v("SI", 256, 384), T.lp[:])], behind=[x], lat=5000.0)
    late_ = len(ops)
    halves(256)
    for o in ops[late_ - 5:]:
        o["rank"] = 0.0
    ts(v("F0"), v("JF"), -15.0, A.add, col(2), A.is_equal)
    act(col(17), row(11), scale=1.0 / 64)
    act(v("FT"), v("F0"), scale=col(16))
    act(v("FK"), v("F0"), scale=col(17))
    act(v("FM"), v("F0"), scale=two(3))
    act(v("FN"), v("F0"), scale=-1.0)
    lin(col(42), two(8), -1.0, 1.0)
    act(v("FL"), v("F0"), scale=two(8))
    act(v("K89"), ident, scale=col(42))
    act(v("P56"), v("I2", 125, 253), scale=two(5))
    ts(v("GM"), v("J16"), col(2), A.is_equal)
    act(col(18), col(16), scale=-1.0)
    act(col(19), row(11), scale=1.0 / 8)
    act(v("NT"), v("GM"), scale=col(18))
    act(v("KV"), v("GM"), scale=col(19))
    for c0, c1, bank in ((0, 128, "PT"), (128, 512, "PK"), (512, NG, "PX")):
        o = v(bank, 0, c1 - c0)
        mm([(o, v("D11"), v("GS", c0, c1), True, False), (o, v("D11"), v("SL", 0, c1 - c0), False, False), (o, v("D12"), v("YY", c0, c1), False, True)])
        ts(v("VV", c0, c1), o, col(13), A.add)
    extra[0] = SETUP[1]
    for d in range(7):
        lst = v("SNL", 8 * d, 8 * d + 8)
        if d:
            (cp if RENUM == "v" else act)(v("YY", GH * d, GH * d + GH), ind(v("TW", 0, E), lst))
        cp(ind(v("TW", 0, E), lst), v("VV", GH * d, GH * d + GH))
    extra[0] = SETUP[0]
    ts(v("QI", 0, 48), v("QI", 48, 96), 63, A.bitwise_and)
    ts(v("QI", 48, 96), v("QI", 48, 96), 0xFC0, A.bitwise_and)
    cp(v("QH"), v("QI"))
    dma("s", [(v("QF", p=slice(8 * j, 8 * j + 8)), v("QH", 48 * j, 48 * j + 48)) for j in range(3)])
    act(v("I32F"), v("I2"))
    for s in range(3):
        cp(v("CAL", 256 * s, 256 * s + 256), v("CA", 256 * s, 256 * s + 256))
    act(col(20), col(2), scale=1.0 / 16)
    ts(exact("WC", 120, 128), v("J8", 0, 8), col(20), A.is_equal, -1.0, A.mult)
    ts(pint(2), pint(0), 7, A.bitwise_and)
    cp(col(32), pint(2))
    ts(v("WB"), v("J8"), col(32), A.is_equal, 1.0 / 256, A.mult)
    act(v("W0"), v("WB"), scale=256.0)
    sel(v("W0"), v("W0"), [[1, 128]], A.is_ge, 0.0, 0, -1, first)
    ts(pint(3), pint(0), 3, A.arith_shift_right)
    cp(col(27), pint(3))
    ts(col(28), pint(2), 16.0, A.mult, col(27), A.add)
    ts(col(29), col(27), 15.0, A.is_equal, 1000.0, A.mult)
    ts(col(30), col(28), 1.0, A.add, col(29), A.add)
    ts(col(31), col(28), 1000.0, A.add, col(29), A.subtract)
    ts(v("FH", 128, 256), v("JF", 0, 128), col(28), A.is_equal)
    ts(v("FH", 256, 384), v("JF", 0, 128), col(30), A.is_equal)
    tt(v("FH", 0, 128), v("FH", 128, 256), v("FH", 256, 384), A.subtract)
    ts(v("F15"), v("JF"), col(31), A.is_equal, -3072.0, A.mult)
    for q in range(4):
        x = sel(v("BC", 512 * q, 512 * q + 512), v("AG"), [[-1, 4], [-16, 8], [0, 16]], A.is_equal, 0.0, -4 * q, 1, first)
        sel(v("BC", 512 * q, 512 * q + 384), v("BC", 512 * q, 512 * q + 384), [[-1, 3], [-16, 8], [0, 16]], A.not_equal, -1.0, -4 * q - 1, 1)

    def extract(t, qs, bank, b0, f, pre=None, close=True):
        c0, c1 = 64 * min(qs), 64 * max(qs) + 64
        if pre:
            mm([(v(bank, b0 + c0, b0 + c1), v(pre), v("TW", 256 * (t % 3) + c0, 256 * (t % 3) + c1), True, False)])
        for h in qs:
            for k0_ in range(0, 16, RUNS if t else 16):
                mm([(v(bank, b0 + 64 * h, b0 + 64 * h + 64), win(f, k), v("XX%d" % (t % 3), 1024 * h + k, 1024 * h + 1024, 16),
                     k == 0 and not pre, k == 15 and close and (not pre or h == qs[-1])) for k in range(k0_, k0_ + (RUNS if t else 16))])

    def prep(t, qs=(3, 2, 1, 0), bt="PT", bk="PK"):
        c0, c1, lh = 64 * min(qs), 64 * max(qs) + 64, "LH%d" % (t % 3)
        extract(t, qs, bt, 0, "FT", "NT")
        if bk != bt:
            extract(t, qs, bk, 0, "FK", "KV", False)
        else:
            extract(t, qs, bt, 256, "FM")
        act(v(lh, c0, c1), v(bt, c0, c1), AF.Abs)
        act(v("YI", c0, c1), v(lh, c0, c1), AF.Identity, bias=160.0 - 15.5 / 32, scale=1.0 / 32)
        if bk != bt:
            extract(t, qs, bt, 256, "FM")
        else:
            extract(t, qs, bk, 0, "FK", "KV", False)
        mm([(v(bk, c0, c1), ident, v("YI", c0, c1), False, True)])
        half, (bnl, ml, ss, mt) = HALFLISTS[t], [v(x, 256 * (t % 2) + c0, 256 * (t % 2) + c1) for x in ("BNL", "ML", "SS", "MT")]
        if t == R - 1 or not half:
            ts(bnl, v(bk, c0, c1), 64.0, A.mult, -10240.0, A.add)
        if not half:
            cp(ml, v(bt, 256 + c0, 256 + c1))
            ts(mt, ml, -float(HOLE), A.add)
            if c0 % 128 == 0:
                ts(v("SS", c0, c0 + 128), v("BNL", c0, c0 + 128), -float(E), A.add)
            return
        if t < R - 1:
            lin(ss, v(bk, c0, c1), 64.0, -10240.0 - E)
        lin(mt, v(bt, 256 + c0, 256 + c1), 1.0, -float(HOLE))
        if half:
            if t < R - 1:
                ts(bnl, ss, float(E), A.add)
            ts(ml, mt, float(HOLE), A.add)
        for o in ops[-4:] if t else ():
            o["urge"] = AHEAD[t]

    def k_gather(t, chunks=(3, 2, 1, 0)):
        w = 256 // len(KV[t])
        for c in [x for q in chunks for x in range(64 * q + 64 - w, 64 * q - 1, -w)]:
            o, src = v("KG", 16 * c, 16 * (c + w)), ind(v("SW", KB, KH), v("BNL", 256 * (t % 2) + c, 256 * (t % 2) + c + w))
            me = ts(o, src, -1.0, A.mult, 249.0, A.add) if KV[t][c // w] == "v" else lin(o, src, -1.0, 249.0)
            if t:
                ops[me]["urge"] = URGE[t]

    def decay(t):
        rg = "RG%d" % (t % 2)
        for c in range(8):
            bank, h, r = DB[c % 2], 1 - c // 4, c % 4
            mm([(v(bank, q, 512, 4), v("BC", 128 * (4 * q + r), 128 * (4 * q + r + 1)), v("LH%d" % (t % 3), 128 * h, 128 * h + 128), True, True) for q in range(4)])
            o = dict(v(rg, 2048 * h + r, 2048 * h + 2048, 4), reg=[(rg, 8192 * h + 2048 * r, 8192 * h + 2048 * r + 2048)])
            act(o, v(bank), AF.Exp, bias=-DROP if r == 3 else None, scale=v("BT", 0, 1))

    def elect(t, j, b0, b1):
        pr, c0, c1, s = "PR%d_" % (t % 3), 16 * b0, 16 * b1, 256 * (t % 3)
        cut, m0 = c0 + SPLIT[t][j], 256 * (t % 2)
        if cut < c1:
            tt(v(pr, 16 * cut, 16 * c1), ind(v("AW", 0, DUMP), v("ML", m0 + cut, m0 + c1)), v("KG", 16 * cut, 16 * c1), A.mult)
        for c in range(c0, cut, WCH):
            ce = min(cut, c + WCH)
            act(v("AS", 16 * c, 16 * ce), ind(v("AW", 0, DUMP), v("ML", m0 + c, m0 + ce)))
            scan(v(pr, 16 * c, 16 * ce), v("AS", 16 * c, 16 * ce), v("KG", 16 * c, 16 * ce), 0.0, A.max, A.mult)
        tot, cum = v(ABANKS[t][j], 256, 256 + c1 - c0), v(ABANKS[t][j], 0, c1 - c0)
        mm([(cum, v("WC", 120 - 8 * k, 248 - 8 * k), v(pr, 16 * c0 + k, 16 * c1, 16), k == 0, k == 15) for k in range(16)])
        (cp if WSV[t][j] == "v" else act)(v("WS", c0, c1), cum)
        mm([(tot, v("WB", p=p16), v("QF", s + c0, s + c1, p=p16), True, False), (tot, v("WB"), v("WS", c0, c1), False, True), (cum, v("W0"), v("WS", c0, c1), True, True)])
        tt(v("THR", c0, c1), tot, v("UR", 256 * t + c0, 256 * t + c1), A.mult)
        tt(v("HIT", c0, c1), cum, v("THR", c0, c1), A.is_gt)

    def elected(t, bank, hs, c0, c1):
        one = v(bank, 384, 384 + c1 - c0)
        mm([(one, v("FH", 0, 128), v("HIT", c0, c1), True, True)])
        for h in hs:
            tt(v("PD", 256 * h + c0, 256 * h + c1), one, v(("MT", "SS", "CT")[h], 256 * (t % 2) + c0, 256 * (t % 2) + c1), A.mult)

    def raise_(t, bank, parts, h, byscan):
        s, lo, hi = 256 * (t % 3), min(x[0] for x in parts), max(x[1] for x in parts)
        n, q0 = hi - lo, 256 * h
        if byscan:
            mm([(v(bank, 0, 16 * n), ident, v("DG", 0, 16 * n), True, False), (v(bank, 0, 16 * n), v("GM"), v("PD", q0 + 16 * lo, q0 + 16 * hi), False, True)])
            xs, x1 = v("XL", q0 + 16 * lo + 15, q0 + 16 * hi, 16), lambda b: v("XL", q0 + 16 * b + 15, q0 + 16 * b + 16)
        else:
            xs, x1 = v(bank, 0, n), lambda b: v(bank, b - lo, b - lo + 1)
            mm([(xs, win("F0", a), v("PD", q0 + 16 * lo + a, q0 + 16 * hi, 16), a == 0, a == 15) for a in range(16)])
        seg = SEGW * (16 * h + lo)
        for j, (b0, b1) in enumerate(parts):
            y0, m = 128 + 160 * j, b1 - b0
            mm([(v(bank, y0, y0 + 8 * m * (m + 1)), ident, v("TRI", 0, 8 * m * (m + 1)), True, False)] +
               [(v(bank, y0 + 8 * i * (i + 1), y0 + 8 * (i + 1) * (i + 2)), v("GM"), v("PD", q0 + 16 * b0, q0 + 16 * (b0 + i + 1)), False, i == m - 1) for i in range(m)])
        if byscan:
            scan(v("XL", q0 + 16 * lo, q0 + 16 * hi), v("RS", 0, 16 * n), v(bank, 0, 16 * n), 0.0, A.min, A.max)
        if LBA[t][h] == "a":
            lin(spots("EE", seg + SEGW - 1, seg + SEGW * n, SEGW), xs, -1.0 / 4096, col(24 + h))
        else:
            ts(spots("EE", seg + SEGW - 1, seg + SEGW * n, SEGW), xs, -1.0 / 4096, A.mult, col(24 + h), A.add)
        old = exact("L1C", 16 * h + lo, 16 * h + hi)
        if not h:
            ts(old, xs, 0.0, A.max, float(HOLE - PAD), A.add)
        for j, (b0, b1) in enumerate(parts):
            for i in range(b1 - b0):
                e, y = SEGW * (16 * h + b0 + i + 1) - 1, 128 + 160 * j + 8 * i * (i + 1)
                ts(exact("EE", e - 16 * (i + 1), e), v(bank, y, y + 16 * (i + 1)), x1(b0 + i), A.not_equal, -0.5, A.add)
        scan(exact("OF", seg + SEGW - 18, seg + SEGW * n), exact("EE", seg + SEGW - 18, seg + SEGW * n), v("RST", SEGW - 18, SEGW * n), 0.0, A.min, A.max)
        ts(exact("L1", 16 * h + lo, 16 * h + hi), spots("OF", seg + SEGW - 1, seg + SEGW * n, SEGW), -4096.0, A.mult, col(22 + h), A.add)
        if h:
            (cp if NVK == "v" else act)(v("NV", q0 + 16 * lo, q0 + 16 * hi), ind(v("AW", KB, RWN), exact("L1", 16 + lo, 16 + hi)))
        else:
            tt(v("NV", 16 * lo, 16 * hi), ind(v("AW", PAD, DUMP), old), v("CAP", s + 16 * lo, s + 16 * hi), A.min)
        for b0, b1 in parts:
            tt(ind(v("SW", KB, RWN) if h else v("SW", 0, KB), exact("L1", 16 * h + b0, 16 * h + b1)), v("NV", q0 + 16 * b0, q0 + 16 * b1), v("OH", s + 16 * b0, s + 16 * b1), A.add)

    def raise_k(t, bank, lo, hi):
        s, c0, c1 = 256 * (t % 3), 16 * lo, 16 * hi
        mm([(v(bank, 0, c1 - c0), ident, v("DG", 0, c1 - c0), True, False), (v(bank, 0, c1 - c0), v("GM"), v("PD", 256 + c0, 256 + c1), False, True)])
        scan(v("XK", c0, c1), v("RS", 0, c1 - c0), v(bank, 0, c1 - c0), 0.0, A.min, A.max)
        xs = v("XK", c0 + 15, c1, 16)
        mm([(v(bank, dl, c1 - c0, 16), v("SH", 128 * dl, 128 * dl + 128), xs, True, True) for dl in range(16)])
        lin(v("LK", c0, c1, 16), xs, -1.0, col(25))
        act(v("EK", c0, c1), v(bank, 0, c1 - c0), AF.Square, scale=128.0)
        scan(v("OK", c0, c1), v("EK", c0, c1), v("LK", c0, c1), 0.0, A.min, A.max)
        ts(v("L2", 2 * lo, 2 * hi, 2), v("OK", c0 + 15, c1, 16), -1.0, A.mult, col(23), A.add)
        ts(v("L1", 16 + lo, 16 + hi), xs, float(E), A.add)
        act(v("NV", 256 + c0, 256 + c1), ind(v("AW", KB, RWN), v("L1", 16 + lo, 16 + hi)))
        for b in range(hi - 1, lo - 1, -1):
            tt(ind(v("SW", KB, RWN), v("L2", 2 * b, 2 * b + 1)), v("NV", 256 + 16 * b, 272 + 16 * b), v("OH", s + 16 * b, s + 16 * b + 16), A.add)

    def lam(t):
        rg = "RG%d" % (t % 2)
        for h in (1, 0):
            c0, c1, bank = 128 * h, 128 * h + 128, SBK[h % 2]
            for c in range(16 * c0, 16 * c1, PIECE):
                scan(v("SC", c, c + PIECE), v("PR%d_" % (t % 3), c, c + PIECE), dict(v(rg, c, c + PIECE), reg=[(rg, 8192 * h, 8192 * h + 8192)]), 0.0, A.add, A.mult)
            for k in (3, 7, 11, 15):
                mm([(v(bank, c0, c1), pos32, v("SC", 16 * c0 + k, 16 * c1, 16), k == 3, k == 15)])
            act(v("LAM", c0, c1), v(bank, c0, c1), scale=-float(np.exp(DROP)))
            ops[dma("s", [(T.yl[:, 256 * t + c0:256 * t + c1], v("LAM", c0, c1))])]["due"] = DUE[t]

    def candidates(t):
        own, (b1, b2) = v("TW", 256 * t, 256 * t + 256), CBANKS
        par = v(b1, 256, 272)
        mm([(par, win("F0", a), v("PD", 512 + a, 768, 16), a == 0, False) for a in range(16)])
        mm([(par, win("F15", a), v("HIT", a, 256, 16), False, a == 15) for a in range(16)])
        tt(v("SM", 0, 16), par, v("PB", 32 + 16 * t, 48 + 16 * t), A.min)
        ts(v("IX1"), v("SM", 0, 16), 4096.0, A.add)
        ts(v("IX2"), par, 4096.0, A.add, 2943.0, A.min)
        for c in range(4):
            mm([(v(b2, 0, 256), win("FN", b), v("PR%d_" % t, 256 * b, 256 * b + 256), b == 0, b == 15) for b in range(4 * c, 4 * c + 4)])
        scan(v("MN"), v("BSEG"), v(b2, 0, 256), 0.0, A.add, A.min)

    def replace(t):
        own, b1 = v("TW", 256 * t, 256 * t + 256), RBANK or CBANKS[0]
        act(v("NX1"), ind(v("TW"), v("IX1")))
        mm([(v(b1, 256, 512), v("K89"), own, True, False), (v(b1, 256, 512), v("P56"), v("NX1"), False, True)])
        act(own, v(b1, 256, 512))
        act(v("NX2"), ind(v("TW"), v("IX2")))
        up_ = v(b1, 256, 272)
        mm([(up_, win("FL", b), v("NX2", 16 * b, 16 * b + 16), b == 0, b == 15) for b in range(16)])
        ts(v("MI", 0, 16), v("MN", 15, 256, 16), 16.0, A.mult, 15.0, A.add)
        ts(v("MI", 16, 32), v("MI", 0, 16), 15, A.bitwise_and)
        tt(v("SM", 32, 48), v("MI", 16, 32), v("PB", 0, 16), A.add)
        ts(v("SM", 48, 64), up_, 4000.0, A.is_gt, 8192.0, A.mult)
        tt(v("SM", 64, 80), v("SM", 32, 48), v("SM", 48, 64), A.add)
        tt(v("SM", 80, 96), v("SM", 64, 80), v("PB", 16, 32), A.min)
        cp(v("PL"), v("SM", 80, 96))
        ts(v("NC"), up_, 2943.0, A.min)
        act(v("NX"), ind(v("TW"), v("NC")))
        cp(ind(v("XX%d" % t), v("PL")), v("NX"))

    lin(col(21, p24), col(0, p24), 16.0, -256.0)
    ts(v("GK", p=p24), v("J16", p=p24), col(21, p24), A.is_equal)
    for h, bank in enumerate(("PW", "PX")):
        mm([(v(bank, 0, 384), v("GK", p=p24), v("QF", 384 * h, 384 * h + 384, p=p24), True, True)])
        ts(v("OH", 384 * h, 384 * h + 384), v(bank, 0, 384), col(1), A.is_equal)
    ts(v("CAP", 0, 256), v("OH", 0, 256), -1.0, A.mult, 15.0, A.add)
    ts(v("CAP", 256, 768), v("OH", 256, 768), -1.0, A.mult, 15.0, A.add)
    for i in range(4):
        ts(exact("TRI", 8 * i * (i + 3), 8 * i * (i + 3) + 16), v("JF", 0, 16), col(1), A.is_ge, 8192.0, A.mult)
    x = act(v("SEG"), v("KI"), AF.Exp, scale=-100.0)
    ops[x]["cost"] += 1300.0
    ts(v("DG"), v("KI", 0, 128), col(1), A.not_equal, -8192.0, A.mult)
    lin(v("RS"), v("SEG", 0, 128), -32768.0, 16384.0)
    fill(v("RST"), -1.0)
    for i in range(4):
        fill(spots("RST", SEGW * (i + 1) - 18 - 16 * i, 8 * SEGW, 4 * SEGW), 0.5)
        fill(spots("RST", SEGW * (i + 1) - 1, 8 * SEGW, 4 * SEGW), (i - 2048.0) / 4096)
    dma("s", [(v("EE", 8 * SEGW * c, 8 * SEGW * (c + 1)), v("RST")) for c in range(4)], after=sent, lat=3500.0)
    lin(col(22), col(1), 4.0, float(DUMP + 3 - 2048))
    lin(col(23), col(1), 1.0, float(E + 16)) if KOLD else lin(col(23), col(1), 4.0, 19.0)
    lin(col(24), col(1), 4.0 / 4096, (DUMP + 3 - HOLE - 2048) / 4096.0)
    lin(col(25), col(1), 1.0, 16.0) if KOLD else lin(col(25), col(1), 4.0 / 4096, (19 - 2048) / 4096.0)
    if KOLD:
        iota(v("LK"), [[0, 256]], 0, 0, True, first)
        fill(v("SH", 0, 128), 0.0)
    extra[0] = 0.0
    for d0, d1 in ((1, 4), (4, 8), (8, 12), (12, 16)) if KOLD else ():
        o, m = v("SH", 128 * d0, 128 * d1), d1 - d0
        sel(o, v("AG", 0, 128 * m), [[-1, m], [0, 8], [1, 16]], A.is_ge, 0.0, -d0, 0, sent)
        sel(o, o, [[1, m], [-1, 128]], A.is_equal, 0.0, d0, 1)
        sel(o, o, [[0, m], [-1, 128]], A.not_equal, -1.0, 0, 1)
    extra[0] = SETUP[0]
    ts(v("CT"), v("CAL", 0, 512), -1024.0, A.add)
    act(v("BT", 0, 1), v("BE", 0, 1), scale=-1.0)
    act(col(37), col(1), scale=256.0)
    lin(v("PB", 0, 16), v("JF", 0, 16), 16.0, col(37))
    lin(col(38), col(1), 1.0, 4096.0)
    lin(v("PB", 16, 32), v("JF", 0, 16), 16.0, col(38))
    for t in range(2):
        lin(v("PB", 32 + 16 * t, 48 + 16 * t), v("PB", 16, 32), 1.0, 2944.0 + 256 * t - 8192.0)
    lin(v("BSEG"), v("SEG"), 4096.0625, -0.0625)
    extra[0] = PICKS0
    for c in (0, 448):
        (cp if WHO[c // 448] == "v" else act)(v("YY", NG + c, NG + c + 448), ind(v("TW", 0, E), v("SNL", c // 16, c // 16 + 28)))
    extra[0] = 0.0
    for c, (who, qs) in enumerate(FIRST):
        for q_ in qs:
            for h, eng in enumerate(who):
                n_ = 64 // len(who)
                c0 = 64 * q_ + n_ * h
                (cp if eng == "v" else act)(v("XX0", 16 * c0, 16 * (c0 + n_)), ind(v("TW", 0, 2944), v("CAL", c0, c0 + n_)))
        prep(0, qs, *B0[c])
        k_gather(0, qs)

    def chains():
        mm([(v("PT", 0, 112), win("FM", a), v("YY", a, 1792, 16), a == 0, a == 15) for a in range(16)])
        act(v("YU"), v("PT", 0, 112))
        mm([(v("PT", 0, 112), roll32, v("YU"), True, True)])
        ts(v("YT", 0, 56), v("PT", 0, 56), float(NG), A.is_lt)
        ts(v("YT", 56, 112), v("PT", 0, 56), float(NG), A.add)
        ts(v("LST"), v("PT", 56, 112), float(NG), A.add)
        tt(v("YT", 112, 168), v("YT", 0, 56), v("YT", 56, 112), A.mult)
        tt(v("YT", 0, 56), v("YT", 112, 168), v("PT", 56, 112), A.max)
        cp(v("PRV"), v("YT", 0, 56))

    for t in range(R):
        tag[0], phase[0] = 1, t + PH["prep"][t]
        if t < 2:
            w = 256 // len(LATER[t])
            for c in range(256 - w, -1, -w):
                (cp if LATER[t][c // w] == "v" else act)(v("XX%d" % (t + 1), 16 * c, 16 * (c + w)), ind(v("TW", 0, 2944), v("CAL", 256 * t + 256 + c, 256 * t + 256 + c + w)))
        extra[0] = SOON[t]
        if 0 < t < R - 1:
            prep(t + 1, bk="PT" if PB1 else "PK")
        extra[0] = SOON[t + 2] if t < 3 else 0.0
        phase[0] = t + PH["replace"]
        if t == 1:
            dma("s", [(v("TW", 0, E, p=slice(row_, 128, 16)), v("S3", c, c + 128)) for row_, c in ((8, 256), (9, 640))])
            dma("s", [(v("TW", 2944, 3456, p=slice(row_, 128, 16)), v("TW", 0, 512, p=slice(row_ + 3, 128, 16))) for row_ in (5, 6)])
        if t in (1, 2) and not RBANK:
            replace(t - 1)
        extra[0] = 0.0
        if t == 3:
            mm([(v("PT", 0, 128), win("FM", a), v("TW", a, E, 16), a == 0, a == 15) for a in range(16)])
            act(v("W1"), v("PT", 0, 128))
            mm([(v("PT", 0, 128), roll32, v("W1"), True, True)])
            ts(v("W2"), v("PT", 0, 128), float(NG), A.is_lt, float(NG), A.mult)
            tt(v("W3"), v("W2"), v("PT", 0, 128), A.add)
            cp(v("MAPL"), v("W3"))
        for j, parts in enumerate(PARTS[t]):
            tag[0], extra[0], b0, b1, phase[0] = 0, EARLY[j], parts[-1][0], parts[0][1], float(t)
            elect(t, j, b0, b1)
            elected(t, ABANKS[t][j], (0,), 16 * b0, 16 * b1)
            raise_(t, ABANKS[t][j], parts, 0, XLV[j])
        tag[0], extra[0] = 1, 0.0
        if t == 0:
            chains()
            prep(1)
        tag[0], extra[0], phase[0] = 1, KBOOST, t + PH["raise"]
        for bank, b in zip(KBANKS, (8, 0)) if t < R - 1 else ():
            elected(t, bank, (1, 2) if t < 2 else (1,), 16 * b, 16 * b + 128)
            if KOLD:
                raise_k(t, bank, b, b + 8)
            else:
                raise_(t, bank, [(b + 4, b + 8), (b, b + 4)], 1, XLK)
        if t in (1, 2) and RBANK:
            extra[0] = SOON[t + 2]
            replace(t - 1)
        if t == 1 and RBANK:
            candidates(t)
        tag[0], extra[0], phase[0] = 0, 0.0, t + PH["chain"]
        buf = "BUF" if t % 2 == 0 else "BUG"
        sent, came = exchange("SW", GHO, buf, NG, -1, calls=X1)
        through(buf, 0, [(ident, "GN", 0), (roll, "SW", GUN)], both=BOTH[t], plus=241.0)
        if t < R - 1:
            dma("s", [(v("AW", OWN, OWN + E), v("SW", OWN, OWN + E))], after=sent[:SHADOW], lat=3000.0)
        for d in range(7):
            c = NG + GH * d
            tt(v(buf, c, c + GH), ind(v(buf, 0, c), v("PRV", 8 * d, 8 * d + 8)), v(buf, c, c + GH), A.add)
        if t < R - 1:
            for (c0, c1), eng in zip(PICK, PICKS[t]):
                o, src = v("GN", c0, c1), ind(v(buf, 0, 2 * NG), v("LST", c0 // 16, c1 // 16)) if c0 < NG - GH else v(buf, NG + c0, NG + c1)
                ts(o, src, -241.0, A.add) if eng == "v" else lin(o, src, 1.0, -241.0)
            sent, came = exchange("GN", 0, "AW", GHO, 1, calls=X2)
            through("AW", GUN, [(unroll, "GN", 0)])
            tag[0] = 1
            iota(v("SW", GUN, PAD), [[0, 2 * NG]], 0, 0, True, sent[-1:])
            if t < R - 2:
                dma("s", [(v("AW", KB, KH), v("SW", KB, KH))], after=came, lat=3000.0)
            phase[0] = t + PH["gather"]
            k_gather(t + 1)
            phase[0] = t + PH["parents"]
            if t < (1 if RBANK else 2):
                candidates(t)
            tag[0], phase[0] = 2, t + PH["decay"][t]
            decay(t)
        else:
            phase[0] = t + PH["decay"][t]
            decay(t)
            phase[0] = t + PH["chain"]
            for c in range(4):
                bank = v(BANKS[c % 2], 0, 512)
                mm([(bank, roll, v("SW", OWN + 512 * c, OWN + 512 * c + 512), True, True)])
                lin(v("BUF", OWN + 512 * c, OWN + 512 * c + 512), bank, 1.0, 241.0)
            for c0, c1, eng in FINAL:
                o, src = v("RG1", c0, c1), ind(v("BUF"), v("MAPL", c0 // 16, c1 // 16))
                ts(o, src, -241.0, A.add) if eng == "v" else lin(o, src, 1.0, -241.0)
                dma("s" if eng == "v" else "a", [(T.ya[0:112, c0:c1], v("RG1", c0, c1, p=up)), (T.ya[112:128, c0:c1], v("RG1", c0, c1, p=down))])
        tag[0], phase[0] = 2, t + PH["lam"][t]
        lam(t)

    n = len(ops)
    succ = [[] for _ in range(n)]
    for i, o in enumerate(ops):
        if o["kind"] == "r":
            o["deps"] = set(o["gaps"])
        for d in o["deps"]:
            succ[d].append(i)

    def gap(d, i):
        if ops[i]["kind"] == "r":
            return ops[i]["gaps"][d]
        if ops[i]["q"] == ops[d]["q"] == "t" or d in ops[i]["behind"]:
            return 0.0
        return ops[d]["lat"] + SYNC

    if n not in ORDER:
        pred, rng = [sorted(o["deps"]) for o in ops], np.random.default_rng(SEED)
        anc, fp = [0] * n, []
        for i in range(n):
            m_ = 0
            for d in pred[i]:
                m_ |= anc[d]
            fp.append([(d, gap(d, i)) for d in pred[i] if ops[d]["lat"] > 150.0 or ops[i]["kind"] == "r" or not (m_ >> d) & 1])
            for d in pred[i]:
                m_ |= 1 << d
            anc[i] = m_
        lat, views = [o["lat"] for o in ops], []
        for per, put, sync, slow, fix, pe in VIEWS:
            cost = [(o["cost"] + o.get("picked", 0.0) * (per - GATHER) + o.get("put", 0.0) * (put - SCATTER) + (fix if o["q"] == "v" else 0.0)) * (slow if o["kind"] == "c" else 1.0)
                    * (pe if o["q"] == "t" else 1.0) for o in ops]
            into = [[(d, cost[d] + (w - SYNC + sync if w and ops[i]["kind"] != "r" else w)) for d, w in fp[i]] for i in range(n)]
            out = [[] for _ in range(n)]
            for i in range(n):
                for d, w in into[i]:
                    out[d].append((i, w))
            views.append((cost, into, out))
        before, after_ = [-1] * n, [-1] * n

        def fit(key, cost, out, npred, head):
            left, est, start, busy = list(npred), list(head), [0.0] * n, {q: ([], []) for q in Q}
            place = [0] * n
            for x, i in enumerate(sorted(range(n), key=lambda j: key[j])):
                place[i] = x
            ready = sorted((-place[i], i) for i in range(n) if not left[i])
            while ready:
                i = ready.pop()[1]
                t0, c, q = est[i], cost[i], ops[i]["q"]
                if q is not None:
                    begins, stops = busy[q]
                    lo, hi = 0, len(stops)
                    while lo < hi:
                        mid_ = (lo + hi) // 2
                        if stops[mid_] <= t0:
                            lo = mid_ + 1
                        else:
                            hi = mid_
                    while lo < len(stops) and begins[lo] < t0 + c:
                        t0 = max(t0, stops[lo])
                        lo += 1
                    begins.insert(lo, t0)
                    stops.insert(lo, t0 + c)
                start[i] = t0
                fresh = False
                for j, w in out[i]:
                    if t0 + w > est[j]:
                        est[j] = t0 + w
                    left[j] -= 1
                    if not left[j]:
                        ready.append((-place[j], j))
                        fresh = True
                if fresh:
                    ready.sort()
            return start

        def link(x, first_=-1, last_=-1):
            for a_, b_ in zip([first_] + x, x + [last_]):
                if a_ >= 0:
                    after_[a_] = b_
                if b_ >= 0:
                    before[b_] = a_

        def sort(part, inside, fs):
            left = {i: npre[i] + (before[i] in inside) for i in part}
            todo = [i for i in part if not left[i]]
            for i in todo:
                for j, w in fs[i]:
                    if j in inside:
                        left[j] -= 1
                        if not left[j]:
                            todo.append(j)
                j = after_[i]
                if j in inside:
                    left[j] -= 1
                    if not left[j]:
                        todo.append(j)
            return todo

        def times(todo, view, r, tail):
            cost, fp, fs = view
            for i in todo:
                d = before[i]
                x = r[d] + cost[d] if d >= 0 else 0.0
                for d, w in fp[i]:
                    if r[d] + w > x:
                        x = r[d] + w
                r[i] = x
            span = 0.0
            for i in reversed(todo):
                j = after_[i]
                x = cost[i] + (tail[j] if j >= 0 and tail[j] > lat[i] else lat[i])
                for j, w in fs[i]:
                    if w + tail[j] > x:
                        x = w + tail[j]
                tail[i] = x
                if r[i] + x > span:
                    span = r[i] + x
            return span

        def guess(new, first_, last_, r, tail, cost, fp, fs):
            t0, head = (r[first_] + cost[first_] if first_ >= 0 else 0.0), []
            for i in new:
                for d, w in fp[i]:
                    if r[d] + w > t0:
                        t0 = r[d] + w
                head.append(t0)
                t0 += cost[i]
            t1, worst = (tail[last_] if last_ >= 0 else 0.0), 0.0
            for i, h in zip(reversed(new), reversed(head)):
                t1 = max(t1 + cost[i], cost[i] + lat[i])
                for j, w in fs[i]:
                    if w + tail[j] > t1:
                        t1 = w + tail[j]
                worst = max(worst, h + t1)
            return worst

        heads, tails = [[0.0] * n for x in views], [[0.0] * n for x in views]
        best, nin, nout = None, [len(x) for x in fp], [len(x) for x in views[0][2]]
        urge, due, boost = [o.get("urge", 0.0) for o in ops], [o.get("due", 0.0) for o in ops], [o["rank"] for o in ops]
        for i in range(n - 1, -1, -1):
            boost[i] = max([boost[i]] + [boost[j] for j, w in views[0][2][i] if boost[j] > SETUP[0] > 0])
        for start_ in range(STARTS):
            cost, into, out = views[BUILD[start_ % len(BUILD)]]
            fore = [[(j, w + urge[i]) for j, w in out[i]] for i in range(n)]
            back = [[(d, w - cost[d] + cost[i] + urge[d]) for d, w in into[i]] for i in range(n)]
            level = [0.0] * n
            for i in range(n - 1, -1, -1):
                level[i] = max([w + level[j] for j, w in fore[i]] + [cost[i] + lat[i] + due[i]])
            key, mine = [-x for x in level], None
            if PHASED:
                turn = [o["phase"] for o in ops]
                for i in range(n - 1, -1, -1):
                    turn[i] = min([turn[i]] + [turn[j] for j, w in out[i]])
                key = [1e7 * turn[i] - level[i] for i in range(n)]
            for it in range(PASSES):
                noise = rng.random(n) * (NOISE if start_ >= len(BUILD) or it else 0.0)
                fw = fit([key[i] - boost[i] + float(noise[i]) for i in range(n)], cost, fore, nin, [0.0] * n)
                order_ = sorted(range(n), key=lambda i: (fw[i], i))
                for q in Q:
                    link([i for i in order_ if ops[i]["q"] == q])
                total = sum(times(order_, x, r, tail) * w for x, r, tail, w in zip(views, heads, tails, WEIGHT))
                if mine is None or total < mine[0]:
                    mine = (total, order_, fw)
                base = fw if total <= mine[0] + SLIP else mine[2]
                bw = fit([-(base[i] + cost[i]) - boost[i] for i in range(n)], cost, back, nout, [(lat[i] if not out[i] else 0.0) + due[i] for i in range(n)])
                key = [-(bw[i] + cost[i]) for i in range(n)]
            if best is None or mine[0] < best[0]:
                best = mine + (BUILD[start_ % len(BUILD)],)
        cost, into, out = views[best[3]]
        key, now_ = list(best[2]), best[0]
        for it in range(STEPS):
            for q in Q:
                link([i for i in best[1] if ops[i]["q"] == q])
            j = it % len(views)
            span = times(best[1], views[j], heads[j], tails[j])
            on = [i for i in range(n) if heads[j][i] + tails[j][i] > span - NEAR]
            mid = best[2][on[int(rng.integers(len(on)))]]
            wide, push = float(rng.random()) * WIDE, float(rng.random()) * PUSH
            key = list(best[2])
            for i in on:
                if abs(best[2][i] - mid) < wide:
                    key[i] -= push
            fw = fit(key, cost, out, nin, [0.0] * n)
            order_ = sorted(range(n), key=lambda i: (fw[i], i))
            for q in Q:
                link([i for i in order_ if ops[i]["q"] == q])
            total = sum(times(order_, x, r, tail) * w for x, r, tail, w in zip(views, heads, tails, WEIGHT))
            if total <= best[0]:
                best = (total, order_, fw, best[3])
        for q in Q:
            link([i for i in best[1] if ops[i]["q"] == q])
        every, order_ = set(range(n)), best[1]
        for sweep in range(SWEEPS):
            size = STRETCH[sweep % len(STRETCH)]
            for p0 in range(-(sweep % 2) * size // 4, n - size // 2, size // 2):
                npre = [len(x) for x in fp]
                order_ = sort(order_, every, views[0][2])
                for x, r, tail in zip(views, heads, tails):
                    times(order_, x, r, tail)
                order_.sort(key=lambda i: heads[0][i] + heads[-1][i])
                part = order_[max(p0, 0):p0 + size]
                inside = set(part)
                npre = {i: sum(d in inside for d, w in fp[i]) for i in part}
                lines = {q: [i for i in part if ops[i]["q"] == q] for q in Q}
                ends = {q: (before[x[0]], after_[x[-1]]) for q, x in lines.items() if x}
                tabu, best_, now_, undo = {}, None, None, None
                for it in range(MOVES):
                    todo = sort(part, inside, views[0][2])
                    total = sum(times(todo, x, r, tail) * w for x, r, tail, w in zip(views, heads, tails, WEIGHT)) if len(todo) == len(part) else 1e18
                    if now_ is not None and total > now_ + SLACK:
                        lines[undo[0]] = undo[1]
                        link(undo[1], *ends[undo[0]])
                        todo = sort(part, inside, views[0][2])
                        total = sum(times(todo, x, r, tail) * w for x, r, tail, w in zip(views, heads, tails, WEIGHT))
                    now_ = total
                    if best_ is None or total < best_[0] - 1.0:
                        best_ = (total, {q: x[:] for q, x in lines.items()})
                    (cost, fp_, fs), r, tail = views[it % len(views)], heads[it % len(views)], tails[it % len(views)]
                    span = max(r[i] + tail[i] for i in part)
                    on, moves = set(i for i in part if r[i] + tail[i] > span - 0.01), []
                    for u in sorted(on):
                        w_ = after_[u]
                        if w_ not in on or r[w_] > r[u] + cost[u] + 0.01:
                            continue
                        run_, x = [u], before[u]
                        for k_ in range(FAR):
                            f = run_[0]
                            if any(d == f or r[d] + cost[d] > r[f] + cost[f] for d, w in fp_[w_]):
                                break
                            if tabu.get((w_, f), -1) < it and (k_ < REACH or x < 0 or r[f] - r[x] - cost[x] > 0.6 * cost[w_]):
                                moves.append((guess([w_] + run_, before[f], after_[w_], r, tail, cost, fp_, fs), w_, f, 0, run_[:]))
                            if x not in inside:
                                break
                            run_.insert(0, x)
                            x = before[x]
                        run_, x = [w_], after_[w_]
                        for k_ in range(FAR):
                            f = run_[-1]
                            if any(j == f or tail[j] > tail[f] for j, w in fs[u]):
                                break
                            if tabu.get((f, u), -1) < it and (k_ < REACH or x < 0 or r[x] - r[f] - cost[f] > 0.6 * cost[u]):
                                moves.append((guess(run_ + [u], before[u], after_[f], r, tail, cost, fp_, fs), u, f, 1, run_[:]))
                            if x not in inside:
                                break
                            run_.append(x)
                            x = after_[x]
                    if not moves:
                        tabu, now_ = {}, None
                        continue
                    e_, x, f, side, run_ = min(moves, key=lambda m_: m_[0] + float(rng.random()) * JITTER)
                    q = ops[x]["q"]
                    undo = (q, lines[q][:])
                    lines[q].remove(x)
                    lines[q].insert(lines[q].index(f) + side, x)
                    link(lines[q], *ends[q])
                    tabu[(x, f) if side == 0 else (f, x)] = it + TENURE
                    for y in run_:
                        tabu[(y, x) if side == 0 else (x, y)] = it + TENURE
                for q, x in best_[1].items():
                    if x:
                        link(x, *ends[q])
        npre = [len(x) for x in fp]
        order_ = sort(order_, every, views[0][2])
        ORDER[n] = ([times(order_, x, r, tail) for x, r, tail in zip(views, heads, tails)], order_)
    order = ORDER[n][1]
    place = {i: x for x, i in enumerate(order)}

    ESEM = {"v": "ev", "a": "ea", "t": "et", "g": "eg"}
    count = {x: 0 for x in SEMAPHORES}
    known, waited = {q: {} for q in Q}, {}
    token, seen = {}, {}

    def wait(q, sem, val, also=()):
        if known[q].get(sem, 0) < val:
            Q[q].wait_ge(T.sem[sem], val)
            known[q][sem] = val
            if q == "g":
                waited[sem] = val
        for s_ in also:
            known[q][s_] = max(known[q].get(s_, 0), also[s_])

    for i in order:
        o = ops[i]
        q = o["q"]
        if o["kind"] == "r":
            count[o["sem"]] += o["n"]
            token[i] = (o["sem"], count[o["sem"]])
            continue
        need = {}
        for d in o["deps"]:
            if q == ops[d]["q"] == "t" or d in o["behind"]:
                continue
            sem, val = token[d]
            if val > need.get(sem, (0, 0))[0]:
                need[sem] = (val, d)
        for sem in sorted(need, key=lambda s_: -place[need[s_][1]]):
            wait(q, sem, need[sem][0], seen.get(need[sem][1], ()) if COVER else ())
        seen[i] = dict(known[q])
        if o["kind"] == "x":
            o["calls"][0]()
            sem, k = o["sem"], o["n"]
        elif o["kind"] == "d":
            sem, k = o["sem"], 16 * len(o["calls"])
            for c in o["calls"]:
                c().then_inc(T.sem[sem], 16)
        else:
            sem, k = ESEM[q], 1
            for c in o["calls"][:-1]:
                c()
            o["calls"][-1]().then_inc(T.sem[sem], 1)
        count[sem] += k
        token[i] = (sem, count[sem])
    last = {token[i][0]: x for x, i in enumerate(order)}
    for sem in sorted(last, key=lambda s_: last[s_]):
        if waited.get(sem, 0) < count[sem]:
            g.wait_ge(T.sem[sem], count[sem])
